import numpy as np, ml_dtypes
CORES = [35,38,43,46]
N = 4
BF = ml_dtypes.bfloat16
def gentries(a):
    return np.ascontiguousarray(a.reshape(8, 16, -1).transpose(0, 2, 1)).reshape(8, -1)
def gtable(e):
    e = np.asarray(e); return np.ascontiguousarray(e.reshape(8, -1, 16).transpose(0, 2, 1)).reshape(128, -1).astype(np.int32)
W, Q, L, C, S, ST, RO, TH = 4096, 16, 256, 64, 256, 2, 4, 9
K = Q * C
GM = (W - L) // (C - 1)
def val(rng, shape, even):
    if even: return rng.integers(0, 256, shape)
    return np.minimum(np.exp2(8.01 * rng.random(shape)).astype(np.int64) - 1, 255)
def items(rng, B, z, share, even):
    v = np.ascontiguousarray(B[np.arange(8)[None, :, None], z].transpose(0, 2 - 1, 3, 2))
    return np.where(rng.random(v.shape, dtype=np.float32) < share, val(rng, v.shape, even), v)
def parts(rng, even):
    per = rng.integers(7, 41, 8); V = rng.integers(0, 4, (8, 40)); ph = rng.integers(0, 40, (N, 8)); e = rng.integers(0, 40, (N, 8, Q)); G8 = np.arange(8)[None, :, None]
    B = np.repeat(val(rng, (8, 1, 16), even), 4, axis=1); B = np.where(rng.random(B.shape) < (0.6 if even else 0.75), val(rng, B.shape, even), B)
    z = V[G8, (np.arange(W) + ph[..., None]) % per[None, :, None]]
    z = np.where(rng.random(z.shape) < rng.choice(np.array([0.01, 0.02, 0.04, 0.06]), (N, 8, 1)), rng.integers(0, 4, z.shape), z)
    u = V[G8[..., None], (np.arange(L) + e[..., None]) % per[None, :, None, None]]
    u = np.where(rng.random(u.shape) < 0.015, rng.integers(0, 4, u.shape), u).reshape(N, 8, Q * L)
    T = items(rng, B, z, 0.08, even); P = items(rng, B, u, 0.08, even)
    eb = e[(np.arange(N)[:, None] + np.arange(RO)[None, :]) % N].transpose(0, 2, 1, 3)
    h = (ph[:, :, None, None] - eb).astype(np.int32)[..., None] + np.arange(W - L + 1, dtype=np.int32)
    hit = h % per.astype(np.int32)[None, :, None, None, None] == 0
    sc = rng.random(hit.shape, dtype=np.float32); f = rng.choice(np.array([0.02, 0.05, 0.15, 0.4], np.float32), (N, 8, 1, 1, 1))
    st = np.sort(np.argpartition(np.where(hit, sc * f, sc), C, axis=-1)[..., :C], axis=-1)
    x = rng.random((N, 8, Q, L)); y = rng.random((N, 8, 16, Q))
    if not even: x = x ** rng.choice(np.array([0.2, 1.0, 5.0]), (N, 8, Q, 1)); y = y ** rng.choice(np.array([0.3, 1.0, 4.0]), (N, 8, 1, Q))
    d = np.arange(L); wt = np.minimum(d + (x * (L - d)).astype(np.int64), L - 1)
    wt = np.where(rng.random(wt.shape) < 0.4, 0, wt)
    return T, P, wt, np.minimum((L * y).astype(np.int64), L - 1), np.ascontiguousarray(st).astype(np.int64)
def pack(T, P, wt, O, st):
    return {"txt": np.ascontiguousarray(T.reshape(N, 128, W)).astype(np.float32).astype(BF), "pat": np.ascontiguousarray(P.reshape(N, 128, Q * L)).astype(np.float32).astype(BF),
            "wit": np.ascontiguousarray(wt.reshape(N, 8, Q * L)).astype(np.int32), "prb": np.ascontiguousarray(O.reshape(N, 128, Q)).astype(np.int32),
            "cd": np.stack([gtable(a.reshape(8, RO * K)) for a in st])}
def runs(rng, n):
    gap = np.ones(C, np.int64); gap[0] = 0
    gap[1 + rng.permutation(C - 1)[:n - 1]] = 2 + rng.integers(0, GM - 1, n - 1)
    a = np.add.accumulate(gap); return a + int(rng.integers(0, W - L - int(a[-1]) + 1))
def still(rng, T, P, wt, O, g):
    X = rng.integers(0, 256, (1, 16, 1)); T[:, g] = X; P[:, g] = X; P[:, g, :, L - 1::L] = 255 - X
    wt[:, g] = 0; wt[:, g, :, 1] = L - 1; O[:, g] = rng.integers(0, L - 2, (N, 16, Q)); return X
def shares(rng, n):
    if rng.random() < 0.5:
        c = np.full(Q, n // Q); c[rng.permutation(Q)[:n - Q * (n // Q)]] += 1; return c
    c = np.ones(Q, np.int64); left = n - Q
    for p in rng.permutation(Q):
        k = min(C - 1, left); c[p] += k; left -= k
    return c
def setup_inputs(rng):
    return pack(*parts(rng, True))
def setup_inputs_spread(rng):
    return pack(*parts(rng, False))
def setup_inputs_ends(rng):
    cut = np.array([0, TH - 1, TH, 16]); row = np.arange(16)[:, None]
    def rec(n):
        v = 255 * (row < cut[rng.choice(4, (N, 8, 1, n), p=np.array([0.45, 0.3, 0.1, 0.15]))])
        return np.where(rng.random((N, 8, 1, n)) < 0.06, 255 * rng.integers(0, 2, (N, 8, 16, n)), v)
    T = rec(W); P = rec(Q * L); wt = (L - 1) * rng.integers(0, 2, (N, 8, Q, L)); O = (L - 1) * rng.integers(0, 2, (N, 8, 16, Q))
    O = np.where(rng.random(O.shape) < 0.1, rng.choice(np.array([1, L - 2]), O.shape), O)
    st = np.zeros((N, 8, RO, Q, C), np.int64); lo = np.arange(C); hi = W - L - lo[::-1]; last = np.concatenate([lo[:C - 2], np.array([W - 2 * L + 1, W - L])])
    for q in range(N):
        for g in range(8):
            for t in range(RO):
                for p in range(Q):
                    k = int(rng.integers(0, 4)); h = int(rng.integers(1, C))
                    if g == 7 or k == 2: st[q, g, t, p] = last
                    elif k == 0: st[q, g, t, p] = np.concatenate([lo[:h], hi[h:]])
                    elif k == 1: st[q, g, t, p] = np.concatenate([np.array([0, L - 1]), hi[2:]])
                    else: st[q, g, t, p] = np.concatenate([2 * lo[:h], W - L - 2 * lo[:C - h][::-1]])
    T[:, 7, :, :C + L] = 0; T[:, 7, :, W - 2 * L + 1] = 0; T[:, 7, :, W - L] = 255; T[:, 7, :, W - 1] = 255
    P[:, 7, :, 0::L] = 0; P[:, 7, :, L - 2::L] = 0; P[:, 7, :, L - 1::L] = 255
    wt[:, 7, :, 1] = L - 1; wt[:, 7, :, L - 1] = 0
    O[:, 7] = (L - 1) * rng.integers(0, 2, (N, 16, Q)); O[:, 7, 5] = 0; O[:, 7, 6] = L - 1
    return pack(T, P, wt, O, st)
def setup_inputs_corners(rng):
    T, P, wt, O, st = parts(rng, True); goal = (S, S + 1, S - 1, K, Q)
    for g in range(6):
        X = still(rng, T, P, wt, O, g)[0, :, 0]
        for q in range(N):
            for p in range(Q):
                if (g < 5 and rng.random() < 0.3) or (g == 5 and q % 2 == 0):
                    P[q, g, :, p * L + int(O[q, g, int(rng.choice(np.array([0, 7, 15]))), p])] = 255 - X
            for t in range(RO):
                c = shares(rng, S if g == 5 else goal[(g + q + t) % 5])
                for p in range(Q): st[q, g, t, p] = runs(rng, int(c[p]))
    X = still(rng, T, P, wt, O, 6); P[::2, 6, :, L - 2::L] = 255 - X; H = W // 2
    for q in range(N):
        for t in range(RO):
            for p in range(Q):
                s0 = int(rng.integers(0, H - L - C + 2)) if (q + t) % 2 == 0 else int(rng.integers(H, W - L - C + 2))
                st[q, 6, t, p] = s0 + np.arange(C)
    k = rng.integers(0, 3, (N, Q, L)); wt[:, 7] = np.where(k == 0, 0, np.where(k == 1, np.arange(L), L - 1))
    v = rng.choice(np.array([0, L - 1, L // 2, 3]), (2, N, 1, Q)); O[:, 7] = np.where(rng.random((N, 16, Q)) < 0.5, v[0], v[1])
    for q in range(N):
        for t in range(0, RO, 2):
            s0 = int(rng.integers(0, W - L - K + 2)); st[q, 7, t] = s0 + np.arange(K).reshape(Q, C)
    wt[0, 7, 0, 1] = L - 1; wt[0, 7, 1, 1] = 0; wt[0, 7, 2, 1] = L - 1; O[0, 7, :, 1] = 3 * rng.integers(0, 2, 16)
    tx, pt = T[0, 7], P[0, 7]; a, b = int(st[0, 7, 0, 1, 0]), int(st[0, 7, 0, 1, C - 1])
    for s in (a, b):
        for o in (0, 3): tx[:, s + o] = pt[:, L + o]
    pt[:, 2 * L - 2] = 255 - tx[:, a + L - 2]; pt[:, 2 * L - 1] = 255 - tx[:, b + L - 1]
    return pack(T, P, wt, O, st)
def setup_inputs_crowd(rng):
    T, P, wt, O, st = parts(rng, True)
    for g in range(8):
        if g % 2 == 0:
            still(rng, T, P, wt, O, g); o = int(rng.integers(0, L - 2)); O[:, g, 0] = o
            for q in range(N):
                if g % 4 == 2: O[q, g, 0, int(rng.integers(0, Q))] = (o + 1) % (L - 2)
                for t in range(RO): st[q, g, t] = runs(rng, S // Q)[None, :]
        else:
            D = int(rng.integers(8, min(28, GM) + 1)); z = int(rng.integers(0, D))
            X = rng.integers(0, 256, 16); Y = X.copy(); i = rng.permutation(16)[:TH]; Y[i] = 255 - Y[i]; XY = np.stack([X, Y], axis=1)
            h = rng.integers(0, 2, D); v = np.concatenate([h, h]); v[z] = 0; v[z + D] = 1
            P[:, g] = XY[:, v[np.arange(Q * L) % L % (2 * D)]]; wt[:, g] = 0
            o = rng.integers(0, L - 1, (N, 16, Q)); o = o + (o % D == z); o[:, 15] = z + D * rng.integers(0, 2, (N, Q)); O[:, g] = o
            for q in range(N):
                s0 = int(rng.integers(0, W - L - (C - 1) * D + 1)); st[q, g] = s0 + D * np.arange(C)
                u = v[(np.arange(W) - s0) % (2 * D)]
                if g % 4 == 3: u = np.where(rng.random(W) < 0.01, 1 - u, u)
                T[q, g] = XY[:, u]
    return pack(T, P, wt, O, st)
def check_inputs(d):
    bad = []
    for k, lo, hi in (("txt", 0, 255), ("pat", 0, 255), ("wit", 0, L - 1), ("prb", 0, L - 1), ("cd", 0, W - L)):
        v = np.asarray(d[k]).astype(np.float64)
        if not (np.min(v) >= lo and np.max(v) <= hi): bad.append("range of " + k)
        if np.any(v != np.floor(v)): bad.append("whole numbers of " + k)
    w = np.asarray(d["wit"]).astype(np.int64).reshape(N, 8, Q, L)
    if np.any((w != 0) & (w < np.arange(L))): bad.append("a witness of wit is 0 or at least its distance")
    s = np.stack([gentries(a) for a in d["cd"]]).astype(np.int64).reshape(N, 8, RO, Q, C)
    if np.any(s[..., 1:] <= s[..., :-1]): bad.append("rising starts of cd")
    return bad
def unlike(x, y):
    return np.add.reduce((x != y).astype(np.int64), axis=0) >= TH
def reference(txt, pat, wit, prb, cd):
    T = txt.astype(np.float32).astype(np.int64).reshape(N, 8, 16, W); P = pat.astype(np.float32).astype(np.int64).reshape(N, 8, 16, Q * L)
    wt = wit.astype(np.int64).reshape(N, 8, Q * L); O = prb.astype(np.int64).reshape(N, 8, 16, Q)
    st = np.stack([gentries(a) for a in cd]).astype(np.int64).reshape(N, 8, RO, K); pl = np.arange(K) // C
    for t in range(RO):
        for r in range(N):
            b = (r + t) % N
            for g in range(8):
                tx, pt, wv, ov, a = T[r, g], P[b, g], wt[b, g], O[b, g], st[r, g, t]
                live = np.arange(K)
                for stage in range(ST):
                    i, j = live[:-1], live[1:]; d = a[j] - a[i]
                    ok = (pl[i] == pl[j]) & (d < L); i, j, d = i[ok], j[ok], d[ok]
                    w = wv[pl[i] * L + d]; ok = w > 0; i, j, d, w = i[ok], j[ok], d[ok], w[ok]
                    y = tx[:, a[i] + w]; dead = np.zeros(K, bool)
                    dead[i[unlike(pt[:, pl[i] * L + w], y)]] = True
                    dead[j[unlike(pt[:, pl[j] * L + w - d], y)]] = True
                    live = live[~dead[live]]
                s = live[:S]
                if len(s) == 0: continue
                p = pl[s]; o = ov[:, p]
                bad = unlike(tx[:, a[s] + o], pt[:, p * L + o])
                fail = np.any(bad, axis=0); m = np.argmax(bad, axis=0); of = o[m, np.arange(len(s))]
                x = np.unique((a[s] + o[0])[~fail]); tx[:, x] = 255 - tx[:, x]
                d = a[s][1:] - a[s][:-1]; c = (p[1:] == p[:-1]) & fail[1:] & ~fail[:-1] & (of[1:] + d < L)
                place, first = np.unique((p[1:] * L + d)[c], return_index=True); wv[place] = (of[1:] + d)[c][first]
                who, first = np.unique(p[fail], return_index=True); mf = m[fail][first]
                for q, k in zip(who, mf): ov[:, q] = np.concatenate([ov[k:k + 1, q], ov[:k, q], ov[k + 1:, q]])
    return {"yt": T.reshape(N, 128, W).astype(np.float32).astype(BF), "yw": wt.astype(np.float32), "yo": O.reshape(N, 128, Q).astype(np.float32)}

@@ -1,0 +1,623 @@
+from concourse.bass import IndirectOffsetOnAxis
+from concourse.mybir import AluOpType as ALU, ActivationFunctionType as AF
+
+N = 4
+BIG = 8192.0
+WW = 4240
+TW = 4368
+STEP_DMA = True
+ROUND = 1.5 * 2.0 ** 23
+SHARE = 24
+PIECES = ("V", "mats", "THo")
+
+F, B, I, U = "float32", "bfloat16", "int32", "uint16"
+MATS = "BO LT Id A1 nBO nI B256 B8k nB8k I8k B4k Wm S0 ShI dOT XO".split()
+SCRATCH = {}
+for _n, _c, _d in (
+    ("TX", TW, B), ("P0", 4096, B), ("P1", 4096, B), ("P2", 4096, B), ("P3", 4096, B),
+    ("W0", WW, B), ("W1", WW, B), ("CT", 272, B), ("cdi", 256, I), ("witi", 256, I), ("prbi", 16, I),
+    ("ip", 8, I), ("iw", 8, I), ("col", 32, F), ("ia", 32, I), ("ib", 16, I), ("oa", 32, U), ("ob", 16, U), ("orr", 8, U),
+    ("G1", 512, F), ("G2", 512, F), ("A", 264, F), ("Ah", 256, B), ("Al", 256, B), ("KX", 256, F), ("EX", 256, B), ("MX", 256, B), ("DL", 264, F), ("QB", 256, F),
+    ("oW1", 256, U), ("ix", 256, B), ("iq16", 128, B), ("iqm", 256, B), ("Z", 144, B), ("M", 128 * len(MATS), B), ("Mf", 384, F),
+    ("Sel", 2048, B), ("KR", 256, B), ("half", 256, B), ("MW", 1024, B), ("MD", 256, B), ("MH", 256, B), ("MC", 256, B), ("tm", 64, F),
+    ("tb", 256, B), ("dW", 8, F), ("dX", 16, F), ("KD", 64, F), ("z0", 16, B), ("xz", 16, B),
+    ("GW", 1024, B), ("WS", 1024, B), ("oP", 64, U), ("TQ", 128, F), ("oTQ", 128, U), ("PG", 4096, B),
+    ("NN", 4096, B), ("N2", 1024, B), ("th", 128, F), ("lv", 128, F), ("dead", 64, F),
+    ("GS", 72, F), ("HS", 72, F), ("d2", 32, F), ("oW2", 32, U), ("ai", 32, F), ("qb", 32, F), ("x1", 64, F),
+    ("THo", 72, F), ("THe", 72, F), ("K", 128, F), ("dead2", 64, F), ("cum", 64, B), ("ones", 64, F), ("dK", 64, F), ("u0", 64, F),
+    ("oR", 64, U), ("step", 272, B), ("inv", 256, B), ("ngt", 8, F), ("same", 256, B), ("oPP", 256, U), ("oTT", 256, U),
+    ("V", 1024, F), ("CW", 6144, F), ("dO", 16, B),
+    ("sg", 272, B), ("sn", 256, B), ("f1", 256, B), ("f0", 256, B), ("t1", 256, B), ("t2", 256, B),
+    ("DM", 256, F), ("KS", 256, F), ("E", 256, B), ("YS", 256, B), ("y1", 16, F), ("y2", 16, F), ("oX", 16, U), ("oX2", 32, U),
+    ("FV", 256, B), ("sv", 512, B), ("CS", 264, F), ("e1", 8, F), ("oE", 8, U), ("R", 16, I), ("R2", 16, I), ("sl", 16, F), ("to", 16, B),
+    ("le", 16, F), ("uo", 16, F), ("su", 64, U), ("lu", 64, U), ("lw", 512, B), ("so", 64, B), ("O", 160, B),
+):
+    SCRATCH[_n] = ("sbuf", [128, _c], _d)
+SCRATCH["TL"] = ("dram", [4, 128, 256], B)
+SCRATCH["TS"] = ("dram", [4, 128, 256], B)
+SCRATCH["TDa"] = ("dram", [8, 4096], B)
+SCRATCH["TDb"] = ("dram", [8, 4096], B)
+for _t in range(8):
+    SCRATCH["B%d" % _t] = ("psum", [128, 512], F)
+
+NDMA = 60
+SEMAPHORES = (["qv", "qa", "qt", "qg", "loc"] + ["d%d" % k for k in range(NDMA)]
+              + ["r%s%d" % (k, t) for k in "uvotp" for t in range(4)])
+
+
+def _emit(g, T, ops):
+    lastw, readers, banks, deps = {}, {}, {}, []
+    for j, (q, kind, fn, rd, wr) in enumerate(ops):
+        d = set()
+        for k in rd + wr:
+            if k[0] == "#":
+                acc = banks.setdefault(k, {})
+                d.update(i for qq, i in acc.items() if qq != q)
+                acc[q] = j
+        for k in rd:
+            if k[0] != "#" and k in lastw:
+                d.add(lastw[k])
+        for k in wr:
+            if k[0] == "#":
+                continue
+            d.update(readers.get(k, []))
+            i = lastw.get(k)
+            if i is not None and not (k in PIECES and ops[i][0] == q):
+                d.add(i)
+        for k in rd:
+            if k[0] != "#":
+                readers.setdefault(k, []).append(j)
+        for k in wr:
+            if k[0] != "#":
+                lastw[k] = j
+                readers[k] = []
+        d.discard(j)
+        deps.append(sorted(i for i in d if ops[i][1] != "s" and not (q == "t" and ops[i][0] == "t")))
+    need = set()
+    for j, d in enumerate(deps):
+        last = {}
+        for i in d:
+            if ops[i][1] == "c":
+                last[ops[i][0]] = i
+        deps[j] = [i for i in d if ops[i][1] != "c"] + list(last.values())
+        need.update(last.values())
+    Q = {"v": g.vector, "a": g.scalar, "t": g.tensor, "g": g, "y": g.sync}
+    cnt = {"v": 0, "a": 0, "t": 0, "g": 0}
+    tok, seen, ndma, loc = {}, {q: {} for q in Q}, 0, 0
+    for j, (q, kind, fn, rd, wr) in enumerate(ops):
+        if kind == "r":
+            tok[j] = fn
+            continue
+        for i in deps[j]:
+            s, n = tok[i]
+            if seen[q].get(s, 0) < n:
+                Q[q].wait_ge(T.sem[s], n)
+                seen[q][s] = n
+        if kind == "s":
+            loc += fn()
+            continue
+        ins = fn()
+        if kind == "d":
+            tok[j] = ("d%d" % ndma, 16)
+            ndma += 1
+            ins.then_inc(T.sem[tok[j][0]], 16)
+        elif j in need:
+            cnt[q] += 1
+            tok[j] = ("q" + q, cnt[q])
+            ins.then_inc(T.sem["q" + q], 1)
+    end = {}
+    for s, n in tok.values():
+        end[s] = max(end.get(s, 0), n)
+    end["loc"] = loc
+    for s, n in end.items():
+        if max(seen[q].get(s, 0) for q in Q) < n:
+            g.wait_ge(T.sem[s], n)
+
+
+def rank_program(g, core, T, topo):
+    rank = T.rank_of(core)
+    if rank is None:
+        return
+    ops = []
+    v, a, pe = g.vector, g.scalar, g.tensor
+
+    def op(q, fn, r="", w="", kind="c"):
+        ops.append([q, kind, fn, r.split(), w.split()])
+
+    def ts(out, in0, s1, o0, s2=None, o1=None, r="", w=""):
+        if o1 is None:
+            op("v", lambda: v.tensor_scalar(out, in0, s1, None, o0), r, w)
+        else:
+            op("v", lambda: v.tensor_scalar(out, in0, s1, s2, o0, o1), r, w)
+
+    def tt(out, in0, in1, o, r="", w=""):
+        op("v", lambda: v.tensor_tensor(out, in0, in1, o), r, w)
+
+    def cp(out, in_, r="", w=""):
+        op("v", lambda: v.tensor_copy(out, in_), r, w)
+
+    def ms(ap, c, w):
+        op("v", lambda: v.memset(ap, c), "", w)
+
+    def scan(out, d0, d1, init, o0, o1, r="", w=""):
+        op("v", lambda: v.tensor_tensor_scan(out, d0, d1, init, o0, o1), r, w)
+
+    def act(out, in_, fn=AF.Identity, bias=0.0, scale=1.0, r="", w=""):
+        if bias is None:
+            op("a", lambda: a.activation(out, in_, fn), r, w)
+        else:
+            op("a", lambda: a.activation(out, in_, fn, bias=bias, scale=scale), r, w)
+
+    def mm1(out, l, x, st, sp, r, w):
+        op("t", lambda: pe.matmul(out, l, x, st, sp), r, w)
+
+    def mm(out, terms, r, w):
+        for k, (l, x) in enumerate(terms):
+            mm1(out, l, x, k == 0, k == len(terms) - 1, r, w)
+
+    def dma(q, out, in_, r="", w=""):
+        e = {"g": g, "y": g.sync, "a": g.scalar}[q]
+        op(q, lambda: e.dma_start(out, in_), r, w, "d")
+
+    def iota(out, pat, base, cm, w, flt=False):
+        if flt:
+            op("g", lambda: g.iota(out, pat, base, cm, allow_small_or_imprecise_dtypes=True), "", w)
+        else:
+            op("g", lambda: g.iota(out, pat, base, cm), "", w)
+
+    def lanes(src, dst, bulk):
+        e = topo.engines(src, dst)
+        return e[:len(e) // 2] if bulk else e[len(e) // 2:]
+
+    def send(k, out, in_, sem, bulk, r):
+        dst = T.cores[(rank - k) % N]
+        e = lanes(core, dst, bulk)
+        rid, pid, _ = topo.addr(dst)
+
+        def fn():
+            g.remote_dma(out, in_, T.sem[sem], T.sem.loc, pid, rid, sum(1 << x for x in e))
+            return len(e)
+        op("g", fn, r, "", "s")
+
+    def recv(k, sem, bulk, w):
+        src = T.cores[(rank + k) % N]
+        ops.append(["r", "r", (sem, len(lanes(src, core, bulk))), [], w.split()])
+
+    col = T.col
+    cR, cG, cG15, c4R, cM32, c256, c256b, cR1, cIs0, cN0, cB1, cB0, cP, c75, cSn, c64, cSg, cRn, cRf = (col[:, k:k + 1] for k in range(19))
+    BO, LT, Id, A1, nBO, nI, B256, B8k, nB8k, I8k, B4k, Wm, S0, ShI, dOT, XO = (T.M[:, 128 * k:128 * k + 128] for k in range(len(MATS)))
+    Idf, nIdf, S0f = (T.Mf[:, 128 * k:128 * k + 128] for k in range(3))
+    P = [T.P0, T.P1, T.P2, T.P3]
+    W = [T.W0, T.W1]
+    Bk = [T["B%d" % t] for t in range(8)]
+    TD = [T.TDa, T.TDb]
+    add, sub, mul, mx, mn = ALU.add, ALU.subtract, ALU.mult, ALU.max, ALU.min
+    eq, ge, gt, lt, le, ne = ALU.is_equal, ALU.is_ge, ALU.is_gt, ALU.is_lt, ALU.is_le, ALU.not_equal
+
+    def O(t, lo=0, hi=16):
+        return T.O[:, 32 * t + 16 + lo:32 * t + 16 + hi]
+
+    dma("y", T.cdi[:], T.cd[:], w="cdi")
+    dma("a", T.witi[:], T.wit[:], w="witi")
+    dma("a", T.P0[:], T.pat[:], w="P0")
+    dma("y", T.TX[:, 0:4096], T.txt[:], w="TX")
+    dma("y", T.prbi[:], T.prb[:], w="prbi")
+    iota(T.ip[:, 0:1], [[0, 1]], 0, 1, "ip0")
+    iota(T.ia[:], [[64, 4], [1, 4], [0, 2]], 0, 0, "ia")
+    iota(T.ib[:], [[32, 16]], 0, 0, "ib")
+    iota(T.iqm[:], [[0, 16], [1, 16]], 0, 0, "iqm", True)
+    iota(T.ix[:], [[1, 256]], 0, 0, "ix", True)
+    iota(T.iq16[:], [[16, 8], [0, 16]], 0, 0, "iq16", True)
+    ms(T.CT[:, 256:272], 0.0, "CTp")
+    ts(T.ip[:, 1:2], T.ip[:, 0:1], 15, ALU.bitwise_and, r="ip0", w="ip1")
+    ts(T.ip[:, 2:3], T.ip[:, 0:1], 31, ALU.bitwise_and, r="ip0", w="ip2")
+    cp(cP, T.ip[:, 0:1], "ip0", "cP")
+    ts(c4R, T.ip[:, 1:2], 4.0, mul, r="ip1", w="c4R")
+    cp(cM32, T.ip[:, 2:3], "ip2", "cM32")
+    cp(cR, T.ip[:, 1:2], "ip1", "cR")
+    ts(T.oa[:], T.ia[:], c4R, add, r="ia c4R", w="oa")
+    ts(T.ob[:], T.ib[:], cM32, add, r="ib cM32", w="ob")
+    tt(cG, cP, cR, sub, "cP cR", "cG")
+    ts(c256, cR, 256.0, mul, r="cR", w="c256")
+    ts(c256b, cR, 256.0, mul, 256.0, add, r="cR", w="c256b")
+    ts(T.tm[:, 0:16], T.iqm[:, 0:16], cR, lt, -512.0, mul, r="iqm cR", w="tm0")
+    ts(T.tm[:, 16:32], T.iqm[:, 0:16], cR, eq, 256.0, mul, r="iqm cR", w="tm1")
+    ts(T.tm[:, 32:48], T.iqm[:, 0:16], 15.0, eq, -512.0, mul, r="iqm", w="tm2")
+    tt(T.tm[:, 48:64], T.tm[:, 0:16], T.tm[:, 16:32], add, "tm0 tm1", "tm3")
+    ms(T.CT[:, 0:1], 0.0, "CT0")
+    tt(T.MW[:, 0:16], T.tm[:, 48:64], T.tm[:, 32:48], add, "tm3 tm2", "MW")
+    n = 16
+    while n < 1024:
+        act(T.MW[:, n:2 * n], T.MW[:, 0:n], r="MW", w="MW")
+        n *= 2
+    act(T.Sel[:, 0:1024], T.MW[:], scale=0.0, bias=1.0, r="MW", w="Sel")
+    act(T.Sel[:, 1024:2048], T.MW[:], scale=0.0, bias=1.0, r="MW", w="Sel")
+    ms(T.A[:, 256:264], 0.0, "Ap")
+    ts(cG15, cG, 15.0, add, r="cG", w="cG15")
+    cp(T.G1[:], T.cdi[:, 0:256].indirect(T.oa[:, 0:32]), "cdi oa", "G1")
+    cp(T.CT[:, 1:256], T.witi[:, 1:256], "witi", "CT")
+    op("v", lambda: v.transpose(T.G2[:], T.G1[:]), "G1", "G2")
+    ts(BO, T.iq16[:], cG, eq, r="iq16 cG", w="BO")
+    cp(T.A[:, 0:256], T.G2[:, 0:512].indirect(T.ob[:, 0:16]), "G2 ob", "A")
+    ts(Id, T.ix[:, 0:128], cP, eq, r="ix cP", w="Id")
+    tt(T.DL[:, 1:256], T.A[:, 1:256], T.A[:, 0:255], sub, "A", "DL")
+    ts(T.Z[:], T.ix[:, 0:144], cG15, eq, r="ix cG15", w="Z")
+    op("v", lambda: v.memset(T.DL[:, 64:257:64], BIG), "DL", "DL")
+    ts(cR1, cR, 1.0, add, r="cR", w="cR1")
+    ts(T.oW1[:, 0:64], T.DL[:, 1:65], 256.0, mn, r="DL", w="oW1a")
+    act(T.GW[:, 512:1024], T.CT[:, 0:272].indirect(T.oW1[:, 32:64]), r="CT CT0 CTp oW1a", w="GWb")
+    act(T.QB[:], T.DL[:, 1:257], scale=-1.0, bias=c256, r="DL c256", w="QB")
+    act(T.G2[:, 256:512], T.A[:, 0:256], bias=64.0, r="A", w="G2")
+    act(T.Ah[:], T.G2[:, 256:512], r="G2", w="Ah")
+    ts(cIs0, cR, 0.0, eq, r="cR", w="cIs0")
+    cp(T.GW[:, 0:512], T.CT[:, 0:272].indirect(T.oW1[:, 0:32]), "CT CT0 CTp oW1a", "GWa")
+
+    def fill(ap, n, c, w):
+        iota(ap, [[0, n]], c, 0, w, True)
+
+    def keep(out, in_, cmp, other, base, r, w):
+        op("g", lambda: g.affine_select(out, in_, [[1, 128]], cmp, other, base, -1), r, w)
+
+    fill(T.GS[:, 64:72], 8, int(BIG), "GSp")
+    fill(T.HS[:, 64:72], 8, 0, "HSp")
+    fill(T.THo[:], 72, 0, "THo")
+    fill(T.THe[:], 72, 0, "THe THa")
+    fill(T.N2[:, 512:528], 16, 0, "N2p")
+    fill(T.ones[:], 64, 1, "ones")
+    fill(T.step[:, 0:16], 16, 0, "stepp")
+    fill(T.sg[:, 0:16], 16, 1, "sgp")
+    fill(T.W1[:, 4096:WW], WW - 4096, 0, "W1p")
+    fill(T.W0[:, 4096:WW], WW - 4096, 0, "W0p")
+    send(1, T.TL[0], T.CT[:, 0:256], "rt0", False, "CT CT0")
+    keep(LT, BO, gt, 0.0, 0, "BO", "LT")
+    keep(ShI, BO, eq, 0.0, -1, "BO", "ShI")
+    send(1, T.P1[:], T.P0[:], "rp1", True, "P0")
+
+    def consts(part):
+        if part == 0:
+            op("g", lambda: g.affine_select(T.Sel[:], T.Sel[:], [[-1, 16], [-16, 8], [0, 16]], eq, 0.0, 0, 1), "Sel", "Sel")
+            ms(cRn, -ROUND, "cRn")
+            ms(cRf, ROUND - 64, "cRn")
+            keep(ShI, ShI, ne, -1.0, 0, "ShI", "ShI")
+            fill(T.TX[:, 4096:TW], TW - 4096, 0, "TXp")
+            fill(T.CS[:], 264, 0, "CS")
+            ts(cN0, cR, 0.0, gt, 256.0, mul, r="cR", w="cN0")
+            for dst, src, s in ((B256, BO, cN0), (nBO, BO, -1.0), (B8k, BO, BIG), (nB8k, BO, -BIG), (I8k, Id, BIG), (S0, BO, cIs0), (nI, Id, -1.0),
+                                (Idf, Id, 1.0), (nIdf, Id, -1.0), (Wm, BO, cR1), (S0f, BO, cIs0)):
+                act(dst, src, scale=s, r="BO Id cN0 cR1 cIs0", w="mats")
+        elif part == 1:
+            tt(T.Al[:], T.G2[:, 256:512], T.Ah[:], sub, "G2 Ah", "Al")
+            ms(T.O[:, 15:160:32], 0.0, "Op")
+            cp(O(0), T.prbi[:], "prbi", "O0")
+            ts(T.iw[:, 0:1], T.ip[:, 0:1], 4, ALU.arith_shift_right, r="ip0", w="iw")
+            ts(T.orr[:], T.ix[:, 0:8], 0.0, mul, cR, add, r="ix cR", w="orr")
+            starts(0)
+        elif part == 2:
+            ts(c64, cR, 64.0, mul, 1024.0, add, r="cR", w="c64")
+            ms(c75, 7.5, "c75")
+            ms(T.su[:], 0, "sup")
+            ms(cSn, -255.5, "cSn")
+            ts(T.KD[:], T.ix[:, 0:64], c64, add, r="ix c64", w="KD")
+            tt(A1, Id, LT, sub, "Id LT", "A1")
+            ts(cB1, cR, -0.5, mul, -8.0, add, r="cR", w="cB1")
+            ts(cB0, cR, -0.5, mul, 0.5, add, r="cR", w="cB0")
+            act(T.half[:], T.ix[:], scale=0.0, bias=0.5, r="ix", w="mats")
+            act(T.KR[:], T.ix[:], scale=-32.0, r="ix", w="mats")
+            act(T.tb[:], T.ix[:], scale=0.0, bias=16.0, r="ix", w="mats")
+        elif part == 3:
+            ts(T.MD[:], T.iqm[:], cR, eq, r="iqm cR", w="MD")
+            ts(T.MH[:], T.iqm[:], cR, lt, r="iqm cR", w="MH")
+        elif part == 4:
+            ts(T.MC[:], T.iqm[:], cR, lt, r="iqm cR", w="MC")
+            ts(T.y1[:], T.ix[:, 0:16], 16.0, mul, cR, add, r="ix cR", w="y1")
+            ts(T.MC[:, 0:256:16], T.iqm[:, 0:256:16], cR, lt, BIG, mul, r="iqm cR", w="MC")
+            ts(T.dW[:], T.y1[:, 0:8], 4112.5, add, r="y1", w="dW")
+            ts(T.dX[:], T.y1[:], 4112.5 - BIG, add, r="y1", w="dX")
+            ts(c4R, cR, -1.0, add, r="cR", w="c4R")
+            ts(cSg, cIs0, -2 * BIG, mul, BIG, add, r="cIs0", w="cSg")
+            ts(T.MX[:], T.iqm[:], c4R, eq, -2.0, mul, r="iqm c4R", w="MX")
+            tt(T.MX[:], T.MX[:], T.MH[:], add, "MH MX", "MX")
+            ts(T.oW1[:, 64:256], T.DL[:, 65:257], 256.0, mn, c256, add, r="DL c256", w="oW1b")
+        else:
+            cp(T.e1[:, 4:5], T.witi[:, 0:1], "witi", "e14")
+            ts(T.xz[:], T.iqm[:, 0:16], cR, eq, T.e1[:, 4:5], mul, r="iqm cR e14", w="xz")
+            mm(T.B7[:, 160:176], [(BO, T.xz[:])], "BO xz", "#7")
+            act(T.z0[:], T.B7[:, 160:176], r="#7", w="z0")
+
+    def count(out, buf, lo, n, r, w):
+        mm(out, [(T.Z[:, 15 - m:143 - m], buf[:, lo + m:lo + 16 * n:16]) for m in range(16)], r + " Z", w)
+
+    def expand(t):
+        recv(1, "rt%d" % (t - 1), False, "TL%d" % (t - 1))
+        dma("y", TD[t % 2][:], T.TL[t - 1], "TL%d" % (t - 1), "TD%d" % (t % 2))
+        op("g", lambda: g.indirect_dma_start(W[t % 2][:, 0:4096], None, TD[t % 2][:], IndirectOffsetOnAxis(ap=T.iw[:, 0:1], axis=0),
+                                             bounds_check=7), "TD%d iw" % (t % 2), "W%d" % (t % 2), "d")
+
+    def rows(q, out_of, t, r, w):
+        if STEP_DMA:
+            dma(q, out_of(0, 8), W[t % 2][0:128:16, 0:4096], r, w)
+        else:
+            for k in range(8):
+                dma(q, out_of(k, k + 1), W[t % 2][16 * k:16 * k + 1, 0:4096], r, w + str(k))
+
+    def apply_u(t, between):
+        b = 16 * (t - 1)
+        recv(1, "ru%d" % (t - 1), False, "lu%d" % (t - 1))
+        recv(1, "rv%d" % (t - 1), False, "lw%d" % (t - 1))
+        for k in range(7, -1, -1):
+            cp(W[t % 2][:, 0:WW].indirect(T.lu[:, b + 2 * k:b + 2 * k + 1]), T.lw[:, 8 * b + 16 * k:8 * b + 16 * k + 16],
+               "lu%d lw%d W%d W%dp" % (t - 1, t - 1, t % 2, t % 2), "W%d" % (t % 2))
+            if between:
+                flip_b(13 - k, 14 - k)
+
+    def equals(n, key, bk, out, spare, r, w):
+        tt(T.DM[:, 0:n], key, T.MD[:, 0:n], mul, bk + " MD", "DM")
+        scan(T.KS[:, n - 1::-1], T.MH[:, n - 1::-1], T.DM[:, n - 1::-1], 0.0, mul, add, "MH DM", "KS")
+        tt(T.E[:, 0:n], key, T.KS[:, 0:n], eq, bk + " KS", "E")
+        scan(T.YS[:, n - 1::-1], T.E[:, n - 1::-1], T.MC[:, n - 1::-1], 0.0, add, mul, "E MC", "YS")
+        tt(T.y1[:, 0:n // 16], T.YS[:, 0:n:16], T.KS[:, 0:n:16], add, "YS KS", "y1")
+        tt(out, T.y1[:, 0:n // 16], spare, mn, "y1 " + r, w)
+
+    def starts(t):
+        for p in range(16):
+            s = T.Sel[:, 128 * p:128 * p + 128]
+            mm(Bk[2 + p // 8][:, 64 * (p % 8):64 * (p % 8) + 64], [(s, T.Ah[:, 64 * t:64 * t + 64]), (s, T.Al[:, 64 * t:64 * t + 64])],
+               "Sel Ah Al", "#%d" % (2 + p // 8))
+
+    def places_a(t, part):
+        if part == 0:
+            scan(T.CS[:, 1:257], T.same[:], T.B7[:, 256:512], 0.0, mul, mx, "same #7", "CS")
+            cp(T.R[:], T.CS[:, 0:264].indirect(T.oE[:, 0:1]), "CS oE", "R")
+            return
+        ts(T.R2[:], T.R[:], 31, ALU.bitwise_and, r="R", w="R2")
+        ts(T.sl[:], T.R2[:], cR1, eq, r="R2 cR1", w="sl")
+        ts(T.le[:], T.R2[:], cR, gt, r="R2 cR", w="le")
+        tt(T.to[:], T.sl[:], O(t), mul, "sl O%d" % t, "to")
+        mm(T.B7[:, 128:144], [(ShI, O(t)), (T.Z[:, 15:143], T.to[:])], "ShI Z to O%d" % t, "#7")
+
+    def places_b(t, part):
+        so = T.so[:, 16 * t:16 * t + 16]
+        if part == 0:
+            tt(T.uo[:], T.B7[:, 128:144], T.le[:], mul, "#7 le", "uo")
+            return
+        tt(so, T.uo[:], O(t), add, "uo O%d" % t, "so%d" % t)
+        send(1, O(t + 1), so, "ro%d" % t, False, "so%d" % t)
+
+    def flip_a():
+        tt(T.E[:], T.B0[:, 256:512], T.EX[:], lt, "#0 EX", "E")
+        scan(T.YS[:, 255::-1], T.MX[:, 255::-1], T.E[:, 255::-1], 0.0, mul, add, "E MX", "YS")
+        ts(T.y2[:], T.YS[:, 0:256:16], cSg, mul, r="YS cSg", w="y2")
+        tt(T.y1[:], T.y2[:], T.KX[:, 0:256:16], add, "y2 KX", "y1")
+        tt(T.y2[:], T.y1[:], T.dX[:], mn, "y1 dX", "y2")
+        ts(T.oX[:], T.y2[:], BIG - 0.5, add, r="y2", w="oX")
+        act(T.FV[:], T.TX[:, 0:TW].indirect(T.oX[:, 0:16]), scale=-1.0, bias=255.0, r="TX TXp oX", w="FV")
+        ts(T.oX2[:, 0:32:2], T.y2[:], BIG - 0.5, add, r="y2", w="oX2")
+
+    def flip_b(lo, hi):
+        for k in range(lo, hi):
+            cp(T.TX[:, 0:TW].indirect(T.oX2[:, 2 * k:2 * k + 1]), T.FV[:, 16 * k:16 * k + 16], "FV oX2", "TX TXp")
+
+    for t in range(4):
+        Pt, pk, ok = P[t], "P%d" % t, "O%d" % t
+        if t == 0:
+            win, wk, cw = T.CT[:, 0:272], "CT CT0 CTp", 0.0
+        else:
+            win, wk, cw = W[t % 2][:, 0:WW], "W%d W%dp" % (t % 2, t % 2), c256
+        s0 = 64 * t
+        TXw = T.TX[:, 0:4096]
+        scan(T.WS[:], T.GW[:], T.MW[:], 0.0, mx, add, "GWa GWb MW", "WS")
+        w1 = T.WS[:, 15:1024:16]
+        ts(T.oP[:], w1, c256b, add, r="WS c256b", w="oP")
+        tt(T.TQ[:, 0:64], w1, T.A[:, s0:s0 + 64], add, "WS A", "TQa")
+        tt(T.TQ[:, 64:128], w1, T.QB[:, s0:s0 + 64], add, "WS QB", "TQb")
+        if t > 0:
+            flip_b(14, 15)
+        ts(T.oTQ[:], T.TQ[:], 256.0, add, r="TQa TQb", w="oTQ")
+        if t > 0:
+            recv(t, "rp%d" % t, True, pk)
+        for h in range(4):
+            o = T.oP[:, 32 * h:32 * h + 32] if h < 2 else T.oTQ[:, 32 * h:32 * h + 32]
+            act(T.PG[:, 512 * h:512 * h + 512], Pt[:, 0:4096].indirect(o), r=pk + (" oP" if h < 2 else " oTQ"), w="PG%d" % h)
+        if t > 0:
+            send(1, T.TL[t], T.TS[t], "rt%d" % t, False, " ".join("TS%d%s" % (t, x) for x in [""] + list("01234567")))
+            flip_b(15, 16)
+        else:
+            consts(0)
+        for h in range(4):
+            tt(T.NN[:, 512 * h:512 * h + 512], TXw.indirect(T.oTQ[:, 32 * (h % 2):32 * (h % 2) + 32]), T.PG[:, 512 * h:512 * h + 512], eq,
+               "TX oTQ PG%d" % h, "N%d" % h)
+            if h % 2:
+                count(T.B0[:, 32 * (h - 1):32 * (h - 1) + 64], T.NN, 512 * (h - 1), 64, "N%d N%d" % (h - 1, h), "#0")
+        act(T.CW[:, 0:256], T.ix[:], scale=0.0, bias=cRf, r="ix cRn", w="CWa")
+        act(T.CW[:, 3072:3328], T.ix[:], AF.Silu if t == 0 else AF.Identity, scale=0.0, r="ix", w="CWb")
+        if t > 0:
+            places_a(t - 1, 1)
+        ts(T.th[:, 0:64], w1, -256.0, gt, 8.0, mul, r="WS", w="tha")
+        ts(T.th[:, 64:128], w1, -256.0, gt, 8.0, mul, r="WS", w="thb")
+        if t == 0:
+            consts(1)
+        tt(T.lv[:], T.B0[:, 0:128], T.th[:], lt, "#0 tha thb", "lv")
+        if t > 0:
+            places_b(t - 1, 0)
+        tt(T.dead[:], T.lv[:, 0:64], T.lv[:, 63:127], mx, "lv", "dead")
+        if t > 0:
+            places_b(t - 1, 1)
+        expand(t + 1)
+        scan(T.GS[:, 1:64], T.dead[:, 0:63], T.DL[:, s0 + 1:s0 + 64], BIG, mul, add, "dead DL", "GS")
+        scan(T.HS[:, 63::-1], T.DL[:, s0 + 64:s0:-1], T.dead[:, 63::-1], 0.0, add, mul, "dead DL", "HS")
+        act(T.x1[:], T.dead[:], scale=1000.0, r="dead", w="x1")
+        tt(T.d2[:], T.HS[:, 2:65:2], T.GS[:, 2:65:2], add, "HS GS HSp GSp", "d2")
+        ts(T.oW2[:], T.d2[:], 256.0, mn, cw, add, r="d2 c256", w="oW2")
+        act(T.GW[:, 256:512], win.indirect(T.oW2[:, 16:32]), r=wk + " oW2", w="GWb")
+        cp(T.GW[:, 0:256], win.indirect(T.oW2[:, 0:16]), wk + " oW2", "GWa")
+        tt(T.ai[:], T.A[:, s0 + 2:s0 + 65:2], T.GS[:, 2:65:2], sub, "A Ap GS GSp", "ai")
+        ts(T.qb[:], T.d2[:], -1.0, mul, c256, add, r="d2 c256", w="qb")
+        scan(T.WS[:, 0:512], T.GW[:, 0:512], T.MW[:, 0:512], 0.0, mx, add, "GWa GWb MW", "WS")
+        w2 = T.WS[:, 15:512:16]
+        ts(T.oP[:, 0:32], w2, c256b, add, r="WS c256b", w="oP")
+        tt(T.TQ[:, 0:32], w2, T.ai[:], add, "WS ai", "TQa")
+        tt(T.TQ[:, 32:64], w2, T.qb[:], add, "WS qb", "TQb")
+        ts(T.oTQ[:, 0:64], T.TQ[:, 0:64], 256.0, add, r="TQa TQb", w="oTQ")
+        act(T.PG[:, 0:512], Pt[:, 0:4096].indirect(T.oP[:, 0:32]), r=pk + " oP", w="PG0")
+        act(T.PG[:, 512:1008], Pt[:, 0:4096].indirect(T.oTQ[:, 32:63]), r=pk + " oTQ", w="PG1")
+        th = T.THe[:, 33:65]
+        ts(th, w2, -256.0, gt, 8.0, mul, r="WS", w="THe")
+        tt(T.THo[:, 0:32], th, T.x1[:, 1:64:2], add, "THe x1", "THo")
+        tt(T.th[:, 0:32], th, T.dead[:, 1:64:2], mul, "THe dead", "tha")
+        tt(T.THo[:, 33:64], T.THe[:, 33:64], T.dead[:, 2:64:2], mul, "THe dead", "THo")
+        tt(T.N2[:, 0:512], TXw.indirect(T.oTQ[:, 0:32]), T.PG[:, 0:512], eq, "TX oTQ PG0", "N2a")
+        tt(T.N2[:, 528:1024], TXw.indirect(T.oTQ[:, 0:31]), T.PG[:, 512:1008], eq, "TX oTQ PG1", "N2b")
+        count(T.B0[:, 0:64], T.N2, 0, 64, "N2a N2b N2p", "#0")
+        if t > 0:
+            recv(1, "ro%d" % (t - 1), False, ok)
+        for p in range(16):
+            act(T.V[:, p:1024:16], Bk[2 + p // 8][:, 64 * (p % 8):64 * (p % 8) + 64], bias=O(t, p, p + 1),
+                r="#%d %s" % (2 + p // 8, ok), w="V")
+        tt(T.dO[:], O(t), O(t, -1, 15), sub, ok + " Op", "dO")
+        tt(T.THe[:, 0:32], T.th[:, 0:32], T.x1[:, 0:64:2], add, "tha x1", "THa")
+        tt(XO, T.dO[:, 0:16].indirect(T.orr[:, 0:8]), BO, mul, "dO orr BO", "XO")
+        mm(T.B5[:, 0:128], [(XO, Id)], "XO Id", "#5")
+        act(dOT, T.B5[:, 0:128], r="#5", w="dOT")
+        if t == 0:
+            consts(2)
+        if t == 1:
+            consts(5)
+        tt(T.K[:, 1:128:2], T.B0[:, 0:64], T.THo[:, 0:64], lt, "#0 THo", "Ko")
+        tt(T.K[:, 0:128:2], T.B0[:, 0:64], T.THe[:, 0:64], lt, "#0 THe THa", "Ke")
+        tt(T.dead2[:], T.K[:, 0:64], T.K[:, 64:128], mx, "Ko Ke", "dead2")
+        scan(T.cum[:], T.ones[:], T.dead2[:], 0.0, add, sub, "ones dead2", "cum")
+        mm(T.B5[:, 128:129], [(LT, T.cum[:, 63:64])], "LT cum", "#5")
+        mm(T.B6[:, 130:131], [(BO, T.cum[:, 63:64])], "BO cum", "#6")
+        base = T.B5[:, 128:129]
+        tt(T.dK[:], T.dead2[:], T.KD[:], mul, "dead2 KD", "dK")
+        tt(T.u0[:], T.dK[:], T.cum[:], mx, "dK cum", "u0")
+        st, stp = T.step[:, 16:272], T.step[:, 15:271]
+        ts(st, T.ix[:], base, ge, r="ix #5", w="step")
+        ts(T.oR[:], T.u0[:], base, add, -1.0, add, r="u0 #5", w="oR")
+        act(T.ngt[:, 0:1], T.B6[:, 130:131], bias=1.0, scale=-1.0, r="#6", w="ngt")
+        act(T.inv[:], T.ix[:], AF.Relu, bias=T.ngt[:, 0:1], r="ix ngt", w="inv")
+        mm(T.B4[:, 256:512], [(dOT, st), (B256, st)], "dOT step mats", "#4")
+        k = 64 - SHARE
+        act(T.CW[:, 3072:6144].indirect(T.oR[:, k:64]), T.V[:, 16 * k:1024], AF.Silu, bias=None, r="oR V", w="CWb")
+        ts(T.CW[:, 0:3072].indirect(T.oR[:, 0:16]), T.V[:, 0:256], 1.0, mul, ROUND - 64, add, r="oR V", w="CWa")
+        cp(T.oPP[:], T.B4[:, 256:512], "#4", "oPP")
+        ts(T.CW[:, 0:3072].indirect(T.oR[:, 16:k]), T.V[:, 256:16 * k], 1.0, mul, ROUND - 64, add, r="oR V", w="CWa")
+
+        def items(h):
+            act(T.PG[:, 512 * h:512 * h + 512], Pt[:, 0:4096].indirect(T.oPP[:, 32 * h:32 * h + 32]), r=pk + " oPP", w="PG%d" % h)
+
+        items(0)
+        items(1)
+        tt(T.G2[:, 0:256], T.CW[:, 0:256], T.CW[:, 3072:3328], add, "CWa CWb", "G2")
+        vv = T.B5[:, 256:512]
+        for k, (l, x) in enumerate(((dOT, st), (B8k, st), (nB8k, stp), (I8k, T.inv[:]))):
+            mm1(vv, l, x, k == 0, False, "dOT step stepp inv mats", "#5")
+        mm(T.B4[:, 0:256], [(dOT, st)], "dOT step", "#4")
+        mm1(T.B3[:, 0:256], S0, T.half[:], True, False, "mats", "#3")
+        mm1(T.B6[:, 0:128], B256, T.step[:, 16:272:2], True, False, "step mats", "#6")
+        mm1(T.B6[:, 0:128], S0, T.half[:, 0:128], False, False, "mats", "#6")
+        ts(T.oTT[:], T.G2[:, 0:256], -ROUND, add, r="G2", w="oTT")
+        act(T.G1[:, 8:264], T.G2[:, 0:256], bias=cRn, r="G2 cRn", w="G1")
+        mm1(vv, Idf, T.G1[:, 8:264], False, False, "G1 mats", "#5")
+        mm1(vv, nIdf, T.G1[:, 7:263], False, True, "G1 mats", "#5")
+        items(2)
+        items(3)
+
+        def score(lo, hi, x):
+            mm(T.B2[:, lo:hi], [(A1, T.sg[:, 16 + lo:16 + hi]), (nBO, T.sg[:, 15 + lo:15 + hi]), (nI, T.sn[:, lo:hi])],
+               "A1 mats sn sgp " + " ".join("sg%d" % k for k in range(hi // 64)), "#2")
+            act(T.f1[:, lo:hi], T.B2[:, lo:hi], AF.Relu, bias=cB1, scale=0.5, r="#2 cB1", w="f1" + x)
+
+        def named(lo, hi, x):
+            fk = "f1" + x
+            tt(T.t1[:, lo:hi], T.B5[:, 256 + lo:256 + hi], T.f1[:, lo:hi], mul, "#5 " + fk, "t1" + x)
+            tt(T.t2[:, lo:hi], T.B4[:, lo:hi], T.f1[:, lo:hi], mul, "#4 " + fk, "t2" + x)
+
+        def slots(lo, hi, x):
+            for k, (l, y) in enumerate(((BO, T.t1[:, lo:hi:2]), (BO, T.t1[:, lo + 1:hi:2]), (nBO, T.t2[:, lo:hi:2]), (nBO, T.t2[:, lo + 1:hi:2]))):
+                mm1(T.B6[:, lo // 2:hi // 2], l, y, False, hi == 256 and k == 3, "mats BO t1%s%s" % (x, " t2" + x if k > 1 else ""), "#6")
+
+        def place0(lo, hi):
+            mm1(T.B3[:, lo:hi], S0f, T.G1[:, 8 + lo:8 + hi], False, hi == 256, "G1 mats", "#3")
+
+        for h in range(4):
+            nk = "N%d N%d" % (2 * h, 2 * h + 1)
+            for j in (2 * h, 2 * h + 1):
+                tt(T.NN[:, 512 * j:512 * j + 512], TXw.indirect(T.oTT[:, 32 * j:32 * j + 32]), T.PG[:, 512 * j:512 * j + 512], eq,
+                   "TX oTT PG%d" % j, "N%d" % j)
+            count(Bk[h % 2][:, 0:64], T.NN, 1024 * h, 64, nk, "#%d" % (h % 2))
+            if h < 2:
+                items(2 * h + 4)
+                items(2 * h + 5)
+            if h == 1:
+                act(T.sn[:], vv, AF.Sign, bias=cSn, r="#5 cSn", w="sn")
+            act(T.sg[:, 16 + 64 * h:80 + 64 * h], Bk[h % 2][:, 0:64], AF.Sign, bias=c75, scale=-1.0, r="#%d c75" % (h % 2), w="sg%d" % h)
+            if h == 0:
+                place0(0, 96)
+            if h == 1:
+                place0(96, 256)
+            if h == 2:
+                score(0, 128, "a")
+        if t == 0:
+            consts(3)
+        tt(T.DM[:], T.B3[:, 0:256], T.MD[:], mul, "#3 MD", "DM")
+        named(0, 128, "a")
+        scan(T.KX[:, 255::-1], T.MH[:, 255::-1], T.DM[:, 255::-1], 0.0, mul, add, "MH DM", "KX")
+        ts(T.e1[:, 0:1], T.cum[:, 63:64], base, add, 256.0, mn, r="cum #5", w="e10")
+        slots(0, 128, "a")
+        score(128, 256, "b")
+        tt(T.EX[:], T.B3[:, 0:256], T.KX[:], eq, "#3 KX", "EX")
+        ts(T.e1[:, 2:3], T.e1[:, 0:1], base, le, 1000.0, mul, r="e10 #5", w="e12")
+        if t == 0:
+            consts(4)
+        named(128, 256, "b")
+        ts(T.oE[:, 0:1], T.e1[:, 0:1], T.e1[:, 2:3], add, 257.0, mn, r="e10 e12", w="oE")
+        slots(128, 256, "b")
+        b = 16 * t
+        mm(T.B7[:, 0:128], [(BO, T.t1[:, 0:256:2]), (BO, T.t1[:, 1:256:2])], "BO t1a t1b", "#7")
+        act(T.sv[:, 8 * b:8 * b + 128], T.B7[:, 0:128], r="#7", w="sv%d" % t)
+        send(1, T.lw[:, 8 * b:8 * b + 128], T.sv[:, 8 * b:8 * b + 128], "rv%d" % t, False, "sv%d" % t)
+        mm(T.B0[:, 256:512], [(Id, T.inv[:]), (S0, T.tb[:]), (BO, T.sg[:, 16:272])], "inv Id BO sg0 sg1 sg2 sg3 mats", "#0")
+        mm(T.B2[:, 256:512], [(A1, T.sg[:, 16:272])], "A1 sg0 sg1 sg2 sg3", "#2")
+        act(T.f0[:], T.B2[:, 256:512], AF.Relu, bias=cB0, scale=0.5, r="#2 cB0", w="f0")
+        mm(T.B1[:, 256:512], [(BO, st), (nBO, stp)], "step stepp mats BO", "#1")
+        act(T.same[:], T.B1[:, 256:512], AF.Relu, bias=1.0, scale=-1.0, r="#1", w="same")
+        mm(T.B7[:, 256:512], [(B8k, T.f0[:]), (Wm, T.f0[:]), (S0, T.KR[:])], "f0 mats", "#7")
+        equals(128, T.B6[:, 0:128], "#6", T.y2[:, 0:8], T.dW[:], "dW", "y2")
+        ts(T.su[:, b:b + 16:2], T.y2[:, 0:8], -0.5, add, r="y2 sup", w="su%d" % t)
+        send(1, T.lu[:, b:b + 16], T.su[:, b:b + 16], "ru%d" % t, False, "su%d" % t)
+        if t < 2:
+            send(t + 2, P[t + 2][:], T.P0[:], "rp%d" % (t + 2), True, "P0")
+        if t < 3:
+            flip_a()
+            starts(t + 1)
+            places_a(t, 0)
+            flip_b(0, 6)
+            apply_u(t + 1, True)
+            wn, wnk = W[(t + 1) % 2], "W%d W%dp" % ((t + 1) % 2, (t + 1) % 2)
+            act(T.GW[:, 512:1024], wn[:, 0:WW].indirect(T.oW1[:, s0 + 96:s0 + 128]), r=wnk + " oW1b", w="GWb")
+            rows("y", lambda i, j, t=t: T.TS[t + 1, 16 * i:16 * j, :], t + 1, wnk, "TS%d" % (t + 1))
+            cp(T.GW[:, 0:512], wn[:, 0:WW].indirect(T.oW1[:, s0 + 64:s0 + 96]), wnk + " oW1b", "GWa")
+        else:
+            flip_a()
+            places_a(3, 0)
+            mark = len(ops)
+            places_a(3, 1)
+            places_b(3, 0)
+            places_b(3, 1)
+            rest = ops[mark:]
+            del ops[mark:]
+            for k in range(16):
+                flip_b(k, k + 1)
+                while rest:
+                    ops.append(rest.pop(0))
+                    if ops[-1][0] == "v" and (not rest or rest[0][0] == "v"):
+                        break
+            dma("y", T.yt[:, 0:2048], T.TX[:, 0:2048], "TX", "yta")
+            dma("a", T.yt[:, 2048:4096], T.TX[:, 2048:4096], "TX", "ytb")
+            apply_u(4, False)
+            cp(T.W0[:, 0:4096:256], T.z0[:], "z0 W0", "W0")
+            rows("g", lambda i, j: T.yw[i:j, :], 4, "W0", "yw")
+            recv(1, "ro3", False, "O4")
+            dma("g", T.yo[:], O(4), "O4", "yo")
+    _emit(g, T, ops)

@@ -6,8 +6,11 @@ BIG = 8192.0
 WW = 4240
 TW = 4368
 STEP_DMA = True
+ORDER = []
+TRIES = [(w, s, x) for w in (110.0, 140.0, 170.0, 200.0) for s in (0.0, 30.0, 70.0, 110.0) for x in (280.0, 320.0)]
+GATHER, SCATTER, LINK = 1.55, 3.8, 2500.0
 ROUND = 1.5 * 2.0 ** 23
-SHARE = 24
+SHARE = 28
 PIECES = ("V", "mats", "THo")
 
 F, B, I, U = "float32", "bfloat16", "int32", "uint16"
@@ -45,34 +48,113 @@ SEMAPHORES = (["qv", "qa", "qt", "qg", "loc"] + ["d%d" % k for k in range(NDMA)]
               + ["r%s%d" % (k, t) for k in "uvotp" for t in range(4)])
 
 
-def _emit(g, T, ops):
-    lastw, readers, banks, deps = {}, {}, {}, []
-    for j, (q, kind, fn, rd, wr) in enumerate(ops):
-        d = set()
-        for k in rd + wr:
-            if k[0] == "#":
-                acc = banks.setdefault(k, {})
-                d.update(i for qq, i in acc.items() if qq != q)
-                acc[q] = j
-        for k in rd:
-            if k[0] != "#" and k in lastw:
-                d.add(lastw[k])
-        for k in wr:
-            if k[0] == "#":
+def _span(ops, deps, order, wake):
+    sent = {o[5][2]: j for j, o in enumerate(ops) if o[1] == "s"}
+    end, free = {}, {}
+    for j in order:
+        q, c = ops[j][0], ops[j][5]
+        if q == "r":
+            end[j] = end[sent[ops[j][2][0]]]
+            continue
+        s = max([free.get(q, 0.0)] + [end[i] + wake for i in deps[j]])
+        free[q], end[j] = s + c[0], s + c[1]
+    return max(end.values())
+
+
+def _order(ops, deps, WAKE, SLACK, LONG):
+    n = len(ops)
+    pre = [[(i, ops[i][5][1] + WAKE) for i in d] for d in deps]
+    last, sent = {}, {o[5][2]: j for j, o in enumerate(ops) if o[1] == "s"}
+    for j, o in enumerate(ops):
+        if o[1] == "r":
+            pre[j].append((sent[o[2][0]], ops[sent[o[2][0]]][5][1]))
+        elif o[0] not in "va" or o[5][0] > LONG or o[1] == "d":
+            if o[0] in last:
+                pre[j].append((last[o[0]], ops[last[o[0]]][5][0]))
+            last[o[0]] = j
+    post = [[] for _ in ops]
+    for j in range(n):
+        for i, c in pre[j]:
+            post[i].append((j, c))
+    left = [len(p) for p in pre]
+    tail, todo, stack = [0.0] * n, [len(p) for p in post], [j for j in range(n) if not post[j]]
+    while stack:
+        j = stack.pop()
+        tail[j] = max([ops[j][5][1]] + [c + tail[i] for i, c in post[j]])
+        for i, c in pre[j]:
+            todo[i] -= 1
+            if not todo[i]:
+                stack.append(i)
+    ready, free, order = [0.0] * n, {}, []
+    cand = {}
+    for j in range(n):
+        if not left[j]:
+            cand.setdefault(ops[j][0], []).append(j)
+    while len(order) < n:
+        best = None
+        for q, c in cand.items():
+            if not c:
                 continue
+            f = free.get(q, 0.0)
+            hot = max(c, key=lambda j: (max(f, ready[j]) + tail[j], -j))
+            bound = max(f, ready[hot]) + tail[hot] + SLACK
+            pick = hot
+            for j in sorted(c, key=lambda j: (max(f, ready[j]), -tail[j], j)):
+                if j == hot or max(f, ready[j]) + ops[j][5][0] + tail[hot] <= bound:
+                    pick = j
+                    break
+            s = max(f, ready[pick])
+            if best is None or s < best[0]:
+                best = (s, q, pick)
+        s, q, j = best
+        cand[q].remove(j)
+        order.append(j)
+        if q != "r":
+            free[q] = s + ops[j][5][0]
+        for i, c in post[j]:
+            ready[i] = max(ready[i], s + c)
+            left[i] -= 1
+            if not left[i]:
+                cand.setdefault(ops[i][0], []).append(i)
+    return order
+
+
+def _emit(g, T, ops):
+    writers, readers, banks, deps = {}, {}, {}, []
+    for j, (q, kind, fn, rd, wr, cost) in enumerate(ops):
+        d = set()
+        for k in set(rd + wr):
+            if k[0] == "#":
+                acc = banks.setdefault(k, [])
+                n = len(acc) - 1
+                while n >= 0 and ops[acc[n]][0] == q:
+                    n -= 1
+                while n >= 0 and ops[acc[n]][0] != q:
+                    d.add(acc[n])
+                    n -= 1
+                acc.append(j)
+        for k in rd:
+            d.update(writers.get(k, []))
+        for k in wr:
             d.update(readers.get(k, []))
-            i = lastw.get(k)
-            if i is not None and not (k in PIECES and ops[i][0] == q):
-                d.add(i)
+            d.update(i for i in writers.get(k, []) if k not in PIECES or ops[i][0] != q)
         for k in rd:
             if k[0] != "#":
                 readers.setdefault(k, []).append(j)
         for k in wr:
-            if k[0] != "#":
-                lastw[k] = j
+            if k in PIECES:
+                writers.setdefault(k, []).append(j)
+            elif k[0] != "#":
+                writers[k] = [j]
                 readers[k] = []
         d.discard(j)
         deps.append(sorted(i for i in d if ops[i][1] != "s" and not (q == "t" and ops[i][0] == "t")))
+    if not ORDER:
+        ORDER.extend(min((_order(ops, deps, w, s, x) for w, s, x in TRIES), key=lambda o: _span(ops, deps, o, 90.0) + _span(ops, deps, o, 170.0)))
+    order = ORDER
+    place = {j: n for n, j in enumerate(order)}
+    ops = [ops[j][:5] for j in order]
+    deps = [sorted(place[i] for i in deps[j]) for j in order]
     need = set()
     for j, d in enumerate(deps):
         last = {}
@@ -121,35 +203,49 @@ def rank_program(g, core, T, topo):
     ops = []
     v, a, pe = g.vector, g.scalar, g.tensor
 
-    def op(q, fn, r="", w="", kind="c"):
-        ops.append([q, kind, fn, r.split(), w.split()])
+    def op(q, fn, r="", w="", kind="c", cost=400.0, lat=0.0, name=None):
+        ops.append([q, kind, fn, r.split(), w.split(), (cost, cost + lat, name)])
+
+    def ns(out, in_, r, more=(), k=None):
+        for x in r.split():
+            if x in ("oX2", "oR") or x[:2] == "lu":
+                return 50 + in_.shape[1] * SCATTER, out, in_
+            if x[0] == "o" and x != "ones":
+                return 50 + out.shape[1] * GATHER, out, in_
+        if k is None:
+            k = 0.5 if all("16" in str(x.dtype) for x in (out, in_) + tuple(more)) else 1.0
+        return 40 + max(64, out.shape[1] * k), out, in_
 
     def ts(out, in0, s1, o0, s2=None, o1=None, r="", w=""):
+        c, out, in0 = ns(out, in0, r)
         if o1 is None:
-            op("v", lambda: v.tensor_scalar(out, in0, s1, None, o0), r, w)
+            op("v", lambda: v.tensor_scalar(out, in0, s1, None, o0), r, w, cost=c)
         else:
-            op("v", lambda: v.tensor_scalar(out, in0, s1, s2, o0, o1), r, w)
+            op("v", lambda: v.tensor_scalar(out, in0, s1, s2, o0, o1), r, w, cost=c)
 
     def tt(out, in0, in1, o, r="", w=""):
-        op("v", lambda: v.tensor_tensor(out, in0, in1, o), r, w)
+        c, out, in0 = ns(out, in0, r, k=1.0 if "#" in r else 2.0)
+        op("v", lambda: v.tensor_tensor(out, in0, in1, o), r, w, cost=c)
 
     def cp(out, in_, r="", w=""):
-        op("v", lambda: v.tensor_copy(out, in_), r, w)
+        c, out, in_ = ns(out, in_, r)
+        op("v", lambda: v.tensor_copy(out, in_), r, w, cost=c)
 
     def ms(ap, c, w):
-        op("v", lambda: v.memset(ap, c), "", w)
+        op("v", lambda: v.memset(ap, c), "", w, cost=104.0)
 
     def scan(out, d0, d1, init, o0, o1, r="", w=""):
-        op("v", lambda: v.tensor_tensor_scan(out, d0, d1, init, o0, o1), r, w)
+        op("v", lambda: v.tensor_tensor_scan(out, d0, d1, init, o0, o1), r, w, cost=ns(out, d0, "", (d1,))[0])
 
     def act(out, in_, fn=AF.Identity, bias=0.0, scale=1.0, r="", w=""):
+        c, out, in_ = ns(out, in_, r, k=1.0)
         if bias is None:
-            op("a", lambda: a.activation(out, in_, fn), r, w)
+            op("a", lambda: a.activation(out, in_, fn), r, w, cost=c + 20)
         else:
-            op("a", lambda: a.activation(out, in_, fn, bias=bias, scale=scale), r, w)
+            op("a", lambda: a.activation(out, in_, fn, bias=bias, scale=scale), r, w, cost=c + 20)
 
     def mm1(out, l, x, st, sp, r, w):
-        op("t", lambda: pe.matmul(out, l, x, st, sp), r, w)
+        op("t", lambda: pe.matmul(out, l, x, st, sp), r, w, cost=10 + max(64, x.shape[1]) * (4 if "32" in str(x.dtype) else 1))
 
     def mm(out, terms, r, w):
         for k, (l, x) in enumerate(terms):
@@ -157,13 +253,13 @@ def rank_program(g, core, T, topo):
 
     def dma(q, out, in_, r="", w=""):
         e = {"g": g, "y": g.sync, "a": g.scalar}[q]
-        op(q, lambda: e.dma_start(out, in_), r, w, "d")
+        op(q, lambda: e.dma_start(out, in_), r, w, "d", 60.0, 7500.0 if w in ("P0", "TX") else 4500.0 if w[:2] == "yt" else 2200.0)
 
     def iota(out, pat, base, cm, w, flt=False):
         if flt:
-            op("g", lambda: g.iota(out, pat, base, cm, allow_small_or_imprecise_dtypes=True), "", w)
+            op("g", lambda: g.iota(out, pat, base, cm, allow_small_or_imprecise_dtypes=True), "", w, cost=130.0 + 2 * out.shape[1])
         else:
-            op("g", lambda: g.iota(out, pat, base, cm), "", w)
+            op("g", lambda: g.iota(out, pat, base, cm), "", w, cost=130.0 + 2 * out.shape[1])
 
     def lanes(src, dst, bulk):
         e = topo.engines(src, dst)
@@ -177,11 +273,11 @@ def rank_program(g, core, T, topo):
         def fn():
             g.remote_dma(out, in_, T.sem[sem], T.sem.loc, pid, rid, sum(1 << x for x in e))
             return len(e)
-        op("g", fn, r, "", "s")
+        op("g", fn, r, "", "s", 500.0, 20000.0 if bulk else LINK, sem)
 
     def recv(k, sem, bulk, w):
         src = T.cores[(rank + k) % N]
-        ops.append(["r", "r", (sem, len(lanes(src, core, bulk))), [], w.split()])
+        ops.append(["r", "r", (sem, len(lanes(src, core, bulk))), [], w.split(), (0.0, 0.0, None)])
 
     col = T.col
     cR, cG, cG15, c4R, cM32, c256, c256b, cR1, cIs0, cN0, cB1, cB0, cP, c75, cSn, c64, cSg, cRn, cRf = (col[:, k:k + 1] for k in range(19))
@@ -230,15 +326,15 @@ def rank_program(g, core, T, topo):
     while n < 1024:
         act(T.MW[:, n:2 * n], T.MW[:, 0:n], r="MW", w="MW")
         n *= 2
-    act(T.Sel[:, 0:1024], T.MW[:], scale=0.0, bias=1.0, r="MW", w="Sel")
-    act(T.Sel[:, 1024:2048], T.MW[:], scale=0.0, bias=1.0, r="MW", w="Sel")
     ms(T.A[:, 256:264], 0.0, "Ap")
     ts(cG15, cG, 15.0, add, r="cG", w="cG15")
+    op("v", lambda: v.memset(T.Sel[:, 0:1024], 1.0), "", "Sel", cost=552.0)
+    op("v", lambda: v.memset(T.Sel[:, 1024:2048], 1.0), "", "Selb", cost=552.0)
     cp(T.G1[:], T.cdi[:, 0:256].indirect(T.oa[:, 0:32]), "cdi oa", "G1")
     cp(T.CT[:, 1:256], T.witi[:, 1:256], "witi", "CT")
-    op("v", lambda: v.transpose(T.G2[:], T.G1[:]), "G1", "G2")
+    op("v", lambda: v.transpose(T.G2[:], T.G1[:]), "G1", "G2 G2b")
     ts(BO, T.iq16[:], cG, eq, r="iq16 cG", w="BO")
-    cp(T.A[:, 0:256], T.G2[:, 0:512].indirect(T.ob[:, 0:16]), "G2 ob", "A")
+    cp(T.A[:, 0:256], T.G2[:, 0:512].indirect(T.ob[:, 0:16]), "G2 G2b ob", "A")
     ts(Id, T.ix[:, 0:128], cP, eq, r="ix cP", w="Id")
     tt(T.DL[:, 1:256], T.A[:, 1:256], T.A[:, 0:255], sub, "A", "DL")
     ts(T.Z[:], T.ix[:, 0:144], cG15, eq, r="ix cG15", w="Z")
@@ -275,7 +371,7 @@ def rank_program(g, core, T, topo):
 
     def consts(part):
         if part == 0:
-            op("g", lambda: g.affine_select(T.Sel[:], T.Sel[:], [[-1, 16], [-16, 8], [0, 16]], eq, 0.0, 0, 1), "Sel", "Sel")
+            op("g", lambda: g.affine_select(T.Sel[:], T.Sel[:], [[-1, 16], [-16, 8], [0, 16]], eq, 0.0, 0, 1), "Sel Selb", "Sel", cost=4400.0)
             ms(cRn, -ROUND, "cRn")
             ms(cRf, ROUND - 64, "cRn")
             keep(ShI, ShI, ne, -1.0, 0, "ShI", "ShI")
@@ -303,7 +399,6 @@ def rank_program(g, core, T, topo):
             ts(cB0, cR, -0.5, mul, 0.5, add, r="cR", w="cB0")
             act(T.half[:], T.ix[:], scale=0.0, bias=0.5, r="ix", w="mats")
             act(T.KR[:], T.ix[:], scale=-32.0, r="ix", w="mats")
-            act(T.tb[:], T.ix[:], scale=0.0, bias=16.0, r="ix", w="mats")
         elif part == 3:
             ts(T.MD[:], T.iqm[:], cR, eq, r="iqm cR", w="MD")
             ts(T.MH[:], T.iqm[:], cR, lt, r="iqm cR", w="MH")
@@ -331,7 +426,7 @@ def rank_program(g, core, T, topo):
         recv(1, "rt%d" % (t - 1), False, "TL%d" % (t - 1))
         dma("y", TD[t % 2][:], T.TL[t - 1], "TL%d" % (t - 1), "TD%d" % (t % 2))
         op("g", lambda: g.indirect_dma_start(W[t % 2][:, 0:4096], None, TD[t % 2][:], IndirectOffsetOnAxis(ap=T.iw[:, 0:1], axis=0),
-                                             bounds_check=7), "TD%d iw" % (t % 2), "W%d" % (t % 2), "d")
+                                             bounds_check=7), "TD%d iw" % (t % 2), "W%d" % (t % 2), "d", 1700.0, 6000.0)
 
     def rows(q, out_of, t, r, w):
         if STEP_DMA:
@@ -384,14 +479,15 @@ def rank_program(g, core, T, topo):
         send(1, O(t + 1), so, "ro%d" % t, False, "so%d" % t)
 
     def flip_a():
-        tt(T.E[:], T.B0[:, 256:512], T.EX[:], lt, "#0 EX", "E")
-        scan(T.YS[:, 255::-1], T.MX[:, 255::-1], T.E[:, 255::-1], 0.0, mul, add, "E MX", "YS")
-        ts(T.y2[:], T.YS[:, 0:256:16], cSg, mul, r="YS cSg", w="y2")
-        tt(T.y1[:], T.y2[:], T.KX[:, 0:256:16], add, "y2 KX", "y1")
-        tt(T.y2[:], T.y1[:], T.dX[:], mn, "y1 dX", "y2")
-        ts(T.oX[:], T.y2[:], BIG - 0.5, add, r="y2", w="oX")
+        x1, x2, x3 = T.tm[:, 0:16], T.tm[:, 16:32], T.tm[:, 32:48]
+        tt(T.EX[:], T.B0[:, 256:512], T.EX[:], lt, "#0 EX", "EX")
+        scan(T.GW[:, 255::-1], T.MX[:, 255::-1], T.EX[:, 255::-1], 0.0, mul, add, "EX MX", "GWa GWb")
+        ts(x1, T.GW[:, 0:256:16], cSg, mul, r="GWa cSg", w="tm0")
+        tt(x2, x1, T.KX[:, 0:256:16], add, "tm0 KX", "tm1")
+        tt(x3, x2, T.dX[:], mn, "tm1 dX", "tm2")
+        ts(T.oX[:], x3, BIG - 0.5, add, r="tm2", w="oX")
         act(T.FV[:], T.TX[:, 0:TW].indirect(T.oX[:, 0:16]), scale=-1.0, bias=255.0, r="TX TXp oX", w="FV")
-        ts(T.oX2[:, 0:32:2], T.y2[:], BIG - 0.5, add, r="y2", w="oX2")
+        ts(T.oX2[:, 0:32:2], x3, BIG - 0.5, add, r="tm2", w="oX2")
 
     def flip_b(lo, hi):
         for k in range(lo, hi):
@@ -415,19 +511,20 @@ def rank_program(g, core, T, topo):
         ts(T.oTQ[:], T.TQ[:], 256.0, add, r="TQa TQb", w="oTQ")
         if t > 0:
             recv(t, "rp%d" % t, True, pk)
-        for h in range(4):
-            o = T.oP[:, 32 * h:32 * h + 32] if h < 2 else T.oTQ[:, 32 * h:32 * h + 32]
-            act(T.PG[:, 512 * h:512 * h + 512], Pt[:, 0:4096].indirect(o), r=pk + (" oP" if h < 2 else " oTQ"), w="PG%d" % h)
+        for h in range(8):
+            o = T.oP[:, 16 * h:16 * h + 16] if h < 4 else T.oTQ[:, 16 * h:16 * h + 16]
+            act(T.PG[:, 512 * h:512 * h + 256], Pt[:, 0:4096].indirect(o), r=pk + (" oP" if h < 4 else " oTQ"), w="PG%d" % h)
         if t > 0:
             send(1, T.TL[t], T.TS[t], "rt%d" % t, False, " ".join("TS%d%s" % (t, x) for x in [""] + list("01234567")))
             flip_b(15, 16)
         else:
             consts(0)
-        for h in range(4):
-            tt(T.NN[:, 512 * h:512 * h + 512], TXw.indirect(T.oTQ[:, 32 * (h % 2):32 * (h % 2) + 32]), T.PG[:, 512 * h:512 * h + 512], eq,
-               "TX oTQ PG%d" % h, "N%d" % h)
-            if h % 2:
-                count(T.B0[:, 32 * (h - 1):32 * (h - 1) + 64], T.NN, 512 * (h - 1), 64, "N%d N%d" % (h - 1, h), "#0")
+        for h in range(8):
+            tt(T.NN[:, 256 * h:256 * h + 256], TXw.indirect(T.oTQ[:, 16 * (h % 4):16 * (h % 4) + 16]), T.PG[:, 512 * h:512 * h + 256], eq,
+               "TX oTQ PG%d" % h, "N%d%s" % (h // 2, "ab"[h % 2]))
+            if h % 4 == 3:
+                count(T.B0[:, 16 * (h - 3):16 * (h - 3) + 64], T.NN, 256 * (h - 3), 64,
+                      " ".join("N%d%s" % (k, x) for k in (h // 2 - 1, h // 2) for x in "ab"), "#0")
         act(T.CW[:, 0:256], T.ix[:], scale=0.0, bias=cRf, r="ix cRn", w="CWa")
         act(T.CW[:, 3072:3328], T.ix[:], AF.Silu if t == 0 else AF.Identity, scale=0.0, r="ix", w="CWb")
         if t > 0:
@@ -448,8 +545,8 @@ def rank_program(g, core, T, topo):
         act(T.x1[:], T.dead[:], scale=1000.0, r="dead", w="x1")
         tt(T.d2[:], T.HS[:, 2:65:2], T.GS[:, 2:65:2], add, "HS GS HSp GSp", "d2")
         ts(T.oW2[:], T.d2[:], 256.0, mn, cw, add, r="d2 c256", w="oW2")
-        act(T.GW[:, 256:512], win.indirect(T.oW2[:, 16:32]), r=wk + " oW2", w="GWb")
-        cp(T.GW[:, 0:256], win.indirect(T.oW2[:, 0:16]), wk + " oW2", "GWa")
+        act(T.GW[:, 192:512], win.indirect(T.oW2[:, 12:32]), r=wk + " oW2", w="GWb")
+        cp(T.GW[:, 0:192], win.indirect(T.oW2[:, 0:12]), wk + " oW2", "GWa")
         tt(T.ai[:], T.A[:, s0 + 2:s0 + 65:2], T.GS[:, 2:65:2], sub, "A Ap GS GSp", "ai")
         ts(T.qb[:], T.d2[:], -1.0, mul, c256, add, r="d2 c256", w="qb")
         scan(T.WS[:, 0:512], T.GW[:, 0:512], T.MW[:, 0:512], 0.0, mx, add, "GWa GWb MW", "WS")
@@ -458,24 +555,28 @@ def rank_program(g, core, T, topo):
         tt(T.TQ[:, 0:32], w2, T.ai[:], add, "WS ai", "TQa")
         tt(T.TQ[:, 32:64], w2, T.qb[:], add, "WS qb", "TQb")
         ts(T.oTQ[:, 0:64], T.TQ[:, 0:64], 256.0, add, r="TQa TQb", w="oTQ")
-        act(T.PG[:, 0:512], Pt[:, 0:4096].indirect(T.oP[:, 0:32]), r=pk + " oP", w="PG0")
-        act(T.PG[:, 512:1008], Pt[:, 0:4096].indirect(T.oTQ[:, 32:63]), r=pk + " oTQ", w="PG1")
+        for h in range(4):
+            n = 16 if h < 3 else 15
+            o = T.oP[:, 16 * h:16 * h + 16] if h < 2 else T.oTQ[:, 16 * h:16 * h + n]
+            act(T.PG[:, 512 * h:512 * h + 16 * n], Pt[:, 0:4096].indirect(o), r=pk + (" oP" if h < 2 else " oTQ"), w="PG%d" % h)
+        for h in range(4):
+            n, lo = 16 if h < 3 else 15, 256 * h + 16 * (h // 2)
+            tt(T.N2[:, lo:lo + 16 * n], TXw.indirect(T.oTQ[:, 16 * (h % 2):16 * (h % 2) + n]), T.PG[:, 512 * h:512 * h + 16 * n], eq,
+               "TX oTQ PG%d" % h, "N2%d" % h)
+        count(T.B0[:, 0:64], T.N2, 0, 64, "N20 N21 N22 N23 N2p", "#0")
         th = T.THe[:, 33:65]
         ts(th, w2, -256.0, gt, 8.0, mul, r="WS", w="THe")
-        tt(T.THo[:, 0:32], th, T.x1[:, 1:64:2], add, "THe x1", "THo")
-        tt(T.th[:, 0:32], th, T.dead[:, 1:64:2], mul, "THe dead", "tha")
-        tt(T.THo[:, 33:64], T.THe[:, 33:64], T.dead[:, 2:64:2], mul, "THe dead", "THo")
-        tt(T.N2[:, 0:512], TXw.indirect(T.oTQ[:, 0:32]), T.PG[:, 0:512], eq, "TX oTQ PG0", "N2a")
-        tt(T.N2[:, 528:1024], TXw.indirect(T.oTQ[:, 0:31]), T.PG[:, 512:1008], eq, "TX oTQ PG1", "N2b")
-        count(T.B0[:, 0:64], T.N2, 0, 64, "N2a N2b N2p", "#0")
         if t > 0:
             recv(1, "ro%d" % (t - 1), False, ok)
         for p in range(16):
             act(T.V[:, p:1024:16], Bk[2 + p // 8][:, 64 * (p % 8):64 * (p % 8) + 64], bias=O(t, p, p + 1),
                 r="#%d %s" % (2 + p // 8, ok), w="V")
         tt(T.dO[:], O(t), O(t, -1, 15), sub, ok + " Op", "dO")
-        tt(T.THe[:, 0:32], T.th[:, 0:32], T.x1[:, 0:64:2], add, "tha x1", "THa")
+        tt(T.th[:, 0:32], th, T.dead[:, 1:64:2], mul, "THe dead", "tha")
         tt(XO, T.dO[:, 0:16].indirect(T.orr[:, 0:8]), BO, mul, "dO orr BO", "XO")
+        tt(T.THo[:, 0:32], th, T.x1[:, 1:64:2], add, "THe x1", "THo")
+        tt(T.THo[:, 33:64], T.THe[:, 33:64], T.dead[:, 2:64:2], mul, "THe dead", "THo")
+        tt(T.THe[:, 0:32], T.th[:, 0:32], T.x1[:, 0:64:2], add, "tha x1", "THa")
         mm(T.B5[:, 0:128], [(XO, Id)], "XO Id", "#5")
         act(dOT, T.B5[:, 0:128], r="#5", w="dOT")
         if t == 0:
@@ -492,8 +593,8 @@ def rank_program(g, core, T, topo):
         tt(T.dK[:], T.dead2[:], T.KD[:], mul, "dead2 KD", "dK")
         tt(T.u0[:], T.dK[:], T.cum[:], mx, "dK cum", "u0")
         st, stp = T.step[:, 16:272], T.step[:, 15:271]
-        ts(st, T.ix[:], base, ge, r="ix #5", w="step")
         ts(T.oR[:], T.u0[:], base, add, -1.0, add, r="u0 #5", w="oR")
+        ts(st, T.ix[:], base, ge, r="ix #5", w="step")
         act(T.ngt[:, 0:1], T.B6[:, 130:131], bias=1.0, scale=-1.0, r="#6", w="ngt")
         act(T.inv[:], T.ix[:], AF.Relu, bias=T.ngt[:, 0:1], r="ix ngt", w="inv")
         mm(T.B4[:, 256:512], [(dOT, st), (B256, st)], "dOT step mats", "#4")
@@ -508,7 +609,8 @@ def rank_program(g, core, T, topo):
 
         items(0)
         items(1)
-        tt(T.G2[:, 0:256], T.CW[:, 0:256], T.CW[:, 3072:3328], add, "CWa CWb", "G2")
+        tt(T.G2[:, 0:128], T.CW[:, 0:128], T.CW[:, 3072:3200], add, "CWa CWb", "G2")
+        tt(T.G2[:, 128:256], T.CW[:, 128:256], T.CW[:, 3200:3328], add, "CWa CWb", "G2b")
         vv = T.B5[:, 256:512]
         for k, (l, x) in enumerate(((dOT, st), (B8k, st), (nB8k, stp), (I8k, T.inv[:]))):
             mm1(vv, l, x, k == 0, False, "dOT step stepp inv mats", "#5")
@@ -516,8 +618,9 @@ def rank_program(g, core, T, topo):
         mm1(T.B3[:, 0:256], S0, T.half[:], True, False, "mats", "#3")
         mm1(T.B6[:, 0:128], B256, T.step[:, 16:272:2], True, False, "step mats", "#6")
         mm1(T.B6[:, 0:128], S0, T.half[:, 0:128], False, False, "mats", "#6")
-        ts(T.oTT[:], T.G2[:, 0:256], -ROUND, add, r="G2", w="oTT")
-        act(T.G1[:, 8:264], T.G2[:, 0:256], bias=cRn, r="G2 cRn", w="G1")
+        ts(T.oTT[:, 0:128], T.G2[:, 0:128], -ROUND, add, r="G2", w="oTT0")
+        ts(T.oTT[:, 128:256], T.G2[:, 128:256], -ROUND, add, r="G2b", w="oTT1")
+        act(T.G1[:, 8:264], T.G2[:, 0:256], bias=cRn, r="G2 G2b cRn", w="G1")
         mm1(vv, Idf, T.G1[:, 8:264], False, False, "G1 mats", "#5")
         mm1(vv, nIdf, T.G1[:, 7:263], False, True, "G1 mats", "#5")
         items(2)
@@ -541,16 +644,18 @@ def rank_program(g, core, T, topo):
             mm1(T.B3[:, lo:hi], S0f, T.G1[:, 8 + lo:8 + hi], False, hi == 256, "G1 mats", "#3")
 
         for h in range(4):
-            nk = "N%d N%d" % (2 * h, 2 * h + 1)
+            nk = "N%da N%da" % (2 * h, 2 * h + 1)
             for j in (2 * h, 2 * h + 1):
                 tt(T.NN[:, 512 * j:512 * j + 512], TXw.indirect(T.oTT[:, 32 * j:32 * j + 32]), T.PG[:, 512 * j:512 * j + 512], eq,
-                   "TX oTT PG%d" % j, "N%d" % j)
+                   "TX oTT%d PG%d" % (j // 4, j), "N%da N%db" % (j, j))
             count(Bk[h % 2][:, 0:64], T.NN, 1024 * h, 64, nk, "#%d" % (h % 2))
             if h < 2:
                 items(2 * h + 4)
                 items(2 * h + 5)
             if h == 1:
                 act(T.sn[:], vv, AF.Sign, bias=cSn, r="#5 cSn", w="sn")
+            if h == 3:
+                act(T.tb[:], T.inv[:], bias=16.0, r="inv", w="tb")
             act(T.sg[:, 16 + 64 * h:80 + 64 * h], Bk[h % 2][:, 0:64], AF.Sign, bias=c75, scale=-1.0, r="#%d c75" % (h % 2), w="sg%d" % h)
             if h == 0:
                 place0(0, 96)
@@ -564,12 +669,15 @@ def rank_program(g, core, T, topo):
         named(0, 128, "a")
         scan(T.KX[:, 255::-1], T.MH[:, 255::-1], T.DM[:, 255::-1], 0.0, mul, add, "MH DM", "KX")
         ts(T.e1[:, 0:1], T.cum[:, 63:64], base, add, 256.0, mn, r="cum #5", w="e10")
-        slots(0, 128, "a")
+        mm1(T.B0[:, 256:512], Id, T.tb[:], True, False, "tb Id", "#0")
         score(128, 256, "b")
+        mm1(T.B0[:, 256:512], BO, T.sg[:, 16:272], False, True, "BO sg0 sg1 sg2 sg3", "#0")
+        slots(0, 128, "a")
         tt(T.EX[:], T.B3[:, 0:256], T.KX[:], eq, "#3 KX", "EX")
         ts(T.e1[:, 2:3], T.e1[:, 0:1], base, le, 1000.0, mul, r="e10 #5", w="e12")
         if t == 0:
             consts(4)
+        flip_a()
         named(128, 256, "b")
         ts(T.oE[:, 0:1], T.e1[:, 0:1], T.e1[:, 2:3], add, 257.0, mn, r="e10 e12", w="oE")
         slots(128, 256, "b")
@@ -577,7 +685,6 @@ def rank_program(g, core, T, topo):
         mm(T.B7[:, 0:128], [(BO, T.t1[:, 0:256:2]), (BO, T.t1[:, 1:256:2])], "BO t1a t1b", "#7")
         act(T.sv[:, 8 * b:8 * b + 128], T.B7[:, 0:128], r="#7", w="sv%d" % t)
         send(1, T.lw[:, 8 * b:8 * b + 128], T.sv[:, 8 * b:8 * b + 128], "rv%d" % t, False, "sv%d" % t)
-        mm(T.B0[:, 256:512], [(Id, T.inv[:]), (S0, T.tb[:]), (BO, T.sg[:, 16:272])], "inv Id BO sg0 sg1 sg2 sg3 mats", "#0")
         mm(T.B2[:, 256:512], [(A1, T.sg[:, 16:272])], "A1 sg0 sg1 sg2 sg3", "#2")
         act(T.f0[:], T.B2[:, 256:512], AF.Relu, bias=cB0, scale=0.5, r="#2 cB0", w="f0")
         mm(T.B1[:, 256:512], [(BO, st), (nBO, stp)], "step stepp mats BO", "#1")
@@ -589,7 +696,6 @@ def rank_program(g, core, T, topo):
         if t < 2:
             send(t + 2, P[t + 2][:], T.P0[:], "rp%d" % (t + 2), True, "P0")
         if t < 3:
-            flip_a()
             starts(t + 1)
             places_a(t, 0)
             flip_b(0, 6)
@@ -599,7 +705,6 @@ def rank_program(g, core, T, topo):
             rows("y", lambda i, j, t=t: T.TS[t + 1, 16 * i:16 * j, :], t + 1, wnk, "TS%d" % (t + 1))
             cp(T.GW[:, 0:512], wn[:, 0:WW].indirect(T.oW1[:, s0 + 64:s0 + 96]), wnk + " oW1b", "GWa")
         else:
-            flip_a()
             places_a(3, 0)
             mark = len(ops)
             places_a(3, 1)

@@ -3,14 +3,15 @@ from concourse.mybir import AluOpType as ALU, ActivationFunctionType as AF
 
 N = 4
 BIG = 8192.0
-WW = 4240
+WW = 4112
+WS = 8224
 TW = 4368
 STEP_DMA = True
 ORDER = []
-TRIES = [(w, s, x) for w in (110.0, 140.0, 170.0, 200.0) for s in (0.0, 30.0, 70.0, 110.0) for x in (280.0, 320.0)]
+TRIES = [(w, s, x, k) for w in (200.0, 230.0, 260.0) for s in (0.0, 50.0, 100.0, 150.0) for x in (280.0, 330.0) for k in range(24)]
 GATHER, SCATTER, LINK = 1.55, 3.8, 2500.0
 ROUND = 1.5 * 2.0 ** 23
-SHARE = 28
+SHARE = 30
 PIECES = ("V", "mats", "THo")
 
 F, B, I, U = "float32", "bfloat16", "int32", "uint16"
@@ -18,11 +19,11 @@ MATS = "BO LT Id A1 nBO nI B256 B8k nB8k I8k B4k Wm S0 ShI dOT XO".split()
 SCRATCH = {}
 for _n, _c, _d in (
     ("TX", TW, B), ("P0", 4096, B), ("P1", 4096, B), ("P2", 4096, B), ("P3", 4096, B),
-    ("W0", WW, B), ("W1", WW, B), ("CT", 272, B), ("cdi", 256, I), ("witi", 256, I), ("prbi", 16, I),
+    ("W0", WS, B), ("W1", WS, B), ("CT", 272, B), ("cdi", 256, I), ("witi", 256, I), ("prbi", 16, I),
     ("ip", 8, I), ("iw", 8, I), ("col", 32, F), ("ia", 32, I), ("ib", 16, I), ("oa", 32, U), ("ob", 16, U), ("orr", 8, U),
     ("G1", 512, F), ("G2", 512, F), ("A", 264, F), ("Ah", 256, B), ("Al", 256, B), ("KX", 256, F), ("EX", 256, B), ("MX", 256, B), ("DL", 264, F), ("QB", 256, F),
     ("oW1", 256, U), ("ix", 256, B), ("iq16", 128, B), ("iqm", 256, B), ("Z", 144, B), ("M", 128 * len(MATS), B), ("Mf", 384, F),
-    ("Sel", 2048, B), ("KR", 256, B), ("half", 256, B), ("MW", 1024, B), ("MD", 256, B), ("MH", 256, B), ("MC", 256, B), ("tm", 64, F),
+    ("Sel", 2048, B), ("KR", 256, B), ("half", 256, B), ("MW", 1024, B), ("MD", 256, B), ("MH", 256, B), ("MC", 1024, B), ("tm", 64, F),
     ("tb", 256, B), ("dW", 8, F), ("dX", 16, F), ("KD", 64, F), ("z0", 16, B), ("xz", 16, B),
     ("GW", 1024, B), ("WS", 1024, B), ("oP", 64, U), ("TQ", 128, F), ("oTQ", 128, U), ("PG", 4096, B),
     ("NN", 4096, B), ("N2", 1024, B), ("th", 128, F), ("lv", 128, F), ("dead", 64, F),
@@ -31,7 +32,7 @@ for _n, _c, _d in (
     ("oR", 64, U), ("step", 272, B), ("inv", 256, B), ("ngt", 8, F), ("same", 256, B), ("oPP", 256, U), ("oTT", 256, U),
     ("V", 1024, F), ("CW", 6144, F), ("dO", 16, B),
     ("sg", 272, B), ("sn", 256, B), ("f1", 256, B), ("f0", 256, B), ("t1", 256, B), ("t2", 256, B),
-    ("DM", 256, F), ("KS", 256, F), ("E", 256, B), ("YS", 256, B), ("y1", 16, F), ("y2", 16, F), ("oX", 16, U), ("oX2", 32, U),
+    ("DM", 256, F), ("KS", 256, F), ("E", 1024, B), ("YS", 1024, B), ("y1", 16, F), ("y2", 16, F), ("oX", 16, U), ("oX2", 32, U),
     ("FV", 256, B), ("sv", 512, B), ("CS", 264, F), ("e1", 8, F), ("oE", 8, U), ("R", 16, I), ("R2", 16, I), ("sl", 16, F), ("to", 16, B),
     ("le", 16, F), ("uo", 16, F), ("su", 64, U), ("lu", 64, U), ("lw", 512, B), ("so", 64, B), ("O", 160, B),
 ):
@@ -61,7 +62,7 @@ def _span(ops, deps, order, wake):
     return max(end.values())
 
 
-def _order(ops, deps, WAKE, SLACK, LONG):
+def _order(ops, deps, WAKE, SLACK, LONG, seed):
     n = len(ops)
     pre = [[(i, ops[i][5][1] + WAKE) for i in d] for d in deps]
     last, sent = {}, {o[5][2]: j for j, o in enumerate(ops) if o[1] == "s"}
@@ -85,6 +86,8 @@ def _order(ops, deps, WAKE, SLACK, LONG):
             todo[i] -= 1
             if not todo[i]:
                 stack.append(i)
+    if seed:
+        tail = [x + (j * 2654435761 * seed + seed) % 1000003 % 240 for j, x in enumerate(tail)]
     ready, free, order = [0.0] * n, {}, []
     cand = {}
     for j in range(n):
@@ -150,7 +153,7 @@ def _emit(g, T, ops):
         d.discard(j)
         deps.append(sorted(i for i in d if ops[i][1] != "s" and not (q == "t" and ops[i][0] == "t")))
     if not ORDER:
-        ORDER.extend(min((_order(ops, deps, w, s, x) for w, s, x in TRIES), key=lambda o: _span(ops, deps, o, 90.0) + _span(ops, deps, o, 170.0)))
+        ORDER.extend(min((_order(ops, deps, *x) for x in TRIES), key=lambda o: _span(ops, deps, o, 180.0) + _span(ops, deps, o, 270.0)))
     order = ORDER
     place = {j: n for n, j in enumerate(order)}
     ops = [ops[j][:5] for j in order]
@@ -253,7 +256,7 @@ def rank_program(g, core, T, topo):
 
     def dma(q, out, in_, r="", w=""):
         e = {"g": g, "y": g.sync, "a": g.scalar}[q]
-        op(q, lambda: e.dma_start(out, in_), r, w, "d", 60.0, 7500.0 if w in ("P0", "TX") else 4500.0 if w[:2] == "yt" else 2200.0)
+        op(q, lambda: e.dma_start(out, in_), r, w, "d", 60.0, 7500.0 if w in ("P0", "TX") else 4500.0 if w[:2] == "yt" else 2600.0)
 
     def iota(out, pat, base, cm, w, flt=False):
         if flt:
@@ -280,7 +283,7 @@ def rank_program(g, core, T, topo):
         ops.append(["r", "r", (sem, len(lanes(src, core, bulk))), [], w.split(), (0.0, 0.0, None)])
 
     col = T.col
-    cR, cG, cG15, c4R, cM32, c256, c256b, cR1, cIs0, cN0, cB1, cB0, cP, c75, cSn, c64, cSg, cRn, cRf = (col[:, k:k + 1] for k in range(19))
+    cR, cG, cG15, c4R, cM32, c256, c256b, cR1, cIs0, cN0, cB1, cB0, cP, c75, cSn, c64, cSg, cRn, cRf, cD, cSi = (col[:, k:k + 1] for k in range(21))
     BO, LT, Id, A1, nBO, nI, B256, B8k, nB8k, I8k, B4k, Wm, S0, ShI, dOT, XO = (T.M[:, 128 * k:128 * k + 128] for k in range(len(MATS)))
     Idf, nIdf, S0f = (T.Mf[:, 128 * k:128 * k + 128] for k in range(3))
     P = [T.P0, T.P1, T.P2, T.P3]
@@ -377,6 +380,8 @@ def rank_program(g, core, T, topo):
             keep(ShI, ShI, ne, -1.0, 0, "ShI", "ShI")
             fill(T.TX[:, 4096:TW], TW - 4096, 0, "TXp")
             fill(T.CS[:], 264, 0, "CS")
+            iota(T.YS[:], [[-16, 8], [1, 128]], 0, 0, "YS", True)
+            fill(T.E[:], 1024, 0, "Ep")
             ts(cN0, cR, 0.0, gt, 256.0, mul, r="cR", w="cN0")
             for dst, src, s in ((B256, BO, cN0), (nBO, BO, -1.0), (B8k, BO, BIG), (nB8k, BO, -BIG), (I8k, Id, BIG), (S0, BO, cIs0), (nI, Id, -1.0),
                                 (Idf, Id, 1.0), (nIdf, Id, -1.0), (Wm, BO, cR1), (S0f, BO, cIs0)):
@@ -391,7 +396,6 @@ def rank_program(g, core, T, topo):
         elif part == 2:
             ts(c64, cR, 64.0, mul, 1024.0, add, r="cR", w="c64")
             ms(c75, 7.5, "c75")
-            ms(T.su[:], 0, "sup")
             ms(cSn, -255.5, "cSn")
             ts(T.KD[:], T.ix[:, 0:64], c64, add, r="ix c64", w="KD")
             tt(A1, Id, LT, sub, "Id LT", "A1")
@@ -403,11 +407,12 @@ def rank_program(g, core, T, topo):
             ts(T.MD[:], T.iqm[:], cR, eq, r="iqm cR", w="MD")
             ts(T.MH[:], T.iqm[:], cR, lt, r="iqm cR", w="MH")
         elif part == 4:
-            ts(T.MC[:], T.iqm[:], cR, lt, r="iqm cR", w="MC")
-            ts(T.y1[:], T.ix[:, 0:16], 16.0, mul, cR, add, r="ix cR", w="y1")
-            ts(T.MC[:, 0:256:16], T.iqm[:, 0:256:16], cR, lt, BIG, mul, r="iqm cR", w="MC")
-            ts(T.dW[:], T.y1[:, 0:8], 4112.5, add, r="y1", w="dW")
-            ts(T.dX[:], T.y1[:], 4112.5 - BIG, add, r="y1", w="dX")
+            ts(T.MC[:], T.YS[:], cR, lt, r="YS cR", w="MC")
+            ts(c64, cR, 32.0, mul, 4128.0, add, r="cR", w="c64")
+            ts(T.dW[:], T.ix[:, 0:8], 512.0, mul, c64, add, r="ix c64", w="dW")
+            tt(T.MC[:, 0:1024:128], T.MC[:, 0:1024:128], T.dW[:], mul, "MC dW", "MC")
+            ts(cD, cR, 4112.0, add, r="cR", w="cD")
+            ts(cSi, cIs0, -2 / BIG, mul, 1 / BIG, add, r="cIs0", w="cSg")
             ts(c4R, cR, -1.0, add, r="cR", w="c4R")
             ts(cSg, cIs0, -2 * BIG, mul, BIG, add, r="cIs0", w="cSg")
             ts(T.MX[:], T.iqm[:], c4R, eq, -2.0, mul, r="iqm c4R", w="MX")
@@ -439,19 +444,22 @@ def rank_program(g, core, T, topo):
         b = 16 * (t - 1)
         recv(1, "ru%d" % (t - 1), False, "lu%d" % (t - 1))
         recv(1, "rv%d" % (t - 1), False, "lw%d" % (t - 1))
-        for k in range(7, -1, -1):
-            cp(W[t % 2][:, 0:WW].indirect(T.lu[:, b + 2 * k:b + 2 * k + 1]), T.lw[:, 8 * b + 16 * k:8 * b + 16 * k + 16],
-               "lu%d lw%d W%d W%dp" % (t - 1, t - 1, t % 2, t % 2), "W%d" % (t % 2))
-            if between:
-                flip_b(13 - k, 14 - k)
+        cp(W[t % 2][:, 0:WS].indirect(T.lu[:, b:b + 8]), T.lw[:, 8 * b:8 * b + 128],
+           "lu%d lw%d W%d W%dp" % (t - 1, t - 1, t % 2, t % 2), "W%d" % (t % 2))
+        if between:
+            flip_b(6, 14)
 
     def equals(n, key, bk, out, spare, r, w):
         tt(T.DM[:, 0:n], key, T.MD[:, 0:n], mul, bk + " MD", "DM")
         scan(T.KS[:, n - 1::-1], T.MH[:, n - 1::-1], T.DM[:, n - 1::-1], 0.0, mul, add, "MH DM", "KS")
-        tt(T.E[:, 0:n], key, T.KS[:, 0:n], eq, bk + " KS", "E")
-        scan(T.YS[:, n - 1::-1], T.E[:, n - 1::-1], T.MC[:, n - 1::-1], 0.0, add, mul, "E MC", "YS")
-        tt(T.y1[:, 0:n // 16], T.YS[:, 0:n:16], T.KS[:, 0:n:16], add, "YS KS", "y1")
-        tt(out, T.y1[:, 0:n // 16], spare, mn, "y1 " + r, w)
+        for k in range(8):
+            ts(T.E[:, 128 * k:144 * k + 16], T.B6[:, 0:16 * k + 16], T.KS[:, 16 * k:16 * k + 1], eq, r=bk + " KS Ep", w="E%d" % k)
+        scan(T.YS[:, 1023::-1], T.E[:, 1023::-1], T.MC[:, 1023::-1], 0.0, mx, mul, " ".join("E%d" % k for k in range(8)) + " MC", "YS")
+        tt(T.y1[:, 0:8], T.YS[:, 0:1024:128], T.KS[:, 0:n:16], mx, "YS KS", "y1")
+        ts(out, T.y1[:, 0:8], -0.5, add, r="y1", w=w)
+
+    def place0(lo, hi):
+        mm1(T.B3[:, lo:hi], S0f, T.G1[:, 8 + lo:8 + hi], False, hi == 256, "G1 mats", "#3")
 
     def starts(t):
         for p in range(16):
@@ -479,15 +487,14 @@ def rank_program(g, core, T, topo):
         send(1, O(t + 1), so, "ro%d" % t, False, "so%d" % t)
 
     def flip_a():
-        x1, x2, x3 = T.tm[:, 0:16], T.tm[:, 16:32], T.tm[:, 32:48]
+        x1, x2 = T.tm[:, 0:16], T.tm[:, 16:32]
+        ts(x1, T.KX[:, 0:256:16], BIG - 0.5, add, cSi, mul, r="KX cSg", w="tm0")
         tt(T.EX[:], T.B0[:, 256:512], T.EX[:], lt, "#0 EX", "EX")
         scan(T.GW[:, 255::-1], T.MX[:, 255::-1], T.EX[:, 255::-1], 0.0, mul, add, "EX MX", "GWa GWb")
-        ts(x1, T.GW[:, 0:256:16], cSg, mul, r="GWa cSg", w="tm0")
-        tt(x2, x1, T.KX[:, 0:256:16], add, "tm0 KX", "tm1")
-        tt(x3, x2, T.dX[:], mn, "tm1 dX", "tm2")
-        ts(T.oX[:], x3, BIG - 0.5, add, r="tm2", w="oX")
+        tt(x2, T.GW[:, 0:256:16], x1, add, "GWa tm0", "tm1")
+        ts(T.oX[:], x2, cSg, mul, cD, mn, r="tm1 cSg cD", w="oX")
         act(T.FV[:], T.TX[:, 0:TW].indirect(T.oX[:, 0:16]), scale=-1.0, bias=255.0, r="TX TXp oX", w="FV")
-        ts(T.oX2[:, 0:32:2], x3, BIG - 0.5, add, r="tm2", w="oX2")
+        ts(T.oX2[:, 0:32:2], x2, cSg, mul, cD, mn, r="tm1 cSg cD", w="oX2")
 
     def flip_b(lo, hi):
         for k in range(lo, hi):
@@ -545,8 +552,8 @@ def rank_program(g, core, T, topo):
         act(T.x1[:], T.dead[:], scale=1000.0, r="dead", w="x1")
         tt(T.d2[:], T.HS[:, 2:65:2], T.GS[:, 2:65:2], add, "HS GS HSp GSp", "d2")
         ts(T.oW2[:], T.d2[:], 256.0, mn, cw, add, r="d2 c256", w="oW2")
-        act(T.GW[:, 192:512], win.indirect(T.oW2[:, 12:32]), r=wk + " oW2", w="GWb")
-        cp(T.GW[:, 0:192], win.indirect(T.oW2[:, 0:12]), wk + " oW2", "GWa")
+        act(T.GW[:, 256:512], win.indirect(T.oW2[:, 16:32]), r=wk + " oW2", w="GWb")
+        cp(T.GW[:, 0:256], win.indirect(T.oW2[:, 0:16]), wk + " oW2", "GWa")
         tt(T.ai[:], T.A[:, s0 + 2:s0 + 65:2], T.GS[:, 2:65:2], sub, "A Ap GS GSp", "ai")
         ts(T.qb[:], T.d2[:], -1.0, mul, c256, add, r="d2 c256", w="qb")
         scan(T.WS[:, 0:512], T.GW[:, 0:512], T.MW[:, 0:512], 0.0, mx, add, "GWa GWb MW", "WS")
@@ -609,8 +616,8 @@ def rank_program(g, core, T, topo):
 
         items(0)
         items(1)
-        tt(T.G2[:, 0:128], T.CW[:, 0:128], T.CW[:, 3072:3200], add, "CWa CWb", "G2")
-        tt(T.G2[:, 128:256], T.CW[:, 128:256], T.CW[:, 3200:3328], add, "CWa CWb", "G2b")
+        tt(T.G2[:, 8:136], T.CW[:, 0:128], T.CW[:, 3072:3200], add, "CWa CWb", "G2")
+        tt(T.G2[:, 136:264], T.CW[:, 128:256], T.CW[:, 3200:3328], add, "CWa CWb", "G2b")
         vv = T.B5[:, 256:512]
         for k, (l, x) in enumerate(((dOT, st), (B8k, st), (nB8k, stp), (I8k, T.inv[:]))):
             mm1(vv, l, x, k == 0, False, "dOT step stepp inv mats", "#5")
@@ -618,9 +625,9 @@ def rank_program(g, core, T, topo):
         mm1(T.B3[:, 0:256], S0, T.half[:], True, False, "mats", "#3")
         mm1(T.B6[:, 0:128], B256, T.step[:, 16:272:2], True, False, "step mats", "#6")
         mm1(T.B6[:, 0:128], S0, T.half[:, 0:128], False, False, "mats", "#6")
-        ts(T.oTT[:, 0:128], T.G2[:, 0:128], -ROUND, add, r="G2", w="oTT0")
-        ts(T.oTT[:, 128:256], T.G2[:, 128:256], -ROUND, add, r="G2b", w="oTT1")
-        act(T.G1[:, 8:264], T.G2[:, 0:256], bias=cRn, r="G2 G2b cRn", w="G1")
+        ts(T.oTT[:, 0:128], T.G2[:, 8:136], -ROUND, add, r="G2", w="oTT0")
+        ts(T.oTT[:, 128:256], T.G2[:, 136:264], -ROUND, add, r="G2b", w="oTT1")
+        act(T.G1[:, 8:264], T.G2[:, 8:264], bias=cRn, r="G2 G2b cRn", w="G1")
         mm1(vv, Idf, T.G1[:, 8:264], False, False, "G1 mats", "#5")
         mm1(vv, nIdf, T.G1[:, 7:263], False, True, "G1 mats", "#5")
         items(2)
@@ -640,15 +647,18 @@ def rank_program(g, core, T, topo):
             for k, (l, y) in enumerate(((BO, T.t1[:, lo:hi:2]), (BO, T.t1[:, lo + 1:hi:2]), (nBO, T.t2[:, lo:hi:2]), (nBO, T.t2[:, lo + 1:hi:2]))):
                 mm1(T.B6[:, lo // 2:hi // 2], l, y, False, hi == 256 and k == 3, "mats BO t1%s%s" % (x, " t2" + x if k > 1 else ""), "#6")
 
-        def place0(lo, hi):
-            mm1(T.B3[:, lo:hi], S0f, T.G1[:, 8 + lo:8 + hi], False, hi == 256, "G1 mats", "#3")
 
         for h in range(4):
             nk = "N%da N%da" % (2 * h, 2 * h + 1)
             for j in (2 * h, 2 * h + 1):
                 tt(T.NN[:, 512 * j:512 * j + 512], TXw.indirect(T.oTT[:, 32 * j:32 * j + 32]), T.PG[:, 512 * j:512 * j + 512], eq,
                    "TX oTT%d PG%d" % (j // 4, j), "N%da N%db" % (j, j))
-            count(Bk[h % 2][:, 0:64], T.NN, 1024 * h, 64, nk, "#%d" % (h % 2))
+            if h == 1:
+                place0(0, 96)
+            if h == 2:
+                place0(96, 256)
+            bk = (0, 1, 7, 1)[h]
+            count(Bk[bk][:, 0:64], T.NN, 1024 * h, 64, nk, "#%d" % bk)
             if h < 2:
                 items(2 * h + 4)
                 items(2 * h + 5)
@@ -656,11 +666,7 @@ def rank_program(g, core, T, topo):
                 act(T.sn[:], vv, AF.Sign, bias=cSn, r="#5 cSn", w="sn")
             if h == 3:
                 act(T.tb[:], T.inv[:], bias=16.0, r="inv", w="tb")
-            act(T.sg[:, 16 + 64 * h:80 + 64 * h], Bk[h % 2][:, 0:64], AF.Sign, bias=c75, scale=-1.0, r="#%d c75" % (h % 2), w="sg%d" % h)
-            if h == 0:
-                place0(0, 96)
-            if h == 1:
-                place0(96, 256)
+            act(T.sg[:, 16 + 64 * h:80 + 64 * h], Bk[bk][:, 0:64], AF.Sign, bias=c75, scale=-1.0, r="#%d c75" % bk, w="sg%d" % h)
             if h == 2:
                 score(0, 128, "a")
         if t == 0:
@@ -690,9 +696,8 @@ def rank_program(g, core, T, topo):
         mm(T.B1[:, 256:512], [(BO, st), (nBO, stp)], "step stepp mats BO", "#1")
         act(T.same[:], T.B1[:, 256:512], AF.Relu, bias=1.0, scale=-1.0, r="#1", w="same")
         mm(T.B7[:, 256:512], [(B8k, T.f0[:]), (Wm, T.f0[:]), (S0, T.KR[:])], "f0 mats", "#7")
-        equals(128, T.B6[:, 0:128], "#6", T.y2[:, 0:8], T.dW[:], "dW", "y2")
-        ts(T.su[:, b:b + 16:2], T.y2[:, 0:8], -0.5, add, r="y2 sup", w="su%d" % t)
-        send(1, T.lu[:, b:b + 16], T.su[:, b:b + 16], "ru%d" % t, False, "su%d" % t)
+        equals(128, T.B6[:, 0:128], "#6", T.su[:, b:b + 8], None, "", "su%d" % t)
+        send(1, T.lu[:, b:b + 8], T.su[:, b:b + 8], "ru%d" % t, False, "su%d" % t)
         if t < 2:
             send(t + 2, P[t + 2][:], T.P0[:], "rp%d" % (t + 2), True, "P0")
         if t < 3:

@@ -3,38 +3,43 @@ from concourse.mybir import AluOpType as ALU, ActivationFunctionType as AF
 
 N = 4
 BIG = 8192.0
+HOLD = 65536.0
 WW = 4112
 WS = 8224
 TW = 4368
-STEP_DMA = True
 ORDER = []
 TRIES = [(w, s, x, k) for w in (200.0, 230.0, 260.0) for s in (0.0, 50.0, 100.0, 150.0) for x in (280.0, 330.0) for k in range(24)]
 GATHER, SCATTER, LINK = 1.55, 3.8, 2500.0
 ROUND = 1.5 * 2.0 ** 23
 SHARE = 30
-PIECES = ("V", "mats", "THo")
+WSH = 32
+SPLIT = (3,)
+PIECES = ("V",)
+TRI = [8 * k * (k + 1) for k in range(9)]
 
 F, B, I, U = "float32", "bfloat16", "int32", "uint16"
-MATS = "BO LT Id A1 nBO nI B256 B8k nB8k I8k B4k Wm S0 ShI dOT XO".split()
+MATS = "BO LT Id A1 nBO nI B256 B8k nB8k I8k nB4k nI8k nI8 S0 nS0 ShI L0 Mx dOT XO".split()
 SCRATCH = {}
 for _n, _c, _d in (
     ("TX", TW, B), ("P0", 4096, B), ("P1", 4096, B), ("P2", 4096, B), ("P3", 4096, B),
     ("W0", WS, B), ("W1", WS, B), ("CT", 272, B), ("cdi", 256, I), ("witi", 256, I), ("prbi", 16, I),
-    ("ip", 8, I), ("iw", 8, I), ("col", 32, F), ("ia", 32, I), ("ib", 16, I), ("oa", 32, U), ("ob", 16, U), ("orr", 8, U),
-    ("G1", 512, F), ("G2", 512, F), ("A", 264, F), ("Ah", 256, B), ("Al", 256, B), ("KX", 256, F), ("EX", 256, B), ("MX", 256, B), ("DL", 264, F), ("QB", 256, F),
-    ("oW1", 256, U), ("ix", 256, B), ("iq16", 128, B), ("iqm", 256, B), ("Z", 144, B), ("M", 128 * len(MATS), B), ("Mf", 384, F),
-    ("Sel", 2048, B), ("KR", 256, B), ("half", 256, B), ("MW", 1024, B), ("MD", 256, B), ("MH", 256, B), ("MC", 1024, B), ("tm", 64, F),
-    ("tb", 256, B), ("dW", 8, F), ("dX", 16, F), ("KD", 64, F), ("z0", 16, B), ("xz", 16, B),
-    ("GW", 1024, B), ("WS", 1024, B), ("oP", 64, U), ("TQ", 128, F), ("oTQ", 128, U), ("PG", 4096, B),
-    ("NN", 4096, B), ("N2", 1024, B), ("th", 128, F), ("lv", 128, F), ("dead", 64, F),
-    ("GS", 72, F), ("HS", 72, F), ("d2", 32, F), ("oW2", 32, U), ("ai", 32, F), ("qb", 32, F), ("x1", 64, F),
-    ("THo", 72, F), ("THe", 72, F), ("K", 128, F), ("dead2", 64, F), ("cum", 64, B), ("ones", 64, F), ("dK", 64, F), ("u0", 64, F),
-    ("oR", 64, U), ("step", 272, B), ("inv", 256, B), ("ngt", 8, F), ("same", 256, B), ("oPP", 256, U), ("oTT", 256, U),
-    ("V", 1024, F), ("CW", 6144, F), ("dO", 16, B),
-    ("sg", 272, B), ("sn", 256, B), ("f1", 256, B), ("f0", 256, B), ("t1", 256, B), ("t2", 256, B),
-    ("DM", 256, F), ("KS", 256, F), ("E", 1024, B), ("YS", 1024, B), ("y1", 16, F), ("y2", 16, F), ("oX", 16, U), ("oX2", 32, U),
-    ("FV", 256, B), ("sv", 512, B), ("CS", 264, F), ("e1", 8, F), ("oE", 8, U), ("R", 16, I), ("R2", 16, I), ("sl", 16, F), ("to", 16, B),
-    ("le", 16, F), ("uo", 16, F), ("su", 64, U), ("lu", 64, U), ("lw", 512, B), ("so", 64, B), ("O", 160, B),
+    ("ip", 8, I), ("iw", 8, I), ("col", 32, F), ("ia", 32, I), ("ib", 16, I), ("oa", 32, U), ("ob", 16, U), ("orr", 64, U),
+    ("G1", 512, F), ("G2", 512, F), ("A", 264, F), ("A64", 256, F), ("Ah", 256, B), ("Al", 256, B), ("DL", 264, F),
+    ("KX", 256, F), ("ZX", 256, B), ("ZS", 256, B), ("MX", 256, B), ("MK", 256, B), ("LV", 256, B), ("m16", 80, B),
+    ("M4", 256, B), ("Z4", 136, B), ("RES", 256, B), ("oK", 8, U), ("iq4", 16, B), ("dd", 128, B),
+    ("oW1", 256, U), ("ix", 256, B), ("iq16", 128, B), ("iqm", 16, B), ("Z", 144, B), ("M", 128 * len(MATS), B), ("Mf", 384, F),
+    ("Sel", 2048, B), ("DX", 256, F), ("MW", 1024, B), ("MWk", 128, B), ("MC", 592, B), ("tm", 64, F),
+    ("dW", 16, F), ("KD", 64, F), ("z0", 16, B), ("xz", 16, B), ("K0", 128, B),
+    ("GW", 1024, B), ("WS", 1024, B), ("oP", 64, U), ("oTQ", 128, U), ("PG", 4096, B),
+    ("NN", 4096, B), ("N1", 2048, B), ("sz", 72, B), ("T1", 64, B), ("TH", 128, B), ("dead", 64, B),
+    ("GS", 72, F), ("D2", 72, F), ("oW2", 32, U),
+    ("K", 128, F), ("dead2", 64, F), ("cum", 64, B), ("ones", 64, F), ("dK", 64, F), ("u0", 64, F),
+    ("oR", 64, U), ("step", 272, B), ("inv", 256, B), ("ngt", 8, F), ("oPP", 256, U), ("oTT", 256, U),
+    ("V", 1024, F), ("CW", WS, F), ("dO", 16, B),
+    ("sg", 272, B), ("sn", 256, B), ("f1", 256, B), ("G0", 256, B), ("d0", 256, B), ("t1", 256, B), ("t2", 256, B),
+    ("KS", 128, F), ("KT", 16, F), ("E", 576, B), ("YS", 592, B), ("oY", 2, U), ("y1", 16, F), ("x1", 16, F), ("x2", 16, F),
+    ("oXg", 16, U), ("oX2", 32, U), ("FV", 256, B), ("sv", 512, B), ("CS", 264, F), ("e1", 8, F), ("oE", 8, U),
+    ("Dp", 16, B), ("uo", 16, B), ("su", 64, U), ("lu", 64, U), ("lw", 512, B), ("so", 64, B), ("O", 160, B), ("o32", 32, F),
 ):
     SCRATCH[_n] = ("sbuf", [128, _c], _d)
 SCRATCH["TL"] = ("dram", [4, 128, 256], B)
@@ -211,9 +216,9 @@ def rank_program(g, core, T, topo):
 
     def ns(out, in_, r, more=(), k=None):
         for x in r.split():
-            if x in ("oX2", "oR") or x[:2] == "lu":
+            if x[:3] == "oX2" or x[:2] in ("lu", "oR", "oS"):
                 return 50 + in_.shape[1] * SCATTER, out, in_
-            if x[0] == "o" and x != "ones":
+            if x[0] == "o" and x not in ("ones", "o32"):
                 return 50 + out.shape[1] * GATHER, out, in_
         if k is None:
             k = 0.5 if all("16" in str(x.dtype) for x in (out, in_) + tuple(more)) else 1.0
@@ -254,9 +259,9 @@ def rank_program(g, core, T, topo):
         for k, (l, x) in enumerate(terms):
             mm1(out, l, x, k == 0, k == len(terms) - 1, r, w)
 
-    def dma(q, out, in_, r="", w=""):
+    def dma(q, out, in_, r="", w="", lat=2600.0):
         e = {"g": g, "y": g.sync, "a": g.scalar}[q]
-        op(q, lambda: e.dma_start(out, in_), r, w, "d", 60.0, 7500.0 if w in ("P0", "TX") else 4500.0 if w[:2] == "yt" else 2600.0)
+        op(q, lambda: e.dma_start(out, in_), r, w, "d", 60.0, lat)
 
     def iota(out, pat, base, cm, w, flt=False):
         if flt:
@@ -282,10 +287,19 @@ def rank_program(g, core, T, topo):
         src = T.cores[(rank + k) % N]
         ops.append(["r", "r", (sem, len(lanes(src, core, bulk))), [], w.split(), (0.0, 0.0, None)])
 
+    def fill(ap, n, c, w):
+        iota(ap, [[0, n]], c, 0, w, True)
+
+    def keep(out, in_, cmp, other, base, r, w):
+        op("g", lambda: g.affine_select(out, in_, [[1, 128]], cmp, other, base, -1), r, w)
+
     col = T.col
-    cR, cG, cG15, c4R, cM32, c256, c256b, cR1, cIs0, cN0, cB1, cB0, cP, c75, cSn, c64, cSg, cRn, cRf, cD, cSi = (col[:, k:k + 1] for k in range(21))
-    BO, LT, Id, A1, nBO, nI, B256, B8k, nB8k, I8k, B4k, Wm, S0, ShI, dOT, XO = (T.M[:, 128 * k:128 * k + 128] for k in range(len(MATS)))
+    (cR, cG, cG15, c4R, cM32, c256, c256b, cR1, cIs0, cN0, cB1, cG0, cP, c75, cSn, c64, cSg, cRn, cRf, cD, cSi, cX1, cE, cNs0, cW, cRm, cY,
+     cR4, cB4, cK) = (col[:, k:k + 1] for k in range(30))
+    (BO, LT, Id, A1, nBO, nI, B256, B8k, nB8k, I8k, nB4k, nI8k, nI8, S0, nS0, ShI, L0, Mx, dOT, XO
+     ) = (T.M[:, 128 * k:128 * k + 128] for k in range(len(MATS)))
     Idf, nIdf, S0f = (T.Mf[:, 128 * k:128 * k + 128] for k in range(3))
+    Z0 = T.Z[:, 15:143]
     P = [T.P0, T.P1, T.P2, T.P3]
     W = [T.W0, T.W1]
     Bk = [T["B%d" % t] for t in range(8)]
@@ -296,15 +310,35 @@ def rank_program(g, core, T, topo):
     def O(t, lo=0, hi=16):
         return T.O[:, 32 * t + 16 + lo:32 * t + 16 + hi]
 
+    def spread(out, k, n, r, w):
+        act(out, T.m16[:, 16 * k:16 * k + 16].indirect(T.orr[:, 0:n]), r=r + " orr", w=w)
+
+    def lanes_of(t):
+        lo, s0 = 128 * t, 64 * t
+        cp(T.G1[:, lo:lo + 128], T.cdi[:, 0:256].indirect(T.oa[:, 8 * t:8 * t + 8]), "cdi oa", "G1")
+        op("v", lambda: v.transpose(T.G2[:, lo:lo + 128], T.G1[:, lo:lo + 128]), "G1", "G2 G2b", cost=168.0)
+        (cp if t == 0 else act)(T.A[:, s0:s0 + 64], T.G2[:, lo:lo + 128].indirect(T.ob[:, 0:4]), r="G2 ob", w="A%d" % t)
+        tt(T.DL[:, s0 + 1:s0 + 64], T.A[:, s0 + 1:s0 + 64], T.A[:, s0:s0 + 63], sub, "A%d" % t, "DL%d" % t)
+        if t == 0:
+            ts(T.oW1[:, 0:64], T.DL[:, 1:65], 256.0, mn, r="DL0 DLp", w="oW10")
+        else:
+            ts(T.oW1[:, s0:s0 + 64], T.DL[:, s0 + 1:s0 + 65], 256.0, mn, c256, add, r="DL%d DLp c256" % t, w="oW1%d" % t)
+
+    def halves_of(t):
+        s0 = 64 * t
+        act(T.A64[:, s0:s0 + 64], T.A[:, s0:s0 + 64], bias=64.0, r="A%d" % t, w="A64%d" % t)
+        act(T.Ah[:, s0:s0 + 64], T.A[:, s0:s0 + 64], bias=64.0, r="A%d" % t, w="Ah%d" % t)
+        tt(T.Al[:, s0:s0 + 64], T.A64[:, s0:s0 + 64], T.Ah[:, s0:s0 + 64], sub, "A64%d Ah%d" % (t, t), "Al%d" % t)
+
     dma("y", T.cdi[:], T.cd[:], w="cdi")
     dma("a", T.witi[:], T.wit[:], w="witi")
-    dma("a", T.P0[:], T.pat[:], w="P0")
-    dma("y", T.TX[:, 0:4096], T.txt[:], w="TX")
-    dma("y", T.prbi[:], T.prb[:], w="prbi")
+    dma("y", T.P0[:], T.pat[:], w="P0", lat=5500.0)
+    dma("y", T.TX[:, 0:4096], T.txt[:], w="TX", lat=7500.0)
+    dma("a", T.prbi[:], T.prb[:], w="prbi")
     iota(T.ip[:, 0:1], [[0, 1]], 0, 1, "ip0")
     iota(T.ia[:], [[64, 4], [1, 4], [0, 2]], 0, 0, "ia")
-    iota(T.ib[:], [[32, 16]], 0, 0, "ib")
-    iota(T.iqm[:], [[0, 16], [1, 16]], 0, 0, "iqm", True)
+    iota(T.ib[:, 0:4], [[32, 4]], 0, 0, "ib")
+    iota(T.iqm[:], [[1, 16]], 0, 0, "iqm", True)
     iota(T.ix[:], [[1, 256]], 0, 0, "ix", True)
     iota(T.iq16[:], [[16, 8], [0, 16]], 0, 0, "iq16", True)
     ms(T.CT[:, 256:272], 0.0, "CTp")
@@ -315,53 +349,41 @@ def rank_program(g, core, T, topo):
     cp(cM32, T.ip[:, 2:3], "ip2", "cM32")
     cp(cR, T.ip[:, 1:2], "ip1", "cR")
     ts(T.oa[:], T.ia[:], c4R, add, r="ia c4R", w="oa")
-    ts(T.ob[:], T.ib[:], cM32, add, r="ib cM32", w="ob")
+    ts(T.ob[:, 0:4], T.ib[:, 0:4], cM32, add, r="ib cM32", w="ob")
+    ts(T.orr[:], T.ix[:, 0:64], 0.0, mul, cR, add, r="ix cR", w="orr")
     tt(cG, cP, cR, sub, "cP cR", "cG")
     ts(c256, cR, 256.0, mul, r="cR", w="c256")
     ts(c256b, cR, 256.0, mul, 256.0, add, r="cR", w="c256b")
-    ts(T.tm[:, 0:16], T.iqm[:, 0:16], cR, lt, -512.0, mul, r="iqm cR", w="tm0")
-    ts(T.tm[:, 16:32], T.iqm[:, 0:16], cR, eq, 256.0, mul, r="iqm cR", w="tm1")
-    ts(T.tm[:, 32:48], T.iqm[:, 0:16], 15.0, eq, -512.0, mul, r="iqm", w="tm2")
+    ts(T.tm[:, 0:16], T.iqm[:], cR, lt, -512.0, mul, r="iqm cR", w="tm0")
+    ts(T.tm[:, 16:32], T.iqm[:], cR, eq, 256.0, mul, r="iqm cR", w="tm1")
+    ts(T.tm[:, 32:48], T.iqm[:], 15.0, eq, -512.0, mul, r="iqm", w="tm2")
     tt(T.tm[:, 48:64], T.tm[:, 0:16], T.tm[:, 16:32], add, "tm0 tm1", "tm3")
     ms(T.CT[:, 0:1], 0.0, "CT0")
-    tt(T.MW[:, 0:16], T.tm[:, 48:64], T.tm[:, 32:48], add, "tm3 tm2", "MW")
-    n = 16
-    while n < 1024:
-        act(T.MW[:, n:2 * n], T.MW[:, 0:n], r="MW", w="MW")
-        n *= 2
-    ms(T.A[:, 256:264], 0.0, "Ap")
+    tt(T.m16[:, 0:16], T.tm[:, 48:64], T.tm[:, 32:48], add, "tm3 tm2", "m0")
+    spread(T.MW[:], 0, 64, "m0", "MW")
+    ms(T.A[:, 256:264], 0.0, "A4")
+    ms(T.DL[:, 64:257:64], BIG, "DLp")
     ts(cG15, cG, 15.0, add, r="cG", w="cG15")
     op("v", lambda: v.memset(T.Sel[:, 0:1024], 1.0), "", "Sel", cost=552.0)
     op("v", lambda: v.memset(T.Sel[:, 1024:2048], 1.0), "", "Selb", cost=552.0)
-    cp(T.G1[:], T.cdi[:, 0:256].indirect(T.oa[:, 0:32]), "cdi oa", "G1")
+    lanes_of(0)
     cp(T.CT[:, 1:256], T.witi[:, 1:256], "witi", "CT")
-    op("v", lambda: v.transpose(T.G2[:], T.G1[:]), "G1", "G2 G2b")
     ts(BO, T.iq16[:], cG, eq, r="iq16 cG", w="BO")
-    cp(T.A[:, 0:256], T.G2[:, 0:512].indirect(T.ob[:, 0:16]), "G2 G2b ob", "A")
     ts(Id, T.ix[:, 0:128], cP, eq, r="ix cP", w="Id")
-    tt(T.DL[:, 1:256], T.A[:, 1:256], T.A[:, 0:255], sub, "A", "DL")
     ts(T.Z[:], T.ix[:, 0:144], cG15, eq, r="ix cG15", w="Z")
-    op("v", lambda: v.memset(T.DL[:, 64:257:64], BIG), "DL", "DL")
     ts(cR1, cR, 1.0, add, r="cR", w="cR1")
-    ts(T.oW1[:, 0:64], T.DL[:, 1:65], 256.0, mn, r="DL", w="oW1a")
-    act(T.GW[:, 512:1024], T.CT[:, 0:272].indirect(T.oW1[:, 32:64]), r="CT CT0 CTp oW1a", w="GWb")
-    act(T.QB[:], T.DL[:, 1:257], scale=-1.0, bias=c256, r="DL c256", w="QB")
-    act(T.G2[:, 256:512], T.A[:, 0:256], bias=64.0, r="A", w="G2")
-    act(T.Ah[:], T.G2[:, 256:512], r="G2", w="Ah")
+    act(T.GW[:, 512:1024], T.CT[:, 0:272].indirect(T.oW1[:, 32:64]), r="CT CT0 CTp oW10", w="GWb")
     ts(cIs0, cR, 0.0, eq, r="cR", w="cIs0")
-    cp(T.GW[:, 0:512], T.CT[:, 0:272].indirect(T.oW1[:, 0:32]), "CT CT0 CTp oW1a", "GWa")
-
-    def fill(ap, n, c, w):
-        iota(ap, [[0, n]], c, 0, w, True)
-
-    def keep(out, in_, cmp, other, base, r, w):
-        op("g", lambda: g.affine_select(out, in_, [[1, 128]], cmp, other, base, -1), r, w)
-
+    cp(T.GW[:, 0:512], T.CT[:, 0:272].indirect(T.oW1[:, 0:32]), "CT CT0 CTp oW10", "GWa")
+    for dst, s, w in ((Idf, 1.0, "Idf"), (nIdf, -1.0, "nIdf"), (nI8, -8.0, "nI8")):
+        act(dst, Id, scale=s, r="Id", w=w)
+    act(T.K0[:, 0:64], T.ix[:, 0:64], scale=0.0, bias=256.0, r="ix", w="K0a")
+    act(T.K0[:, 64:128], T.ix[:, 0:64], scale=0.0, bias=c256b, r="ix c256b", w="K0b")
+    iota(T.iq4[:], [[0, 4], [1, 4]], 0, 0, "iq4", True)
+    fill(T.N1[:, 1024:1040], 16, 0, "N1p")
+    fill(T.sz[:, 0:1], 1, 0, "szp")
     fill(T.GS[:, 64:72], 8, int(BIG), "GSp")
-    fill(T.HS[:, 64:72], 8, 0, "HSp")
-    fill(T.THo[:], 72, 0, "THo")
-    fill(T.THe[:], 72, 0, "THe THa")
-    fill(T.N2[:, 512:528], 16, 0, "N2p")
+    fill(T.D2[:, 64:72], 8, int(BIG), "D2p")
     fill(T.ones[:], 64, 1, "ones")
     fill(T.step[:, 0:16], 16, 0, "stepp")
     fill(T.sg[:, 0:16], 16, 1, "sgp")
@@ -376,23 +398,36 @@ def rank_program(g, core, T, topo):
         if part == 0:
             op("g", lambda: g.affine_select(T.Sel[:], T.Sel[:], [[-1, 16], [-16, 8], [0, 16]], eq, 0.0, 0, 1), "Sel Selb", "Sel", cost=4400.0)
             ms(cRn, -ROUND, "cRn")
-            ms(cRf, ROUND - 64, "cRn")
+            ms(cRf, ROUND - 64, "cRf")
             keep(ShI, ShI, ne, -1.0, 0, "ShI", "ShI")
             fill(T.TX[:, 4096:TW], TW - 4096, 0, "TXp")
-            fill(T.CS[:], 264, 0, "CS")
-            iota(T.YS[:], [[-16, 8], [1, 128]], 0, 0, "YS", True)
-            fill(T.E[:], 1024, 0, "Ep")
+            fill(T.CS[:, 256:264], 8, 0, "CSp")
+            fill(T.YS[:, 576:592], 16, 0, "YSp")
+            fill(T.KT[:], 16, 0, "KT")
+            mm(T.B6[:, 0:131], [(Id, T.Z[:, 12 - 4 * k:143 - 4 * k]) for k in range(4)], "Id Z", "#6")
+            act(T.Z4[:, 0:131], T.B6[:, 0:131], scale=1 / 32, r="#6", w="Z4")
+            ts(T.ip[:, 3:4], T.ip[:, 1:2], 2, ALU.arith_shift_right, r="ip1", w="ip3")
+            cp(cR4, T.ip[:, 3:4], "ip3", "cR4")
+            ts(T.tm[:, 0:16], T.iq4[:], cR4, lt, -2.0, mul, r="iq4 cR4", w="tm0")
+            ts(T.tm[:, 16:32], T.iq4[:], cR4, eq, r="iq4 cR4", w="tm1")
+            tt(T.m16[:, 64:80], T.tm[:, 0:16], T.tm[:, 16:32], add, "tm0 tm1", "m4")
+            spread(T.M4[:], 4, 16, "m4", "M4 M4a M4b")
+            ts(cB4, cR4, 3.0, eq, -2.0, add, r="cR4", w="cB4")
             ts(cN0, cR, 0.0, gt, 256.0, mul, r="cR", w="cN0")
-            for dst, src, s in ((B256, BO, cN0), (nBO, BO, -1.0), (B8k, BO, BIG), (nB8k, BO, -BIG), (I8k, Id, BIG), (S0, BO, cIs0), (nI, Id, -1.0),
-                                (Idf, Id, 1.0), (nIdf, Id, -1.0), (Wm, BO, cR1), (S0f, BO, cIs0)):
-                act(dst, src, scale=s, r="BO Id cN0 cR1 cIs0", w="mats")
+            ts(cNs0, cIs0, -1.0, mul, r="cIs0", w="cNs0")
+            for dst, src, s, w in ((B256, BO, cN0, "B256"), (nBO, BO, -1.0, "nBO"), (B8k, BO, BIG, "B8k"), (nB8k, BO, -BIG, "nB8k"),
+                                   (I8k, Id, BIG, "I8k"), (S0, BO, cIs0, "S0"), (nI, Id, -1.0, "nI"), (S0f, BO, cIs0, "S0f"),
+                                   (nS0, BO, cNs0, "nS0"), (nB4k, BO, -HOLD / 16, "nB4k"), (nI8k, Id, -BIG, "nI8k")):
+                act(dst, src, scale=s, r="BO Id cN0 cIs0 cNs0", w=w)
         elif part == 1:
-            tt(T.Al[:], T.G2[:, 256:512], T.Ah[:], sub, "G2 Ah", "Al")
+            halves_of(0)
             ms(T.O[:, 15:160:32], 0.0, "Op")
             cp(O(0), T.prbi[:], "prbi", "O0")
             ts(T.iw[:, 0:1], T.ip[:, 0:1], 4, ALU.arith_shift_right, r="ip0", w="iw")
-            ts(T.orr[:], T.ix[:, 0:8], 0.0, mul, cR, add, r="ix cR", w="orr")
-            starts(0)
+            ts(T.ip[:, 4:5], T.ip[:, 1:2], 1, ALU.arith_shift_right, r="ip1", w="ip4")
+            ts(cK, T.ip[:, 4:5], 4.0, mul, 3.0, add, r="ip4", w="cK")
+            ts(T.oK[:], T.ix[:, 0:8], 32.0, mul, cK, add, r="ix cK", w="oK")
+            lanes_of(1)
         elif part == 2:
             ts(c64, cR, 64.0, mul, 1024.0, add, r="cR", w="c64")
             ms(c75, 7.5, "c75")
@@ -400,32 +435,57 @@ def rank_program(g, core, T, topo):
             ts(T.KD[:], T.ix[:, 0:64], c64, add, r="ix c64", w="KD")
             tt(A1, Id, LT, sub, "Id LT", "A1")
             ts(cB1, cR, -0.5, mul, -8.0, add, r="cR", w="cB1")
-            ts(cB0, cR, -0.5, mul, 0.5, add, r="cR", w="cB0")
-            act(T.half[:], T.ix[:], scale=0.0, bias=0.5, r="ix", w="mats")
-            act(T.KR[:], T.ix[:], scale=-32.0, r="ix", w="mats")
-        elif part == 3:
-            ts(T.MD[:], T.iqm[:], cR, eq, r="iqm cR", w="MD")
-            ts(T.MH[:], T.iqm[:], cR, lt, r="iqm cR", w="MH")
-        elif part == 4:
-            ts(T.MC[:], T.YS[:], cR, lt, r="YS cR", w="MC")
-            ts(c64, cR, 32.0, mul, 4128.0, add, r="cR", w="c64")
-            ts(T.dW[:], T.ix[:, 0:8], 512.0, mul, c64, add, r="ix c64", w="dW")
-            tt(T.MC[:, 0:1024:128], T.MC[:, 0:1024:128], T.dW[:], mul, "MC dW", "MC")
-            ts(cD, cR, 4112.0, add, r="cR", w="cD")
-            ts(cSi, cIs0, -2 / BIG, mul, 1 / BIG, add, r="cIs0", w="cSg")
-            ts(c4R, cR, -1.0, add, r="cR", w="c4R")
+            ts(T.m16[:, 16:32], T.iqm[:], 0.0, eq, -2 * HOLD, mul, r="iqm", w="m1")
+            spread(T.LV[:], 1, 16, "m1", "LV")
+            ts(T.tm[:, 0:16], T.iqm[:], cR, gt, -BIG, mul, r="iqm cR", w="tm0")
+            ts(T.tm[:, 16:32], T.iqm[:], cR, eq, HOLD, mul, r="iqm cR", w="tm1")
+            tt(T.tm[:, 32:48], T.tm[:, 0:16], T.tm[:, 16:32], add, "tm0 tm1", "tm2")
+            tt(T.m16[:, 32:48], T.tm[:, 32:48], T.m16[:, 16:32], add, "tm2 m1", "m2")
+            spread(T.MK[:], 2, 16, "m2", "MK")
+            ts(cRm, cR, -1.0, add, r="cR", w="cRm")
+            ts(T.tm[:, 0:16], T.iqm[:], cRm, eq, -2.0, mul, r="iqm cRm", w="tm0")
+            ts(T.tm[:, 16:32], T.iqm[:], cR, lt, r="iqm cR", w="tm1")
+            tt(T.m16[:, 48:64], T.tm[:, 0:16], T.tm[:, 16:32], add, "tm0 tm1", "m3")
+            spread(T.MX[:], 3, 16, "m3", "MX")
+            act(T.MWk[:], T.MW[:, 0:128], scale=32.0, r="MW", w="MWk")
+            ts(cSi, cIs0, -2 / BIG, mul, 1 / BIG, add, r="cIs0", w="cSi")
+            ts(cX1, cSi, HOLD + BIG, mul, r="cSi", w="cX1")
             ts(cSg, cIs0, -2 * BIG, mul, BIG, add, r="cIs0", w="cSg")
-            ts(T.MX[:], T.iqm[:], c4R, eq, -2.0, mul, r="iqm c4R", w="MX")
-            tt(T.MX[:], T.MX[:], T.MH[:], add, "MH MX", "MX")
-            ts(T.oW1[:, 64:256], T.DL[:, 65:257], 256.0, mn, c256, add, r="DL c256", w="oW1b")
+            ts(cD, cR, 4112.0, add, r="cR", w="cD")
+        elif part == 3:
+            for k in range(8):
+                ts(T.MC[:, TRI[k]:TRI[k + 1]], T.ix[:, 0:16 * k + 16], -16.0 * k, add, cR, lt, r="ix cR", w="MC%d" % k)
+            ts(cW, cR, 32.0, mul, 4128.0, add, r="cR", w="cW")
+            ts(T.dW[:], T.ix[:, 0:16], 512.0, mul, cW, add, r="ix cW", w="dW")
+            ts(T.dW[:, 0:1], T.dW[:, 0:1], cN0, mul, 1 / 256, mul, r="dW cN0", w="dW")
+            ts(cY, cR1, cR, mul, 8.0, mul, r="cR cR1", w="cY")
+            ts(T.e1[:, 0:1], cR, 568.0, add, r="cR", w="e10")
+            ts(T.oY[:, 0:1], cY, T.e1[:, 0:1], mn, r="cY e10", w="oY oS")
+            cp(T.MC[:, 0:592].indirect(T.oY[:, 0:1]), T.dW[:], "oS dW", " ".join("MC%d" % k for k in range(8)))
+            tt(L0, LT, Z0, add, "LT Z", "L0")
+            tt(Mx, Id, Z0, sub, "Id Z", "Mx")
+            ts(T.e1[:, 1:2], cR, -0.5, mul, 1.0, add, r="cR", w="e11")
+            ts(cG0, cIs0, -8.0, mul, T.e1[:, 1:2], add, r="cIs0 e11", w="cG0")
+            halves_of(1)
+        elif part == 4:
+            for t in (2, 3):
+                lanes_of(t)
+                halves_of(t)
         else:
             cp(T.e1[:, 4:5], T.witi[:, 0:1], "witi", "e14")
-            ts(T.xz[:], T.iqm[:, 0:16], cR, eq, T.e1[:, 4:5], mul, r="iqm cR e14", w="xz")
+            ts(T.xz[:], T.iqm[:], cR, eq, T.e1[:, 4:5], mul, r="iqm cR e14", w="xz")
             mm(T.B7[:, 160:176], [(BO, T.xz[:])], "BO xz", "#7")
             act(T.z0[:], T.B7[:, 160:176], r="#7", w="z0")
 
-    def count(out, buf, lo, n, r, w):
-        mm(out, [(T.Z[:, 15 - m:143 - m], buf[:, lo + m:lo + 16 * n:16]) for m in range(16)], r + " Z", w)
+    def count(out, buf, lo, n, r, w, fresh=True):
+        for m in range(16):
+            mm1(out, T.Z[:, 15 - m:143 - m], buf[:, lo + m:lo + 16 * n:16], fresh and m == 0, m == 15, r + " Z", w)
+
+    def quick(bk, lo, k0, k1, r):
+        mm(Bk[bk][:, 4 * k0:4 * k1], [(T.Z4[:, 3 - q:131 - q], T.N1[:, lo + 16 * k0 + q:lo + 16 * k1:4]) for q in range(4)], r + " Z4", "#%d" % bk)
+
+    def pick(bk, k0, k1, w):
+        scan(T.RES[:, 4 * k0:4 * k1], Bk[bk][:, 4 * k0:4 * k1], T.M4[:, 4 * k0:4 * k1], 0.0, mx, add, "#%d M4 M4a M4b" % bk, w)
 
     def expand(t):
         recv(1, "rt%d" % (t - 1), False, "TL%d" % (t - 1))
@@ -433,73 +493,68 @@ def rank_program(g, core, T, topo):
         op("g", lambda: g.indirect_dma_start(W[t % 2][:, 0:4096], None, TD[t % 2][:], IndirectOffsetOnAxis(ap=T.iw[:, 0:1], axis=0),
                                              bounds_check=7), "TD%d iw" % (t % 2), "W%d" % (t % 2), "d", 1700.0, 6000.0)
 
-    def rows(q, out_of, t, r, w):
-        if STEP_DMA:
-            dma(q, out_of(0, 8), W[t % 2][0:128:16, 0:4096], r, w)
-        else:
-            for k in range(8):
-                dma(q, out_of(k, k + 1), W[t % 2][16 * k:16 * k + 1, 0:4096], r, w + str(k))
-
-    def apply_u(t, between):
+    def apply_u(t, win, wk):
         b = 16 * (t - 1)
         recv(1, "ru%d" % (t - 1), False, "lu%d" % (t - 1))
         recv(1, "rv%d" % (t - 1), False, "lw%d" % (t - 1))
-        cp(W[t % 2][:, 0:WS].indirect(T.lu[:, b:b + 8]), T.lw[:, 8 * b:8 * b + 128],
-           "lu%d lw%d W%d W%dp" % (t - 1, t - 1, t % 2, t % 2), "W%d" % (t % 2))
-        if between:
-            flip_b(6, 14)
+        cp(win[:, 0:WS].indirect(T.lu[:, b:b + 8]), T.lw[:, 8 * b:8 * b + 128], "lu%d lw%d %s" % (t - 1, t - 1, wk), wk)
 
-    def equals(n, key, bk, out, spare, r, w):
-        tt(T.DM[:, 0:n], key, T.MD[:, 0:n], mul, bk + " MD", "DM")
-        scan(T.KS[:, n - 1::-1], T.MH[:, n - 1::-1], T.DM[:, n - 1::-1], 0.0, mul, add, "MH DM", "KS")
-        for k in range(8):
-            ts(T.E[:, 128 * k:144 * k + 16], T.B6[:, 0:16 * k + 16], T.KS[:, 16 * k:16 * k + 1], eq, r=bk + " KS Ep", w="E%d" % k)
-        scan(T.YS[:, 1023::-1], T.E[:, 1023::-1], T.MC[:, 1023::-1], 0.0, mx, mul, " ".join("E%d" % k for k in range(8)) + " MC", "YS")
-        tt(T.y1[:, 0:8], T.YS[:, 0:1024:128], T.KS[:, 0:n:16], mx, "YS KS", "y1")
-        ts(out, T.y1[:, 0:8], -0.5, add, r="y1", w=w)
-
-    def place0(lo, hi):
-        mm1(T.B3[:, lo:hi], S0f, T.G1[:, 8 + lo:8 + hi], False, hi == 256, "G1 mats", "#3")
+    def equals(lo, hi, x):
+        scan(T.KS[:, 16 * lo:16 * hi], T.B6[:, 16 * lo:16 * hi], T.MWk[:, 16 * lo:16 * hi], 0.0, mx, add, "#6 MWk", "KS" + x)
+        for k in range(lo, hi):
+            ts(T.E[:, TRI[k]:TRI[k + 1]], T.B6[:, 0:16 * k + 16], T.KS[:, 16 * k + 15:16 * k + 16], sub, BIG, eq, r="#6 KS" + x, w="E%d" % k)
+        back = slice(TRI[hi] - 1, TRI[lo] - 1 if lo else None, -1)
+        scan(T.YS[:, back], T.E[:, back], T.MC[:, back], 0.0, mx, mul, " ".join("E%d MC%d" % (k, k) for k in range(lo, hi)), "YS" + x)
 
     def starts(t):
         for p in range(16):
             s = T.Sel[:, 128 * p:128 * p + 128]
             mm(Bk[2 + p // 8][:, 64 * (p % 8):64 * (p % 8) + 64], [(s, T.Ah[:, 64 * t:64 * t + 64]), (s, T.Al[:, 64 * t:64 * t + 64])],
-               "Sel Ah Al", "#%d" % (2 + p // 8))
+               "Sel Ah%d Al%d" % (t, t), "#%d" % (2 + p // 8))
 
-    def places_a(t, part):
-        if part == 0:
-            scan(T.CS[:, 1:257], T.same[:], T.B7[:, 256:512], 0.0, mul, mx, "same #7", "CS")
-            cp(T.R[:], T.CS[:, 0:264].indirect(T.oE[:, 0:1]), "CS oE", "R")
-            return
-        ts(T.R2[:], T.R[:], 31, ALU.bitwise_and, r="R", w="R2")
-        ts(T.sl[:], T.R2[:], cR1, eq, r="R2 cR1", w="sl")
-        ts(T.le[:], T.R2[:], cR, gt, r="R2 cR", w="le")
-        tt(T.to[:], T.sl[:], O(t), mul, "sl O%d" % t, "to")
-        mm(T.B7[:, 128:144], [(ShI, O(t)), (T.Z[:, 15:143], T.to[:])], "ShI Z to O%d" % t, "#7")
+    def places(t):
+        st = T.step
+        mm(T.B1[:, 256:512], [(Id, T.G0[:]), (nS0, T.G0[:])], "Id nS0 G0", "#1")
+        mm1(T.B1[:, 0:256], S0, T.G0[:], True, False, "S0 G0", "#1")
+        for k, (l, x) in enumerate(((nBO, st[:, 17:272]), (BO, st[:, 16:271]), (nI, T.inv[:, 1:256]))):
+            mm1(T.B1[:, 0:255], l, x, False, k == 2, "nBO BO nI step inv", "#1")
+        act(T.d0[:], T.B1[:, 0:256], AF.Relu, r="#1", w="d0")
+        scan(T.CS[:, 255::-1], T.d0[:, 255::-1], T.B1[:, 511:255:-1], 0.0, mul, add, "d0 #1", "CS")
+        tt(T.uo[:], T.CS[:, 0:264].indirect(T.oE[:, 0:1]), T.Dp[:], mul, "CS CSp oE Dp", "uo")
+        mm(T.B7[:, 144:160], [(Id, O(t)), (Mx, T.uo[:])], "Id Mx uo O%d" % t, "#7")
+        so, land = (T.so[:, 16 * t:16 * t + 16], O(t + 1)) if t < 3 else (T.o32[:, 0:16], T.o32[:, 16:32])
+        act(so, T.B7[:, 144:160], r="#7", w="so%d" % t)
+        send(1, land, so, "ro%d" % t, False, "so%d" % t)
 
-    def places_b(t, part):
-        so = T.so[:, 16 * t:16 * t + 16]
-        if part == 0:
-            tt(T.uo[:], T.B7[:, 128:144], T.le[:], mul, "#7 le", "uo")
-            return
-        tt(so, T.uo[:], O(t), add, "uo O%d" % t, "so%d" % t)
-        send(1, O(t + 1), so, "ro%d" % t, False, "so%d" % t)
+    def held(lo, hi, x):
+        back = slice(hi - 1, lo - 1 if lo else None, -1)
+        scan(T.KX[:, back], T.B3[:, back], T.MK[:, back], -HOLD, mx, add, "#3 MK", "KX" + x)
+        tt(T.DX[:, lo:hi], T.KX[:, lo:hi], T.B3[:, lo:hi], sub, "#3 KX" + x, "DX" + x)
 
-    def flip_a():
-        x1, x2 = T.tm[:, 0:16], T.tm[:, 16:32]
-        ts(x1, T.KX[:, 0:256:16], BIG - 0.5, add, cSi, mul, r="KX cSg", w="tm0")
-        tt(T.EX[:], T.B0[:, 256:512], T.EX[:], lt, "#0 EX", "EX")
-        scan(T.GW[:, 255::-1], T.MX[:, 255::-1], T.EX[:, 255::-1], 0.0, mul, add, "EX MX", "GWa GWb")
-        tt(x2, T.GW[:, 0:256:16], x1, add, "GWa tm0", "tm1")
-        ts(T.oX[:], x2, cSg, mul, cD, mn, r="tm1 cSg cD", w="oX")
-        act(T.FV[:], T.TX[:, 0:TW].indirect(T.oX[:, 0:16]), scale=-1.0, bias=255.0, r="TX TXp oX", w="FV")
-        ts(T.oX2[:, 0:32:2], x2, cSg, mul, cD, mn, r="tm1 cSg cD", w="oX2")
+    def accepted(lo, hi, r):
+        mm(T.B3[:, 256 + lo:256 + hi], [(S0, T.LV[:, lo:hi]), (nI8k, T.inv[:, lo:hi]), (nB4k, T.sg[:, 16 + lo:16 + hi])],
+           "S0 LV nI8k inv nB4k " + r, "#3")
 
-    def flip_b(lo, hi):
+    def flip_a(lo, hi, x):
+        back = slice(hi - 1, lo - 1 if lo else None, -1)
+        k0, k1 = lo // 16, hi // 16
+        tt(T.ZX[:, lo:hi], T.B3[:, 256 + lo:256 + hi], T.DX[:, lo:hi], eq, "#3 DX" + x, "ZX" + x)
+        scan(T.ZS[:, back], T.MX[:, back], T.ZX[:, back], 0.0, mul, add, "MX ZX" + x, "ZS" + x)
+        tt(T.x2[:, k0:k1], T.ZS[:, lo:hi:16], T.x1[:, k0:k1], add, "x1 ZS" + x, "x2" + x)
+        ts(T.oX2[:, 2 * k0:2 * k1:2], T.x2[:, k0:k1], cSg, mul, cD, mn, r="cSg cD x2" + x, w="oX2" + x)
+
+    def flip_b(lo, hi, t):
         for k in range(lo, hi):
-            cp(T.TX[:, 0:TW].indirect(T.oX2[:, 2 * k:2 * k + 1]), T.FV[:, 16 * k:16 * k + 16], "FV oX2", "TX TXp")
+            x = ("ab"[k // 8] if t in SPLIT else "b")
+            cp(T.TX[:, 0:TW].indirect(T.oX2[:, 2 * k:2 * k + 1]), T.FV[:, 16 * k:16 * k + 16], "FV oX2" + x, "TX TXp")
 
+    def offsets1(t):
+        s0 = 64 * t
+        mm1(T.B4[:, 0:128], Id, T.K0[:], True, False, "Id K0a K0b", "#4")
+        mm1(T.B4[:, 0:64], Idf, T.A[:, s0:s0 + 64], False, False, "Idf A%d" % t, "#4")
+        mm1(T.B4[:, 64:128], nIdf, T.DL[:, s0 + 1:s0 + 65], False, False, "nIdf DLp DL%d" % t, "#4")
+
+    offsets1(0)
     for t in range(4):
         Pt, pk, ok = P[t], "P%d" % t, "O%d" % t
         if t == 0:
@@ -511,88 +566,91 @@ def rank_program(g, core, T, topo):
         scan(T.WS[:], T.GW[:], T.MW[:], 0.0, mx, add, "GWa GWb MW", "WS")
         w1 = T.WS[:, 15:1024:16]
         ts(T.oP[:], w1, c256b, add, r="WS c256b", w="oP")
-        tt(T.TQ[:, 0:64], w1, T.A[:, s0:s0 + 64], add, "WS A", "TQa")
-        tt(T.TQ[:, 64:128], w1, T.QB[:, s0:s0 + 64], add, "WS QB", "TQb")
+        act(T.sz[:, 1:65], w1, AF.Sign, bias=256.0, r="WS", w="sz")
+        mm1(T.B4[:, 0:64], Id, w1, False, False, "Id WS", "#4")
+        mm1(T.B4[:, 64:128], Id, w1, False, True, "Id WS", "#4")
+        cp(T.oTQ[:], T.B4[:, 0:128], "#4", "oTQ")
         if t > 0:
-            flip_b(14, 15)
-        ts(T.oTQ[:], T.TQ[:], 256.0, add, r="TQa TQb", w="oTQ")
-        if t > 0:
+            flip_b(14, 16, t - 1)
             recv(t, "rp%d" % t, True, pk)
         for h in range(8):
-            o = T.oP[:, 16 * h:16 * h + 16] if h < 4 else T.oTQ[:, 16 * h:16 * h + 16]
-            act(T.PG[:, 512 * h:512 * h + 256], Pt[:, 0:4096].indirect(o), r=pk + (" oP" if h < 4 else " oTQ"), w="PG%d" % h)
+            n = 16 if h < 7 else 15
+            o = T.oP[:, 16 * h:16 * h + 16] if h < 4 else T.oTQ[:, 16 * h:16 * h + n]
+            act(T.PG[:, 512 * h:512 * h + 16 * n], Pt[:, 0:4096].indirect(o), r=pk + (" oP" if h < 4 else " oTQ"), w="PG%d" % h)
         if t > 0:
-            send(1, T.TL[t], T.TS[t], "rt%d" % t, False, " ".join("TS%d%s" % (t, x) for x in [""] + list("01234567")))
-            flip_b(15, 16)
+            send(1, T.TL[t], T.TS[t], "rt%d" % t, False, "TS%d" % t)
         else:
             consts(0)
+        mm1(T.B0[:, 0:64], nI8, T.sz[:, 1:65], True, False, "nI8 sz", "#0")
+        act(T.M4[:, 3:256:4], T.sz[:, 0:64], scale=-0.25, bias=cB4, r="sz szp cB4 M4", w="M4a M4b")
         for h in range(8):
-            tt(T.NN[:, 256 * h:256 * h + 256], TXw.indirect(T.oTQ[:, 16 * (h % 4):16 * (h % 4) + 16]), T.PG[:, 512 * h:512 * h + 256], eq,
-               "TX oTQ PG%d" % h, "N%d%s" % (h // 2, "ab"[h % 2]))
-            if h % 4 == 3:
-                count(T.B0[:, 16 * (h - 3):16 * (h - 3) + 64], T.NN, 256 * (h - 3), 64,
-                      " ".join("N%d%s" % (k, x) for k in (h // 2 - 1, h // 2) for x in "ab"), "#0")
-        act(T.CW[:, 0:256], T.ix[:], scale=0.0, bias=cRf, r="ix cRn", w="CWa")
+            n, lo = 16 if h < 7 else 15, 256 * h + 16 * (h // 4)
+            tt(T.N1[:, lo:lo + 16 * n], TXw.indirect(T.oTQ[:, 16 * (h % 4):16 * (h % 4) + n]), T.PG[:, 512 * h:512 * h + 16 * n], eq,
+               "TX oTQ PG%d" % h, "Q%d" % h)
+            if h == 3:
+                count(T.B0[:, 0:64], T.N1, 0, 64, "Q0 Q1 Q2 Q3", "#0", False)
+                act(T.T1[:], T.B0[:, 0:64], AF.Sign, scale=-1.0, bias=-0.5, r="#0", w="T1")
+            if h > 3:
+                quick(1 if h < 7 else 6, 1024, (0, 17, 33, 49)[h - 4], (17, 33, 49, 64)[h - 4], "N1p Q%d" % h)
+        pick(1, 0, 49, "RESa")
+        pick(6, 49, 64, "RESb")
+        act(T.CW[:, 0:256], T.ix[:], scale=0.0, bias=cRf, r="ix cRf", w="CWa")
         act(T.CW[:, 3072:3328], T.ix[:], AF.Silu if t == 0 else AF.Identity, scale=0.0, r="ix", w="CWb")
-        if t > 0:
-            places_a(t - 1, 1)
-        ts(T.th[:, 0:64], w1, -256.0, gt, 8.0, mul, r="WS", w="tha")
-        ts(T.th[:, 64:128], w1, -256.0, gt, 8.0, mul, r="WS", w="thb")
         if t == 0:
             consts(1)
-        tt(T.lv[:], T.B0[:, 0:128], T.th[:], lt, "#0 tha thb", "lv")
-        if t > 0:
-            places_b(t - 1, 0)
-        tt(T.dead[:], T.lv[:, 0:64], T.lv[:, 63:127], mx, "lv", "dead")
-        if t > 0:
-            places_b(t - 1, 1)
-        expand(t + 1)
-        scan(T.GS[:, 1:64], T.dead[:, 0:63], T.DL[:, s0 + 1:s0 + 64], BIG, mul, add, "dead DL", "GS")
-        scan(T.HS[:, 63::-1], T.DL[:, s0 + 64:s0:-1], T.dead[:, 63::-1], 0.0, add, mul, "dead DL", "HS")
-        act(T.x1[:], T.dead[:], scale=1000.0, r="dead", w="x1")
-        tt(T.d2[:], T.HS[:, 2:65:2], T.GS[:, 2:65:2], add, "HS GS HSp GSp", "d2")
-        ts(T.oW2[:], T.d2[:], 256.0, mn, cw, add, r="d2 c256", w="oW2")
+            starts(0)
+        else:
+            recv(1, "ro%d" % (t - 1), False, ok)
+        X2 = T.B4[:, 128:192]
+        mm1(X2, Id, T.K0[:, 32:96], True, False, "Id K0a K0b", "#4")
+        mm1(X2[:, 0:32], Idf, T.A[:, s0 + 2:s0 + 65:2], False, False, "Idf A%d A%d" % (t, t + 1), "#4")
+        tt(T.dead[:], T.RES[:, 3:256:4], T.T1[:], lt, "RESa RESb T1", "dead")
+        if t < 3:
+            expand(t + 1)
+        scan(T.GS[:, 1:64], T.dead[:, 0:63], T.DL[:, s0 + 1:s0 + 64], BIG, mul, add, "dead DL%d" % t, "GS")
+        scan(T.D2[:, 63:0:-1], T.dead[:, 63:0:-1], T.GS[:, 63:0:-1], BIG, mul, mx, "dead GS", "D2")
+        ts(T.oW2[:], T.D2[:, 2:65:2], 256.0, mn, cw, add, r="D2 D2p c256", w="oW2")
         act(T.GW[:, 256:512], win.indirect(T.oW2[:, 16:32]), r=wk + " oW2", w="GWb")
         cp(T.GW[:, 0:256], win.indirect(T.oW2[:, 0:16]), wk + " oW2", "GWa")
-        tt(T.ai[:], T.A[:, s0 + 2:s0 + 65:2], T.GS[:, 2:65:2], sub, "A Ap GS GSp", "ai")
-        ts(T.qb[:], T.d2[:], -1.0, mul, c256, add, r="d2 c256", w="qb")
-        scan(T.WS[:, 0:512], T.GW[:, 0:512], T.MW[:, 0:512], 0.0, mx, add, "GWa GWb MW", "WS")
-        w2 = T.WS[:, 15:512:16]
-        ts(T.oP[:, 0:32], w2, c256b, add, r="WS c256b", w="oP")
-        tt(T.TQ[:, 0:32], w2, T.ai[:], add, "WS ai", "TQa")
-        tt(T.TQ[:, 32:64], w2, T.qb[:], add, "WS qb", "TQb")
-        ts(T.oTQ[:, 0:64], T.TQ[:, 0:64], 256.0, add, r="TQa TQb", w="oTQ")
-        for h in range(4):
-            n = 16 if h < 3 else 15
-            o = T.oP[:, 16 * h:16 * h + 16] if h < 2 else T.oTQ[:, 16 * h:16 * h + n]
-            act(T.PG[:, 512 * h:512 * h + 16 * n], Pt[:, 0:4096].indirect(o), r=pk + (" oP" if h < 2 else " oTQ"), w="PG%d" % h)
-        for h in range(4):
-            n, lo = 16 if h < 3 else 15, 256 * h + 16 * (h // 2)
-            tt(T.N2[:, lo:lo + 16 * n], TXw.indirect(T.oTQ[:, 16 * (h % 2):16 * (h % 2) + n]), T.PG[:, 512 * h:512 * h + 16 * n], eq,
-               "TX oTQ PG%d" % h, "N2%d" % h)
-        count(T.B0[:, 0:64], T.N2, 0, 64, "N20 N21 N22 N23 N2p", "#0")
-        th = T.THe[:, 33:65]
-        ts(th, w2, -256.0, gt, 8.0, mul, r="WS", w="THe")
-        if t > 0:
-            recv(1, "ro%d" % (t - 1), False, ok)
+        mm1(X2[:, 0:32], nIdf, T.GS[:, 2:65:2], False, False, "nIdf GS GSp", "#4")
+        mm1(X2[:, 32:64], nIdf, T.D2[:, 2:65:2], False, False, "nIdf D2 D2p", "#4")
+        for k, (lo, c, b) in enumerate(((1, 1, -1.0), (0, 1, -3.0), (65, 0, -3.0), (64, 0, -1.0))):
+            act(T.TH[:, lo:lo + 63:2], T.dead[:, c:64:2], scale=2.0, bias=b, r="dead", w="TH%d" % k)
         for p in range(16):
             act(T.V[:, p:1024:16], Bk[2 + p // 8][:, 64 * (p % 8):64 * (p % 8) + 64], bias=O(t, p, p + 1),
                 r="#%d %s" % (2 + p // 8, ok), w="V")
         tt(T.dO[:], O(t), O(t, -1, 15), sub, ok + " Op", "dO")
-        tt(T.th[:, 0:32], th, T.dead[:, 1:64:2], mul, "THe dead", "tha")
         tt(XO, T.dO[:, 0:16].indirect(T.orr[:, 0:8]), BO, mul, "dO orr BO", "XO")
-        tt(T.THo[:, 0:32], th, T.x1[:, 1:64:2], add, "THe x1", "THo")
-        tt(T.THo[:, 33:64], T.THe[:, 33:64], T.dead[:, 2:64:2], mul, "THe dead", "THo")
-        tt(T.THe[:, 0:32], T.th[:, 0:32], T.x1[:, 0:64:2], add, "tha x1", "THa")
+        scan(T.WS[:, 0:512], T.GW[:, 0:512], T.MW[:, 0:512], 0.0, mx, add, "GWa GWb MW", "WS")
+        w2 = T.WS[:, 15:512:16]
+        ts(T.oP[:, 0:32], w2, c256b, add, r="WS c256b", w="oP")
+        act(T.sz[:, 1:33], w2, AF.Sign, bias=256.0, r="WS", w="sz")
+        mm1(X2[:, 0:32], Id, w2, False, False, "Id WS", "#4")
+        mm1(X2[:, 32:64], Id, w2, False, True, "Id WS", "#4")
+        cp(T.oTQ[:, 0:64], X2, "#4", "oTQ")
+        for h in range(4):
+            n = 16 if h < 3 else 15
+            o = T.oP[:, 16 * h:16 * h + 16] if h < 2 else T.oTQ[:, 16 * h:16 * h + n]
+            act(T.PG[:, 512 * h:512 * h + 16 * n], Pt[:, 0:4096].indirect(o), r=pk + (" oP" if h < 2 else " oTQ"), w="PG%d" % h)
+        act(T.M4[:, 3:128:4], T.sz[:, 1:33], scale=-0.25, bias=cB4, r="sz cB4 M4", w="M4a")
+        act(T.M4[:, 131:256:4], T.sz[:, 0:32], scale=-0.25, bias=cB4, r="sz szp cB4 M4", w="M4b")
         mm(T.B5[:, 0:128], [(XO, Id)], "XO Id", "#5")
         act(dOT, T.B5[:, 0:128], r="#5", w="dOT")
+        mm(T.B7[:, 128:144], [(ShI, O(t))], "ShI " + ok, "#7")
+        act(T.Dp[:], T.B7[:, 128:144], r="#7", w="Dp")
+        for h in range(4):
+            n, lo = 16 if h < 3 else 15, 512 + 256 * h + 16 * (h // 2)
+            tt(T.N1[:, lo:lo + 16 * n], TXw.indirect(T.oTQ[:, 16 * (h % 2):16 * (h % 2) + n]), T.PG[:, 512 * h:512 * h + 16 * n], eq,
+               "TX oTQ PG%d" % h, "Q%d" % (h + 2))
+            quick(1 if h < 3 else 0, 512, (0, 16, 32, 49)[h], (16, 32, 49, 64)[h], "N1p Q%d" % (h + 2))
+        pick(1, 0, 49, "RESa")
+        pick(0, 49, 64, "RESb")
         if t == 0:
             consts(2)
         if t == 1:
             consts(5)
-        tt(T.K[:, 1:128:2], T.B0[:, 0:64], T.THo[:, 0:64], lt, "#0 THo", "Ko")
-        tt(T.K[:, 0:128:2], T.B0[:, 0:64], T.THe[:, 0:64], lt, "#0 THe THa", "Ke")
-        tt(T.dead2[:], T.K[:, 0:64], T.K[:, 64:128], mx, "Ko Ke", "dead2")
+        tt(T.K[:], T.RES[:, 0:256].indirect(T.oK[:]), T.TH[:], lt, "RESa RESb oK TH0 TH1 TH2 TH3", "K")
+        tt(T.dead2[:], T.K[:, 0:64], T.K[:, 64:128], mx, "K", "dead2")
         scan(T.cum[:], T.ones[:], T.dead2[:], 0.0, add, sub, "ones dead2", "cum")
         mm(T.B5[:, 128:129], [(LT, T.cum[:, 63:64])], "LT cum", "#5")
         mm(T.B6[:, 130:131], [(BO, T.cum[:, 63:64])], "BO cum", "#6")
@@ -604,7 +662,7 @@ def rank_program(g, core, T, topo):
         ts(st, T.ix[:], base, ge, r="ix #5", w="step")
         act(T.ngt[:, 0:1], T.B6[:, 130:131], bias=1.0, scale=-1.0, r="#6", w="ngt")
         act(T.inv[:], T.ix[:], AF.Relu, bias=T.ngt[:, 0:1], r="ix ngt", w="inv")
-        mm(T.B4[:, 256:512], [(dOT, st), (B256, st)], "dOT step mats", "#4")
+        mm(T.B4[:, 256:512], [(dOT, st), (B256, st)], "dOT step B256", "#4")
         k = 64 - SHARE
         act(T.CW[:, 3072:6144].indirect(T.oR[:, k:64]), T.V[:, 16 * k:1024], AF.Silu, bias=None, r="oR V", w="CWb")
         ts(T.CW[:, 0:3072].indirect(T.oR[:, 0:16]), T.V[:, 0:256], 1.0, mul, ROUND - 64, add, r="oR V", w="CWa")
@@ -618,116 +676,128 @@ def rank_program(g, core, T, topo):
         items(1)
         tt(T.G2[:, 8:136], T.CW[:, 0:128], T.CW[:, 3072:3200], add, "CWa CWb", "G2")
         tt(T.G2[:, 136:264], T.CW[:, 128:256], T.CW[:, 3200:3328], add, "CWa CWb", "G2b")
-        vv = T.B5[:, 256:512]
-        for k, (l, x) in enumerate(((dOT, st), (B8k, st), (nB8k, stp), (I8k, T.inv[:]))):
-            mm1(vv, l, x, k == 0, False, "dOT step stepp inv mats", "#5")
+        if t == 3:
+            recv(1, "rt3", False, "TL3")
+            dma("g", T.CW[0:128:16, 0:4096], T.TL[3], "TL3", "CWa CWb")
+        vv = {"a": (T.B5[:, 256:384], "#5"), "b": (T.B0[:, 256:384], "#0")}
+        for x, lo in (("a", 0), ("b", 128)):
+            for k, (l, y) in enumerate(((dOT, st), (B8k, st), (nB8k, stp), (I8k, T.inv[:]))):
+                mm1(vv[x][0], l, y[:, lo:lo + 128], k == 0, False, "dOT step stepp inv B8k nB8k I8k", vv[x][1])
         mm(T.B4[:, 0:256], [(dOT, st)], "dOT step", "#4")
-        mm1(T.B3[:, 0:256], S0, T.half[:], True, False, "mats", "#3")
-        mm1(T.B6[:, 0:128], B256, T.step[:, 16:272:2], True, False, "step mats", "#6")
-        mm1(T.B6[:, 0:128], S0, T.half[:, 0:128], False, False, "mats", "#6")
         ts(T.oTT[:, 0:128], T.G2[:, 8:136], -ROUND, add, r="G2", w="oTT0")
         ts(T.oTT[:, 128:256], T.G2[:, 136:264], -ROUND, add, r="G2b", w="oTT1")
         act(T.G1[:, 8:264], T.G2[:, 8:264], bias=cRn, r="G2 G2b cRn", w="G1")
-        mm1(vv, Idf, T.G1[:, 8:264], False, False, "G1 mats", "#5")
-        mm1(vv, nIdf, T.G1[:, 7:263], False, True, "G1 mats", "#5")
+        mm1(vv["a"][0], Idf, T.G1[:, 8:136], False, False, "G1 Idf", "#5")
+        mm1(vv["a"][0], nIdf, T.G1[:, 7:135], False, True, "G1 nIdf", "#5")
         items(2)
         items(3)
 
         def score(lo, hi, x):
             mm(T.B2[:, lo:hi], [(A1, T.sg[:, 16 + lo:16 + hi]), (nBO, T.sg[:, 15 + lo:15 + hi]), (nI, T.sn[:, lo:hi])],
-               "A1 mats sn sgp " + " ".join("sg%d" % k for k in range(hi // 64)), "#2")
+               "A1 nBO nI sgp sn" + x + " " + " ".join("sg%d" % k for k in range(hi // 64)), "#2")
             act(T.f1[:, lo:hi], T.B2[:, lo:hi], AF.Relu, bias=cB1, scale=0.5, r="#2 cB1", w="f1" + x)
 
         def named(lo, hi, x):
             fk = "f1" + x
-            tt(T.t1[:, lo:hi], T.B5[:, 256 + lo:256 + hi], T.f1[:, lo:hi], mul, "#5 " + fk, "t1" + x)
+            tt(T.t1[:, lo:hi], vv[x][0], T.f1[:, lo:hi], mul, vv[x][1] + " " + fk, "t1" + x)
             tt(T.t2[:, lo:hi], T.B4[:, lo:hi], T.f1[:, lo:hi], mul, "#4 " + fk, "t2" + x)
 
         def slots(lo, hi, x):
+            mm1(T.B6[:, lo // 2:hi // 2], B256, T.step[:, 16 + lo:16 + hi:2], True, False, "step B256", "#6")
             for k, (l, y) in enumerate(((BO, T.t1[:, lo:hi:2]), (BO, T.t1[:, lo + 1:hi:2]), (nBO, T.t2[:, lo:hi:2]), (nBO, T.t2[:, lo + 1:hi:2]))):
-                mm1(T.B6[:, lo // 2:hi // 2], l, y, False, hi == 256 and k == 3, "mats BO t1%s%s" % (x, " t2" + x if k > 1 else ""), "#6")
+                mm1(T.B6[:, lo // 2:hi // 2], l, y, False, k == 3, "nBO BO t1%s%s" % (x, " t2" + x if k > 1 else ""), "#6")
 
+        def old_text():
+            ts(T.oXg[:], T.KX[:, 0:256:16], HOLD, add, r="KXa KXb", w="oXg")
+            act(T.FV[:], T.TX[:, 0:TW].indirect(T.oXg[:]), scale=-1.0, bias=255.0, r="TX TXp oXg", w="FV")
+            act(T.x1[:], T.KX[:, 0:256:16], scale=cSi, bias=cX1, r="KXa KXb cSi cX1", w="x1")
 
+        split = t in SPLIT
         for h in range(4):
-            nk = "N%da N%da" % (2 * h, 2 * h + 1)
+            nk = "N%d N%d" % (2 * h, 2 * h + 1)
             for j in (2 * h, 2 * h + 1):
                 tt(T.NN[:, 512 * j:512 * j + 512], TXw.indirect(T.oTT[:, 32 * j:32 * j + 32]), T.PG[:, 512 * j:512 * j + 512], eq,
-                   "TX oTT%d PG%d" % (j // 4, j), "N%da N%db" % (j, j))
+                   "TX oTT%d PG%d" % (j // 4, j), "N%d" % j)
             if h == 1:
-                place0(0, 96)
+                mm1(T.B3[:, 0:128], S0f, T.G1[:, 8:136], True, True, "G1 S0f", "#3")
             if h == 2:
-                place0(96, 256)
-            bk = (0, 1, 7, 1)[h]
+                mm1(T.B3[:, 128:256], S0f, T.G1[:, 136:264], True, True, "G1 S0f", "#3")
+                if split:
+                    held(0, 128, "a")
+                    held(128, 256, "b")
+            bk = (6, 1, 7, 1)[h]
+            if h == 3:
+                tt(T.dd[:], T.G1[:, 136:264], T.G1[:, 135:263], sub, "G1", "dd")
             count(Bk[bk][:, 0:64], T.NN, 1024 * h, 64, nk, "#%d" % bk)
+            if h == 3:
+                mm1(vv["b"][0], Id, T.dd[:], False, True, "Id dd", "#0")
+                ops.insert(len(ops) - 11, ops.pop())
+                act(T.sn[:, 128:256], vv["b"][0], AF.Sign, bias=cSn, r="#0 cSn", w="snb")
             if h < 2:
                 items(2 * h + 4)
                 items(2 * h + 5)
             if h == 1:
-                act(T.sn[:], vv, AF.Sign, bias=cSn, r="#5 cSn", w="sn")
-            if h == 3:
-                act(T.tb[:], T.inv[:], bias=16.0, r="inv", w="tb")
+                act(T.sn[:, 0:128], vv["a"][0], AF.Sign, bias=cSn, r="#5 cSn", w="sna")
             act(T.sg[:, 16 + 64 * h:80 + 64 * h], Bk[bk][:, 0:64], AF.Sign, bias=c75, scale=-1.0, r="#%d c75" % bk, w="sg%d" % h)
             if h == 2:
                 score(0, 128, "a")
+                if split:
+                    accepted(0, 128, "sg0 sg1")
+                    old_text()
+                    flip_a(0, 128, "a")
         if t == 0:
             consts(3)
-        tt(T.DM[:], T.B3[:, 0:256], T.MD[:], mul, "#3 MD", "DM")
+        if not split:
+            held(0, 256, "b")
+            old_text()
         named(0, 128, "a")
-        scan(T.KX[:, 255::-1], T.MH[:, 255::-1], T.DM[:, 255::-1], 0.0, mul, add, "MH DM", "KX")
-        ts(T.e1[:, 0:1], T.cum[:, 63:64], base, add, 256.0, mn, r="cum #5", w="e10")
-        mm1(T.B0[:, 256:512], Id, T.tb[:], True, False, "tb Id", "#0")
-        score(128, 256, "b")
-        mm1(T.B0[:, 256:512], BO, T.sg[:, 16:272], False, True, "BO sg0 sg1 sg2 sg3", "#0")
         slots(0, 128, "a")
-        tt(T.EX[:], T.B3[:, 0:256], T.KX[:], eq, "#3 KX", "EX")
-        ts(T.e1[:, 2:3], T.e1[:, 0:1], base, le, 1000.0, mul, r="e10 #5", w="e12")
-        if t == 0:
-            consts(4)
-        flip_a()
+        score(128, 256, "b")
+        equals(0, 4, "a")
+        if split:
+            flip_b(0, 8, t)
+            accepted(128, 256, "sg2 sg3")
+            flip_a(128, 256, "b")
+        else:
+            accepted(0, 256, "sg0 sg1 sg2 sg3")
+            flip_a(0, 256, "b")
         named(128, 256, "b")
-        ts(T.oE[:, 0:1], T.e1[:, 0:1], T.e1[:, 2:3], add, 257.0, mn, r="e10 e12", w="oE")
         slots(128, 256, "b")
         b = 16 * t
         mm(T.B7[:, 0:128], [(BO, T.t1[:, 0:256:2]), (BO, T.t1[:, 1:256:2])], "BO t1a t1b", "#7")
         act(T.sv[:, 8 * b:8 * b + 128], T.B7[:, 0:128], r="#7", w="sv%d" % t)
+        mm(T.B2[:, 256:512], [(L0, T.sg[:, 16:272])], "L0 sg0 sg1 sg2 sg3", "#2")
+        act(T.G0[:], T.B2[:, 256:512], AF.Relu, bias=cG0, scale=-0.5, r="#2 cG0", w="G0")
         send(1, T.lw[:, 8 * b:8 * b + 128], T.sv[:, 8 * b:8 * b + 128], "rv%d" % t, False, "sv%d" % t)
-        mm(T.B2[:, 256:512], [(A1, T.sg[:, 16:272])], "A1 sg0 sg1 sg2 sg3", "#2")
-        act(T.f0[:], T.B2[:, 256:512], AF.Relu, bias=cB0, scale=0.5, r="#2 cB0", w="f0")
-        mm(T.B1[:, 256:512], [(BO, st), (nBO, stp)], "step stepp mats BO", "#1")
-        act(T.same[:], T.B1[:, 256:512], AF.Relu, bias=1.0, scale=-1.0, r="#1", w="same")
-        mm(T.B7[:, 256:512], [(B8k, T.f0[:]), (Wm, T.f0[:]), (S0, T.KR[:])], "f0 mats", "#7")
-        equals(128, T.B6[:, 0:128], "#6", T.su[:, b:b + 8], None, "", "su%d" % t)
+        act(cE, T.cum[:, 63:64], AF.Relu, bias=256.0, scale=-256.0, r="cum", w="cE")
+        ts(T.oE[:, 0:1], base, cE, add, 256.0, mn, r="cE #5", w="oE")
+        equals(4, 8, "b")
+        act(T.KT[:, 0:8], T.KS[:, 15:128:16], bias=BIG, r="KSa KSb", w="KT")
+        tt(T.y1[:], T.YS[:, 0:592].indirect(T.oY[:, 0:1]), T.KT[:], mx, "YSa YSb YSp oY KT", "y1")
+        cp(T.su[:, b:b + 8], T.y1[:, 0:8], "y1", "su%d" % t)
         send(1, T.lu[:, b:b + 8], T.su[:, b:b + 8], "ru%d" % t, False, "su%d" % t)
+        places(t)
         if t < 2:
             send(t + 2, P[t + 2][:], T.P0[:], "rp%d" % (t + 2), True, "P0")
+        if t == 0:
+            consts(4)
         if t < 3:
             starts(t + 1)
-            places_a(t, 0)
-            flip_b(0, 6)
-            apply_u(t + 1, True)
+            offsets1(t + 1)
+            flip_b(8 if split else 0, 10, t)
             wn, wnk = W[(t + 1) % 2], "W%d W%dp" % ((t + 1) % 2, (t + 1) % 2)
-            act(T.GW[:, 512:1024], wn[:, 0:WW].indirect(T.oW1[:, s0 + 96:s0 + 128]), r=wnk + " oW1b", w="GWb")
-            rows("y", lambda i, j, t=t: T.TS[t + 1, 16 * i:16 * j, :], t + 1, wnk, "TS%d" % (t + 1))
-            cp(T.GW[:, 0:512], wn[:, 0:WW].indirect(T.oW1[:, s0 + 64:s0 + 96]), wnk + " oW1b", "GWa")
+            apply_u(t + 1, wn, wnk)
+            flip_b(10, 14, t)
+            act(T.GW[:, 16 * WSH:1024], wn[:, 0:WW].indirect(T.oW1[:, s0 + 64 + WSH:s0 + 128]), r=wnk + " oW1%d" % (t + 1), w="GWb")
+            dma("y", T.TS[t + 1], wn[0:128:16, 0:4096], wnk, "TS%d" % (t + 1))
+            cp(T.GW[:, 0:16 * WSH], wn[:, 0:WW].indirect(T.oW1[:, s0 + 64:s0 + 64 + WSH]), wnk + " oW1%d" % (t + 1), "GWa")
         else:
-            places_a(3, 0)
-            mark = len(ops)
-            places_a(3, 1)
-            places_b(3, 0)
-            places_b(3, 1)
-            rest = ops[mark:]
-            del ops[mark:]
-            for k in range(16):
-                flip_b(k, k + 1)
-                while rest:
-                    ops.append(rest.pop(0))
-                    if ops[-1][0] == "v" and (not rest or rest[0][0] == "v"):
-                        break
-            dma("y", T.yt[:, 0:2048], T.TX[:, 0:2048], "TX", "yta")
-            dma("a", T.yt[:, 2048:4096], T.TX[:, 2048:4096], "TX", "ytb")
-            apply_u(4, False)
-            cp(T.W0[:, 0:4096:256], T.z0[:], "z0 W0", "W0")
-            rows("g", lambda i, j: T.yw[i:j, :], 4, "W0", "yw")
-            recv(1, "ro3", False, "O4")
-            dma("g", T.yo[:], O(4), "O4", "yo")
+            flip_b(8 if split else 0, 16, t)
+            dma("y", T.yt[:, 0:2048], T.TX[:, 0:2048], "TX", "yta", lat=4500.0)
+            dma("a", T.yt[:, 2048:4096], T.TX[:, 2048:4096], "TX", "ytb", lat=4500.0)
+            recv(1, "ro3", False, "o32")
+            dma("y", T.yo[:], T.o32[:, 16:32], "o32", "yo")
+            apply_u(4, T.CW, "CWa CWb")
+            cp(T.CW[:, 0:4096:256], T.z0[:], "z0 CWa", "CWa CWb")
+            dma("a", T.yw[:], T.CW[0:128:16, 0:4096], "CWa CWb", "yw")
     _emit(g, T, ops)

@@ -6,38 +6,46 @@ BIG = 8192.0
 HOLD = 65536.0
 WW = 4112
 WS = 8224
-TW = 4368
+TW = 4128
 ORDER = []
-TRIES = [(w, s, x, k) for w in (200.0, 230.0, 260.0) for s in (0.0, 50.0, 100.0, 150.0) for x in (280.0, 330.0) for k in range(24)]
-GATHER, SCATTER, LINK = 1.55, 3.8, 2500.0
+TRIES, MOVES = 16, 400
+PACES = ((0.83, 1.0, 1.9, 150.0, 110.0, 10.0, 400.0, 0.42), (0.87, 1.3, 3.1, 190.0, 128.0, 10.0, 700.0, 0.45),
+         (1.1, 1.0, 2.5, 170.0, 122.0, 10.0, 500.0, 0.72), (1.15, 1.7, 4.5, 240.0, 165.0, 20.0, 1100.0, 0.6))
+LINK = 2300.0
 ROUND = 1.5 * 2.0 ** 23
-SHARE = 30
-WSH = 32
-SPLIT = (3,)
+SHARE = 34
+WSH = 24
+SPLIT = (0, 1, 2, 3)
+EARLY = True
+ONE = True
+URGENT = None
+ALL8 = True
+DDV = True
+QUICK = QUICK2 = True
 PIECES = ("V",)
 TRI = [8 * k * (k + 1) for k in range(9)]
 
 F, B, I, U = "float32", "bfloat16", "int32", "uint16"
-MATS = "BO LT Id A1 nBO nI B256 B8k nB8k I8k nB4k nI8k nI8 S0 nS0 ShI L0 Mx dOT XO".split()
+MATS = "BO LT Id A1 nBO nI B256 B8k nB8k BN nB4k nS8k nI8 S0 nS0 ShI L0 Mx dOT dO0 XO nI4k Bx nBx".split()
 SCRATCH = {}
 for _n, _c, _d in (
     ("TX", TW, B), ("P0", 4096, B), ("P1", 4096, B), ("P2", 4096, B), ("P3", 4096, B),
     ("W0", WS, B), ("W1", WS, B), ("CT", 272, B), ("cdi", 256, I), ("witi", 256, I), ("prbi", 16, I),
-    ("ip", 8, I), ("iw", 8, I), ("col", 32, F), ("ia", 32, I), ("ib", 16, I), ("oa", 32, U), ("ob", 16, U), ("orr", 64, U),
-    ("G1", 512, F), ("G2", 512, F), ("A", 264, F), ("A64", 256, F), ("Ah", 256, B), ("Al", 256, B), ("DL", 264, F),
+    ("ip", 8, I), ("iw", 8, I), ("col", 40, F), ("ia", 32, I), ("ib", 16, I), ("oa", 32, U), ("ob", 16, U), ("orr", 64, U),
+    ("G1", 512, F), ("G2", 512, F), ("A", 264, F), ("A64", 256, F), ("Ah", 264, B), ("Al", 264, B), ("DL", 264, F), ("DB", 256, B),
     ("KX", 256, F), ("ZX", 256, B), ("ZS", 256, B), ("MX", 256, B), ("MK", 256, B), ("LV", 256, B), ("m16", 80, B),
-    ("M4", 256, B), ("Z4", 136, B), ("RES", 256, B), ("oK", 8, U), ("iq4", 16, B), ("dd", 128, B),
+    ("M4", 256, B), ("Z4", 136, B), ("RES", 256, B), ("oK", 8, U), ("iq4", 16, B), ("dd", 256, B), ("fine", 512, B),
     ("oW1", 256, U), ("ix", 256, B), ("iq16", 128, B), ("iqm", 16, B), ("Z", 144, B), ("M", 128 * len(MATS), B), ("Mf", 384, F),
     ("Sel", 2048, B), ("DX", 256, F), ("MW", 1024, B), ("MWk", 128, B), ("MC", 592, B), ("tm", 64, F),
-    ("dW", 16, F), ("KD", 64, F), ("z0", 16, B), ("xz", 16, B), ("K0", 128, B),
+    ("dW", 16, F), ("z0", 16, B), ("xz", 16, B), ("K0", 128, B),
     ("GW", 1024, B), ("WS", 1024, B), ("oP", 64, U), ("oTQ", 128, U), ("PG", 4096, B),
-    ("NN", 4096, B), ("N1", 2048, B), ("sz", 72, B), ("T1", 64, B), ("TH", 128, B), ("dead", 64, B),
-    ("GS", 72, F), ("D2", 72, F), ("oW2", 32, U),
-    ("K", 128, F), ("dead2", 64, F), ("cum", 64, B), ("ones", 64, F), ("dK", 64, F), ("u0", 64, F),
-    ("oR", 64, U), ("step", 272, B), ("inv", 256, B), ("ngt", 8, F), ("oPP", 256, U), ("oTT", 256, U),
+    ("NN", 4096, B), ("N1", 2048, B), ("sz", 72, B), ("T1", 128, B), ("Z2", 136, B), ("TH", 200, B), ("s2", 72, B), ("dead", 64, B),
+    ("GS", 72, B), ("D2", 72, B), ("oW2", 32, U),
+    ("K", 128, F), ("dead2", 64, F), ("cum", 64, B), ("ones", 256, B), ("dK", 64, F), ("u0", 64, F),
+    ("oR", 64, U), ("step", 272, B), ("oPP", 256, U), ("oTT", 256, U),
     ("V", 1024, F), ("CW", WS, F), ("dO", 16, B),
-    ("sg", 272, B), ("sn", 256, B), ("f1", 256, B), ("G0", 256, B), ("d0", 256, B), ("t1", 256, B), ("t2", 256, B),
-    ("KS", 128, F), ("KT", 16, F), ("E", 576, B), ("YS", 592, B), ("oY", 2, U), ("y1", 16, F), ("x1", 16, F), ("x2", 16, F),
+    ("sg", 352, B), ("sn", 256, B), ("G0", 256, B), ("d0", 256, B), ("t1", 256, B), ("t2", 256, B),
+    ("KS", 128, F), ("KT", 32, F), ("E", 576, B), ("YS", 576, B), ("oY", 8, U), ("y1", 32, F), ("x1", 16, F), ("x2", 16, F),
     ("oXg", 16, U), ("oX2", 32, U), ("FV", 256, B), ("sv", 512, B), ("CS", 264, F), ("e1", 8, F), ("oE", 8, U),
     ("Dp", 16, B), ("uo", 16, B), ("su", 64, U), ("lu", 64, U), ("lw", 512, B), ("so", 64, B), ("O", 160, B), ("o32", 32, F),
 ):
@@ -51,30 +59,51 @@ for _t in range(8):
 
 NDMA = 60
 SEMAPHORES = (["qv", "qa", "qt", "qg", "loc"] + ["d%d" % k for k in range(NDMA)]
-              + ["r%s%d" % (k, t) for k in "uvotp" for t in range(4)])
+              + ["r%s%d" % (k, t) for k in "uvwxotp" for t in range(4)])
 
 
-def _span(ops, deps, order, wake):
-    sent = {o[5][2]: j for j, o in enumerate(ops) if o[1] == "s"}
-    end, free = {}, {}
-    for j in order:
-        q, c = ops[j][0], ops[j][5]
-        if q == "r":
-            end[j] = end[sent[ops[j][2][0]]]
-            continue
-        s = max([free.get(q, 0.0)] + [end[i] + wake for i in deps[j]])
-        free[q], end[j] = s + c[0], s + c[1]
-    return max(end.values())
+def _place(ops, before, after, floor, rank):
+    n = len(ops)
+    left, ready, start, gaps = [len(p) for p in before], list(floor), [0.0] * n, {}
+    cand = [j for j in range(n) if not left[j]]
+    while cand:
+        j = min(cand, key=lambda x: rank[x])
+        cand.remove(j)
+        s, c = ready[j], ops[j][5][0]
+        if ops[j][0] != "r":
+            used = gaps.setdefault(ops[j][0], [])
+            lo, hi = 0, len(used)
+            while lo < hi:
+                mid = (lo + hi) // 2
+                if used[mid][1] <= s:
+                    lo = mid + 1
+                else:
+                    hi = mid
+            while lo < len(used) and s + c > used[lo][0]:
+                s = max(s, used[lo][1])
+                lo += 1
+            used.insert(lo, (s, s + c))
+        start[j] = s
+        for i, d in after[j]:
+            ready[i] = max(ready[i], s + d)
+            left[i] -= 1
+            if not left[i]:
+                cand.append(i)
+    return start
 
 
-def _order(ops, deps, WAKE, SLACK, LONG, seed):
+def _graph(ops, deps, WAKE):
     n = len(ops)
     pre = [[(i, ops[i][5][1] + WAKE) for i in d] for d in deps]
     last, sent = {}, {o[5][2]: j for j, o in enumerate(ops) if o[1] == "s"}
     for j, o in enumerate(ops):
         if o[1] == "r":
-            pre[j].append((sent[o[2][0]], ops[sent[o[2][0]]][5][1]))
-        elif o[0] not in "va" or o[5][0] > LONG or o[1] == "d":
+            pre[j].append((sent[o[2][2]], ops[sent[o[2][2]]][5][1]))
+        elif o[0] == "t":
+            if o[4][0] in last:
+                pre[j].append((last[o[4][0]], ops[last[o[4][0]]][5][0]))
+            last[o[4][0]] = j
+        elif o[0] not in "va":
             if o[0] in last:
                 pre[j].append((last[o[0]], ops[last[o[0]]][5][0]))
             last[o[0]] = j
@@ -82,49 +111,111 @@ def _order(ops, deps, WAKE, SLACK, LONG, seed):
     for j in range(n):
         for i, c in pre[j]:
             post[i].append((j, c))
-    left = [len(p) for p in pre]
-    tail, todo, stack = [0.0] * n, [len(p) for p in post], [j for j in range(n) if not post[j]]
-    while stack:
-        j = stack.pop()
-        tail[j] = max([ops[j][5][1]] + [c + tail[i] for i, c in post[j]])
-        for i, c in pre[j]:
-            todo[i] -= 1
-            if not todo[i]:
-                stack.append(i)
-    if seed:
-        tail = [x + (j * 2654435761 * seed + seed) % 1000003 % 240 for j, x in enumerate(tail)]
-    ready, free, order = [0.0] * n, {}, []
-    cand = {}
-    for j in range(n):
-        if not left[j]:
-            cand.setdefault(ops[j][0], []).append(j)
-    while len(order) < n:
-        best = None
-        for q, c in cand.items():
-            if not c:
+    return pre, post, [[(i, ops[j][5][0] + c - ops[i][5][0]) for i, c in pre[j]] for j in range(n)]
+
+
+def _order(timed, deps):
+    n = len(deps)
+    graphs = [_graph(ops, deps, m[3]) for ops, m in zip(timed, PACES)]
+    best, rank = None, list(range(n))
+    for k in range(TRIES):
+        ops, (pre, post, back) = timed[k % len(PACES)], graphs[k % len(PACES)]
+        if k >= len(PACES):
+            rank = best[2]
+        start = _place(ops, pre, post, [0.0] * n, rank)
+        late = _place(ops, post, back, [o[5][1] - o[5][0] for o in ops], [-start[j] - ops[j][5][0] for j in range(n)])
+        start = _place(ops, pre, post, [0.0] * n, [-late[j] - ops[j][5][0] for j in range(n)])
+        new = _polish(timed, deps, graphs[0], sorted(range(n), key=lambda j: (start[j], j)))
+        if best is None or new[0] < best[0]:
+            best = new
+    return best[1]
+
+
+def _polish(timed, deps, graph, order):
+    pre, post = [[i for i, c in p] for p in graph[0]], [[i for i, c in p] for p in graph[1]]
+    sent = {o[5][2]: j for j, o in enumerate(timed[0]) if o[1] == "s"}
+    queue = [o[0] for o in timed[0]]
+    need = [[sent[o[2][2]]] if o[1] == "r" else d for o, d in zip(timed[0], deps)]
+
+    def run(order, k):
+        ops, end, free, last, why = timed[k], [0.0] * len(order), {}, {}, [None] * len(order)
+        for j in order:
+            q, c, s, w = queue[j], ops[j][5], -1.0, PACES[k][3]
+            if q == "r":
+                end[j], why[j] = end[need[j][0]], (need[j][0], False)
                 continue
-            f = free.get(q, 0.0)
-            hot = max(c, key=lambda j: (max(f, ready[j]) + tail[j], -j))
-            bound = max(f, ready[hot]) + tail[hot] + SLACK
-            pick = hot
-            for j in sorted(c, key=lambda j: (max(f, ready[j]), -tail[j], j)):
-                if j == hot or max(f, ready[j]) + ops[j][5][0] + tail[hot] <= bound:
-                    pick = j
-                    break
-            s = max(f, ready[pick])
-            if best is None or s < best[0]:
-                best = (s, q, pick)
-        s, q, j = best
-        cand[q].remove(j)
-        order.append(j)
-        if q != "r":
-            free[q] = s + ops[j][5][0]
-        for i, c in post[j]:
-            ready[i] = max(ready[i], s + c)
-            left[i] -= 1
-            if not left[i]:
-                cand.setdefault(ops[i][0], []).append(i)
-    return order
+            for i in need[j]:
+                if end[i] + w > s:
+                    s, why[j] = end[i] + w, (i, False)
+            if free.get(q, 0.0) > s:
+                s, why[j] = free.get(q, 0.0), (last[q], True) if q in last else None
+            free[q], last[q], end[j] = s + c[0], j, s + c[1]
+        return end, why
+
+    def total(order):
+        runs = [run(order, k) for k in range(len(PACES))]
+        return sum(max(e) / m[4] for (e, w), m in zip(runs, PACES)), runs
+
+    def moves(order, k, end, why):
+        ops, w = timed[k], PACES[k][3]
+        start = [e - o[5][1] for e, o in zip(end, ops)]
+        ready = [max([end[i] + w for i in d] + [0.0]) for d in need]
+        own, full, nxt, line = [o[5][1] for o in ops], [0.0] * len(order), {}, {}
+        for j in reversed(order):
+            full[j] = max(own[j], ops[j][5][0] + nxt[queue[j]]) if queue[j] in nxt and queue[j] != "r" else own[j]
+            nxt[queue[j]] = full[j]
+            for i in need[j]:
+                own[i] = max(own[i], ops[i][5][1] + (0.0 if queue[j] == "r" else w) + full[j])
+        for j in order:
+            line.setdefault(queue[j], []).append(j)
+        at = {j: x for q in line for x, j in enumerate(line[q])}
+        j, out, span = end.index(max(end)), [], max(end)
+        while why[j]:
+            if why[j][1] and queue[j] in "vat":
+                ln, b = line[queue[j]], at[j]
+                for a, z, up in [(b - d, b, True) for d in range(1, 7)] + [(b - 1, b + d, False) for d in range(1, 4)]:
+                    if a < 0 or z + 1 >= len(ln):
+                        continue
+                    part = [ln[z]] + ln[a:z] if up else ln[a + 1:z + 1] + [ln[a]]
+                    s, far = start[ln[a - 1]] + ops[ln[a - 1]][5][0] if a else 0.0, 0.0
+                    for x in part:
+                        s = max(s, ready[x])
+                        far = max(far, s + own[x])
+                        s += ops[x][5][0]
+                    far = max(far, s + full[ln[z + 1]])
+                    if far < span - 8:
+                        out.append((span - far, ln[a], ln[z], up))
+            j = why[j][0]
+        return out
+
+    least, runs = total(order)
+    failed, n, mark = set(), 0, least
+    while n < MOVES:
+        cand = sorted((m for k in range(len(PACES)) for m in moves(order, k, *runs[k]) if m[1:] not in failed), reverse=True)
+        if not cand:
+            if least >= mark:
+                break
+            failed, mark = set(), least
+        for gain, i, j, up in cand[:6]:
+            if (i, j, up) in failed:
+                continue
+            failed.add((i, j, up))
+            place = {x: k for k, x in enumerate(order)}
+            move, todo, lo, hi = set(), [j if up else i], place[i], place[j]
+            while todo:
+                x = todo.pop()
+                if x not in move:
+                    move.add(x)
+                    todo.extend(y for y in (pre if up else post)[x] if lo <= place[y] <= hi)
+            if lo >= hi or (i in move and j in move):
+                continue
+            a, b = [x for x in order[lo:hi + 1] if x in move], [x for x in order[lo:hi + 1] if x not in move]
+            new = order[:lo] + (a + b if up else b + a) + order[hi + 1:]
+            span, r = total(new)
+            n += 1
+            if span < least:
+                order, least, runs = new, span, r
+    return least, order, [e - o[5][1] for e, o in zip(runs[1][0], timed[1])]
 
 
 def _emit(g, T, ops):
@@ -158,7 +249,10 @@ def _emit(g, T, ops):
         d.discard(j)
         deps.append(sorted(i for i in d if ops[i][1] != "s" and not (q == "t" and ops[i][0] == "t")))
     if not ORDER:
-        ORDER.extend(min((_order(ops, deps, *x) for x in TRIES), key=lambda o: _span(ops, deps, o, 180.0) + _span(ops, deps, o, 270.0)))
+        def timed_by(m):
+            busy = [o[5][0][0] + o[5][0][1] * m[o[5][0][2]] + (m[5] if o[0] in "va" and o[1] == "c" and not o[5][0][2] else 0) for o in ops]
+            return [o[:5] + [(c, c + o[5][1], o[5][2])] for o, c in zip(ops, busy)]
+        ORDER.extend(_order([timed_by(m) for m in PACES], deps))
     order = ORDER
     place = {j: n for n, j in enumerate(order)}
     ops = [ops[j][:5] for j in order]
@@ -176,7 +270,7 @@ def _emit(g, T, ops):
     tok, seen, ndma, loc = {}, {q: {} for q in Q}, 0, 0
     for j, (q, kind, fn, rd, wr) in enumerate(ops):
         if kind == "r":
-            tok[j] = fn
+            tok[j] = fn[:2]
             continue
         for i in deps[j]:
             s, n = tok[i]
@@ -206,23 +300,35 @@ def _emit(g, T, ops):
 
 def rank_program(g, core, T, topo):
     rank = T.rank_of(core)
+    helper = [min(h for h in topo.cores_of(c) if T.rank_of(h) is None and topo.die(h) == topo.die(c)
+                  and all(topo.may_write(h, d) for d in T.cores)) for c in T.cores]
     if rank is None:
+        if core in helper:
+            r = helper.index(core)
+            g.wait_ge(T.sem.rp0, len(topo.engines(T.cores[r], core)))
+            for k in range(1, N):
+                rid, pid, _ = topo.addr(T.cores[(r - k) % N])
+                g.remote_dma(T["P%d" % k][:], T.P0[:], T.sem["rp%d" % k], T.sem.loc, pid, rid, topo.mask(core, T.cores[(r - k) % N]))
+            g.wait_ge(T.sem.loc, sum(len(topo.engines(core, d)) for d in T.cores if d != T.cores[r]))
         return
     ops = []
     v, a, pe = g.vector, g.scalar, g.tensor
 
     def op(q, fn, r="", w="", kind="c", cost=400.0, lat=0.0, name=None):
-        ops.append([q, kind, fn, r.split(), w.split(), (cost, cost + lat, name)])
+        ops.append([q, kind, fn, r.split(), w.split(), (cost if isinstance(cost, tuple) else (cost, 0, 0), lat, name)])
 
-    def ns(out, in_, r, more=(), k=None):
+    def stays():
+        ops[-1][5] = ops[-1][5][:2] + ("stays",)
+
+    def ns(out, in_, r, more=(), k=None, fix=0):
         for x in r.split():
             if x[:3] == "oX2" or x[:2] in ("lu", "oR", "oS"):
-                return 50 + in_.shape[1] * SCATTER, out, in_
+                return (50 + fix, in_.shape[1], 2), out, in_
             if x[0] == "o" and x not in ("ones", "o32"):
-                return 50 + out.shape[1] * GATHER, out, in_
+                return (50 + fix, out.shape[1], 1), out, in_
         if k is None:
             k = 0.5 if all("16" in str(x.dtype) for x in (out, in_) + tuple(more)) else 1.0
-        return 40 + max(64, out.shape[1] * k), out, in_
+        return (fix, max(64, out.shape[1] * k), 0), out, in_
 
     def ts(out, in0, s1, o0, s2=None, o1=None, r="", w=""):
         c, out, in0 = ns(out, in0, r)
@@ -240,20 +346,20 @@ def rank_program(g, core, T, topo):
         op("v", lambda: v.tensor_copy(out, in_), r, w, cost=c)
 
     def ms(ap, c, w):
-        op("v", lambda: v.memset(ap, c), "", w, cost=104.0)
+        op("v", lambda: v.memset(ap, c), "", w, cost=(0, 64, 0))
 
     def scan(out, d0, d1, init, o0, o1, r="", w=""):
         op("v", lambda: v.tensor_tensor_scan(out, d0, d1, init, o0, o1), r, w, cost=ns(out, d0, "", (d1,))[0])
 
     def act(out, in_, fn=AF.Identity, bias=0.0, scale=1.0, r="", w=""):
-        c, out, in_ = ns(out, in_, r, k=1.0)
+        c, out, in_ = ns(out, in_, r, k=1.0, fix=18)
         if bias is None:
-            op("a", lambda: a.activation(out, in_, fn), r, w, cost=c + 20)
+            op("a", lambda: a.activation(out, in_, fn), r, w, cost=c)
         else:
-            op("a", lambda: a.activation(out, in_, fn, bias=bias, scale=scale), r, w, cost=c + 20)
+            op("a", lambda: a.activation(out, in_, fn, bias=bias, scale=scale), r, w, cost=c)
 
     def mm1(out, l, x, st, sp, r, w):
-        op("t", lambda: pe.matmul(out, l, x, st, sp), r, w, cost=10 + max(64, x.shape[1]) * (4 if "32" in str(x.dtype) else 1))
+        op("t", lambda: pe.matmul(out, l, x, st, sp), r, w, cost=(10, max(64, x.shape[1]) * (4 if "32" in str(x.dtype) else 1), 7))
 
     def mm(out, terms, r, w):
         for k, (l, x) in enumerate(terms):
@@ -265,27 +371,27 @@ def rank_program(g, core, T, topo):
 
     def iota(out, pat, base, cm, w, flt=False):
         if flt:
-            op("g", lambda: g.iota(out, pat, base, cm, allow_small_or_imprecise_dtypes=True), "", w, cost=130.0 + 2 * out.shape[1])
+            op("g", lambda: g.iota(out, pat, base, cm, allow_small_or_imprecise_dtypes=True), "", w, cost=(130, 2 * out.shape[1], 0))
         else:
-            op("g", lambda: g.iota(out, pat, base, cm), "", w, cost=130.0 + 2 * out.shape[1])
+            op("g", lambda: g.iota(out, pat, base, cm), "", w, cost=(130, 2 * out.shape[1], 0))
 
     def lanes(src, dst, bulk):
         e = topo.engines(src, dst)
-        return e[:len(e) // 2] if bulk else e[len(e) // 2:]
+        return e if bulk is None or bulk or ALL8 else e[len(e) // 2:]
 
     def send(k, out, in_, sem, bulk, r):
-        dst = T.cores[(rank - k) % N]
+        dst = helper[rank] if bulk else T.cores[(rank - k) % N]
         e = lanes(core, dst, bulk)
         rid, pid, _ = topo.addr(dst)
 
         def fn():
             g.remote_dma(out, in_, T.sem[sem], T.sem.loc, pid, rid, sum(1 << x for x in e))
             return len(e)
-        op("g", fn, r, "", "s", 500.0, 20000.0 if bulk else LINK, sem)
+        op("g", fn, r, "", "s", (0, 1, 6), LINK + {"u": 0, "v": 300, "p": 19000}.get(sem[1], 1200 * (sem != "ro3")), sem)
 
     def recv(k, sem, bulk, w):
-        src = T.cores[(rank + k) % N]
-        ops.append(["r", "r", (sem, len(lanes(src, core, bulk))), [], w.split(), (0.0, 0.0, None)])
+        src = (helper if bulk else T.cores)[(rank + k) % N]
+        ops.append(["r", "r", (sem, len(lanes(src, core, bulk)), "rp0" if bulk else sem), [], w.split(), ((0, 0, 0), 0.0, None)])
 
     def fill(ap, n, c, w):
         iota(ap, [[0, n]], c, 0, w, True)
@@ -295,8 +401,8 @@ def rank_program(g, core, T, topo):
 
     col = T.col
     (cR, cG, cG15, c4R, cM32, c256, c256b, cR1, cIs0, cN0, cB1, cG0, cP, c75, cSn, c64, cSg, cRn, cRf, cD, cSi, cX1, cE, cNs0, cW, cRm, cY,
-     cR4, cB4, cK) = (col[:, k:k + 1] for k in range(30))
-    (BO, LT, Id, A1, nBO, nI, B256, B8k, nB8k, I8k, nB4k, nI8k, nI8, S0, nS0, ShI, L0, Mx, dOT, XO
+     cR4, cB4, cK, cNz, cNzB, cS8k, cH0, cH1, cB5, cH0b, cH1b) = (col[:, k:k + 1] for k in range(38))
+    (BO, LT, Id, A1, nBO, nI, B256, B8k, nB8k, BN, nB4k, nS8k, nI8, S0, nS0, ShI, L0, Mx, dOT, dO0, XO, nI4k, Bx, nBx
      ) = (T.M[:, 128 * k:128 * k + 128] for k in range(len(MATS)))
     Idf, nIdf, S0f = (T.Mf[:, 128 * k:128 * k + 128] for k in range(3))
     Z0 = T.Z[:, 15:143]
@@ -316,9 +422,10 @@ def rank_program(g, core, T, topo):
     def lanes_of(t):
         lo, s0 = 128 * t, 64 * t
         cp(T.G1[:, lo:lo + 128], T.cdi[:, 0:256].indirect(T.oa[:, 8 * t:8 * t + 8]), "cdi oa", "G1")
-        op("v", lambda: v.transpose(T.G2[:, lo:lo + 128], T.G1[:, lo:lo + 128]), "G1", "G2 G2b", cost=168.0)
+        op("v", lambda: v.transpose(T.G2[:, lo:lo + 128], T.G1[:, lo:lo + 128]), "G1", "G2 G2b", cost=(40, 128, 0))
         (cp if t == 0 else act)(T.A[:, s0:s0 + 64], T.G2[:, lo:lo + 128].indirect(T.ob[:, 0:4]), r="G2 ob", w="A%d" % t)
         tt(T.DL[:, s0 + 1:s0 + 64], T.A[:, s0 + 1:s0 + 64], T.A[:, s0:s0 + 63], sub, "A%d" % t, "DL%d" % t)
+        ts(T.DB[:, s0:s0 + 64], T.DL[:, s0 + 1:s0 + 65], 256.0, mn, r="DL%d DLp" % t, w="DB%d" % t)
         if t == 0:
             ts(T.oW1[:, 0:64], T.DL[:, 1:65], 256.0, mn, r="DL0 DLp", w="oW10")
         else:
@@ -332,8 +439,8 @@ def rank_program(g, core, T, topo):
 
     dma("y", T.cdi[:], T.cd[:], w="cdi")
     dma("a", T.witi[:], T.wit[:], w="witi")
-    dma("y", T.P0[:], T.pat[:], w="P0", lat=5500.0)
-    dma("y", T.TX[:, 0:4096], T.txt[:], w="TX", lat=7500.0)
+    dma("y", T.P0[:], T.pat[:], w="P0", lat=5000.0)
+    dma("y", T.TX[:, 0:4096], T.txt[:], w="TX", lat=6800.0)
     dma("a", T.prbi[:], T.prb[:], w="prbi")
     iota(T.ip[:, 0:1], [[0, 1]], 0, 1, "ip0")
     iota(T.ia[:], [[64, 4], [1, 4], [0, 2]], 0, 0, "ia")
@@ -360,50 +467,58 @@ def rank_program(g, core, T, topo):
     tt(T.tm[:, 48:64], T.tm[:, 0:16], T.tm[:, 16:32], add, "tm0 tm1", "tm3")
     ms(T.CT[:, 0:1], 0.0, "CT0")
     tt(T.m16[:, 0:16], T.tm[:, 48:64], T.tm[:, 32:48], add, "tm3 tm2", "m0")
+    act(T.CW[:, 3072:3328], T.ix[:], AF.Silu, scale=0.0, r="ix", w="CWb")
+    ops[-1][5] = ((1360, 256, 0), 0.0, None)
     spread(T.MW[:], 0, 64, "m0", "MW")
-    ms(T.A[:, 256:264], 0.0, "A4")
+    ms(T.Ah[:, 256:264], 0.0, "Ah4")
+    ms(T.Al[:, 256:264], 0.0, "Al4")
     ms(T.DL[:, 64:257:64], BIG, "DLp")
     ts(cG15, cG, 15.0, add, r="cG", w="cG15")
-    op("v", lambda: v.memset(T.Sel[:, 0:1024], 1.0), "", "Sel", cost=552.0)
-    op("v", lambda: v.memset(T.Sel[:, 1024:2048], 1.0), "", "Selb", cost=552.0)
     lanes_of(0)
+    ms(T.G2[:, 7:8], ROUND + 4096, "G2")
+    halves_of(0)
     cp(T.CT[:, 1:256], T.witi[:, 1:256], "witi", "CT")
     ts(BO, T.iq16[:], cG, eq, r="iq16 cG", w="BO")
     ts(Id, T.ix[:, 0:128], cP, eq, r="ix cP", w="Id")
     ts(T.Z[:], T.ix[:, 0:144], cG15, eq, r="ix cG15", w="Z")
     ts(cR1, cR, 1.0, add, r="cR", w="cR1")
-    act(T.GW[:, 512:1024], T.CT[:, 0:272].indirect(T.oW1[:, 32:64]), r="CT CT0 CTp oW10", w="GWb")
+    act(T.GW[:, 16 * WSH:1024], T.CT[:, 0:272].indirect(T.oW1[:, WSH:64]), r="CT CT0 CTp oW10", w="GWb")
     ts(cIs0, cR, 0.0, eq, r="cR", w="cIs0")
-    cp(T.GW[:, 0:512], T.CT[:, 0:272].indirect(T.oW1[:, 0:32]), "CT CT0 CTp oW10", "GWa")
-    for dst, s, w in ((Idf, 1.0, "Idf"), (nIdf, -1.0, "nIdf"), (nI8, -8.0, "nI8")):
+    cp(T.GW[:, 0:256], T.CT[:, 0:272].indirect(T.oW1[:, 0:16]), "CT CT0 CTp oW10", "GWa")
+    if WSH > 16:
+        cp(T.GW[:, 256:16 * WSH], T.CT[:, 0:272].indirect(T.oW1[:, 16:WSH]), "CT CT0 CTp oW10", "GWc")
+    for dst, s, w in ((nI, -1.0, "nI"), (nI8, -8.0, "nI8")):
         act(dst, Id, scale=s, r="Id", w=w)
-    act(T.K0[:, 0:64], T.ix[:, 0:64], scale=0.0, bias=256.0, r="ix", w="K0a")
+    act(T.K0[:, 0:64], T.ix[:, 0:64], scale=0.0, bias=192.0, r="ix", w="K0a")
     act(T.K0[:, 64:128], T.ix[:, 0:64], scale=0.0, bias=c256b, r="ix c256b", w="K0b")
     iota(T.iq4[:], [[0, 4], [1, 4]], 0, 0, "iq4", True)
     fill(T.N1[:, 1024:1040], 16, 0, "N1p")
     fill(T.sz[:, 0:1], 1, 0, "szp")
+    fill(T.s2[:, 32:33], 1, 0, "s2p")
     fill(T.GS[:, 64:72], 8, int(BIG), "GSp")
     fill(T.D2[:, 64:72], 8, int(BIG), "D2p")
-    fill(T.ones[:], 64, 1, "ones")
+    op("v", lambda: v.memset(T.Sel[:, 0:1024], 1.0), "", "Sel", cost=(0, 512, 0))
+    op("v", lambda: v.memset(T.Sel[:, 1024:2048], 1.0), "", "Selb", cost=(0, 512, 0))
+    op("g", lambda: g.affine_select(T.Sel[:], T.Sel[:], [[-1, 16], [-16, 8], [0, 16]], eq, 0.0, 0, 1), "Sel Selb", "Sel", cost=(170, 4096, 0))
+    send(1, T.TL[0], T.CT[:, 0:256], "rt0", False, "CT CT0")
+    ops[-1][5] = ((3000, 1, 6),) + ops[-1][5][1:]
+    send(0, T.P0[:], T.P0[:], "rp0", True, "P0 TX")
+    keep(ShI, BO, eq, 0.0, -1, "BO", "ShI")
+    keep(ShI, ShI, ne, -1.0, 0, "ShI", "ShI")
+    keep(LT, BO, gt, 0.0, 0, "BO", "LT")
+    fill(T.ones[:], 256, 1, "ones")
     fill(T.step[:, 0:16], 16, 0, "stepp")
     fill(T.sg[:, 0:16], 16, 1, "sgp")
+    fill(T.sg[:, 272:288], 16, 0, "sgq")
+    fill(T.TX[:, 4096:4128], 32, 0, "TXp")
+    fill(T.CS[:, 256:264], 8, 0, "CSp")
+    fill(T.KT[:], 32, 0, "KT KTa KTb")
     fill(T.W1[:, 4096:WW], WW - 4096, 0, "W1p")
     fill(T.W0[:, 4096:WW], WW - 4096, 0, "W0p")
-    send(1, T.TL[0], T.CT[:, 0:256], "rt0", False, "CT CT0")
-    keep(LT, BO, gt, 0.0, 0, "BO", "LT")
-    keep(ShI, BO, eq, 0.0, -1, "BO", "ShI")
-    send(1, T.P1[:], T.P0[:], "rp1", True, "P0")
 
     def consts(part):
         if part == 0:
-            op("g", lambda: g.affine_select(T.Sel[:], T.Sel[:], [[-1, 16], [-16, 8], [0, 16]], eq, 0.0, 0, 1), "Sel Selb", "Sel", cost=4400.0)
-            ms(cRn, -ROUND, "cRn")
             ms(cRf, ROUND - 64, "cRf")
-            keep(ShI, ShI, ne, -1.0, 0, "ShI", "ShI")
-            fill(T.TX[:, 4096:TW], TW - 4096, 0, "TXp")
-            fill(T.CS[:, 256:264], 8, 0, "CSp")
-            fill(T.YS[:, 576:592], 16, 0, "YSp")
-            fill(T.KT[:], 16, 0, "KT")
             mm(T.B6[:, 0:131], [(Id, T.Z[:, 12 - 4 * k:143 - 4 * k]) for k in range(4)], "Id Z", "#6")
             act(T.Z4[:, 0:131], T.B6[:, 0:131], scale=1 / 32, r="#6", w="Z4")
             ts(T.ip[:, 3:4], T.ip[:, 1:2], 2, ALU.arith_shift_right, r="ip1", w="ip3")
@@ -413,14 +528,24 @@ def rank_program(g, core, T, topo):
             tt(T.m16[:, 64:80], T.tm[:, 0:16], T.tm[:, 16:32], add, "tm0 tm1", "m4")
             spread(T.M4[:], 4, 16, "m4", "M4 M4a M4b")
             ts(cB4, cR4, 3.0, eq, -2.0, add, r="cR4", w="cB4")
+            ts(cB5, cR4, 3.0, eq, -3.0, add, r="cR4", w="cB5")
+            mm(T.B7[:, 0:135], [(Id, T.Z[:, 8:143]), (Id, T.Z[:, 0:135])], "Id Z", "#7")
+            act(T.Z2[:, 0:135], T.B7[:, 0:135], r="#7", w="Z2")
+            ts(cH0, cR, 8.0, lt, -1.0, mul, r="cR", w="cH0")
+            ts(cH1, cR, 8.0, ge, -1.0, mul, r="cR", w="cH1")
             ts(cN0, cR, 0.0, gt, 256.0, mul, r="cR", w="cN0")
             ts(cNs0, cIs0, -1.0, mul, r="cIs0", w="cNs0")
-            for dst, src, s, w in ((B256, BO, cN0, "B256"), (nBO, BO, -1.0, "nBO"), (B8k, BO, BIG, "B8k"), (nB8k, BO, -BIG, "nB8k"),
-                                   (I8k, Id, BIG, "I8k"), (S0, BO, cIs0, "S0"), (nI, Id, -1.0, "nI"), (S0f, BO, cIs0, "S0f"),
-                                   (nS0, BO, cNs0, "nS0"), (nB4k, BO, -HOLD / 16, "nB4k"), (nI8k, Id, -BIG, "nI8k")):
-                act(dst, src, scale=s, r="BO Id cN0 cIs0 cNs0", w=w)
+            ts(cNz, cR, 0.0, gt, r="cR", w="cNz")
+            ts(cNzB, cR, 0.0, gt, -BIG, mul, r="cR", w="cNzB")
+            ts(cS8k, cIs0, -BIG, mul, r="cIs0", w="cS8k")
+            for dst, src, s, r, w in ((B256, BO, cN0, "cN0", "B256"), (nBO, BO, -1.0, "", "nBO"), (B8k, BO, BIG, "", "B8k"),
+                                      (nB8k, BO, cNzB, "cNzB", "nB8k"), (BN, BO, cNz, "cNz", "BN"), (S0, BO, cIs0, "cIs0", "S0"),
+                                      (Idf, Id, 1.0, "", "Idf"), (nIdf, Id, -1.0, "", "nIdf"), (S0f, BO, cIs0, "cIs0", "S0f"), (nS0, BO, cNs0, "cNs0", "nS0"),
+                                      (nB4k, BO, -HOLD / 16, "", "nB4k"), (nS8k, BO, cS8k, "cS8k", "nS8k"), (nI4k, Id, -4096.0, "", "nI4k"),
+                                      (Bx, BO, 256.0, "", "Bx"), (nBx, BO, -256.0, "", "nBx")):
+                act(dst, src, scale=s, r="BO Id " + r, w=w)
+            act(T.fine[:, 0:256], T.ix[:], scale=0.0, bias=1 / 256, r="ix", w="fine0")
         elif part == 1:
-            halves_of(0)
             ms(T.O[:, 15:160:32], 0.0, "Op")
             cp(O(0), T.prbi[:], "prbi", "O0")
             ts(T.iw[:, 0:1], T.ip[:, 0:1], 4, ALU.arith_shift_right, r="ip0", w="iw")
@@ -428,13 +553,18 @@ def rank_program(g, core, T, topo):
             ts(cK, T.ip[:, 4:5], 4.0, mul, 3.0, add, r="ip4", w="cK")
             ts(T.oK[:], T.ix[:, 0:8], 32.0, mul, cK, add, r="ix cK", w="oK")
             lanes_of(1)
+            halves_of(1)
         elif part == 2:
             ts(c64, cR, 64.0, mul, 1024.0, add, r="cR", w="c64")
             ms(c75, 7.5, "c75")
+            ts(cH0b, cR, 8.0, lt, 7.5, mul, r="cR", w="cH0b")
+            ts(cH1b, cR, 8.0, ge, 7.5, mul, r="cR", w="cH1b")
             ms(cSn, -255.5, "cSn")
-            ts(T.KD[:], T.ix[:, 0:64], c64, add, r="ix c64", w="KD")
+            ts(T.B6[:, 256:320], T.ix[:, 0:64], c64, add, r="ix c64", w="#6 dK")
+            tt(L0, LT, Z0, add, "LT Z", "L0")
             tt(A1, Id, LT, sub, "Id LT", "A1")
-            ts(cB1, cR, -0.5, mul, -8.0, add, r="cR", w="cB1")
+            act(A1, A1, scale=4096.0, r="A1", w="A1")
+            ts(cB1, cR, -4096.0, mul, -18 * 4096.0, add, r="cR", w="cB1")
             ts(T.m16[:, 16:32], T.iqm[:], 0.0, eq, -2 * HOLD, mul, r="iqm", w="m1")
             spread(T.LV[:], 1, 16, "m1", "LV")
             ts(T.tm[:, 0:16], T.iqm[:], cR, gt, -BIG, mul, r="iqm cR", w="tm0")
@@ -449,7 +579,7 @@ def rank_program(g, core, T, topo):
             spread(T.MX[:], 3, 16, "m3", "MX")
             act(T.MWk[:], T.MW[:, 0:128], scale=32.0, r="MW", w="MWk")
             ts(cSi, cIs0, -2 / BIG, mul, 1 / BIG, add, r="cIs0", w="cSi")
-            ts(cX1, cSi, HOLD + BIG, mul, r="cSi", w="cX1")
+            ts(cX1, cSi, HOLD + BIG - ROUND, mul, r="cSi", w="cX1")
             ts(cSg, cIs0, -2 * BIG, mul, BIG, add, r="cIs0", w="cSg")
             ts(cD, cR, 4112.0, add, r="cR", w="cD")
         elif part == 3:
@@ -460,13 +590,15 @@ def rank_program(g, core, T, topo):
             ts(T.dW[:, 0:1], T.dW[:, 0:1], cN0, mul, 1 / 256, mul, r="dW cN0", w="dW")
             ts(cY, cR1, cR, mul, 8.0, mul, r="cR cR1", w="cY")
             ts(T.e1[:, 0:1], cR, 568.0, add, r="cR", w="e10")
-            ts(T.oY[:, 0:1], cY, T.e1[:, 0:1], mn, r="cY e10", w="oY oS")
+            ts(T.oY[:, 0:1], cY, T.e1[:, 0:1], mn, r="cY e10", w="oS")
+            ts(T.oY[:, 2:3], cY, TRI[4] - 1.0, mn, r="cY", w="oY")
+            ts(T.e1[:, 2:3], cR, 64.0, mul, cY, add, r="cR cY", w="e12")
+            ts(T.oY[:, 4:5], T.e1[:, 2:3], float(TRI[4]), add, TRI[8] - 1.0, mn, r="e12 oY", w="oY")
+            ts(T.oY[:, 6:7], cY, TRI[8] - 1.0, mn, r="cY oY", w="oY")
             cp(T.MC[:, 0:592].indirect(T.oY[:, 0:1]), T.dW[:], "oS dW", " ".join("MC%d" % k for k in range(8)))
-            tt(L0, LT, Z0, add, "LT Z", "L0")
             tt(Mx, Id, Z0, sub, "Id Z", "Mx")
             ts(T.e1[:, 1:2], cR, -0.5, mul, 1.0, add, r="cR", w="e11")
             ts(cG0, cIs0, -8.0, mul, T.e1[:, 1:2], add, r="cIs0 e11", w="cG0")
-            halves_of(1)
         elif part == 4:
             for t in (2, 3):
                 lanes_of(t)
@@ -493,18 +625,43 @@ def rank_program(g, core, T, topo):
         op("g", lambda: g.indirect_dma_start(W[t % 2][:, 0:4096], None, TD[t % 2][:], IndirectOffsetOnAxis(ap=T.iw[:, 0:1], axis=0),
                                              bounds_check=7), "TD%d iw" % (t % 2), "W%d" % (t % 2), "d", 1700.0, 6000.0)
 
-    def apply_u(t, win, wk):
-        b = 16 * (t - 1)
-        recv(1, "ru%d" % (t - 1), False, "lu%d" % (t - 1))
-        recv(1, "rv%d" % (t - 1), False, "lw%d" % (t - 1))
-        cp(win[:, 0:WS].indirect(T.lu[:, b:b + 8]), T.lw[:, 8 * b:8 * b + 128], "lu%d lw%d %s" % (t - 1, t - 1, wk), wk)
+    def values(t, h):
+        lo = 128 * t
+        if h:
+            act(T.sv[:, lo:lo + 128], T.B7[:, 0:128], r="#7", w="sv%d" % t)
+            send(1, T.lw[:, lo:lo + 128], T.sv[:, lo:lo + 128], "rv%d" % t, False, "sv%d" % t)
+
+    def keys(t, h):
+        lo, x = 16 * t + 8 * h, "ab"[h]
+        if ONE:
+            if h:
+                lo = 16 * t
+                act(T.KT[:, 0:8], T.KS[:, 15:128:16], bias=BIG, r="KSa KSb", w="KTa")
+                tt(T.y1[:, 0:16], T.YS[:, 0:576].indirect(T.oY[:, 6:7]), T.KT[:, 0:16], mx, "YSa YSb YSc oY KT KTa", "y1")
+                cp(T.su[:, lo:lo + 8], T.y1[:, 0:8], "y1", "su%d" % t)
+                send(1, T.lu[:, lo:lo + 8], T.su[:, lo:lo + 8], "ru%d" % t, URGENT, "su%d" % t)
+            return
+        act(T.KT[:, 16 * h:16 * h + 4], T.KS[:, 64 * h + 15:64 * h + 64:16], bias=BIG, r="KS" + x, w="KT" + x)
+        tt(T.y1[:, 16 * h:16 * h + 16], T.YS[:, 0:TRI[4 * h + 4]].indirect(T.oY[:, 2 * h + 2:2 * h + 3]), T.KT[:, 16 * h:16 * h + 16], mx,
+           "YSa oY KT KT%s YS%s" % (x, x) + " YSc" * h, "y1" + x)
+        cp(T.su[:, lo:lo + 4], T.y1[:, 16 * h:16 * h + 4], "y1" + x, "su%d%d" % (t, h))
+        send(1, T.lu[:, lo:lo + 4], T.su[:, lo:lo + 4], "r%s%d" % ("xu"[h], t), (False, URGENT)[h], "su%d%d" % (t, h))
+
+    def apply_u(t, h, win, wk):
+        lo, n = (16 * t, 8) if ONE else (16 * t + 8 * h, 4)
+        if not h:
+            recv(1, "rv%d" % t, False, "lw%d" % t)
+        if h or not ONE:
+            recv(1, "r%s%d" % ("xu"[h], t), (False, URGENT)[h], "lu%d%d" % (t, h))
+            cp(win[:, 0:WS].indirect(T.lu[:, lo:lo + n]), T.lw[:, 8 * lo:8 * lo + 16 * n], "lu%d%d lw%d %s" % (t, h, t, wk), wk)
 
     def equals(lo, hi, x):
         scan(T.KS[:, 16 * lo:16 * hi], T.B6[:, 16 * lo:16 * hi], T.MWk[:, 16 * lo:16 * hi], 0.0, mx, add, "#6 MWk", "KS" + x)
         for k in range(lo, hi):
             ts(T.E[:, TRI[k]:TRI[k + 1]], T.B6[:, 0:16 * k + 16], T.KS[:, 16 * k + 15:16 * k + 16], sub, BIG, eq, r="#6 KS" + x, w="E%d" % k)
-        back = slice(TRI[hi] - 1, TRI[lo] - 1 if lo else None, -1)
-        scan(T.YS[:, back], T.E[:, back], T.MC[:, back], 0.0, mx, mul, " ".join("E%d MC%d" % (k, k) for k in range(lo, hi)), "YS" + x)
+        for i, j, w in ((lo, hi, "YSa"),) if not lo else ((lo, lo + 2, "YSb"), (lo + 2, hi, "YSc")):
+            back = slice(TRI[j] - 1, TRI[i] - 1 if i else None, -1)
+            scan(T.YS[:, back], T.E[:, back], T.MC[:, back], 0.0, mx, mul, " ".join("E%d MC%d" % (k, k) for k in range(i, j)), w)
 
     def starts(t):
         for p in range(16):
@@ -514,31 +671,44 @@ def rank_program(g, core, T, topo):
 
     def places(t):
         st = T.step
-        mm(T.B1[:, 256:512], [(Id, T.G0[:]), (nS0, T.G0[:])], "Id nS0 G0", "#1")
-        mm1(T.B1[:, 0:256], S0, T.G0[:], True, False, "S0 G0", "#1")
-        for k, (l, x) in enumerate(((nBO, st[:, 17:272]), (BO, st[:, 16:271]), (nI, T.inv[:, 1:256]))):
-            mm1(T.B1[:, 0:255], l, x, False, k == 2, "nBO BO nI step inv", "#1")
+        mm1(T.B1[:, 0:256], BN, st[:, 16:272], True, False, "BN step", "#1")
+        mm1(T.B1[:, 0:255], nBO, st[:, 17:272], False, False, "nBO step", "#1")
+        mm1(T.B1[:, 0:256], S0, T.G0[:], False, True, "S0 G0", "#1")
+        mm(T.B5[:, 256:512], [(Id, T.G0[:]), (nS0, T.G0[:])], "Id nS0 G0", "#5")
         act(T.d0[:], T.B1[:, 0:256], AF.Relu, r="#1", w="d0")
-        scan(T.CS[:, 255::-1], T.d0[:, 255::-1], T.B1[:, 511:255:-1], 0.0, mul, add, "d0 #1", "CS")
+        scan(T.CS[:, 255::-1], T.d0[:, 255::-1], T.B5[:, 511:255:-1], 0.0, mul, add, "d0 #5", "CS")
         tt(T.uo[:], T.CS[:, 0:264].indirect(T.oE[:, 0:1]), T.Dp[:], mul, "CS CSp oE Dp", "uo")
         mm(T.B7[:, 144:160], [(Id, O(t)), (Mx, T.uo[:])], "Id Mx uo O%d" % t, "#7")
         so, land = (T.so[:, 16 * t:16 * t + 16], O(t + 1)) if t < 3 else (T.o32[:, 0:16], T.o32[:, 16:32])
         act(so, T.B7[:, 144:160], r="#7", w="so%d" % t)
         send(1, land, so, "ro%d" % t, False, "so%d" % t)
 
-    def held(lo, hi, x):
-        back = slice(hi - 1, lo - 1 if lo else None, -1)
-        scan(T.KX[:, back], T.B3[:, back], T.MK[:, back], -HOLD, mx, add, "#3 MK", "KX" + x)
-        tt(T.DX[:, lo:hi], T.KX[:, lo:hi], T.B3[:, lo:hi], sub, "#3 KX" + x, "DX" + x)
+    def held():
+        scan(T.KX[:, 255::-1], T.B3[:, 255::-1], T.MK[:, 255::-1], -HOLD, mx, add, "#3 MK", "KX")
+        for lo, x in ((0, "a"), (128, "b")):
+            tt(T.DX[:, lo:lo + 128], T.KX[:, lo:lo + 128], T.B3[:, lo:lo + 128], sub, "#3 KX", "DX" + x)
+        ts(T.oXg[:], T.KX[:, 0:256:16], HOLD - ROUND, add, r="KX", w="oXg")
+        act(T.FV[:], T.TX[:, 0:TW].indirect(T.oXg[:]), scale=-1.0, bias=255.0, r="TX TXp oXg", w="FV")
+        act(T.x1[:], T.KX[:, 0:256:16], scale=cSi, bias=cX1, r="cSi cX1 KX", w="x1")
 
-    def accepted(lo, hi, r):
-        mm(T.B3[:, 256 + lo:256 + hi], [(S0, T.LV[:, lo:hi]), (nI8k, T.inv[:, lo:hi]), (nB4k, T.sg[:, 16 + lo:16 + hi])],
-           "S0 LV nI8k inv nB4k " + r, "#3")
+    def signs(out, l, lo, hi, back, stop, r, w, start=False):
+        mm1(out, l, T.sg[:, 16 + lo - back:16 + hi - back], start, stop and hi < 256, r + " sgp " + " ".join("sg%d" % k for k in range(hi // 64)), w)
+        if hi == 256:
+            mm1(out[:, 192 - lo:256 - lo], l, T.sg[:, 288 - back:352 - back], False, stop, r + " sgq sg4", w)
+
+    def accepted(lo, hi):
+        out, bk = lifted(lo, hi)
+        mm1(out, S0, T.LV[:, lo:hi], True, False, "S0 LV", bk)
+        mm1(out, nS8k, T.step[:, 16 + lo:16 + hi], False, False, "nS8k step", bk)
+        signs(out, nB4k, lo, hi, 0, True, "nB4k", bk)
+
+    def lifted(lo, hi):
+        return (T.B5[:, 384:512], "#5") if hi == 128 else (T.B3[:, 256 + lo:256 + hi], "#3")
 
     def flip_a(lo, hi, x):
         back = slice(hi - 1, lo - 1 if lo else None, -1)
         k0, k1 = lo // 16, hi // 16
-        tt(T.ZX[:, lo:hi], T.B3[:, 256 + lo:256 + hi], T.DX[:, lo:hi], eq, "#3 DX" + x, "ZX" + x)
+        tt(T.ZX[:, lo:hi], lifted(lo, hi)[0], T.DX[:, lo:hi], eq, lifted(lo, hi)[1] + " DX" + x + " DXa" * (not lo), "ZX" + x)
         scan(T.ZS[:, back], T.MX[:, back], T.ZX[:, back], 0.0, mul, add, "MX ZX" + x, "ZS" + x)
         tt(T.x2[:, k0:k1], T.ZS[:, lo:hi:16], T.x1[:, k0:k1], add, "x1 ZS" + x, "x2" + x)
         ts(T.oX2[:, 2 * k0:2 * k1:2], T.x2[:, k0:k1], cSg, mul, cD, mn, r="cSg cD x2" + x, w="oX2" + x)
@@ -550,9 +720,11 @@ def rank_program(g, core, T, topo):
 
     def offsets1(t):
         s0 = 64 * t
-        mm1(T.B4[:, 0:128], Id, T.K0[:], True, False, "Id K0a K0b", "#4")
-        mm1(T.B4[:, 0:64], Idf, T.A[:, s0:s0 + 64], False, False, "Idf A%d" % t, "#4")
-        mm1(T.B4[:, 64:128], nIdf, T.DL[:, s0 + 1:s0 + 65], False, False, "nIdf DLp DL%d" % t, "#4")
+        for bk, lo, n in ((4, 0, 16), (6, 16, 48)):
+            mm1(Bk[bk][:, 0:2 * n], Id, T.K0[:, 64 - n:64 + n], True, False, "Id K0a K0b", "#%d" % bk)
+            mm1(Bk[bk][:, 0:n], Id, T.Ah[:, s0 + lo:s0 + lo + n], False, False, "Id Ah%d" % t, "#%d" % bk)
+            mm1(Bk[bk][:, 0:n], Id, T.Al[:, s0 + lo:s0 + lo + n], False, False, "Id Al%d" % t, "#%d" % bk)
+            mm1(Bk[bk][:, n:2 * n], nI, T.DB[:, s0 + lo:s0 + lo + n], False, False, "nI DB%d" % t, "#%d" % bk)
 
     offsets1(0)
     for t in range(4):
@@ -563,39 +735,61 @@ def rank_program(g, core, T, topo):
             win, wk, cw = W[t % 2][:, 0:WW], "W%d W%dp" % (t % 2, t % 2), c256
         s0 = 64 * t
         TXw = T.TX[:, 0:4096]
-        scan(T.WS[:], T.GW[:], T.MW[:], 0.0, mx, add, "GWa GWb MW", "WS")
         w1 = T.WS[:, 15:1024:16]
-        ts(T.oP[:], w1, c256b, add, r="WS c256b", w="oP")
-        act(T.sz[:, 1:65], w1, AF.Sign, bias=256.0, r="WS", w="sz")
-        mm1(T.B4[:, 0:64], Id, w1, False, False, "Id WS", "#4")
-        mm1(T.B4[:, 64:128], Id, w1, False, True, "Id WS", "#4")
-        cp(T.oTQ[:], T.B4[:, 0:128], "#4", "oTQ")
+        for x, bk, lo, n, r in (("a", 4, 0, 16, "GWa"), ("b", 6, 16, 48, "GWb GWc")):
+            scan(T.WS[:, 16 * lo:16 * (lo + n)], T.GW[:, 16 * lo:16 * (lo + n)], T.MW[:, 0:16 * n], 0.0, mx, add, r + " MW", "WS" + x)
+            ts(T.oP[:, lo:lo + n], w1[:, lo:lo + n], c256b, add, r="c256b WS" + x, w="oP" + x)
+            mm1(Bk[bk][:, 0:n], Id, w1[:, lo:lo + n], False, False, "Id WS" + x, "#%d" % bk)
+            mm1(Bk[bk][:, n:2 * n], Id, w1[:, lo:lo + n], False, True, "Id WS" + x, "#%d" % bk)
+            cp(T.oTQ[:, 2 * lo:2 * (lo + n)], Bk[bk][:, 0:2 * n], "#%d" % bk, "oTQ" + x)
+        act(T.sz[:, 1:65], w1, AF.Sign, bias=256.0, r="WSa WSb", w="sz")
         if t > 0:
             flip_b(14, 16, t - 1)
             recv(t, "rp%d" % t, True, pk)
-        for h in range(8):
-            n = 16 if h < 7 else 15
-            o = T.oP[:, 16 * h:16 * h + 16] if h < 4 else T.oTQ[:, 16 * h:16 * h + n]
-            act(T.PG[:, 512 * h:512 * h + 16 * n], Pt[:, 0:4096].indirect(o), r=pk + (" oP" if h < 4 else " oTQ"), w="PG%d" % h)
+        turn = (0, 4, 1, 2, 3, 5, 6, 7)
+        for h in turn:
+            n, x = 16 if h < 7 else 15, "ab"[h % 4 > 0]
+            lo = 16 if h == 4 else 16 * h
+            o = T.oP[:, lo:lo + 16] if h < 4 else T.oTQ[:, lo:lo + n]
+            act(T.PG[:, 512 * h:512 * h + 16 * n], Pt[:, 0:4096].indirect(o), r=pk + (" oP" if h < 4 else " oTQ") + x, w="PG%d" % h)
         if t > 0:
             send(1, T.TL[t], T.TS[t], "rt%d" % t, False, "TS%d" % t)
         else:
             consts(0)
-        mm1(T.B0[:, 0:64], nI8, T.sz[:, 1:65], True, False, "nI8 sz", "#0")
-        act(T.M4[:, 3:256:4], T.sz[:, 0:64], scale=-0.25, bias=cB4, r="sz szp cB4 M4", w="M4a M4b")
-        for h in range(8):
-            n, lo = 16 if h < 7 else 15, 256 * h + 16 * (h // 4)
-            tt(T.N1[:, lo:lo + 16 * n], TXw.indirect(T.oTQ[:, 16 * (h % 4):16 * (h % 4) + n]), T.PG[:, 512 * h:512 * h + 16 * n], eq,
-               "TX oTQ PG%d" % h, "Q%d" % h)
-            if h == 3:
-                count(T.B0[:, 0:64], T.N1, 0, 64, "Q0 Q1 Q2 Q3", "#0", False)
-                act(T.T1[:], T.B0[:, 0:64], AF.Sign, scale=-1.0, bias=-0.5, r="#0", w="T1")
+        if QUICK:
+            act(T.M4[:, 3:256:4], T.sz[:, 0:64], scale=-0.25, bias=cB5, r="sz szp cB5 M4", w="M4a M4b")
+            ts(T.T1[:, 0:128:2], w1, -256.0, gt, r="WSa WSb", w="T10")
+            act(T.T1[:, 1:128:2], w1, AF.Sign, bias=256.0, r="WSa WSb", w="T11")
+        else:
+            mm1(T.B0[:, 0:64], nI8, T.sz[:, 1:65], True, False, "nI8 sz", "#0")
+            mm1(T.B1[:, 0:64], nI8, T.sz[:, 0:64], True, False, "nI8 sz szp", "#1")
+        for h in turn:
+            n, lo, y = 16 if h < 7 else 15, 256 * h + 16 * (h // 4), 16 * (h % 4) + 16 * (h % 4 > 0)
+            tt(T.N1[:, lo:lo + 16 * n], TXw.indirect(T.oTQ[:, y:y + n]), T.PG[:, 512 * h:512 * h + 16 * n], eq,
+               "TX PG%d oTQ%s" % (h, "ab"[h % 4 > 0]), "Q%d" % h)
+            if not QUICK:
+                if h == 3:
+                    count(T.B0[:, 0:64], T.N1, 0, 64, "Q0 Q1 Q2 Q3", "#0", False)
+                    act(T.T1[:, 64:128], T.B0[:, 0:64], AF.Relu, scale=-100.0, r="#0", w="T1")
+                if h == 7:
+                    count(T.B1[:, 0:64], T.N1, 1024, 64, "Q4 Q5 Q6 Q7 N1p", "#1", False)
+                continue
+            if h in (1, 3):
+                lo = 32 * (h - 1)
+                mm1(T.B0[:, lo:lo + 64], nI8, T.T1[:, lo:lo + 64], True, False, "nI8 T10 T11", "#0")
+                for q in range(8):
+                    mm1(T.B0[:, lo:lo + 64], T.Z2[:, 7 - q:135 - q], T.N1[:, 8 * lo + q:8 * lo + 512:8], False, q == 7, "Z2 Q%d Q%d" % (h - 1, h), "#0")
             if h > 3:
-                quick(1 if h < 7 else 6, 1024, (0, 17, 33, 49)[h - 4], (17, 33, 49, 64)[h - 4], "N1p Q%d" % h)
-        pick(1, 0, 49, "RESa")
-        pick(6, 49, 64, "RESb")
+                quick(1 if h < 7 else 7, 1024, (0, 17, 33, 49)[h - 4], (17, 33, 49, 64)[h - 4], "N1p Q%d" % h)
+        if QUICK:
+            for j, c in enumerate((cH0, cH1)):
+                act(T.TH[:, 64 * j:64 * j + 64], T.B0[:, j:128:2], AF.Sign, scale=c, bias=-0.5, r="#0 cH0 cH1", w="TH%d TH%d" % (2 * j, 2 * j + 1))
+            mm(T.B0[:, 128:192], [(Id, T.TH[:, 0:64]), (Id, T.TH[:, 64:128])], "Id TH0 TH1 TH2 TH3", "#0")
+            pick(1, 0, 49, "RESa")
+            pick(7, 49, 64, "RESb")
         act(T.CW[:, 0:256], T.ix[:], scale=0.0, bias=cRf, r="ix cRf", w="CWa")
-        act(T.CW[:, 3072:3328], T.ix[:], AF.Silu if t == 0 else AF.Identity, scale=0.0, r="ix", w="CWb")
+        if t > 0:
+            act(T.CW[:, 3072:3328], T.ix[:], scale=0.0, r="ix", w="CWb")
         if t == 0:
             consts(1)
             starts(0)
@@ -603,70 +797,96 @@ def rank_program(g, core, T, topo):
             recv(1, "ro%d" % (t - 1), False, ok)
         X2 = T.B4[:, 128:192]
         mm1(X2, Id, T.K0[:, 32:96], True, False, "Id K0a K0b", "#4")
-        mm1(X2[:, 0:32], Idf, T.A[:, s0 + 2:s0 + 65:2], False, False, "Idf A%d A%d" % (t, t + 1), "#4")
-        tt(T.dead[:], T.RES[:, 3:256:4], T.T1[:], lt, "RESa RESb T1", "dead")
+        mm1(X2[:, 0:32], Id, T.Ah[:, s0 + 2:s0 + 65:2], False, False, "Id Ah%d Ah%d" % (t, t + 1), "#4")
+        mm1(X2[:, 0:32], Id, T.Al[:, s0 + 2:s0 + 65:2], False, False, "Id Al%d Al%d" % (t, t + 1), "#4")
+        if QUICK:
+            tt(T.dead[:], T.RES[:, 3:256:4], T.B0[:, 128:192], lt, "RESa RESb #0", "dead")
+        else:
+            tt(T.dead[:], T.B1[:, 0:64], T.T1[:, 64:128], lt, "#1 T1", "dead")
         if t < 3:
             expand(t + 1)
         scan(T.GS[:, 1:64], T.dead[:, 0:63], T.DL[:, s0 + 1:s0 + 64], BIG, mul, add, "dead DL%d" % t, "GS")
         scan(T.D2[:, 63:0:-1], T.dead[:, 63:0:-1], T.GS[:, 63:0:-1], BIG, mul, mx, "dead GS", "D2")
         ts(T.oW2[:], T.D2[:, 2:65:2], 256.0, mn, cw, add, r="D2 D2p c256", w="oW2")
-        act(T.GW[:, 256:512], win.indirect(T.oW2[:, 16:32]), r=wk + " oW2", w="GWb")
+        act(T.GW[:, 256:512], win.indirect(T.oW2[:, 16:32]), r=wk + " oW2", w="GWb GWc")
         cp(T.GW[:, 0:256], win.indirect(T.oW2[:, 0:16]), wk + " oW2", "GWa")
-        mm1(X2[:, 0:32], nIdf, T.GS[:, 2:65:2], False, False, "nIdf GS GSp", "#4")
-        mm1(X2[:, 32:64], nIdf, T.D2[:, 2:65:2], False, False, "nIdf D2 D2p", "#4")
-        for k, (lo, c, b) in enumerate(((1, 1, -1.0), (0, 1, -3.0), (65, 0, -3.0), (64, 0, -1.0))):
-            act(T.TH[:, lo:lo + 63:2], T.dead[:, c:64:2], scale=2.0, bias=b, r="dead", w="TH%d" % k)
+        mm1(X2[:, 0:32], nI, T.GS[:, 2:65:2], False, False, "nI GS GSp", "#4")
+        mm1(X2[:, 32:64], nI, T.D2[:, 2:65:2], False, False, "nI D2 D2p", "#4")
+        if QUICK2:
+            for k, (lo, c, b) in enumerate(((1, 1, -1.0), (0, 1, -3.0), (65, 0, -3.0), (64, 0, -1.0))):
+                act(T.TH[:, lo:lo + 63:2], T.dead[:, c:64:2], scale=2.0, bias=b, r="dead", w="TH%d" % k)
+        else:
+            for k, (lo, b) in enumerate(((0, 0.0), (65, -100.0), (130, 0.0))):
+                act(T.TH[:, lo:lo + 64], T.dead[:], scale=100.0, bias=b, r="dead", w="TH%d" % k + " TH3" * (k < 2) + " TH2" * (k == 1) + " TH1" * (k == 0))
         for p in range(16):
             act(T.V[:, p:1024:16], Bk[2 + p // 8][:, 64 * (p % 8):64 * (p % 8) + 64], bias=O(t, p, p + 1),
                 r="#%d %s" % (2 + p // 8, ok), w="V")
         tt(T.dO[:], O(t), O(t, -1, 15), sub, ok + " Op", "dO")
         tt(XO, T.dO[:, 0:16].indirect(T.orr[:, 0:8]), BO, mul, "dO orr BO", "XO")
-        scan(T.WS[:, 0:512], T.GW[:, 0:512], T.MW[:, 0:512], 0.0, mx, add, "GWa GWb MW", "WS")
         w2 = T.WS[:, 15:512:16]
-        ts(T.oP[:, 0:32], w2, c256b, add, r="WS c256b", w="oP")
-        act(T.sz[:, 1:33], w2, AF.Sign, bias=256.0, r="WS", w="sz")
-        mm1(X2[:, 0:32], Id, w2, False, False, "Id WS", "#4")
-        mm1(X2[:, 32:64], Id, w2, False, True, "Id WS", "#4")
-        cp(T.oTQ[:, 0:64], X2, "#4", "oTQ")
+        for lo, x, r in ((0, "a", "GWa"), (16, "b", "GWb GWc")):
+            scan(T.WS[:, 16 * lo:16 * lo + 256], T.GW[:, 16 * lo:16 * lo + 256], T.MW[:, 0:256], 0.0, mx, add, r + " MW", "WS" + x)
+            ts(T.oP[:, lo:lo + 16], w2[:, lo:lo + 16], c256b, add, r="c256b WS" + x, w="oP" + x)
+        if QUICK2:
+            act(T.sz[:, 1:33], w2, AF.Sign, bias=256.0, r="WSa WSb", w="sz")
+        mm1(X2[:, 0:32], Id, w2, False, False, "Id WSa WSb", "#4")
+        mm1(X2[:, 32:64], Id, w2, False, True, "Id WSa WSb", "#4")
+        cp(T.oTQ[:, 0:64], X2, "#4", "oTQa oTQb")
         for h in range(4):
             n = 16 if h < 3 else 15
             o = T.oP[:, 16 * h:16 * h + 16] if h < 2 else T.oTQ[:, 16 * h:16 * h + n]
-            act(T.PG[:, 512 * h:512 * h + 16 * n], Pt[:, 0:4096].indirect(o), r=pk + (" oP" if h < 2 else " oTQ"), w="PG%d" % h)
-        act(T.M4[:, 3:128:4], T.sz[:, 1:33], scale=-0.25, bias=cB4, r="sz cB4 M4", w="M4a")
-        act(T.M4[:, 131:256:4], T.sz[:, 0:32], scale=-0.25, bias=cB4, r="sz szp cB4 M4", w="M4b")
+            act(T.PG[:, 512 * h:512 * h + 16 * n], Pt[:, 0:4096].indirect(o), r=pk + (" oP" + "ab"[h] if h < 2 else " oTQa oTQb"), w="PG%d" % h)
+        if QUICK2:
+            act(T.M4[:, 3:128:4], T.sz[:, 1:33], scale=-0.25, bias=cB4, r="sz cB4 M4", w="M4a")
+            act(T.M4[:, 131:256:4], T.sz[:, 0:32], scale=-0.25, bias=cB4, r="sz szp cB4 M4", w="M4b")
+        else:
+            ts(T.s2[:, 0:32], w2, -256.0, gt, r="WSa WSb", w="s2a")
+            ts(T.s2[:, 33:65], w2, -256.0, gt, r="WSa WSb", w="s2b")
+            mm1(T.B0[:, 0:64], nI8, T.s2[:, 0:64], True, False, "nI8 s2a s2b s2p", "#0")
         mm(T.B5[:, 0:128], [(XO, Id)], "XO Id", "#5")
-        act(dOT, T.B5[:, 0:128], r="#5", w="dOT")
+        act(dOT, T.B5[:, 0:128], scale=cNz, r="#5 cNz", w="dOT")
+        act(dO0, T.B5[:, 0:128], scale=cIs0, r="#5 cIs0", w="dO0")
+        act(T.fine[:, 256:384], dOT, scale=1 / 256, r="dOT", w="fine")
         mm(T.B7[:, 128:144], [(ShI, O(t))], "ShI " + ok, "#7")
         act(T.Dp[:], T.B7[:, 128:144], r="#7", w="Dp")
         for h in range(4):
             n, lo = 16 if h < 3 else 15, 512 + 256 * h + 16 * (h // 2)
             tt(T.N1[:, lo:lo + 16 * n], TXw.indirect(T.oTQ[:, 16 * (h % 2):16 * (h % 2) + n]), T.PG[:, 512 * h:512 * h + 16 * n], eq,
-               "TX oTQ PG%d" % h, "Q%d" % (h + 2))
-            quick(1 if h < 3 else 0, 512, (0, 16, 32, 49)[h], (16, 32, 49, 64)[h], "N1p Q%d" % (h + 2))
-        pick(1, 0, 49, "RESa")
-        pick(0, 49, 64, "RESb")
+               "TX oTQa oTQb PG%d" % h, "Q%d" % (h + 2))
+            if QUICK2:
+                quick(1 if h < 3 else 0, 512, (0, 16, 32, 49)[h], (16, 32, 49, 64)[h], "N1p Q%d" % (h + 2))
+        if QUICK2:
+            pick(1, 0, 49, "RESa")
+            pick(0, 49, 64, "RESb")
+        else:
+            count(T.B0[:, 0:64], T.N1, 512, 64, "Q2 Q3 Q4 Q5 N1p", "#0", False)
         if t == 0:
             consts(2)
         if t == 1:
             consts(5)
-        tt(T.K[:], T.RES[:, 0:256].indirect(T.oK[:]), T.TH[:], lt, "RESa RESb oK TH0 TH1 TH2 TH3", "K")
-        tt(T.dead2[:], T.K[:, 0:64], T.K[:, 64:128], mx, "K", "dead2")
-        scan(T.cum[:], T.ones[:], T.dead2[:], 0.0, add, sub, "ones dead2", "cum")
+        if QUICK2:
+            tt(T.K[:], T.RES[:, 0:256].indirect(T.oK[:]), T.TH[:, 0:128], lt, "RESa RESb oK TH0 TH1 TH2 TH3", "K Ke")
+        else:
+            tt(T.K[:, 1:128:2], T.B0[:, 0:64], T.TH[:, 1:129:2], lt, "#0 TH0 TH1 TH3", "K")
+            tt(T.K[:, 0:128:2], T.B0[:, 0:64], T.TH[:, 66:194:2], lt, "#0 TH1 TH2 TH3", "Ke")
+        tt(T.dead2[:], T.K[:, 0:64], T.K[:, 64:128], mx, "K Ke", "dead2")
+        scan(T.cum[:], T.ones[:, 0:64], T.dead2[:], 0.0, add, sub, "ones dead2", "cum")
+        mm1(T.B4[:, 256:512], dO0, T.ones[:], True, False, "dO0 ones", "#4")
         mm(T.B5[:, 128:129], [(LT, T.cum[:, 63:64])], "LT cum", "#5")
-        mm(T.B6[:, 130:131], [(BO, T.cum[:, 63:64])], "BO cum", "#6")
+        mm(T.B5[:, 129:130], [(L0, T.cum[:, 63:64])], "L0 cum", "#5")
         base = T.B5[:, 128:129]
-        tt(T.dK[:], T.dead2[:], T.KD[:], mul, "dead2 KD", "dK")
-        tt(T.u0[:], T.dK[:], T.cum[:], mx, "dK cum", "u0")
+        tt(T.B6[:, 320:384], T.B6[:, 256:320], T.dead2[:], mul, "dead2 #6", "#6 dK")
+        tt(T.u0[:], T.B6[:, 320:384], T.cum[:], mx, "dK cum #6", "u0")
         st, stp = T.step[:, 16:272], T.step[:, 15:271]
         ts(T.oR[:], T.u0[:], base, add, -1.0, add, r="u0 #5", w="oR")
-        ts(st, T.ix[:], base, ge, r="ix #5", w="step")
-        act(T.ngt[:, 0:1], T.B6[:, 130:131], bias=1.0, scale=-1.0, r="#6", w="ngt")
-        act(T.inv[:], T.ix[:], AF.Relu, bias=T.ngt[:, 0:1], r="ix ngt", w="inv")
-        mm(T.B4[:, 256:512], [(dOT, st), (B256, st)], "dOT step B256", "#4")
+        ts(st, T.ix[:], T.B5[:, 129:130], ge, r="ix #5", w="step")
+        mm1(T.B4[:, 256:512], dOT, st, False, False, "dOT step", "#4")
+        mm1(T.B4[:, 256:512], B256, st, False, True, "B256 step", "#4")
         k = 64 - SHARE
         act(T.CW[:, 3072:6144].indirect(T.oR[:, k:64]), T.V[:, 16 * k:1024], AF.Silu, bias=None, r="oR V", w="CWb")
         ts(T.CW[:, 0:3072].indirect(T.oR[:, 0:16]), T.V[:, 0:256], 1.0, mul, ROUND - 64, add, r="oR V", w="CWa")
         cp(T.oPP[:], T.B4[:, 256:512], "#4", "oPP")
+        stays()
         ts(T.CW[:, 0:3072].indirect(T.oR[:, 16:k]), T.V[:, 256:16 * k], 1.0, mul, ROUND - 64, add, r="oR V", w="CWa")
 
         def items(h):
@@ -679,38 +899,43 @@ def rank_program(g, core, T, topo):
         if t == 3:
             recv(1, "rt3", False, "TL3")
             dma("g", T.CW[0:128:16, 0:4096], T.TL[3], "TL3", "CWa CWb")
-        vv = {"a": (T.B5[:, 256:384], "#5"), "b": (T.B0[:, 256:384], "#0")}
-        for x, lo in (("a", 0), ("b", 128)):
-            for k, (l, y) in enumerate(((dOT, st), (B8k, st), (nB8k, stp), (I8k, T.inv[:]))):
-                mm1(vv[x][0], l, y[:, lo:lo + 128], k == 0, False, "dOT step stepp inv B8k nB8k I8k", vv[x][1])
-        mm(T.B4[:, 0:256], [(dOT, st)], "dOT step", "#4")
+        vv = T.B5[:, 256:384]
+        for k, (l, y) in enumerate(((dO0, T.ones[:]), (dOT, st), (B8k, st), (nB8k, stp))):
+            mm1(vv, l, y[:, 0:128], k == 0, False, "dO0 ones dOT step stepp B8k nB8k", "#5")
         ts(T.oTT[:, 0:128], T.G2[:, 8:136], -ROUND, add, r="G2", w="oTT0")
         ts(T.oTT[:, 128:256], T.G2[:, 136:264], -ROUND, add, r="G2b", w="oTT1")
-        act(T.G1[:, 8:264], T.G2[:, 8:264], bias=cRn, r="G2 G2b cRn", w="G1")
-        mm1(vv["a"][0], Idf, T.G1[:, 8:136], False, False, "G1 Idf", "#5")
-        mm1(vv["a"][0], nIdf, T.G1[:, 7:135], False, True, "G1 nIdf", "#5")
+        mm(T.B4[:, 0:256], [(dO0, T.fine[:, 0:256]), (T.fine[:, 256:384], st)], "dO0 step fine0 fine", "#4")
+        mm1(vv[:, 0:128], Idf, T.G2[:, 8:136], False, False, "G2 Idf", "#5")
+        mm1(vv[:, 0:128], nIdf, T.G2[:, 7:135], False, True, "G2 nIdf", "#5")
+        if DDV:
+            tt(T.dd[:, 0:128], T.G2[:, 136:264], T.G2[:, 135:263], sub, "G2 G2b", "dd")
+        else:
+            mm(T.B0[:, 384:512], [(Idf, T.G2[:, 136:264]), (nIdf, T.G2[:, 135:263])], "G2 G2b Idf nIdf", "#0")
+            act(T.dd[:, 0:128], T.B0[:, 384:512], r="#0", w="dd")
+        for k, (l, y) in enumerate(((dO0, T.ones[:]), (dOT, st), (B8k, st), (nB8k, stp))):
+            mm1(T.B0[:, 256:384], l, y[:, 128:256], k == 0, False, "dO0 ones dOT step stepp B8k nB8k", "#0")
+        mm1(T.B0[:, 256:384], Id, T.dd[:, 0:128], False, True, "Id dd", "#0")
         items(2)
         items(3)
 
-        def score(lo, hi, x):
-            mm(T.B2[:, lo:hi], [(A1, T.sg[:, 16 + lo:16 + hi]), (nBO, T.sg[:, 15 + lo:15 + hi]), (nI, T.sn[:, lo:hi])],
-               "A1 nBO nI sgp sn" + x + " " + " ".join("sg%d" % k for k in range(hi // 64)), "#2")
-            act(T.f1[:, lo:hi], T.B2[:, lo:hi], AF.Relu, bias=cB1, scale=0.5, r="#2 cB1", w="f1" + x)
-
         def named(lo, hi, x):
-            fk = "f1" + x
-            tt(T.t1[:, lo:hi], vv[x][0], T.f1[:, lo:hi], mul, vv[x][1] + " " + fk, "t1" + x)
-            tt(T.t2[:, lo:hi], T.B4[:, lo:hi], T.f1[:, lo:hi], mul, "#4 " + fk, "t2" + x)
+            mm1(T.B2[:, lo:hi], Id, (T.ones, T.dd)[lo > 0][:, 0:128], True, False, "Id ones" + " dd" * (lo > 0), "#2")
+            mm1(T.B2[:, lo:hi], nI4k, T.sn[:, lo:hi], False, False, "nI4k sn" + x, "#2")
+            signs(T.B2[:, lo:hi], A1, lo, hi, 0, False, "A1", "#2")
+            signs(T.B2[:, lo:hi], nB4k, lo, hi, 1, True, "nB4k", "#2")
+            f = T.t1[:, lo:hi] if lo else T.dd[:, 128:256]
+            act(f, T.B2[:, lo:hi], AF.Relu, bias=cB1, r="#2 cB1", w="t1b" if lo else "f1")
+            if not lo:
+                tt(T.t1[:, lo:hi], vv[:, lo:hi], f, mul, "#5 f1", "t1a")
+            tt(T.t2[:, lo:hi], T.B4[:, lo:hi], f, mn, "#4 " + ("t1b" if lo else "f1"), "t2" + x)
 
         def slots(lo, hi, x):
+            one = [(BO, T.t1[:, k:hi:2]) for k in (lo, lo + 1)]
+            two = [((nBx, Bx)[lo > 0], T.t2[:, k:hi:2]) for k in (lo, lo + 1)]
             mm1(T.B6[:, lo // 2:hi // 2], B256, T.step[:, 16 + lo:16 + hi:2], True, False, "step B256", "#6")
-            for k, (l, y) in enumerate(((BO, T.t1[:, lo:hi:2]), (BO, T.t1[:, lo + 1:hi:2]), (nBO, T.t2[:, lo:hi:2]), (nBO, T.t2[:, lo + 1:hi:2]))):
-                mm1(T.B6[:, lo // 2:hi // 2], l, y, False, k == 3, "nBO BO t1%s%s" % (x, " t2" + x if k > 1 else ""), "#6")
-
-        def old_text():
-            ts(T.oXg[:], T.KX[:, 0:256:16], HOLD, add, r="KXa KXb", w="oXg")
-            act(T.FV[:], T.TX[:, 0:TW].indirect(T.oXg[:]), scale=-1.0, bias=255.0, r="TX TXp oXg", w="FV")
-            act(T.x1[:], T.KX[:, 0:256:16], scale=cSi, bias=cX1, r="KXa KXb cSi cX1", w="x1")
+            for k, (l, y) in enumerate(one if lo else one + two):
+                mm1(T.B6[:, lo // 2:hi // 2], l, y, False, k == (1 if lo else 3), "BO nBx t1" + x + " t2a" * (k > 1), "#6")
+            mm(T.B7[:, lo // 2:hi // 2], one + two if lo else one, "BO Bx t1" + x + " t2b" * (lo > 0), "#7")
 
         split = t in SPLIT
         for h in range(4):
@@ -718,67 +943,59 @@ def rank_program(g, core, T, topo):
             for j in (2 * h, 2 * h + 1):
                 tt(T.NN[:, 512 * j:512 * j + 512], TXw.indirect(T.oTT[:, 32 * j:32 * j + 32]), T.PG[:, 512 * j:512 * j + 512], eq,
                    "TX oTT%d PG%d" % (j // 4, j), "N%d" % j)
+            if h == 0:
+                mm1(T.B3[:, 0:128], S0f, T.G2[:, 8:136], True, True, "G2 S0f", "#3")
             if h == 1:
-                mm1(T.B3[:, 0:128], S0f, T.G1[:, 8:136], True, True, "G1 S0f", "#3")
-            if h == 2:
-                mm1(T.B3[:, 128:256], S0f, T.G1[:, 136:264], True, True, "G1 S0f", "#3")
-                if split:
-                    held(0, 128, "a")
-                    held(128, 256, "b")
+                mm1(T.B3[:, 128:256], S0f, T.G2[:, 136:264], True, True, "G2b S0f", "#3")
+            if h == 2 and split:
+                held()
             bk = (6, 1, 7, 1)[h]
-            if h == 3:
-                tt(T.dd[:], T.G1[:, 136:264], T.G1[:, 135:263], sub, "G1", "dd")
-            count(Bk[bk][:, 0:64], T.NN, 1024 * h, 64, nk, "#%d" % bk)
-            if h == 3:
-                mm1(vv["b"][0], Id, T.dd[:], False, True, "Id dd", "#0")
-                ops.insert(len(ops) - 11, ops.pop())
-                act(T.sn[:, 128:256], vv["b"][0], AF.Sign, bias=cSn, r="#0 cSn", w="snb")
+            if h < 3:
+                count(Bk[bk][:, 0:64], T.NN, 1024 * h, 64, nk, "#%d" % bk)
+                act(T.sg[:, 16 + 64 * h:80 + 64 * h], Bk[bk][:, 0:64], AF.Sign, bias=c75, scale=-1.0, r="#%d c75" % bk, w="sg%d" % h)
+            else:
+                for j in (6, 7):
+                    mm(T.B1[:, 64 * j - 384:64 * j - 320], [(T.Z2[:, 7 - q:135 - q], T.NN[:, 512 * j + q:512 * j + 512:8]) for q in range(8)],
+                       "Z2 N%d" % j, "#1")
+                act(T.sg[:, 208:272], T.B1[:, 0:128:2], AF.Sign, bias=cH0b, scale=cH0, r="#1 cH0 cH0b", w="sg3")
+                act(T.sg[:, 288:352], T.B1[:, 1:128:2], AF.Sign, bias=cH1b, scale=cH1, r="#1 cH1 cH1b", w="sg4")
             if h < 2:
                 items(2 * h + 4)
                 items(2 * h + 5)
             if h == 1:
-                act(T.sn[:, 0:128], vv["a"][0], AF.Sign, bias=cSn, r="#5 cSn", w="sna")
-            act(T.sg[:, 16 + 64 * h:80 + 64 * h], Bk[bk][:, 0:64], AF.Sign, bias=c75, scale=-1.0, r="#%d c75" % bk, w="sg%d" % h)
+                act(T.sn[:, 0:128], vv[:, 0:128], AF.Sign, bias=cSn, r="#5 cSn", w="sna")
+                act(T.sn[:, 128:256], T.B0[:, 256:384], AF.Sign, bias=cSn, r="#0 cSn", w="snb")
             if h == 2:
-                score(0, 128, "a")
                 if split:
-                    accepted(0, 128, "sg0 sg1")
-                    old_text()
+                    accepted(0, 128)
+                named(0, 128, "a")
+                if split:
                     flip_a(0, 128, "a")
         if t == 0:
             consts(3)
         if not split:
-            held(0, 256, "b")
-            old_text()
-        named(0, 128, "a")
+            held()
         slots(0, 128, "a")
-        score(128, 256, "b")
+        named(128, 256, "b")
+        values(t, 0)
         equals(0, 4, "a")
         if split:
             flip_b(0, 8, t)
-            accepted(128, 256, "sg2 sg3")
+            accepted(128, 256)
             flip_a(128, 256, "b")
         else:
-            accepted(0, 256, "sg0 sg1 sg2 sg3")
+            accepted(0, 256)
             flip_a(0, 256, "b")
-        named(128, 256, "b")
         slots(128, 256, "b")
-        b = 16 * t
-        mm(T.B7[:, 0:128], [(BO, T.t1[:, 0:256:2]), (BO, T.t1[:, 1:256:2])], "BO t1a t1b", "#7")
-        act(T.sv[:, 8 * b:8 * b + 128], T.B7[:, 0:128], r="#7", w="sv%d" % t)
-        mm(T.B2[:, 256:512], [(L0, T.sg[:, 16:272])], "L0 sg0 sg1 sg2 sg3", "#2")
-        act(T.G0[:], T.B2[:, 256:512], AF.Relu, bias=cG0, scale=-0.5, r="#2 cG0", w="G0")
-        send(1, T.lw[:, 8 * b:8 * b + 128], T.sv[:, 8 * b:8 * b + 128], "rv%d" % t, False, "sv%d" % t)
+        signs(T.B0[:, 0:256], L0, 0, 256, 0, True, "L0", "#0", True)
+        values(t, 1)
+        act(T.G0[:], T.B0[:, 0:256], AF.Relu, bias=cG0, scale=-0.5, r="#0 cG0", w="G0")
+        keys(t, 0)
         act(cE, T.cum[:, 63:64], AF.Relu, bias=256.0, scale=-256.0, r="cum", w="cE")
         ts(T.oE[:, 0:1], base, cE, add, 256.0, mn, r="cE #5", w="oE")
         equals(4, 8, "b")
-        act(T.KT[:, 0:8], T.KS[:, 15:128:16], bias=BIG, r="KSa KSb", w="KT")
-        tt(T.y1[:], T.YS[:, 0:592].indirect(T.oY[:, 0:1]), T.KT[:], mx, "YSa YSb YSp oY KT", "y1")
-        cp(T.su[:, b:b + 8], T.y1[:, 0:8], "y1", "su%d" % t)
-        send(1, T.lu[:, b:b + 8], T.su[:, b:b + 8], "ru%d" % t, False, "su%d" % t)
+        keys(t, 1)
         places(t)
-        if t < 2:
-            send(t + 2, P[t + 2][:], T.P0[:], "rp%d" % (t + 2), True, "P0")
         if t == 0:
             consts(4)
         if t < 3:
@@ -786,18 +1003,22 @@ def rank_program(g, core, T, topo):
             offsets1(t + 1)
             flip_b(8 if split else 0, 10, t)
             wn, wnk = W[(t + 1) % 2], "W%d W%dp" % ((t + 1) % 2, (t + 1) % 2)
-            apply_u(t + 1, wn, wnk)
+            apply_u(t, 0, wn, wnk)
+            apply_u(t, 1, wn, wnk)
             flip_b(10, 14, t)
             act(T.GW[:, 16 * WSH:1024], wn[:, 0:WW].indirect(T.oW1[:, s0 + 64 + WSH:s0 + 128]), r=wnk + " oW1%d" % (t + 1), w="GWb")
             dma("y", T.TS[t + 1], wn[0:128:16, 0:4096], wnk, "TS%d" % (t + 1))
-            cp(T.GW[:, 0:16 * WSH], wn[:, 0:WW].indirect(T.oW1[:, s0 + 64:s0 + 64 + WSH]), wnk + " oW1%d" % (t + 1), "GWa")
+            cp(T.GW[:, 0:256], wn[:, 0:WW].indirect(T.oW1[:, s0 + 64:s0 + 80]), wnk + " oW1%d" % (t + 1), "GWa")
+            if WSH > 16:
+                cp(T.GW[:, 256:16 * WSH], wn[:, 0:WW].indirect(T.oW1[:, s0 + 80:s0 + 64 + WSH]), wnk + " oW1%d" % (t + 1), "GWc")
         else:
             flip_b(8 if split else 0, 16, t)
             dma("y", T.yt[:, 0:2048], T.TX[:, 0:2048], "TX", "yta", lat=4500.0)
             dma("a", T.yt[:, 2048:4096], T.TX[:, 2048:4096], "TX", "ytb", lat=4500.0)
             recv(1, "ro3", False, "o32")
             dma("y", T.yo[:], T.o32[:, 16:32], "o32", "yo")
-            apply_u(4, T.CW, "CWa CWb")
+            apply_u(3, 0, T.CW, "CWa CWb")
+            apply_u(3, 1, T.CW, "CWa CWb")
             cp(T.CW[:, 0:4096:256], T.z0[:], "z0 CWa", "CWa CWb")
             dma("a", T.yw[:], T.CW[0:128:16, 0:4096], "CWa CWb", "yw")
     _emit(g, T, ops)

@@ -6,47 +6,47 @@ BIG = 8192.0
 HOLD = 65536.0
 WW = 4112
 WS = 8224
-TW = 4128
+TW = 4144
+CW1 = 3200
 ORDER = []
 TRIES, MOVES = 16, 400
 PACES = ((0.83, 1.0, 1.9, 150.0, 110.0, 10.0, 400.0, 0.42), (0.87, 1.3, 3.1, 190.0, 128.0, 10.0, 700.0, 0.45),
          (1.1, 1.0, 2.5, 170.0, 122.0, 10.0, 500.0, 0.72), (1.15, 1.7, 4.5, 240.0, 165.0, 20.0, 1100.0, 0.6))
-LINK = 2300.0
+LINK = 1900.0
+TINY = 2.0 ** -21
+NONE = (-6000.0, -12000.0)
 ROUND = 1.5 * 2.0 ** 23
 SHARE = 34
-WSH = 24
-SPLIT = (0, 1, 2, 3)
-EARLY = True
-ONE = True
-URGENT = None
-ALL8 = True
-DDV = True
-QUICK = QUICK2 = True
-PIECES = ("V",)
-TRI = [8 * k * (k + 1) for k in range(9)]
+PART1 = ((0, 8, 4, "v8"), (8, 28, 6, "v28"), (28, 64, 5, "a64"))
+TURN1 = (("i", 0, 8), ("j", 0, 8), ("i", 8, 28), ("i", 28, 46), ("i", 46, 64), ("j", 8, 28), ("j", 28, 46), ("j", 46, 64))
+PART2 = ((0, 12, 4, "v12"), (12, 32, 6, "a32"))
+TURN2 = (("i", 0, 12), ("i", 12, 32), ("j", 0, 12), ("j", 12, 32))
+PLAIN = (8, 32)
+FIRST, HEAD = 32, 12
+PIECES = ("V", "Sel")
 
 F, B, I, U = "float32", "bfloat16", "int32", "uint16"
-MATS = "BO LT Id A1 nBO nI B256 B8k nB8k BN nB4k nS8k nI8 S0 nS0 ShI L0 Mx dOT dO0 XO nI4k Bx nBx".split()
+MATS = "BO LT Id A1 nBO nI B256 B8k nB8k BN nB4k nS8k nI8 S0 nS0 ShI L0 Mx dOT dO0 XO nI4k Bx nBx qI hI cI n4I".split()
 SCRATCH = {}
 for _n, _c, _d in (
     ("TX", TW, B), ("P0", 4096, B), ("P1", 4096, B), ("P2", 4096, B), ("P3", 4096, B),
     ("W0", WS, B), ("W1", WS, B), ("CT", 272, B), ("cdi", 256, I), ("witi", 256, I), ("prbi", 16, I),
-    ("ip", 8, I), ("iw", 8, I), ("col", 40, F), ("ia", 32, I), ("ib", 16, I), ("oa", 32, U), ("ob", 16, U), ("orr", 64, U),
+    ("ip", 8, I), ("iw", 8, I), ("col", 48, F), ("ia", 32, I), ("ib", 16, I), ("oa", 32, U), ("ob", 16, U), ("orr", 64, U),
     ("G1", 512, F), ("G2", 512, F), ("A", 264, F), ("A64", 256, F), ("Ah", 264, B), ("Al", 264, B), ("DL", 264, F), ("DB", 256, B),
-    ("KX", 256, F), ("ZX", 256, B), ("ZS", 256, B), ("MX", 256, B), ("MK", 256, B), ("LV", 256, B), ("m16", 80, B),
-    ("M4", 256, B), ("Z4", 136, B), ("RES", 256, B), ("oK", 8, U), ("iq4", 16, B), ("dd", 256, B), ("fine", 512, B),
-    ("oW1", 256, U), ("ix", 256, B), ("iq16", 128, B), ("iqm", 16, B), ("Z", 144, B), ("M", 128 * len(MATS), B), ("Mf", 384, F),
-    ("Sel", 2048, B), ("DX", 256, F), ("MW", 1024, B), ("MWk", 128, B), ("MC", 592, B), ("tm", 64, F),
-    ("dW", 16, F), ("z0", 16, B), ("xz", 16, B), ("K0", 128, B),
+    ("KX", 512, F), ("ZX", 512, B), ("ZS", 512, B), ("MX", 512, B), ("MK", 512, B), ("LV", 256, B), ("m16", 128, B), ("or2", 16, U),
+    ("W4", 128, B), ("two", 128, B), ("UU", 192, B), ("A2", 256, F), ("LF", 272, F), ("dd", 256, B), ("fine", 512, B),
+    ("oW1", 256, U), ("ix", 256, B), ("iq16", 128, B), ("iqm", 16, B), ("Z", 144, B), ("M", 128 * len(MATS), B), ("Mf", 768, F),
+    ("Sel", 2048, B), ("MW", 1024, B), ("MWk", 128, B), ("MC", 400, B), ("tm", 64, F),
+    ("z0", 16, B), ("xz", 16, B), ("K0", 128, B),
     ("GW", 1024, B), ("WS", 1024, B), ("oP", 64, U), ("oTQ", 128, U), ("PG", 4096, B),
-    ("NN", 4096, B), ("N1", 2048, B), ("sz", 72, B), ("T1", 128, B), ("Z2", 136, B), ("TH", 200, B), ("s2", 72, B), ("dead", 64, B),
-    ("GS", 72, B), ("D2", 72, B), ("oW2", 32, U),
-    ("K", 128, F), ("dead2", 64, F), ("cum", 64, B), ("ones", 256, B), ("dK", 64, F), ("u0", 64, F),
+    ("NN", 4096, B), ("N1", 2048, B), ("nd", 32, F), ("T1", 136, B), ("Z2", 136, B), ("TH", 128, B), ("T2", 72, B), ("AE", 128, B),
+    ("CJ", 128, B), ("K2", 128, B), ("oW2", 32, U),
+    ("cum", 136, F), ("DD", 128, F), ("ones", 256, B), ("dK", 128, F), ("u0", 64, F),
     ("oR", 64, U), ("step", 272, B), ("oPP", 256, U), ("oTT", 256, U),
     ("V", 1024, F), ("CW", WS, F), ("dO", 16, B),
     ("sg", 352, B), ("sn", 256, B), ("G0", 256, B), ("d0", 256, B), ("t1", 256, B), ("t2", 256, B),
-    ("KS", 128, F), ("KT", 32, F), ("E", 576, B), ("YS", 576, B), ("oY", 8, U), ("y1", 32, F), ("x1", 16, F), ("x2", 16, F),
-    ("oXg", 16, U), ("oX2", 32, U), ("FV", 256, B), ("sv", 512, B), ("CS", 264, F), ("e1", 8, F), ("oE", 8, U),
+    ("KS", 128, F), ("E", 400, F), ("YS", 400, F), ("x1", 16, F), ("x2", 32, F),
+    ("oXg", 16, U), ("oX2", 16, U), ("FV", 256, B), ("sv", 512, B), ("CS", 264, F), ("e1", 8, F), ("oE", 8, U),
     ("Dp", 16, B), ("uo", 16, B), ("su", 64, U), ("lu", 64, U), ("lw", 512, B), ("so", 64, B), ("O", 160, B), ("o32", 32, F),
 ):
     SCRATCH[_n] = ("sbuf", [128, _c], _d)
@@ -59,7 +59,7 @@ for _t in range(8):
 
 NDMA = 60
 SEMAPHORES = (["qv", "qa", "qt", "qg", "loc"] + ["d%d" % k for k in range(NDMA)]
-              + ["r%s%d" % (k, t) for k in "uvwxotp" for t in range(4)])
+              + ["r%s%d" % (k, t) for k in "uvotp" for t in range(4)])
 
 
 def _place(ops, before, after, floor, rank):
@@ -317,12 +317,9 @@ def rank_program(g, core, T, topo):
     def op(q, fn, r="", w="", kind="c", cost=400.0, lat=0.0, name=None):
         ops.append([q, kind, fn, r.split(), w.split(), (cost if isinstance(cost, tuple) else (cost, 0, 0), lat, name)])
 
-    def stays():
-        ops[-1][5] = ops[-1][5][:2] + ("stays",)
-
     def ns(out, in_, r, more=(), k=None, fix=0):
         for x in r.split():
-            if x[:3] == "oX2" or x[:2] in ("lu", "oR", "oS"):
+            if x[:3] == "oX2" or x[:2] in ("lu", "oR"):
                 return (50 + fix, in_.shape[1], 2), out, in_
             if x[0] == "o" and x not in ("ones", "o32"):
                 return (50 + fix, out.shape[1], 1), out, in_
@@ -375,23 +372,18 @@ def rank_program(g, core, T, topo):
         else:
             op("g", lambda: g.iota(out, pat, base, cm), "", w, cost=(130, 2 * out.shape[1], 0))
 
-    def lanes(src, dst, bulk):
-        e = topo.engines(src, dst)
-        return e if bulk is None or bulk or ALL8 else e[len(e) // 2:]
-
     def send(k, out, in_, sem, bulk, r):
         dst = helper[rank] if bulk else T.cores[(rank - k) % N]
-        e = lanes(core, dst, bulk)
         rid, pid, _ = topo.addr(dst)
 
         def fn():
-            g.remote_dma(out, in_, T.sem[sem], T.sem.loc, pid, rid, sum(1 << x for x in e))
-            return len(e)
+            g.remote_dma(out, in_, T.sem[sem], T.sem.loc, pid, rid, topo.mask(core, dst))
+            return len(topo.engines(core, dst))
         op("g", fn, r, "", "s", (0, 1, 6), LINK + {"u": 0, "v": 300, "p": 19000}.get(sem[1], 1200 * (sem != "ro3")), sem)
 
     def recv(k, sem, bulk, w):
         src = (helper if bulk else T.cores)[(rank + k) % N]
-        ops.append(["r", "r", (sem, len(lanes(src, core, bulk)), "rp0" if bulk else sem), [], w.split(), ((0, 0, 0), 0.0, None)])
+        ops.append(["r", "r", (sem, len(topo.engines(src, core)), "rp0" if bulk else sem), [], w.split(), ((0, 0, 0), 0.0, None)])
 
     def fill(ap, n, c, w):
         iota(ap, [[0, n]], c, 0, w, True)
@@ -399,12 +391,15 @@ def rank_program(g, core, T, topo):
     def keep(out, in_, cmp, other, base, r, w):
         op("g", lambda: g.affine_select(out, in_, [[1, 128]], cmp, other, base, -1), r, w)
 
+    def span(name, lo, hi, unit):
+        return " " + " ".join(name + str(k) for k in range(lo // unit, (hi - 1) // unit + 1)) + " "
+
     col = T.col
-    (cR, cG, cG15, c4R, cM32, c256, c256b, cR1, cIs0, cN0, cB1, cG0, cP, c75, cSn, c64, cSg, cRn, cRf, cD, cSi, cX1, cE, cNs0, cW, cRm, cY,
-     cR4, cB4, cK, cNz, cNzB, cS8k, cH0, cH1, cB5, cH0b, cH1b) = (col[:, k:k + 1] for k in range(38))
-    (BO, LT, Id, A1, nBO, nI, B256, B8k, nB8k, BN, nB4k, nS8k, nI8, S0, nS0, ShI, L0, Mx, dOT, dO0, XO, nI4k, Bx, nBx
+    (cR, cG, cG15, c4R, cM32, c256, c256b, cIs0, cN0, cB1, cG0, cP, cSn, c75, cSg, cRf, cD, cSi, cX1, cE, cNs0, cW, cRm, cY,
+     cT, cTe, cNz, cNzB, cS8k, cH0, cH1, cTl, cH0b, cH1b, cA2, c512, cB0, cB1x, cBs, cE2, cD2, cX2) = (col[:, k:k + 1] for k in range(42))
+    (BO, LT, Id, A1, nBO, nI, B256, B8k, nB8k, BN, nB4k, nS8k, nI8, S0, nS0, ShI, L0, Mx, dOT, dO0, XO, nI4k, Bx, nBx, qI, hI, cI, n4I
      ) = (T.M[:, 128 * k:128 * k + 128] for k in range(len(MATS)))
-    Idf, nIdf, S0f = (T.Mf[:, 128 * k:128 * k + 128] for k in range(3))
+    Idf, nIdf, S0f, Idw, LTf, L0f = (T.Mf[:, 128 * k:128 * k + 128] for k in range(6))
     Z0 = T.Z[:, 15:143]
     P = [T.P0, T.P1, T.P2, T.P3]
     W = [T.W0, T.W1]
@@ -412,6 +407,7 @@ def rank_program(g, core, T, topo):
     TD = [T.TDa, T.TDb]
     add, sub, mul, mx, mn = ALU.add, ALU.subtract, ALU.mult, ALU.max, ALU.min
     eq, ge, gt, lt, le, ne = ALU.is_equal, ALU.is_ge, ALU.is_gt, ALU.is_lt, ALU.is_le, ALU.not_equal
+    TXw = T.TX[:, 0:4096]
 
     def O(t, lo=0, hi=16):
         return T.O[:, 32 * t + 16 + lo:32 * t + 16 + hi]
@@ -419,11 +415,49 @@ def rank_program(g, core, T, topo):
     def spread(out, k, n, r, w):
         act(out, T.m16[:, 16 * k:16 * k + 16].indirect(T.orr[:, 0:n]), r=r + " orr", w=w)
 
+    def witnesses(parts, win, off, r):
+        for lo, hi, bk, shares in parts:
+            for sh in shares.split():
+                up = int(sh[1:])
+                (cp if sh[0] == "v" else act)(T.GW[:, 16 * lo:16 * up], win.indirect(off[:, lo:up]), r=r, w=span("GW", lo, up, 2))
+                lo = up
+
+    def offsets(parts):
+        for lo, hi, bk, shares in parts:
+            n, w, x = hi - lo, T.WS[:, 16 * lo + 15:16 * hi:16], span("WS", lo, hi, 2)
+            scan(T.WS[:, 16 * lo:16 * hi], T.GW[:, 16 * lo:16 * hi], T.MW[:, 0:16 * n], 0.0, mx, add, span("GW", lo, hi, 2) + "MW", x)
+            ts(T.oP[:, lo:hi], w, c256b, add, r="c256b" + x, w=span("oP", lo, hi, 2))
+            mm1(Bk[bk][:, 0:n], Id, w, False, False, "Id" + x, "#%d" % bk)
+            mm1(Bk[bk][:, n:2 * n], Id, w, False, True, "Id" + x, "#%d" % bk)
+            cp(T.oTQ[:, 2 * lo:2 * hi], Bk[bk][:, 0:2 * n], "#%d" % bk, span("oTQ", 2 * lo, 2 * hi, 4))
+
+    def duels(parts, turn, plain, low, Pt, pk, after):
+        calls = []
+        for side, lo, hi in turn:
+            p0, p1, bk, sh = [p for p in parts if p[0] <= lo < p[1]][0]
+            swap = p0 >= plain
+            hi2 = hi - (side == "j" and hi == parts[-1][1])
+            y, z = p0 + lo, p1 + lo
+            oy, ry = T.oTQ[:, y:y + hi2 - lo], span("oTQ", y, y + hi - lo, 4)
+            oz, rz = (T.oP[:, lo:hi], span("oP", lo, hi, 2)) if side == "i" else (T.oTQ[:, z:z + hi2 - lo], span("oTQ", z, z + hi - lo, 4))
+            at = 16 * lo + (1024 if side == "j" and not swap else 0)
+            pg, rg = T.PG[:, at:at + 16 * (hi2 - lo)], span("PG", at, at + 16 * (hi - lo), 32)
+            if not swap:
+                act(pg, Pt[:, 0:4096].indirect(oz), r=pk + rz, w=rg)
+            elif side == "i":
+                act(pg, TXw.indirect(oy), r="TX" + ry, w=rg)
+            at = 16 * lo + (low if side == "i" else 1040)
+            calls.append((T.N1[:, at:at + 16 * (hi2 - lo)], Pt[:, 0:4096].indirect(oz) if swap else TXw.indirect(oy), pg,
+                          (pk + rz if swap else "TX" + ry) + rg, span("Q", at, at + 16 * (hi2 - lo), 16), side, hi))
+        for out, in0, pg, r, w, side, hi in calls:
+            tt(out, in0, pg, eq, r, w)
+            after(side, hi)
+
     def lanes_of(t):
         lo, s0 = 128 * t, 64 * t
         cp(T.G1[:, lo:lo + 128], T.cdi[:, 0:256].indirect(T.oa[:, 8 * t:8 * t + 8]), "cdi oa", "G1")
-        op("v", lambda: v.transpose(T.G2[:, lo:lo + 128], T.G1[:, lo:lo + 128]), "G1", "G2 G2b", cost=(40, 128, 0))
-        (cp if t == 0 else act)(T.A[:, s0:s0 + 64], T.G2[:, lo:lo + 128].indirect(T.ob[:, 0:4]), r="G2 ob", w="A%d" % t)
+        op("v", lambda: v.transpose(T.G2[:, lo:lo + 128], T.G1[:, lo:lo + 128]), "G1", "G2 G2a G2b", cost=(40, 128, 0))
+        (cp if t == 0 else act)(T.A[:, s0:s0 + 64], T.G2[:, lo:lo + 128].indirect(T.ob[:, 0:4]), r="G2 G2a G2b ob", w="A%d" % t)
         tt(T.DL[:, s0 + 1:s0 + 64], T.A[:, s0 + 1:s0 + 64], T.A[:, s0:s0 + 63], sub, "A%d" % t, "DL%d" % t)
         ts(T.DB[:, s0:s0 + 64], T.DL[:, s0 + 1:s0 + 65], 256.0, mn, r="DL%d DLp" % t, w="DB%d" % t)
         if t == 0:
@@ -440,7 +474,7 @@ def rank_program(g, core, T, topo):
     dma("y", T.cdi[:], T.cd[:], w="cdi")
     dma("a", T.witi[:], T.wit[:], w="witi")
     dma("y", T.P0[:], T.pat[:], w="P0", lat=5000.0)
-    dma("y", T.TX[:, 0:4096], T.txt[:], w="TX", lat=6800.0)
+    dma("y", TXw, T.txt[:], w="TX", lat=6800.0)
     dma("a", T.prbi[:], T.prb[:], w="prbi")
     iota(T.ip[:, 0:1], [[0, 1]], 0, 1, "ip0")
     iota(T.ia[:], [[64, 4], [1, 4], [0, 2]], 0, 0, "ia")
@@ -467,42 +501,30 @@ def rank_program(g, core, T, topo):
     tt(T.tm[:, 48:64], T.tm[:, 0:16], T.tm[:, 16:32], add, "tm0 tm1", "tm3")
     ms(T.CT[:, 0:1], 0.0, "CT0")
     tt(T.m16[:, 0:16], T.tm[:, 48:64], T.tm[:, 32:48], add, "tm3 tm2", "m0")
-    act(T.CW[:, 3072:3328], T.ix[:], AF.Silu, scale=0.0, r="ix", w="CWb")
+    act(T.CW[:, CW1:CW1 + 256], T.ix[:], AF.Silu, scale=0.0, r="ix", w="CWb")
     ops[-1][5] = ((1360, 256, 0), 0.0, None)
     spread(T.MW[:], 0, 64, "m0", "MW")
-    ms(T.Ah[:, 256:264], 0.0, "Ah4")
-    ms(T.Al[:, 256:264], 0.0, "Al4")
     ms(T.DL[:, 64:257:64], BIG, "DLp")
     ts(cG15, cG, 15.0, add, r="cG", w="cG15")
     lanes_of(0)
-    ms(T.G2[:, 7:8], ROUND + 4096, "G2")
+    ms(T.G2[:, 7:8], 4096 - ROUND, "G2")
     halves_of(0)
     cp(T.CT[:, 1:256], T.witi[:, 1:256], "witi", "CT")
     ts(BO, T.iq16[:], cG, eq, r="iq16 cG", w="BO")
     ts(Id, T.ix[:, 0:128], cP, eq, r="ix cP", w="Id")
     ts(T.Z[:], T.ix[:, 0:144], cG15, eq, r="ix cG15", w="Z")
-    ts(cR1, cR, 1.0, add, r="cR", w="cR1")
-    act(T.GW[:, 16 * WSH:1024], T.CT[:, 0:272].indirect(T.oW1[:, WSH:64]), r="CT CT0 CTp oW10", w="GWb")
     ts(cIs0, cR, 0.0, eq, r="cR", w="cIs0")
-    cp(T.GW[:, 0:256], T.CT[:, 0:272].indirect(T.oW1[:, 0:16]), "CT CT0 CTp oW10", "GWa")
-    if WSH > 16:
-        cp(T.GW[:, 256:16 * WSH], T.CT[:, 0:272].indirect(T.oW1[:, 16:WSH]), "CT CT0 CTp oW10", "GWc")
-    for dst, s, w in ((nI, -1.0, "nI"), (nI8, -8.0, "nI8")):
+    witnesses(PART1, T.CT[:, 0:272], T.oW1[:, 0:64], "CT CT0 CTp oW10")
+    for dst, s, w in ((nI, -1.0, "nI"), (nI8, -1 / 8, "nI8"), (hI, -0.5, "hI")):
         act(dst, Id, scale=s, r="Id", w=w)
     act(T.K0[:, 0:64], T.ix[:, 0:64], scale=0.0, bias=192.0, r="ix", w="K0a")
     act(T.K0[:, 64:128], T.ix[:, 0:64], scale=0.0, bias=c256b, r="ix c256b", w="K0b")
-    iota(T.iq4[:], [[0, 4], [1, 4]], 0, 0, "iq4", True)
     fill(T.N1[:, 1024:1040], 16, 0, "N1p")
-    fill(T.sz[:, 0:1], 1, 0, "szp")
-    fill(T.s2[:, 32:33], 1, 0, "s2p")
-    fill(T.GS[:, 64:72], 8, int(BIG), "GSp")
-    fill(T.D2[:, 64:72], 8, int(BIG), "D2p")
-    op("v", lambda: v.memset(T.Sel[:, 0:1024], 1.0), "", "Sel", cost=(0, 512, 0))
-    op("v", lambda: v.memset(T.Sel[:, 1024:2048], 1.0), "", "Selb", cost=(0, 512, 0))
-    op("g", lambda: g.affine_select(T.Sel[:], T.Sel[:], [[-1, 16], [-16, 8], [0, 16]], eq, 0.0, 0, 1), "Sel Selb", "Sel", cost=(170, 4096, 0))
-    send(1, T.TL[0], T.CT[:, 0:256], "rt0", False, "CT CT0")
-    ops[-1][5] = ((3000, 1, 6),) + ops[-1][5][1:]
-    send(0, T.P0[:], T.P0[:], "rp0", True, "P0 TX")
+    fill(T.T1[:, 0:2], 2, 0, "T1p")
+    fill(T.T2[:, 0:2], 2, 0, "T2p")
+    ts(T.x1[:], T.iqm[:], cR, eq, r="iqm cR", w="x1")
+    for p in range(16):
+        ts(T.Sel[:, 128 * p:128 * p + 128], BO, T.x1[:, p:p + 1], mul, r="BO x1", w="Sel")
     keep(ShI, BO, eq, 0.0, -1, "BO", "ShI")
     keep(ShI, ShI, ne, -1.0, 0, "ShI", "ShI")
     keep(LT, BO, gt, 0.0, 0, "BO", "LT")
@@ -510,29 +532,31 @@ def rank_program(g, core, T, topo):
     fill(T.step[:, 0:16], 16, 0, "stepp")
     fill(T.sg[:, 0:16], 16, 1, "sgp")
     fill(T.sg[:, 272:288], 16, 0, "sgq")
-    fill(T.TX[:, 4096:4128], 32, 0, "TXp")
+    fill(T.TX[:, 4096:TW], TW - 4096, 0, "TXp")
     fill(T.CS[:, 256:264], 8, 0, "CSp")
-    fill(T.KT[:], 32, 0, "KT KTa KTb")
+    fill(T.E[:, 0:98], 98, 0, "E0 E1 KTa")
+    iota(T.YS[:, 0:392], [[0, 8], [1, 49]], 0, 0, "YSa YSb", True)
     fill(T.W1[:, 4096:WW], WW - 4096, 0, "W1p")
     fill(T.W0[:, 4096:WW], WW - 4096, 0, "W0p")
+    send(1, T.TL[0], T.CT[:, 0:256], "rt0", False, "CT CT0")
+    ops[-1][5] = ((3000, 1, 6),) + ops[-1][5][1:]
+    send(0, T.P0[:], T.P0[:], "rp0", True, "P0 TX")
 
     def consts(part):
         if part == 0:
-            ms(cRf, ROUND - 64, "cRf")
-            mm(T.B6[:, 0:131], [(Id, T.Z[:, 12 - 4 * k:143 - 4 * k]) for k in range(4)], "Id Z", "#6")
-            act(T.Z4[:, 0:131], T.B6[:, 0:131], scale=1 / 32, r="#6", w="Z4")
-            ts(T.ip[:, 3:4], T.ip[:, 1:2], 2, ALU.arith_shift_right, r="ip1", w="ip3")
-            cp(cR4, T.ip[:, 3:4], "ip3", "cR4")
-            ts(T.tm[:, 0:16], T.iq4[:], cR4, lt, -2.0, mul, r="iq4 cR4", w="tm0")
-            ts(T.tm[:, 16:32], T.iq4[:], cR4, eq, r="iq4 cR4", w="tm1")
-            tt(T.m16[:, 64:80], T.tm[:, 0:16], T.tm[:, 16:32], add, "tm0 tm1", "m4")
-            spread(T.M4[:], 4, 16, "m4", "M4 M4a M4b")
-            ts(cB4, cR4, 3.0, eq, -2.0, add, r="cR4", w="cB4")
-            ts(cB5, cR4, 3.0, eq, -3.0, add, r="cR4", w="cB5")
+            ms(cRf, ROUND + 64, "cRf")
+            ms(T.LF[:, 264:272], NONE[1] * TINY, "LFp")
             mm(T.B7[:, 0:135], [(Id, T.Z[:, 8:143]), (Id, T.Z[:, 0:135])], "Id Z", "#7")
-            act(T.Z2[:, 0:135], T.B7[:, 0:135], r="#7", w="Z2")
+            act(T.Z2[:, 0:135], T.B7[:, 0:135], scale=1 / 64, r="#7", w="Z2")
             ts(cH0, cR, 8.0, lt, -1.0, mul, r="cR", w="cH0")
             ts(cH1, cR, 8.0, ge, -1.0, mul, r="cR", w="cH1")
+            for j, c in enumerate((cH1, cH0)):
+                act(T.CJ[:, j:128:2], T.ix[:, 0:64], scale=0.0, bias=c, r="ix cH0 cH1", w="CJ%d" % j)
+            act(T.CJ[:], T.CJ[:], scale=2.0, bias=-63 / 128, r="CJ0 CJ1", w="CJ")
+            ts(c512, cR, 512.0, mul, 256.0, add, r="cR", w="c512")
+            ts(cA2, cR, -256.0 * TINY, mul, r="cR", w="cA2")
+            for k, c in enumerate((256.0, c256b, 256.0, c512)):
+                act(T.K2[:, 32 * k:32 * k + 32], T.ix[:, 0:32], scale=0.0, bias=c, r="ix c256b c512", w="K2%d" % k)
             ts(cN0, cR, 0.0, gt, 256.0, mul, r="cR", w="cN0")
             ts(cNs0, cIs0, -1.0, mul, r="cIs0", w="cNs0")
             ts(cNz, cR, 0.0, gt, r="cR", w="cNz")
@@ -540,7 +564,8 @@ def rank_program(g, core, T, topo):
             ts(cS8k, cIs0, -BIG, mul, r="cIs0", w="cS8k")
             for dst, src, s, r, w in ((B256, BO, cN0, "cN0", "B256"), (nBO, BO, -1.0, "", "nBO"), (B8k, BO, BIG, "", "B8k"),
                                       (nB8k, BO, cNzB, "cNzB", "nB8k"), (BN, BO, cNz, "cNz", "BN"), (S0, BO, cIs0, "cIs0", "S0"),
-                                      (Idf, Id, 1.0, "", "Idf"), (nIdf, Id, -1.0, "", "nIdf"), (S0f, BO, cIs0, "cIs0", "S0f"), (nS0, BO, cNs0, "cNs0", "nS0"),
+                                      (Idf, Id, 1.0, "", "Idf"), (Idw, Id, 1 / TINY, "", "Idw"), (qI, Id, 0.25, "", "qI"), (cI, Id, 33 / 128, "", "cI"),
+                                      (n4I, Id, -4.0, "", "n4I"), (nIdf, Id, -1.0, "", "nIdf"), (S0f, BO, cIs0, "cIs0", "S0f"), (nS0, BO, cNs0, "cNs0", "nS0"),
                                       (nB4k, BO, -HOLD / 16, "", "nB4k"), (nS8k, BO, cS8k, "cS8k", "nS8k"), (nI4k, Id, -4096.0, "", "nI4k"),
                                       (Bx, BO, 256.0, "", "Bx"), (nBx, BO, -256.0, "", "nBx")):
                 act(dst, src, scale=s, r="BO Id " + r, w=w)
@@ -549,56 +574,71 @@ def rank_program(g, core, T, topo):
             ms(T.O[:, 15:160:32], 0.0, "Op")
             cp(O(0), T.prbi[:], "prbi", "O0")
             ts(T.iw[:, 0:1], T.ip[:, 0:1], 4, ALU.arith_shift_right, r="ip0", w="iw")
-            ts(T.ip[:, 4:5], T.ip[:, 1:2], 1, ALU.arith_shift_right, r="ip1", w="ip4")
-            ts(cK, T.ip[:, 4:5], 4.0, mul, 3.0, add, r="ip4", w="cK")
-            ts(T.oK[:], T.ix[:, 0:8], 32.0, mul, cK, add, r="ix cK", w="oK")
             lanes_of(1)
             halves_of(1)
         elif part == 2:
-            ts(c64, cR, 64.0, mul, 1024.0, add, r="cR", w="c64")
+            act(cT, cR, scale=68.0, bias=1024.0, r="cR", w="cT")
+            act(T.cum[:, 0:1], cT, r="cT", w="cump")
+            act(cTl, cR, scale=-68.0, bias=-1088.0, r="cR", w="cTl")
+            act(cTe, cTl, scale=-256.0, bias=256.0, r="cTl", w="cTe")
+            ms(T.two[:], 0.0, "two")
+            ms(T.two[:, 3:128:4], 2.0, "two")
+            ms(T.dK[:, 0:128:2], 1.0, "dK")
+            act(T.tm[:, 0:32], T.ix[:, 0:32], scale=2.0, bias=cT, r="ix cT", w="tm0 tm1")
+            act(T.dK[:, 1:64:2], T.tm[:, 0:32], scale=-1.0, r="tm0 tm1", w="dKe")
+            act(T.dK[:, 65:128:2], T.tm[:, 0:32], scale=-1.0, bias=-4.0, r="tm0 tm1", w="dKo")
             ms(c75, 7.5, "c75")
-            ts(cH0b, cR, 8.0, lt, 7.5, mul, r="cR", w="cH0b")
-            ts(cH1b, cR, 8.0, ge, 7.5, mul, r="cR", w="cH1b")
+            act(cH0b, cH0, scale=-7.5 / 64, r="cH0", w="cH0b")
+            act(cH1b, cH1, scale=-7.5 / 64, r="cH1", w="cH1b")
             ms(cSn, -255.5, "cSn")
-            ts(T.B6[:, 256:320], T.ix[:, 0:64], c64, add, r="ix c64", w="#6 dK")
             tt(L0, LT, Z0, add, "LT Z", "L0")
+            act(LTf, LT, r="LT", w="LTf")
+            act(L0f, L0, r="L0", w="L0f")
+            mm(T.B7[:, 176:177], [(LTf, cTl)], "LTf cTl", "#7")
+            mm(T.B7[:, 177:178], [(L0f, cTl)], "L0f cTl", "#7")
+            act(cB0, T.B7[:, 176:177], r="#7", w="cB0")
+            act(cB1x, T.B7[:, 176:177], bias=1.0, r="#7", w="cB1x")
+            act(cBs, T.B7[:, 177:178], scale=-1.0, r="#7", w="cBs")
             tt(A1, Id, LT, sub, "Id LT", "A1")
             act(A1, A1, scale=4096.0, r="A1", w="A1")
-            ts(cB1, cR, -4096.0, mul, -18 * 4096.0, add, r="cR", w="cB1")
+            act(cB1, cR, scale=-4096.0, bias=-18 * 4096.0, r="cR", w="cB1")
             ts(T.m16[:, 16:32], T.iqm[:], 0.0, eq, -2 * HOLD, mul, r="iqm", w="m1")
-            spread(T.LV[:], 1, 16, "m1", "LV")
             ts(T.tm[:, 0:16], T.iqm[:], cR, gt, -BIG, mul, r="iqm cR", w="tm0")
             ts(T.tm[:, 16:32], T.iqm[:], cR, eq, HOLD, mul, r="iqm cR", w="tm1")
             tt(T.tm[:, 32:48], T.tm[:, 0:16], T.tm[:, 16:32], add, "tm0 tm1", "tm2")
             tt(T.m16[:, 32:48], T.tm[:, 32:48], T.m16[:, 16:32], add, "tm2 m1", "m2")
-            spread(T.MK[:], 2, 16, "m2", "MK")
-            ts(cRm, cR, -1.0, add, r="cR", w="cRm")
+            spread(T.MK[:, 0:256], 2, 16, "m2", "MK")
+            cp(T.or2[:, 0:16:2], T.orr[:, 0:8], "orr", "or2")
+            ts(T.or2[:, 1:16:2], T.orr[:, 0:8], 16.0, add, r="orr", w="or3")
+            act(T.m16[:, 64:80], T.m16[:, 16:32], r="m1", w="m4")
+            act(T.m16[:, 80:96], T.tm[:, 32:48], r="tm2", w="m5")
+            act(T.MK[:, 256:512], T.m16[:, 64:96].indirect(T.or2[:]), r="m4 m5 or2 or3", w="MK2")
+            ms(T.LV[:], 0.0, "LV")
+            ms(T.LV[:, 0:256:32], -2 * HOLD, "LV")
+            act(cRm, cR, bias=-1.0, r="cR", w="cRm")
+            ms(cX2, (HOLD + BIG + ROUND) / BIG, "cX2")
             ts(T.tm[:, 0:16], T.iqm[:], cRm, eq, -2.0, mul, r="iqm cRm", w="tm0")
             ts(T.tm[:, 16:32], T.iqm[:], cR, lt, r="iqm cR", w="tm1")
             tt(T.m16[:, 48:64], T.tm[:, 0:16], T.tm[:, 16:32], add, "tm0 tm1", "m3")
-            spread(T.MX[:], 3, 16, "m3", "MX")
+            spread(T.MX[:, 0:256], 3, 16, "m3", "MX")
+            act(T.m16[:, 96:111], T.ones[:, 0:15], r="ones", w="m6")
+            act(T.m16[:, 111:112], cIs0, scale=-2.0, bias=1.0, r="cIs0", w="m6b")
+            act(T.m16[:, 112:128], T.m16[:, 48:64], r="m3", w="m7")
+            act(T.MX[:, 256:512], T.m16[:, 96:128].indirect(T.or2[:]), r="m6 m6b m7 or2 or3", w="MX2")
             act(T.MWk[:], T.MW[:, 0:128], scale=32.0, r="MW", w="MWk")
-            ts(cSi, cIs0, -2 / BIG, mul, 1 / BIG, add, r="cIs0", w="cSi")
-            ts(cX1, cSi, HOLD + BIG - ROUND, mul, r="cSi", w="cX1")
-            ts(cSg, cIs0, -2 * BIG, mul, BIG, add, r="cIs0", w="cSg")
+            act(cSi, cIs0, scale=-2 / BIG, bias=1 / BIG, r="cIs0", w="cSi")
+            act(cX1, cSi, scale=HOLD + BIG + ROUND, r="cSi", w="cX1")
+            act(cSg, cIs0, scale=-2 * BIG, bias=BIG, r="cIs0", w="cSg")
             ts(cD, cR, 4112.0, add, r="cR", w="cD")
+            act(cD2, cR, bias=4128.0, r="cR", w="cD2")
         elif part == 3:
-            for k in range(8):
-                ts(T.MC[:, TRI[k]:TRI[k + 1]], T.ix[:, 0:16 * k + 16], -16.0 * k, add, cR, lt, r="ix cR", w="MC%d" % k)
-            ts(cW, cR, 32.0, mul, 4128.0, add, r="cR", w="cW")
-            ts(T.dW[:], T.ix[:, 0:16], 512.0, mul, cW, add, r="ix cW", w="dW")
-            ts(T.dW[:, 0:1], T.dW[:, 0:1], cN0, mul, 1 / 256, mul, r="dW cN0", w="dW")
-            ts(cY, cR1, cR, mul, 8.0, mul, r="cR cR1", w="cY")
-            ts(T.e1[:, 0:1], cR, 568.0, add, r="cR", w="e10")
-            ts(T.oY[:, 0:1], cY, T.e1[:, 0:1], mn, r="cY e10", w="oS")
-            ts(T.oY[:, 2:3], cY, TRI[4] - 1.0, mn, r="cY", w="oY")
-            ts(T.e1[:, 2:3], cR, 64.0, mul, cY, add, r="cR cY", w="e12")
-            ts(T.oY[:, 4:5], T.e1[:, 2:3], float(TRI[4]), add, TRI[8] - 1.0, mn, r="e12 oY", w="oY")
-            ts(T.oY[:, 6:7], cY, TRI[8] - 1.0, mn, r="cY oY", w="oY")
-            cp(T.MC[:, 0:592].indirect(T.oY[:, 0:1]), T.dW[:], "oS dW", " ".join("MC%d" % k for k in range(8)))
+            act(cY, cR, bias=33.0, r="cR", w="cY")
+            ts(T.MC[:, 0:392], T.YS[:, 0:392], cY, lt, r="YSa YSb cY", w="MC")
+            act(cW, cR, scale=32.0, bias=4128.0, r="cR", w="cW")
+            act(T.MC[:, 1:392:49], T.ix[:, 0:8], scale=512.0, bias=cW, r="ix cW", w="MC")
             tt(Mx, Id, Z0, sub, "Id Z", "Mx")
-            ts(T.e1[:, 1:2], cR, -0.5, mul, 1.0, add, r="cR", w="e11")
-            ts(cG0, cIs0, -8.0, mul, T.e1[:, 1:2], add, r="cIs0 e11", w="cG0")
+            act(T.e1[:, 1:2], cR, scale=-0.5, bias=1.0, r="cR", w="e11")
+            act(cG0, cIs0, scale=-8.0, bias=T.e1[:, 1:2], r="cIs0 e11", w="cG0")
         elif part == 4:
             for t in (2, 3):
                 lanes_of(t)
@@ -609,15 +649,13 @@ def rank_program(g, core, T, topo):
             mm(T.B7[:, 160:176], [(BO, T.xz[:])], "BO xz", "#7")
             act(T.z0[:], T.B7[:, 160:176], r="#7", w="z0")
 
-    def count(out, buf, lo, n, r, w, fresh=True):
+    def count(out, buf, lo, n, r, w):
         for m in range(16):
-            mm1(out, T.Z[:, 15 - m:143 - m], buf[:, lo + m:lo + 16 * n:16], fresh and m == 0, m == 15, r + " Z", w)
+            mm1(out, T.Z[:, 15 - m:143 - m], buf[:, lo + m:lo + 16 * n:16], m == 0, m == 15, r + " Z", w)
 
-    def quick(bk, lo, k0, k1, r):
-        mm(Bk[bk][:, 4 * k0:4 * k1], [(T.Z4[:, 3 - q:131 - q], T.N1[:, lo + 16 * k0 + q:lo + 16 * k1:4]) for q in range(4)], r + " Z4", "#%d" % bk)
-
-    def pick(bk, k0, k1, w):
-        scan(T.RES[:, 4 * k0:4 * k1], Bk[bk][:, 4 * k0:4 * k1], T.M4[:, 4 * k0:4 * k1], 0.0, mx, add, "#%d M4 M4a M4b" % bk, w)
+    def pairs(out, lo, n, stop, r, w):
+        for q in range(8):
+            mm1(out, T.Z2[:, 7 - q:135 - q], T.N1[:, lo + q:lo + 16 * n:8], False, stop and q == 7, r + " Z2", w)
 
     def expand(t):
         recv(1, "rt%d" % (t - 1), False, "TL%d" % (t - 1))
@@ -625,43 +663,29 @@ def rank_program(g, core, T, topo):
         op("g", lambda: g.indirect_dma_start(W[t % 2][:, 0:4096], None, TD[t % 2][:], IndirectOffsetOnAxis(ap=T.iw[:, 0:1], axis=0),
                                              bounds_check=7), "TD%d iw" % (t % 2), "W%d" % (t % 2), "d", 1700.0, 6000.0)
 
-    def values(t, h):
+    def values(t):
         lo = 128 * t
-        if h:
-            act(T.sv[:, lo:lo + 128], T.B7[:, 0:128], r="#7", w="sv%d" % t)
-            send(1, T.lw[:, lo:lo + 128], T.sv[:, lo:lo + 128], "rv%d" % t, False, "sv%d" % t)
+        act(T.sv[:, lo:lo + 128], T.B7[:, 0:128], r="#7", w="sv%d" % t)
+        send(1, T.lw[:, lo:lo + 128], T.sv[:, lo:lo + 128], "rv%d" % t, False, "sv%d" % t)
 
-    def keys(t, h):
-        lo, x = 16 * t + 8 * h, "ab"[h]
-        if ONE:
-            if h:
-                lo = 16 * t
-                act(T.KT[:, 0:8], T.KS[:, 15:128:16], bias=BIG, r="KSa KSb", w="KTa")
-                tt(T.y1[:, 0:16], T.YS[:, 0:576].indirect(T.oY[:, 6:7]), T.KT[:, 0:16], mx, "YSa YSb YSc oY KT KTa", "y1")
-                cp(T.su[:, lo:lo + 8], T.y1[:, 0:8], "y1", "su%d" % t)
-                send(1, T.lu[:, lo:lo + 8], T.su[:, lo:lo + 8], "ru%d" % t, URGENT, "su%d" % t)
-            return
-        act(T.KT[:, 16 * h:16 * h + 4], T.KS[:, 64 * h + 15:64 * h + 64:16], bias=BIG, r="KS" + x, w="KT" + x)
-        tt(T.y1[:, 16 * h:16 * h + 16], T.YS[:, 0:TRI[4 * h + 4]].indirect(T.oY[:, 2 * h + 2:2 * h + 3]), T.KT[:, 16 * h:16 * h + 16], mx,
-           "YSa oY KT KT%s YS%s" % (x, x) + " YSc" * h, "y1" + x)
-        cp(T.su[:, lo:lo + 4], T.y1[:, 16 * h:16 * h + 4], "y1" + x, "su%d%d" % (t, h))
-        send(1, T.lu[:, lo:lo + 4], T.su[:, lo:lo + 4], "r%s%d" % ("xu"[h], t), (False, URGENT)[h], "su%d%d" % (t, h))
+    def keys(t):
+        lo = 16 * t
+        cp(T.su[:, lo:lo + 8], T.YS[:, 0:392:49], "YSa YSb", "su%d" % t)
+        send(1, T.lu[:, lo:lo + 8], T.su[:, lo:lo + 8], "ru%d" % t, False, "su%d" % t)
 
-    def apply_u(t, h, win, wk):
-        lo, n = (16 * t, 8) if ONE else (16 * t + 8 * h, 4)
-        if not h:
-            recv(1, "rv%d" % t, False, "lw%d" % t)
-        if h or not ONE:
-            recv(1, "r%s%d" % ("xu"[h], t), (False, URGENT)[h], "lu%d%d" % (t, h))
-            cp(win[:, 0:WS].indirect(T.lu[:, lo:lo + n]), T.lw[:, 8 * lo:8 * lo + 16 * n], "lu%d%d lw%d %s" % (t, h, t, wk), wk)
+    def apply_u(t, win, wk):
+        recv(1, "rv%d" % t, False, "lw%d" % t)
+        recv(1, "ru%d" % t, False, "lu%d" % t)
+        cp(win[:, 0:WS].indirect(T.lu[:, 16 * t:16 * t + 8]), T.lw[:, 128 * t:128 * t + 128], "lu%d lw%d %s" % (t, t, wk), wk)
 
     def equals(lo, hi, x):
         scan(T.KS[:, 16 * lo:16 * hi], T.B6[:, 16 * lo:16 * hi], T.MWk[:, 16 * lo:16 * hi], 0.0, mx, add, "#6 MWk", "KS" + x)
+        act(T.E[:, 49 * lo:49 * hi:49], T.KS[:, 16 * lo + 15:16 * hi:16], bias=BIG, r="KS" + x, w="KT" + x)
         for k in range(lo, hi):
-            ts(T.E[:, TRI[k]:TRI[k + 1]], T.B6[:, 0:16 * k + 16], T.KS[:, 16 * k + 15:16 * k + 16], sub, BIG, eq, r="#6 KS" + x, w="E%d" % k)
-        for i, j, w in ((lo, hi, "YSa"),) if not lo else ((lo, lo + 2, "YSb"), (lo + 2, hi, "YSc")):
-            back = slice(TRI[j] - 1, TRI[i] - 1 if i else None, -1)
-            scan(T.YS[:, back], T.E[:, back], T.MC[:, back], 0.0, mx, mul, " ".join("E%d MC%d" % (k, k) for k in range(i, j)), w)
+            n = min(48, 16 * k + 16)
+            ts(T.E[:, 49 * k + 49 - n:49 * k + 49], T.B6[:, 16 * k + 16 - n:16 * k + 16], T.KS[:, 16 * k + 15:16 * k + 16], sub, BIG, eq, r="#6 KS" + x, w="E%d" % k)
+        back = slice(49 * hi - 1, 49 * lo - 1 if lo else None, -1)
+        scan(T.YS[:, back], T.E[:, back], T.MC[:, back], 0.0, mx, mul, "MC KT%s " % x + " ".join("E%d" % k for k in range(lo, hi)), "YS" + x)
 
     def starts(t):
         for p in range(16):
@@ -684,12 +708,12 @@ def rank_program(g, core, T, topo):
         send(1, land, so, "ro%d" % t, False, "so%d" % t)
 
     def held():
-        scan(T.KX[:, 255::-1], T.B3[:, 255::-1], T.MK[:, 255::-1], -HOLD, mx, add, "#3 MK", "KX")
-        for lo, x in ((0, "a"), (128, "b")):
-            tt(T.DX[:, lo:lo + 128], T.KX[:, lo:lo + 128], T.B3[:, lo:lo + 128], sub, "#3 KX", "DX" + x)
-        ts(T.oXg[:], T.KX[:, 0:256:16], HOLD - ROUND, add, r="KX", w="oXg")
+        scan(T.KX[:, 255::-1], T.B3[:, 255::-1], T.MK[:, 255::-1], -2 * ROUND, mx, add, "#3 MK", "KX")
+        scan(T.KX[:, 511:255:-1], T.B3[:, 255::-1], T.MK[:, 511:255:-1], -2 * ROUND, mx, add, "#3 MK2", "KX2")
+        ts(T.oXg[:], T.KX[:, 0:256:16], HOLD + ROUND, add, r="KX", w="oXg")
         act(T.FV[:], T.TX[:, 0:TW].indirect(T.oXg[:]), scale=-1.0, bias=255.0, r="TX TXp oXg", w="FV")
-        act(T.x1[:], T.KX[:, 0:256:16], scale=cSi, bias=cX1, r="cSi cX1 KX", w="x1")
+        act(T.x1[:, 0:16:2], T.KX[:, 0:256:32], scale=cSi, bias=cX1, r="cSi cX1 KX", w="x1")
+        act(T.x1[:, 1:16:2], T.KX[:, 16:256:32], scale=1 / BIG, bias=cX2, r="cX2 KX", w="x1b")
 
     def signs(out, l, lo, hi, back, stop, r, w, start=False):
         mm1(out, l, T.sg[:, 16 + lo - back:16 + hi - back], start, stop and hi < 256, r + " sgp " + " ".join("sg%d" % k for k in range(hi // 64)), w)
@@ -697,221 +721,186 @@ def rank_program(g, core, T, topo):
             mm1(out[:, 192 - lo:256 - lo], l, T.sg[:, 288 - back:352 - back], False, stop, r + " sgq sg4", w)
 
     def accepted(lo, hi):
-        out, bk = lifted(lo, hi)
-        mm1(out, S0, T.LV[:, lo:hi], True, False, "S0 LV", bk)
+        out, bk = lifted(lo)
+        mm1(out, S0f, T.G2[:, 8 + lo:8 + hi], True, False, "S0f G2 G2a G2b", bk)
+        mm1(out, S0, T.LV[:, lo:hi], False, False, "S0 LV", bk)
         mm1(out, nS8k, T.step[:, 16 + lo:16 + hi], False, False, "nS8k step", bk)
         signs(out, nB4k, lo, hi, 0, True, "nB4k", bk)
 
-    def lifted(lo, hi):
-        return (T.B5[:, 384:512], "#5") if hi == 128 else (T.B3[:, 256 + lo:256 + hi], "#3")
+    def lifted(lo):
+        return (T.B3[:, 384:512], "#3") if lo else (T.B5[:, 384:512], "#5")
 
     def flip_a(lo, hi, x):
-        back = slice(hi - 1, lo - 1 if lo else None, -1)
         k0, k1 = lo // 16, hi // 16
-        tt(T.ZX[:, lo:hi], lifted(lo, hi)[0], T.DX[:, lo:hi], eq, lifted(lo, hi)[1] + " DX" + x + " DXa" * (not lo), "ZX" + x)
-        scan(T.ZS[:, back], T.MX[:, back], T.ZX[:, back], 0.0, mul, add, "MX ZX" + x, "ZS" + x)
-        tt(T.x2[:, k0:k1], T.ZS[:, lo:hi:16], T.x1[:, k0:k1], add, "x1 ZS" + x, "x2" + x)
-        ts(T.oX2[:, 2 * k0:2 * k1:2], T.x2[:, k0:k1], cSg, mul, cD, mn, r="cSg cD x2" + x, w="oX2" + x)
+        for j, (s, d) in enumerate(((cSg, cD), (BIG, cD2))):
+            y, up = x + str(j), 256 * j
+            back = slice(up + hi - 1, up + lo - 1 if up + lo else None, -1)
+            tt(T.ZX[:, up + lo:up + hi], lifted(lo)[0], T.KX[:, up + lo:up + hi], eq, lifted(lo)[1] + " KX KX2", "ZX" + y)
+            scan(T.ZS[:, back], T.MX[:, back], T.ZX[:, back], 0.0, mul, add, "MX MX2 ZX" + y, "ZS" + y)
+            z = T.x2[:, 16 * j + k0 // 2:16 * j + k1 // 2]
+            tt(z, T.ZS[:, up + lo:up + hi:32], T.x1[:, k0 + j:k1:2], add, "x1 x1b ZS" + y, "x2" + y)
+            ts(T.oX2[:, k0 + j:k1:2], z, s, mul, d, mn, r="cSg cD cD2 x2" + y, w="oX2" + y)
 
-    def flip_b(lo, hi, t):
+    def flip_b(lo, hi):
         for k in range(lo, hi):
-            x = ("ab"[k // 8] if t in SPLIT else "b")
-            cp(T.TX[:, 0:TW].indirect(T.oX2[:, 2 * k:2 * k + 1]), T.FV[:, 16 * k:16 * k + 16], "FV oX2" + x, "TX TXp")
+            x = "ab"[k // 4]
+            cp(T.TX[:, 0:TW].indirect(T.oX2[:, 2 * k:2 * k + 2]), T.FV[:, 32 * k:32 * k + 32], "FV oX2%s0 oX2%s1" % (x, x), "TX TXp")
 
     def offsets1(t):
         s0 = 64 * t
-        for bk, lo, n in ((4, 0, 16), (6, 16, 48)):
+        for lo, hi, bk, sh in PART1:
+            n = hi - lo
             mm1(Bk[bk][:, 0:2 * n], Id, T.K0[:, 64 - n:64 + n], True, False, "Id K0a K0b", "#%d" % bk)
-            mm1(Bk[bk][:, 0:n], Id, T.Ah[:, s0 + lo:s0 + lo + n], False, False, "Id Ah%d" % t, "#%d" % bk)
-            mm1(Bk[bk][:, 0:n], Id, T.Al[:, s0 + lo:s0 + lo + n], False, False, "Id Al%d" % t, "#%d" % bk)
-            mm1(Bk[bk][:, n:2 * n], nI, T.DB[:, s0 + lo:s0 + lo + n], False, False, "nI DB%d" % t, "#%d" % bk)
+            mm1(Bk[bk][:, 0:n], Id, T.Ah[:, s0 + lo:s0 + hi], False, False, "Id Ah%d" % t, "#%d" % bk)
+            mm1(Bk[bk][:, 0:n], Id, T.Al[:, s0 + lo:s0 + hi], False, False, "Id Al%d" % t, "#%d" % bk)
+            mm1(Bk[bk][:, n:2 * n], nI, T.DB[:, s0 + lo:s0 + hi], False, False, "nI DB%d" % t, "#%d" % bk)
 
     offsets1(0)
     for t in range(4):
         Pt, pk, ok = P[t], "P%d" % t, "O%d" % t
-        if t == 0:
-            win, wk, cw = T.CT[:, 0:272], "CT CT0 CTp", 0.0
-        else:
-            win, wk, cw = W[t % 2][:, 0:WW], "W%d W%dp" % (t % 2, t % 2), c256
+        win, wk = (W[t % 2][:, 0:WW], "W%d W%dp" % (t % 2, t % 2)) if t else (T.CT[:, 0:272], "CT CT0 CTp")
         s0 = 64 * t
-        TXw = T.TX[:, 0:4096]
-        w1 = T.WS[:, 15:1024:16]
-        for x, bk, lo, n, r in (("a", 4, 0, 16, "GWa"), ("b", 6, 16, 48, "GWb GWc")):
-            scan(T.WS[:, 16 * lo:16 * (lo + n)], T.GW[:, 16 * lo:16 * (lo + n)], T.MW[:, 0:16 * n], 0.0, mx, add, r + " MW", "WS" + x)
-            ts(T.oP[:, lo:lo + n], w1[:, lo:lo + n], c256b, add, r="c256b WS" + x, w="oP" + x)
-            mm1(Bk[bk][:, 0:n], Id, w1[:, lo:lo + n], False, False, "Id WS" + x, "#%d" % bk)
-            mm1(Bk[bk][:, n:2 * n], Id, w1[:, lo:lo + n], False, True, "Id WS" + x, "#%d" % bk)
-            cp(T.oTQ[:, 2 * lo:2 * (lo + n)], Bk[bk][:, 0:2 * n], "#%d" % bk, "oTQ" + x)
-        act(T.sz[:, 1:65], w1, AF.Sign, bias=256.0, r="WSa WSb", w="sz")
+        w1, WS1 = T.WS[:, 15:1024:16], span("WS", 0, 64, 2)
+        offsets(PART1)
         if t > 0:
-            flip_b(14, 16, t - 1)
+            flip_b(7, 8)
             recv(t, "rp%d" % t, True, pk)
-        turn = (0, 4, 1, 2, 3, 5, 6, 7)
-        for h in turn:
-            n, x = 16 if h < 7 else 15, "ab"[h % 4 > 0]
-            lo = 16 if h == 4 else 16 * h
-            o = T.oP[:, lo:lo + 16] if h < 4 else T.oTQ[:, lo:lo + n]
-            act(T.PG[:, 512 * h:512 * h + 16 * n], Pt[:, 0:4096].indirect(o), r=pk + (" oP" if h < 4 else " oTQ") + x, w="PG%d" % h)
-        if t > 0:
             send(1, T.TL[t], T.TS[t], "rt%d" % t, False, "TS%d" % t)
         else:
             consts(0)
-        if QUICK:
-            act(T.M4[:, 3:256:4], T.sz[:, 0:64], scale=-0.25, bias=cB5, r="sz szp cB5 M4", w="M4a M4b")
-            ts(T.T1[:, 0:128:2], w1, -256.0, gt, r="WSa WSb", w="T10")
-            act(T.T1[:, 1:128:2], w1, AF.Sign, bias=256.0, r="WSa WSb", w="T11")
-        else:
-            mm1(T.B0[:, 0:64], nI8, T.sz[:, 1:65], True, False, "nI8 sz", "#0")
-            mm1(T.B1[:, 0:64], nI8, T.sz[:, 0:64], True, False, "nI8 sz szp", "#1")
-        for h in turn:
-            n, lo, y = 16 if h < 7 else 15, 256 * h + 16 * (h // 4), 16 * (h % 4) + 16 * (h % 4 > 0)
-            tt(T.N1[:, lo:lo + 16 * n], TXw.indirect(T.oTQ[:, y:y + n]), T.PG[:, 512 * h:512 * h + 16 * n], eq,
-               "TX PG%d oTQ%s" % (h, "ab"[h % 4 > 0]), "Q%d" % h)
-            if not QUICK:
-                if h == 3:
-                    count(T.B0[:, 0:64], T.N1, 0, 64, "Q0 Q1 Q2 Q3", "#0", False)
-                    act(T.T1[:, 64:128], T.B0[:, 0:64], AF.Relu, scale=-100.0, r="#0", w="T1")
-                if h == 7:
-                    count(T.B1[:, 0:64], T.N1, 1024, 64, "Q4 Q5 Q6 Q7 N1p", "#1", False)
-                continue
-            if h in (1, 3):
-                lo = 32 * (h - 1)
-                mm1(T.B0[:, lo:lo + 64], nI8, T.T1[:, lo:lo + 64], True, False, "nI8 T10 T11", "#0")
-                for q in range(8):
-                    mm1(T.B0[:, lo:lo + 64], T.Z2[:, 7 - q:135 - q], T.N1[:, 8 * lo + q:8 * lo + 512:8], False, q == 7, "Z2 Q%d Q%d" % (h - 1, h), "#0")
-            if h > 3:
-                quick(1 if h < 7 else 7, 1024, (0, 17, 33, 49)[h - 4], (17, 33, 49, 64)[h - 4], "N1p Q%d" % h)
-        if QUICK:
-            for j, c in enumerate((cH0, cH1)):
-                act(T.TH[:, 64 * j:64 * j + 64], T.B0[:, j:128:2], AF.Sign, scale=c, bias=-0.5, r="#0 cH0 cH1", w="TH%d TH%d" % (2 * j, 2 * j + 1))
-            mm(T.B0[:, 128:192], [(Id, T.TH[:, 0:64]), (Id, T.TH[:, 64:128])], "Id TH0 TH1 TH2 TH3", "#0")
-            pick(1, 0, 49, "RESa")
-            pick(7, 49, 64, "RESb")
+        ts(T.T1[:, 2:130:2], w1, -256.0, gt, r=WS1, w="T10")
+        act(T.T1[:, 3:130:2], w1, AF.Sign, bias=256.0, r=WS1, w="T11")
+        for j in range(2):
+            act(T.A2[:, j:128:2], T.A[:, s0:s0 + 64], scale=TINY, r="A%d" % t, w="A2%d" % j)
+            act(T.A2[:, 128 + j:256:2], T.A[:, s0:s0 + 64], scale=-TINY, bias=cA2 if t else 0.0, r="cA2 A%d" % t, w="A2%d" % (j + 2))
+        J = T.B1[:, 0:128]
+        mm1(J, Id, T.CJ[:], True, False, "Id CJ", "#1")
+        mm1(T.B0[:, 0:128], hI, T.CJ[:], True, False, "hI CJ", "#0")
+        done = {"i": 0, "j": 0}
+
+        def counts1(side, hi):
+            lo, last = done[side], [x[2] for x in TURN1 if x[0] == side][-2:]
+            if hi - lo < 26 and hi not in last[side == "i":]:
+                return
+            if side == "i":
+                pairs(T.B0[:, 2 * lo:2 * hi], 16 * lo, hi - lo, False, span("Q", 16 * lo, 16 * hi, 16), "#0")
+                if hi == 64:
+                    mm1(T.B0[:, 0:128], nI8, T.T1[:, 2:130], False, True, "nI8 T10 T11", "#0")
+            else:
+                lo, up = lo + (lo > 0), min(hi + 1, 64)
+                pairs(J[:, 2 * lo:2 * up], 1024 + 16 * lo, up - lo, hi == 64, "N1p" + span("Q", max(1040, 1024 + 16 * lo), 1024 + 16 * up, 16), "#1")
+                if hi == last[0]:
+                    act(T.TH[:], T.B0[:, 0:128], AF.Sign, scale=-1.0, bias=61 / 256, r="#0", w="TH")
+                    mm1(J, nI8, T.T1[:, 0:128], False, False, "nI8 T10 T11 T1p", "#1")
+                    mm1(J, hI, T.TH[:], False, False, "hI TH", "#1")
+            done[side] = hi
+
+        duels(PART1, TURN1, PLAIN[0], 0, Pt, pk, counts1)
         act(T.CW[:, 0:256], T.ix[:], scale=0.0, bias=cRf, r="ix cRf", w="CWa")
         if t > 0:
-            act(T.CW[:, 3072:3328], T.ix[:], scale=0.0, r="ix", w="CWb")
-        if t == 0:
+            act(T.CW[:, CW1:CW1 + 256], T.ix[:], scale=0.0, r="ix", w="CWb")
+            recv(1, "ro%d" % (t - 1), False, ok)
+        else:
             consts(1)
             starts(0)
-        else:
-            recv(1, "ro%d" % (t - 1), False, ok)
-        X2 = T.B4[:, 128:192]
-        mm1(X2, Id, T.K0[:, 32:96], True, False, "Id K0a K0b", "#4")
-        mm1(X2[:, 0:32], Id, T.Ah[:, s0 + 2:s0 + 65:2], False, False, "Id Ah%d Ah%d" % (t, t + 1), "#4")
-        mm1(X2[:, 0:32], Id, T.Al[:, s0 + 2:s0 + 65:2], False, False, "Id Al%d Al%d" % (t, t + 1), "#4")
-        if QUICK:
-            tt(T.dead[:], T.RES[:, 3:256:4], T.B0[:, 128:192], lt, "RESa RESb #0", "dead")
-        else:
-            tt(T.dead[:], T.B1[:, 0:64], T.T1[:, 64:128], lt, "#1 T1", "dead")
+        for lo, hi, bk, sh in PART2:
+            mm1(Bk[bk][:, 0:2 * (hi - lo)], Id, T.K2[:, 64 * (t > 0) + 32 + lo - hi:64 * (t > 0) + 32 + hi - lo], True, False, "Id K20 K21 K22 K23", "#%d" % bk)
+        scan(T.LF[:, 0:128], J, T.A2[:, 0:128], NONE[0] * TINY, mx, mn, "#1 A20 A21", "LFa")
+        scan(T.LF[:, 263:135:-1], T.B1[:, 127::-1], T.A2[:, 255:127:-1], NONE[1] * TINY, mx, mn, "#1 A22 A23", "LFb")
+        tt(T.nd[:], T.LF[:, 3:128:4], T.LF[:, 140:265:4], add, "LFa LFb LFp", "nd")
+        ts(T.oW2[:], T.nd[:], -1 / TINY, mul, c256b if t else 256.0, mn, r="nd c256b", w="oW2")
         if t < 3:
             expand(t + 1)
-        scan(T.GS[:, 1:64], T.dead[:, 0:63], T.DL[:, s0 + 1:s0 + 64], BIG, mul, add, "dead DL%d" % t, "GS")
-        scan(T.D2[:, 63:0:-1], T.dead[:, 63:0:-1], T.GS[:, 63:0:-1], BIG, mul, mx, "dead GS", "D2")
-        ts(T.oW2[:], T.D2[:, 2:65:2], 256.0, mn, cw, add, r="D2 D2p c256", w="oW2")
-        act(T.GW[:, 256:512], win.indirect(T.oW2[:, 16:32]), r=wk + " oW2", w="GWb GWc")
-        cp(T.GW[:, 0:256], win.indirect(T.oW2[:, 0:16]), wk + " oW2", "GWa")
-        mm1(X2[:, 0:32], nI, T.GS[:, 2:65:2], False, False, "nI GS GSp", "#4")
-        mm1(X2[:, 32:64], nI, T.D2[:, 2:65:2], False, False, "nI D2 D2p", "#4")
-        if QUICK2:
-            for k, (lo, c, b) in enumerate(((1, 1, -1.0), (0, 1, -3.0), (65, 0, -3.0), (64, 0, -1.0))):
-                act(T.TH[:, lo:lo + 63:2], T.dead[:, c:64:2], scale=2.0, bias=b, r="dead", w="TH%d" % k)
-        else:
-            for k, (lo, b) in enumerate(((0, 0.0), (65, -100.0), (130, 0.0))):
-                act(T.TH[:, lo:lo + 64], T.dead[:], scale=100.0, bias=b, r="dead", w="TH%d" % k + " TH3" * (k < 2) + " TH2" * (k == 1) + " TH1" * (k == 0))
+        witnesses(PART2, win, T.oW2, wk + " oW2")
+        for lo, hi, bk, sh in PART2:
+            mm1(Bk[bk][:, 0:hi - lo], Idw, T.LF[:, 3 + 4 * lo:4 * hi:4], False, False, "Idw LFa", "#%d" % bk)
+            mm1(Bk[bk][:, hi - lo:2 * (hi - lo)], Idw, T.nd[:, lo:hi], False, False, "Idw nd", "#%d" % bk)
+        for k in range(4):
+            act(T.AE[:, 64 * (k // 2) + k % 2:64 * (k // 2) + 64:2], T.B1[:, k:128:4], AF.Sign, r="#1", w="AE%d" % k)
+        ae, ao, AE = T.AE[:, 0:64], T.AE[:, 64:128], " AE0 AE1 AE2 AE3"
+        mm(T.B7[:, 192:256], [(Id, ae), (n4I, ao)], "Id n4I" + AE, "#7")
+        act(T.UU[:, 128:192], T.B7[:, 192:256], bias=3.5 + 47.5 / 64, r="#7", w="TI")
+        xi, xj = T.B0[:, 0:64], T.B1[:, 128:192]
+        mm1(xi, Id, ae, True, False, "Id" + AE, "#0")
+        mm1(xi, qI, ao, False, False, "qI" + AE, "#0")
+        mm1(xj, cI, T.ones[:, 0:64], True, False, "cI ones", "#1")
+        mm1(xj, qI, ae, False, False, "qI" + AE, "#1")
         for p in range(16):
             act(T.V[:, p:1024:16], Bk[2 + p // 8][:, 64 * (p % 8):64 * (p % 8) + 64], bias=O(t, p, p + 1),
                 r="#%d %s" % (2 + p // 8, ok), w="V")
         tt(T.dO[:], O(t), O(t, -1, 15), sub, ok + " Op", "dO")
         tt(XO, T.dO[:, 0:16].indirect(T.orr[:, 0:8]), BO, mul, "dO orr BO", "XO")
-        w2 = T.WS[:, 15:512:16]
-        for lo, x, r in ((0, "a", "GWa"), (16, "b", "GWb GWc")):
-            scan(T.WS[:, 16 * lo:16 * lo + 256], T.GW[:, 16 * lo:16 * lo + 256], T.MW[:, 0:256], 0.0, mx, add, r + " MW", "WS" + x)
-            ts(T.oP[:, lo:lo + 16], w2[:, lo:lo + 16], c256b, add, r="c256b WS" + x, w="oP" + x)
-        if QUICK2:
-            act(T.sz[:, 1:33], w2, AF.Sign, bias=256.0, r="WSa WSb", w="sz")
-        mm1(X2[:, 0:32], Id, w2, False, False, "Id WSa WSb", "#4")
-        mm1(X2[:, 32:64], Id, w2, False, True, "Id WSa WSb", "#4")
-        cp(T.oTQ[:, 0:64], X2, "#4", "oTQa oTQb")
-        for h in range(4):
-            n = 16 if h < 3 else 15
-            o = T.oP[:, 16 * h:16 * h + 16] if h < 2 else T.oTQ[:, 16 * h:16 * h + n]
-            act(T.PG[:, 512 * h:512 * h + 16 * n], Pt[:, 0:4096].indirect(o), r=pk + (" oP" + "ab"[h] if h < 2 else " oTQa oTQb"), w="PG%d" % h)
-        if QUICK2:
-            act(T.M4[:, 3:128:4], T.sz[:, 1:33], scale=-0.25, bias=cB4, r="sz cB4 M4", w="M4a")
-            act(T.M4[:, 131:256:4], T.sz[:, 0:32], scale=-0.25, bias=cB4, r="sz szp cB4 M4", w="M4b")
-        else:
-            ts(T.s2[:, 0:32], w2, -256.0, gt, r="WSa WSb", w="s2a")
-            ts(T.s2[:, 33:65], w2, -256.0, gt, r="WSa WSb", w="s2b")
-            mm1(T.B0[:, 0:64], nI8, T.s2[:, 0:64], True, False, "nI8 s2a s2b s2p", "#0")
+        w2, WS2 = T.WS[:, 15:512:16], span("WS", 0, 32, 2)
+        offsets(PART2)
+        ts(T.T2[:, 2:66:2], w2, -256.0, gt, r=WS2, w="T20")
+        act(T.T2[:, 3:66:2], w2, AF.Sign, bias=256.0, r=WS2, w="T21")
         mm(T.B5[:, 0:128], [(XO, Id)], "XO Id", "#5")
         act(dOT, T.B5[:, 0:128], scale=cNz, r="#5 cNz", w="dOT")
         act(dO0, T.B5[:, 0:128], scale=cIs0, r="#5 cIs0", w="dO0")
         act(T.fine[:, 256:384], dOT, scale=1 / 256, r="dOT", w="fine")
         mm(T.B7[:, 128:144], [(ShI, O(t))], "ShI " + ok, "#7")
         act(T.Dp[:], T.B7[:, 128:144], r="#7", w="Dp")
-        for h in range(4):
-            n, lo = 16 if h < 3 else 15, 512 + 256 * h + 16 * (h // 2)
-            tt(T.N1[:, lo:lo + 16 * n], TXw.indirect(T.oTQ[:, 16 * (h % 2):16 * (h % 2) + n]), T.PG[:, 512 * h:512 * h + 16 * n], eq,
-               "TX oTQa oTQb PG%d" % h, "Q%d" % (h + 2))
-            if QUICK2:
-                quick(1 if h < 3 else 0, 512, (0, 16, 32, 49)[h], (16, 32, 49, 64)[h], "N1p Q%d" % (h + 2))
-        if QUICK2:
-            pick(1, 0, 49, "RESa")
-            pick(0, 49, 64, "RESb")
-        else:
-            count(T.B0[:, 0:64], T.N1, 512, 64, "Q2 Q3 Q4 Q5 N1p", "#0", False)
+
+        def counts2(side, hi):
+            if side == "i" and hi == 32:
+                pairs(xi, 512, 32, False, span("Q", 512, 1024, 16), "#0")
+                mm1(xi, nI8, T.T2[:, 2:66], False, True, "nI8 T20 T21", "#0")
+                mm1(xj, nI8, T.T2[:, 0:64], False, False, "nI8 T20 T21 T2p", "#1")
+            elif hi == 32:
+                pairs(xj, 1024, 32, True, "N1p" + span("Q", 1040, 1536, 16), "#1")
+
+        duels(PART2, TURN2, PLAIN[1], 512, Pt, pk, counts2)
         if t == 0:
             consts(2)
         if t == 1:
             consts(5)
-        if QUICK2:
-            tt(T.K[:], T.RES[:, 0:256].indirect(T.oK[:]), T.TH[:, 0:128], lt, "RESa RESb oK TH0 TH1 TH2 TH3", "K Ke")
-        else:
-            tt(T.K[:, 1:128:2], T.B0[:, 0:64], T.TH[:, 1:129:2], lt, "#0 TH0 TH1 TH3", "K")
-            tt(T.K[:, 0:128:2], T.B0[:, 0:64], T.TH[:, 66:194:2], lt, "#0 TH1 TH2 TH3", "Ke")
-        tt(T.dead2[:], T.K[:, 0:64], T.K[:, 64:128], mx, "K Ke", "dead2")
-        scan(T.cum[:], T.ones[:, 0:64], T.dead2[:], 0.0, add, sub, "ones dead2", "cum")
+        ts(T.UU[:, 0:64], xi, 47.5 / 64, lt, 0.5, add, r="#0", w="Ue")
+        tt(T.UU[:, 64:128], xi, T.UU[:, 128:192], lt, "#0 TI", "Uo")
         mm1(T.B4[:, 256:512], dO0, T.ones[:], True, False, "dO0 ones", "#4")
-        mm(T.B5[:, 128:129], [(LT, T.cum[:, 63:64])], "LT cum", "#5")
-        mm(T.B5[:, 129:130], [(L0, T.cum[:, 63:64])], "L0 cum", "#5")
+        tt(T.W4[:, 0:128:2], xj, T.UU[:, 0:64], gt, "#1 Ue", "We")
+        tt(T.W4[:, 1:128:2], xj, T.UU[:, 64:128], gt, "#1 Uo", "Wo")
+        scan(T.cum[:, 1:129], T.W4[:], T.two[:], cT, add, add, "We Wo two cT", "cum")
+        for j, x in enumerate("eo"):
+            scan(T.DD[:, 64 * j:64 * j + 64], T.W4[:, j:128:2], T.dK[:, 64 * j:64 * j + 64], 0.0, mx, mul, "dK dKe dKo W" + x, "D" + x)
         base = T.B5[:, 128:129]
-        tt(T.B6[:, 320:384], T.B6[:, 256:320], T.dead2[:], mul, "dead2 #6", "#6 dK")
-        tt(T.u0[:], T.B6[:, 320:384], T.cum[:], mx, "dK cum #6", "u0")
+        mm(base, [(LTf, T.cum[:, 128:129])], "LTf cum", "#5")
+        mm(T.B7[:, 128:129], [(L0f, T.cum[:, 128:129])], "L0f cum", "#7")
+        for j, x in enumerate("eo"):
+            tt(T.u0[:, 32 * j:32 * j + 32], T.cum[:, 4 * j:128 + j:4], T.DD[:, 64 * j + 1:64 * j + 64:2], add, "cum cump D" + x, "u" + x)
+        for j, x in enumerate("eo"):
+            ts(T.oR[:, j:64:2], T.u0[:, 32 * j:32 * j + 32], base, add, (cB0, cB1x)[j], add, r="#5 cB0 cB1x u" + x, w="R" + x)
         st, stp = T.step[:, 16:272], T.step[:, 15:271]
-        ts(T.oR[:], T.u0[:], base, add, -1.0, add, r="u0 #5", w="oR")
-        ts(st, T.ix[:], T.B5[:, 129:130], ge, r="ix #5", w="step")
+        ts(st, T.ix[:], cBs, add, T.B7[:, 128:129], ge, r="ix cBs #7", w="step")
         mm1(T.B4[:, 256:512], dOT, st, False, False, "dOT step", "#4")
         mm1(T.B4[:, 256:512], B256, st, False, True, "B256 step", "#4")
         k = 64 - SHARE
-        act(T.CW[:, 3072:6144].indirect(T.oR[:, k:64]), T.V[:, 16 * k:1024], AF.Silu, bias=None, r="oR V", w="CWb")
-        ts(T.CW[:, 0:3072].indirect(T.oR[:, 0:16]), T.V[:, 0:256], 1.0, mul, ROUND - 64, add, r="oR V", w="CWa")
+        act(T.CW[:, CW1:2 * CW1].indirect(T.oR[:, k:64]), T.V[:, 16 * k:1024], AF.Silu, bias=None, r="oR Re Ro V", w="CWb")
+        ts(T.CW[:, 0:CW1].indirect(T.oR[:, 0:16]), T.V[:, 0:256], -1.0, mul, ROUND + 64, add, r="oR Re Ro V", w="CWa")
         cp(T.oPP[:], T.B4[:, 256:512], "#4", "oPP")
-        stays()
-        ts(T.CW[:, 0:3072].indirect(T.oR[:, 16:k]), T.V[:, 256:16 * k], 1.0, mul, ROUND - 64, add, r="oR V", w="CWa")
+        ts(T.CW[:, 0:CW1].indirect(T.oR[:, 16:k]), T.V[:, 256:16 * k], -1.0, mul, ROUND + 64, add, r="oR Re Ro V", w="CWa")
+
+        def cuts(h):
+            return zip((32 * h,), (32 * h + 32,)) if h else ((0, HEAD), (HEAD, 32))
 
         def items(h):
-            act(T.PG[:, 512 * h:512 * h + 512], Pt[:, 0:4096].indirect(T.oPP[:, 32 * h:32 * h + 32]), r=pk + " oPP", w="PG%d" % h)
+            for lo, hi in cuts(h):
+                act(T.PG[:, 16 * lo:16 * hi], Pt[:, 0:4096].indirect(T.oPP[:, lo:hi]), r=pk + " oPP", w=span("PG", 16 * lo, 16 * hi, 32))
 
         items(0)
         items(1)
-        tt(T.G2[:, 8:136], T.CW[:, 0:128], T.CW[:, 3072:3200], add, "CWa CWb", "G2")
-        tt(T.G2[:, 136:264], T.CW[:, 128:256], T.CW[:, 3200:3328], add, "CWa CWb", "G2b")
+        for lo, hi, x in ((0, FIRST, "G2"), (FIRST, 128, "G2a"), (128, 256, "G2b")):
+            scan(T.G2[:, 8 + lo:8 + hi], T.CW[:, CW1 + lo:CW1 + hi], T.CW[:, lo:hi], 0.0, mx, sub, "CWa CWb", x)
+            ts(T.oTT[:, lo:hi], T.G2[:, 8 + lo:8 + hi], ROUND, add, r=x, w=span("oTT", lo, hi, 32))
         if t == 3:
             recv(1, "rt3", False, "TL3")
             dma("g", T.CW[0:128:16, 0:4096], T.TL[3], "TL3", "CWa CWb")
         vv = T.B5[:, 256:384]
         for k, (l, y) in enumerate(((dO0, T.ones[:]), (dOT, st), (B8k, st), (nB8k, stp))):
             mm1(vv, l, y[:, 0:128], k == 0, False, "dO0 ones dOT step stepp B8k nB8k", "#5")
-        ts(T.oTT[:, 0:128], T.G2[:, 8:136], -ROUND, add, r="G2", w="oTT0")
-        ts(T.oTT[:, 128:256], T.G2[:, 136:264], -ROUND, add, r="G2b", w="oTT1")
         mm(T.B4[:, 0:256], [(dO0, T.fine[:, 0:256]), (T.fine[:, 256:384], st)], "dO0 step fine0 fine", "#4")
-        mm1(vv[:, 0:128], Idf, T.G2[:, 8:136], False, False, "G2 Idf", "#5")
-        mm1(vv[:, 0:128], nIdf, T.G2[:, 7:135], False, True, "G2 nIdf", "#5")
-        if DDV:
-            tt(T.dd[:, 0:128], T.G2[:, 136:264], T.G2[:, 135:263], sub, "G2 G2b", "dd")
-        else:
-            mm(T.B0[:, 384:512], [(Idf, T.G2[:, 136:264]), (nIdf, T.G2[:, 135:263])], "G2 G2b Idf nIdf", "#0")
-            act(T.dd[:, 0:128], T.B0[:, 384:512], r="#0", w="dd")
+        mm1(vv, Idf, T.G2[:, 8:136], False, False, "G2 G2a Idf", "#5")
+        mm1(vv, nIdf, T.G2[:, 7:135], False, True, "G2 G2a nIdf", "#5")
+        scan(T.dd[:, 0:128], T.G2[:, 136:264], T.G2[:, 135:263], 0.0, mn, sub, "G2a G2b", "dd")
         for k, (l, y) in enumerate(((dO0, T.ones[:]), (dOT, st), (B8k, st), (nB8k, stp))):
             mm1(T.B0[:, 256:384], l, y[:, 128:256], k == 0, False, "dO0 ones dOT step stepp B8k nB8k", "#0")
         mm1(T.B0[:, 256:384], Id, T.dd[:, 0:128], False, True, "Id dd", "#0")
@@ -937,17 +926,17 @@ def rank_program(g, core, T, topo):
                 mm1(T.B6[:, lo // 2:hi // 2], l, y, False, k == (1 if lo else 3), "BO nBx t1" + x + " t2a" * (k > 1), "#6")
             mm(T.B7[:, lo // 2:hi // 2], one + two if lo else one, "BO Bx t1" + x + " t2b" * (lo > 0), "#7")
 
-        split = t in SPLIT
         for h in range(4):
-            nk = "N%d N%d" % (2 * h, 2 * h + 1)
+            nk = "N%d N%d" % (2 * h, 2 * h + 1) + " N0x" * (h == 0)
             for j in (2 * h, 2 * h + 1):
-                tt(T.NN[:, 512 * j:512 * j + 512], TXw.indirect(T.oTT[:, 32 * j:32 * j + 32]), T.PG[:, 512 * j:512 * j + 512], eq,
-                   "TX oTT%d PG%d" % (j // 4, j), "N%d" % j)
+                for lo, hi in cuts(j):
+                    tt(T.NN[:, 16 * lo:16 * hi], TXw.indirect(T.oTT[:, lo:hi]), T.PG[:, 16 * lo:16 * hi], eq,
+                       "TX" + span("oTT", lo, hi, 32) + span("PG", 16 * lo, 16 * hi, 32), "N%d" % j + "x" * (hi == HEAD))
             if h == 0:
-                mm1(T.B3[:, 0:128], S0f, T.G2[:, 8:136], True, True, "G2 S0f", "#3")
+                mm1(T.B3[:, 0:128], S0f, T.G2[:, 8:136], True, True, "G2 G2a S0f", "#3")
             if h == 1:
                 mm1(T.B3[:, 128:256], S0f, T.G2[:, 136:264], True, True, "G2b S0f", "#3")
-            if h == 2 and split:
+            if h == 2:
                 held()
             bk = (6, 1, 7, 1)[h]
             if h < 3:
@@ -963,62 +952,47 @@ def rank_program(g, core, T, topo):
                 items(2 * h + 4)
                 items(2 * h + 5)
             if h == 1:
-                act(T.sn[:, 0:128], vv[:, 0:128], AF.Sign, bias=cSn, r="#5 cSn", w="sna")
+                act(T.sn[:, 0:128], vv, AF.Sign, bias=cSn, r="#5 cSn", w="sna")
                 act(T.sn[:, 128:256], T.B0[:, 256:384], AF.Sign, bias=cSn, r="#0 cSn", w="snb")
             if h == 2:
-                if split:
-                    accepted(0, 128)
+                accepted(0, 128)
                 named(0, 128, "a")
-                if split:
-                    flip_a(0, 128, "a")
+                flip_a(0, 128, "a")
         if t == 0:
             consts(3)
-        if not split:
-            held()
         slots(0, 128, "a")
         named(128, 256, "b")
-        values(t, 0)
         equals(0, 4, "a")
-        if split:
-            flip_b(0, 8, t)
-            accepted(128, 256)
-            flip_a(128, 256, "b")
-        else:
-            accepted(0, 256)
-            flip_a(0, 256, "b")
+        flip_b(0, 4)
+        accepted(128, 256)
+        flip_a(128, 256, "b")
         slots(128, 256, "b")
         signs(T.B0[:, 0:256], L0, 0, 256, 0, True, "L0", "#0", True)
-        values(t, 1)
+        values(t)
         act(T.G0[:], T.B0[:, 0:256], AF.Relu, bias=cG0, scale=-0.5, r="#0 cG0", w="G0")
-        keys(t, 0)
-        act(cE, T.cum[:, 63:64], AF.Relu, bias=256.0, scale=-256.0, r="cum", w="cE")
-        ts(T.oE[:, 0:1], base, cE, add, 256.0, mn, r="cE #5", w="oE")
+        act(cE, T.cum[:, 128:129], AF.Relu, bias=cTe, scale=-256.0, r="cum cTe", w="cE")
+        act(cE2, cE, bias=cB0, r="cE cB0", w="cE2")
+        ts(T.oE[:, 0:1], base, cE2, add, 256.0, mn, r="cE2 #5", w="oE")
         equals(4, 8, "b")
-        keys(t, 1)
+        keys(t)
         places(t)
         if t == 0:
             consts(4)
         if t < 3:
             starts(t + 1)
             offsets1(t + 1)
-            flip_b(8 if split else 0, 10, t)
+            flip_b(4, 7)
             wn, wnk = W[(t + 1) % 2], "W%d W%dp" % ((t + 1) % 2, (t + 1) % 2)
-            apply_u(t, 0, wn, wnk)
-            apply_u(t, 1, wn, wnk)
-            flip_b(10, 14, t)
-            act(T.GW[:, 16 * WSH:1024], wn[:, 0:WW].indirect(T.oW1[:, s0 + 64 + WSH:s0 + 128]), r=wnk + " oW1%d" % (t + 1), w="GWb")
+            apply_u(t, wn, wnk)
+            witnesses(PART1, wn[:, 0:WW], T.oW1[:, s0 + 64:s0 + 128], wnk + " oW1%d" % (t + 1))
             dma("y", T.TS[t + 1], wn[0:128:16, 0:4096], wnk, "TS%d" % (t + 1))
-            cp(T.GW[:, 0:256], wn[:, 0:WW].indirect(T.oW1[:, s0 + 64:s0 + 80]), wnk + " oW1%d" % (t + 1), "GWa")
-            if WSH > 16:
-                cp(T.GW[:, 256:16 * WSH], wn[:, 0:WW].indirect(T.oW1[:, s0 + 80:s0 + 64 + WSH]), wnk + " oW1%d" % (t + 1), "GWc")
         else:
-            flip_b(8 if split else 0, 16, t)
+            flip_b(4, 8)
             dma("y", T.yt[:, 0:2048], T.TX[:, 0:2048], "TX", "yta", lat=4500.0)
             dma("a", T.yt[:, 2048:4096], T.TX[:, 2048:4096], "TX", "ytb", lat=4500.0)
             recv(1, "ro3", False, "o32")
             dma("y", T.yo[:], T.o32[:, 16:32], "o32", "yo")
-            apply_u(3, 0, T.CW, "CWa CWb")
-            apply_u(3, 1, T.CW, "CWa CWb")
+            apply_u(3, T.CW, "CWa CWb")
             cp(T.CW[:, 0:4096:256], T.z0[:], "z0 CWa", "CWa CWb")
             dma("a", T.yw[:], T.CW[0:128:16, 0:4096], "CWa CWb", "yw")
     _emit(g, T, ops)

@@ -9,57 +9,63 @@ WS = 8224
 TW = 4144
 CW1 = 3200
 ORDER = []
-TRIES, MOVES = 16, 400
+TRIES, MOVES = 44, 300
 PACES = ((0.83, 1.0, 1.9, 150.0, 110.0, 10.0, 400.0, 0.42), (0.87, 1.3, 3.1, 190.0, 128.0, 10.0, 700.0, 0.45),
-         (1.1, 1.0, 2.5, 170.0, 122.0, 10.0, 500.0, 0.72), (1.15, 1.7, 4.5, 240.0, 165.0, 20.0, 1100.0, 0.6))
-LINK = 1900.0
+         (1.1, 1.0, 2.5, 170.0, 122.0, 10.0, 500.0, 0.58), (1.2, 1.9, 6.5, 240.0, 185.0, 20.0, 1000.0, 0.6))
+LOADS = (4400.0, 6000.0)
+LINK = 1600.0
+BULK = 16000.0
 TINY = 2.0 ** -21
 NONE = (-6000.0, -12000.0)
 ROUND = 1.5 * 2.0 ** 23
 SHARE = 34
-PART1 = ((0, 8, 4, "v8"), (8, 28, 6, "v28"), (28, 64, 5, "a64"))
+PART1 = ((0, 8, 4, "v8"), (8, 28, 6, "a28"), (28, 64, 5, "v46 a64"))
 TURN1 = (("i", 0, 8), ("j", 0, 8), ("i", 8, 28), ("i", 28, 46), ("i", 46, 64), ("j", 8, 28), ("j", 28, 46), ("j", 46, 64))
+COUNT1 = {"i": (64,), "j": (28, 46, 64)}
+PARTL = ((0, 16, 4, "v16"), (16, 40, 6, "a40"), (40, 64, 5, "a64"))
+TURNL = (("i", 0, 16), ("i", 16, 40), ("i", 40, 64), ("j", 0, 16), ("j", 16, 40), ("j", 40, 64))
+COUNTL = {"i": (40, 64), "j": (40, 64)}
 PART2 = ((0, 12, 4, "v12"), (12, 32, 6, "a32"))
-TURN2 = (("i", 0, 12), ("i", 12, 32), ("j", 0, 12), ("j", 12, 32))
-PLAIN = (8, 32)
+TURN2 = (("i", 0, 12), ("i", 12, 32), ("j", 12, 32), ("j", 0, 12))
+PLAIN = (8, 40, 32)
+MERGE = (64, 40, 64)
+FLIPS = (0, 128, 192, 256)
+NAMES = 128
 FIRST, HEAD = 32, 12
 PIECES = ("V", "Sel")
 
 F, B, I, U = "float32", "bfloat16", "int32", "uint16"
-MATS = "BO LT Id A1 nBO nI B256 B8k nB8k BN nB4k nS8k nI8 S0 nS0 ShI L0 Mx dOT dO0 XO nI4k Bx nBx qI hI cI n4I".split()
+MATS = "BO LT Id A1 nBO nI B256 B8k nB8k BN nB4k nS8k nI8 S0 nS0 ShI L0 Mx dOT dO0 XO nI4k qI hI cI n4I".split()
 SCRATCH = {}
 for _n, _c, _d in (
-    ("TX", TW, B), ("P0", 4096, B), ("P1", 4096, B), ("P2", 4096, B), ("P3", 4096, B),
-    ("W0", WS, B), ("W1", WS, B), ("CT", 272, B), ("cdi", 256, I), ("witi", 256, I), ("prbi", 16, I),
-    ("ip", 8, I), ("iw", 8, I), ("col", 48, F), ("ia", 32, I), ("ib", 16, I), ("oa", 32, U), ("ob", 16, U), ("orr", 64, U),
+    ("X0", TW, B), ("X1", TW, B), ("X2", TW, B), ("X3", TW, B), ("X4", TW, B), ("P0", 4096, B),
+    ("W0", WS, B), ("cdo", 256, I), ("CT", 272, B), ("cdi", 256, I), ("witi", 256, I), ("prbi", 16, I),
+    ("ip", 8, I), ("iw", 8, I), ("col", 48, F), ("ia", 8, I), ("ib", 16, I), ("oa", 8, U), ("ob", 16, U), ("orr", 64, U),
     ("G1", 512, F), ("G2", 512, F), ("A", 264, F), ("A64", 256, F), ("Ah", 264, B), ("Al", 264, B), ("DL", 264, F), ("DB", 256, B),
-    ("KX", 512, F), ("ZX", 512, B), ("ZS", 512, B), ("MX", 512, B), ("MK", 512, B), ("LV", 256, B), ("m16", 128, B), ("or2", 16, U),
-    ("W4", 128, B), ("two", 128, B), ("UU", 192, B), ("A2", 256, F), ("LF", 272, F), ("dd", 256, B), ("fine", 512, B),
-    ("oW1", 256, U), ("ix", 256, B), ("iq16", 128, B), ("iqm", 16, B), ("Z", 144, B), ("M", 128 * len(MATS), B), ("Mf", 768, F),
-    ("Sel", 2048, B), ("MW", 1024, B), ("MWk", 128, B), ("MC", 400, B), ("tm", 64, F),
+    ("KX", 512, F), ("ZX", 512, B), ("ZS", 512, B), ("MX", 512, B), ("MK", 256, B), ("LV", 256, B), ("m16", 128, B), ("or2", 16, U),
+    ("W4", 128, B), ("two", 128, B), ("UU", 192, B), ("A2", 256, F), ("LF", 272, F), ("dd", 256, B),
+    ("oW1", 256, U), ("ix", 256, B), ("iq16", 128, B), ("iqm", 16, B), ("Z", 144, B), ("M", 128 * len(MATS), B), ("Mf", 512, F),
+    ("Sel", 2048, B), ("MW", 16 * max(8, *(p[1] - p[0] for p in PART1 + PART2 + PARTL)), B), ("MWk", 128, B), ("MC", 400, B), ("tm", 64, F),
     ("z0", 16, B), ("xz", 16, B), ("K0", 128, B),
-    ("GW", 1024, B), ("WS", 1024, B), ("oP", 64, U), ("oTQ", 128, U), ("PG", 4096, B),
+    ("GW", 1024, B), ("WS", 1024, B), ("oP", 64, U), ("oTQ", 192, U), ("PG", 4096, B),
     ("NN", 4096, B), ("N1", 2048, B), ("nd", 32, F), ("T1", 136, B), ("Z2", 136, B), ("TH", 128, B), ("T2", 72, B), ("AE", 128, B),
     ("CJ", 128, B), ("K2", 128, B), ("oW2", 32, U),
     ("cum", 136, F), ("DD", 128, F), ("ones", 256, B), ("dK", 128, F), ("u0", 64, F),
     ("oR", 64, U), ("step", 272, B), ("oPP", 256, U), ("oTT", 256, U),
-    ("V", 1024, F), ("CW", WS, F), ("dO", 16, B),
-    ("sg", 352, B), ("sn", 256, B), ("G0", 256, B), ("d0", 256, B), ("t1", 256, B), ("t2", 256, B),
-    ("KS", 128, F), ("E", 400, F), ("YS", 400, F), ("x1", 16, F), ("x2", 32, F),
-    ("oXg", 16, U), ("oX2", 16, U), ("FV", 256, B), ("sv", 512, B), ("CS", 264, F), ("e1", 8, F), ("oE", 8, U),
-    ("Dp", 16, B), ("uo", 16, B), ("su", 64, U), ("lu", 64, U), ("lw", 512, B), ("so", 64, B), ("O", 160, B), ("o32", 32, F),
+    ("V", 1024, F), ("CW", 2 * CW1, F), ("dO", 16, B),
+    ("sg", 352, B), ("sn", 256, B), ("nil", 256, B), ("G0", 256, B), ("d0", 256, B), ("t1", 256, B), ("t2", 256, B),
+    ("KS", 128, F), ("E", 400, F), ("YS", 400, F), ("x1", 16, F), ("xo", 16, F), ("oH", 16, U), ("x2", 32, F),
+    ("sG", 64, U), ("oG", 64, U), ("sX", 96, U), ("lX", 96, U), ("FV", 256, B), ("sv", 128, B), ("CS", 264, F), ("e1", 8, F), ("oE", 8, U),
+    ("Dp", 16, B), ("uo", 16, B), ("su", 8, U), ("O", 160, B), ("o32", 16, F),
 ):
     SCRATCH[_n] = ("sbuf", [128, _c], _d)
-SCRATCH["TL"] = ("dram", [4, 128, 256], B)
-SCRATCH["TS"] = ("dram", [4, 128, 256], B)
-SCRATCH["TDa"] = ("dram", [8, 4096], B)
-SCRATCH["TDb"] = ("dram", [8, 4096], B)
+SCRATCH["TD"] = ("dram", [8, 4096], B)
 for _t in range(8):
     SCRATCH["B%d" % _t] = ("psum", [128, 512], F)
 
 NDMA = 60
 SEMAPHORES = (["qv", "qa", "qt", "qg", "loc"] + ["d%d" % k for k in range(NDMA)]
-              + ["r%s%d" % (k, t) for k in "uvotp" for t in range(4)])
+              + ["r%s%d" % (k, t) for k in "chxfamb" for t in range(4)])
 
 
 def _place(ops, before, after, floor, rank):
@@ -117,11 +123,14 @@ def _graph(ops, deps, WAKE):
 def _order(timed, deps):
     n = len(deps)
     graphs = [_graph(ops, deps, m[3]) for ops, m in zip(timed, PACES)]
-    best, rank = None, list(range(n))
+    best, rank, seed = None, list(range(n)), 1
     for k in range(TRIES):
         ops, (pre, post, back) = timed[k % len(PACES)], graphs[k % len(PACES)]
-        if k >= len(PACES):
-            rank = best[2]
+        if best:
+            rank = []
+            for x in best[2][k % len(PACES)]:
+                seed = (seed * 1103515245 + 12345) % 2147483648
+                rank.append(x + 150.0 * seed / 2147483648)
         start = _place(ops, pre, post, [0.0] * n, rank)
         late = _place(ops, post, back, [o[5][1] - o[5][0] for o in ops], [-start[j] - ops[j][5][0] for j in range(n)])
         start = _place(ops, pre, post, [0.0] * n, [-late[j] - ops[j][5][0] for j in range(n)])
@@ -132,75 +141,109 @@ def _order(timed, deps):
 
 
 def _polish(timed, deps, graph, order):
+    n = len(order)
     pre, post = [[i for i, c in p] for p in graph[0]], [[i for i, c in p] for p in graph[1]]
     sent = {o[5][2]: j for j, o in enumerate(timed[0]) if o[1] == "s"}
-    queue = [o[0] for o in timed[0]]
+    queue = ["vatgyr".index(o[0]) for o in timed[0]]
     need = [[sent[o[2][2]]] if o[1] == "r" else d for o, d in zip(timed[0], deps)]
+    busy = [[o[5][0] for o in ops] for ops in timed]
+    lat = [[o[5][1] for o in ops] for ops in timed]
 
-    def run(order, k):
-        ops, end, free, last, why = timed[k], [0.0] * len(order), {}, {}, [None] * len(order)
-        for j in order:
-            q, c, s, w = queue[j], ops[j][5], -1.0, PACES[k][3]
-            if q == "r":
-                end[j], why[j] = end[need[j][0]], (need[j][0], False)
+    def run(order, k, lo, old):
+        end, free, w, b, l = list(old), [None] * 5, PACES[k][3], busy[k], lat[k]
+        left, x = 5, lo - 1
+        while left and x >= 0:
+            j = order[x]
+            q = queue[j]
+            if q < 5 and free[q] is None:
+                free[q] = end[j] - l[j] + b[j]
+                left -= 1
+            x -= 1
+        free = [f or 0.0 for f in free]
+        for j in order[lo:]:
+            q = queue[j]
+            if q == 5:
+                end[j] = end[need[j][0]]
                 continue
+            s = free[q] - w
             for i in need[j]:
-                if end[i] + w > s:
-                    s, why[j] = end[i] + w, (i, False)
-            if free.get(q, 0.0) > s:
-                s, why[j] = free.get(q, 0.0), (last[q], True) if q in last else None
-            free[q], last[q], end[j] = s + c[0], j, s + c[1]
-        return end, why
+                if end[i] > s:
+                    s = end[i]
+            s += w
+            free[q] = s + b[j]
+            end[j] = s + l[j]
+        return end
 
-    def total(order):
-        runs = [run(order, k) for k in range(len(PACES))]
-        return sum(max(e) / m[4] for (e, w), m in zip(runs, PACES)), runs
+    def total(order, lo, old):
+        runs = [run(order, k, lo, old[k]) for k in range(len(PACES))]
+        return sum((max(e) + 0.1 * sum(e) / n) / m[4] for e, m in zip(runs, PACES)), runs
 
-    def moves(order, k, end, why):
-        ops, w = timed[k], PACES[k][3]
-        start = [e - o[5][1] for e, o in zip(end, ops)]
-        ready = [max([end[i] + w for i in d] + [0.0]) for d in need]
-        own, full, nxt, line = [o[5][1] for o in ops], [0.0] * len(order), {}, {}
+    def moves(order, k, end, line, at):
+        w, b, l = PACES[k][3], busy[k], lat[k]
+        own, full, nxt = list(l), [0.0] * n, [None] * 6
         for j in reversed(order):
-            full[j] = max(own[j], ops[j][5][0] + nxt[queue[j]]) if queue[j] in nxt and queue[j] != "r" else own[j]
-            nxt[queue[j]] = full[j]
+            q = queue[j]
+            f = own[j]
+            if q < 5:
+                if nxt[q] is not None and b[j] + nxt[q] > f:
+                    f = b[j] + nxt[q]
+                nxt[q] = f
+                full[j] = f
+                f += w
+            else:
+                full[j] = f
             for i in need[j]:
-                own[i] = max(own[i], ops[i][5][1] + (0.0 if queue[j] == "r" else w) + full[j])
-        for j in order:
-            line.setdefault(queue[j], []).append(j)
-        at = {j: x for q in line for x, j in enumerate(line[q])}
-        j, out, span = end.index(max(end)), [], max(end)
-        while why[j]:
-            if why[j][1] and queue[j] in "vat":
-                ln, b = line[queue[j]], at[j]
-                for a, z, up in [(b - d, b, True) for d in range(1, 7)] + [(b - 1, b + d, False) for d in range(1, 4)]:
+                if l[i] + f > own[i]:
+                    own[i] = l[i] + f
+        span = max(end)
+        j, out = end.index(span), []
+
+        def ready(x):
+            return max([end[i] for i in need[x]] + [-w]) + w
+        while True:
+            q, s0 = queue[j], end[j] - l[j]
+            if q == 5:
+                j = need[j][0]
+                continue
+            if ready(j) >= s0 - 1e-6:
+                if not need[j]:
+                    break
+                j = max(need[j], key=lambda i: end[i])
+                continue
+            ln, p = line[q], at[j]
+            if q < 3:
+                for a, z, up in [(p - d, p, True) for d in range(1, 7)] + [(p - 1, p + d, False) for d in range(0, 4)]:
                     if a < 0 or z + 1 >= len(ln):
                         continue
                     part = [ln[z]] + ln[a:z] if up else ln[a + 1:z + 1] + [ln[a]]
-                    s, far = start[ln[a - 1]] + ops[ln[a - 1]][5][0] if a else 0.0, 0.0
+                    s, far = end[ln[a - 1]] - l[ln[a - 1]] + b[ln[a - 1]] if a else 0.0, 0.0
                     for x in part:
-                        s = max(s, ready[x])
+                        s = max(s, ready(x))
                         far = max(far, s + own[x])
-                        s += ops[x][5][0]
+                        s += b[x]
                     far = max(far, s + full[ln[z + 1]])
                     if far < span - 8:
                         out.append((span - far, ln[a], ln[z], up))
-            j = why[j][0]
+            if not p:
+                break
+            j = ln[p - 1]
         return out
 
-    least, runs = total(order)
-    failed, n, mark = set(), 0, least
-    while n < MOVES:
-        cand = sorted((m for k in range(len(PACES)) for m in moves(order, k, *runs[k]) if m[1:] not in failed), reverse=True)
+    least, runs = total(order, 0, [[0.0] * n] * len(PACES))
+    failed, tried, mark = set(), 0, least
+    while tried < MOVES:
+        line = [[j for j in order if queue[j] == q] for q in range(5)]
+        at = {j: x for ln in line for x, j in enumerate(ln)}
+        cand = sorted(set(m for k in range(len(PACES)) for m in moves(order, k, runs[k], line, at) if m[1:] not in failed), reverse=True)
         if not cand:
             if least >= mark:
                 break
             failed, mark = set(), least
-        for gain, i, j, up in cand[:6]:
+        place = {x: k for k, x in enumerate(order)}
+        for gain, i, j, up in cand[:16]:
             if (i, j, up) in failed:
                 continue
             failed.add((i, j, up))
-            place = {x: k for k, x in enumerate(order)}
             move, todo, lo, hi = set(), [j if up else i], place[i], place[j]
             while todo:
                 x = todo.pop()
@@ -211,11 +254,13 @@ def _polish(timed, deps, graph, order):
                 continue
             a, b = [x for x in order[lo:hi + 1] if x in move], [x for x in order[lo:hi + 1] if x not in move]
             new = order[:lo] + (a + b if up else b + a) + order[hi + 1:]
-            span, r = total(new)
-            n += 1
+            span, r = total(new, lo, runs)
+            tried += 1
             if span < least:
                 order, least, runs = new, span, r
-    return least, order, [e - o[5][1] for e, o in zip(runs[1][0], timed[1])]
+                for k in range(lo, hi + 1):
+                    place[order[k]] = k
+    return least, order, [[e - x for e, x in zip(r, l)] for r, l in zip(runs, lat)]
 
 
 def _emit(g, T, ops):
@@ -300,16 +345,18 @@ def _emit(g, T, ops):
 
 def rank_program(g, core, T, topo):
     rank = T.rank_of(core)
-    helper = [min(h for h in topo.cores_of(c) if T.rank_of(h) is None and topo.die(h) == topo.die(c)
-                  and all(topo.may_write(h, d) for d in T.cores)) for c in T.cores]
+    helper = [min(h for h in topo.cores_of(c) if T.rank_of(h) is None and topo.die(h) != topo.die(c) and topo.may_write(h, T.cores[(r + 1) % N]))
+              for r, c in enumerate(T.cores)]
     if rank is None:
         if core in helper:
             r = helper.index(core)
-            g.wait_ge(T.sem.rp0, len(topo.engines(T.cores[r], core)))
-            for k in range(1, N):
-                rid, pid, _ = topo.addr(T.cores[(r - k) % N])
-                g.remote_dma(T["P%d" % k][:], T.P0[:], T.sem["rp%d" % k], T.sem.loc, pid, rid, topo.mask(core, T.cores[(r - k) % N]))
-            g.wait_ge(T.sem.loc, sum(len(topo.engines(core, d)) for d in T.cores if d != T.cores[r]))
+            dst = T.cores[(r + 1) % N]
+            rid, pid, _ = topo.addr(dst)
+            for t in range(4):
+                g.wait_ge(T.sem["rh%d" % t], len(topo.engines(T.cores[r], core)))
+                x = T["X%d" % (t + 1)][:, 2048:4096]
+                g.remote_dma(x, x, T.sem["rh%d" % t], T.sem.loc, pid, rid, topo.mask(core, dst))
+            g.wait_ge(T.sem.loc, 4 * len(topo.engines(core, dst)))
         return
     ops = []
     v, a, pe = g.vector, g.scalar, g.tensor
@@ -319,9 +366,9 @@ def rank_program(g, core, T, topo):
 
     def ns(out, in_, r, more=(), k=None, fix=0):
         for x in r.split():
-            if x[:3] == "oX2" or x[:2] in ("lu", "oR"):
+            if x[:2] in ("lX", "su", "oR"):
                 return (50 + fix, in_.shape[1], 2), out, in_
-            if x[0] == "o" and x not in ("ones", "o32"):
+            if x[0] == "o" and x != "ones":
                 return (50 + fix, out.shape[1], 1), out, in_
         if k is None:
             k = 0.5 if all("16" in str(x.dtype) for x in (out, in_) + tuple(more)) else 1.0
@@ -372,18 +419,17 @@ def rank_program(g, core, T, topo):
         else:
             op("g", lambda: g.iota(out, pat, base, cm), "", w, cost=(130, 2 * out.shape[1], 0))
 
-    def send(k, out, in_, sem, bulk, r):
-        dst = helper[rank] if bulk else T.cores[(rank - k) % N]
+    def send(k, out, in_, sem, r):
+        dst = helper[rank] if sem[1] == "h" else T.cores[(rank + k) % N]
         rid, pid, _ = topo.addr(dst)
 
         def fn():
             g.remote_dma(out, in_, T.sem[sem], T.sem.loc, pid, rid, topo.mask(core, dst))
             return len(topo.engines(core, dst))
-        op("g", fn, r, "", "s", (0, 1, 6), LINK + {"u": 0, "v": 300, "p": 19000}.get(sem[1], 1200 * (sem != "ro3")), sem)
+        op("g", fn, r, "", "s", (0, 1, 6), LINK + {"x": BULK, "h": BULK, "c": 2000}.get(sem[1], 0), sem)
 
-    def recv(k, sem, bulk, w):
-        src = (helper if bulk else T.cores)[(rank + k) % N]
-        ops.append(["r", "r", (sem, len(topo.engines(src, core)), "rp0" if bulk else sem), [], w.split(), ((0, 0, 0), 0.0, None)])
+    def recv(k, sem, w):
+        ops.append(["r", "r", (sem, len(topo.engines((helper if sem[1] == "h" else T.cores)[(rank - k) % N], core)), sem), [], w.split(), ((0, 0, 0), 0.0, None)])
 
     def fill(ap, n, c, w):
         iota(ap, [[0, n]], c, 0, w, True)
@@ -395,22 +441,32 @@ def rank_program(g, core, T, topo):
         return " " + " ".join(name + str(k) for k in range(lo // unit, (hi - 1) // unit + 1)) + " "
 
     col = T.col
-    (cR, cG, cG15, c4R, cM32, c256, c256b, cIs0, cN0, cB1, cG0, cP, cSn, c75, cSg, cRf, cD, cSi, cX1, cE, cNs0, cW, cRm, cY,
+    (cR, cG, cG15, c4R, cM32, c256, c256b, cIs0, cN0, cB1, cG0, cP, cSn, c75, cSg, cRf, cD, cSi, cX1, cE, cN8, cW, cRm, cY,
      cT, cTe, cNz, cNzB, cS8k, cH0, cH1, cTl, cH0b, cH1b, cA2, c512, cB0, cB1x, cBs, cE2, cD2, cX2) = (col[:, k:k + 1] for k in range(42))
-    (BO, LT, Id, A1, nBO, nI, B256, B8k, nB8k, BN, nB4k, nS8k, nI8, S0, nS0, ShI, L0, Mx, dOT, dO0, XO, nI4k, Bx, nBx, qI, hI, cI, n4I
+    (BO, LT, Id, A1, nBO, nI, B256, B8k, nB8k, BN, nB4k, nS8k, nI8, S0, nS0, ShI, L0, Mx, dOT, dO0, XO, nI4k, qI, hI, cI, n4I
      ) = (T.M[:, 128 * k:128 * k + 128] for k in range(len(MATS)))
-    Idf, nIdf, S0f, Idw, LTf, L0f = (T.Mf[:, 128 * k:128 * k + 128] for k in range(6))
+    S0f, Idw, LTf, L0f = (T.Mf[:, 128 * k:128 * k + 128] for k in range(4))
     Z0 = T.Z[:, 15:143]
-    P = [T.P0, T.P1, T.P2, T.P3]
-    W = [T.W0, T.W1]
+    X = [T["X%d" % t] for t in range(5)]
     Bk = [T["B%d" % t] for t in range(8)]
-    TD = [T.TDa, T.TDb]
     add, sub, mul, mx, mn = ALU.add, ALU.subtract, ALU.mult, ALU.max, ALU.min
     eq, ge, gt, lt, le, ne = ALU.is_equal, ALU.is_ge, ALU.is_gt, ALU.is_lt, ALU.is_le, ALU.not_equal
-    TXw = T.TX[:, 0:4096]
+    Pw = T.P0[:, 0:4096]
 
     def O(t, lo=0, hi=16):
         return T.O[:, 32 * t + 16 + lo:32 * t + 16 + hi]
+
+    def unit(out, c, w):
+        keep(out, T.nil[:, 0:128], ne, c, 0, "nil", w)
+
+    def put(out, c, w, pattern=None, at=1):
+        n = out.shape[1]
+        op("g", lambda: g.affine_select(out, T.nil[:, 0:n], pattern or [[0, n]], ne if pattern else eq, c, -at, 0), "nil", w, cost=(170, 2 * n, 0))
+
+    def rows(out, c, lo, hi, w):
+        op("g", lambda: g.affine_select(out, T.nil[:, 0:128], [[16, 8], [0, 16]], ne if lo == hi else gt, c, lo, -1), "nil", w)
+        if lo < hi:
+            op("g", lambda: g.affine_select(out, out, [[16, 8], [0, 16]], ge, 0.0, hi, -1), w, w)
 
     def spread(out, k, n, r, w):
         act(out, T.m16[:, 16 * k:16 * k + 16].indirect(T.orr[:, 0:n]), r=r + " orr", w=w)
@@ -422,40 +478,48 @@ def rank_program(g, core, T, topo):
                 (cp if sh[0] == "v" else act)(T.GW[:, 16 * lo:16 * up], win.indirect(off[:, lo:up]), r=r, w=span("GW", lo, up, 2))
                 lo = up
 
-    def offsets(parts):
+    def offsets(parts, merge):
         for lo, hi, bk, shares in parts:
             n, w, x = hi - lo, T.WS[:, 16 * lo + 15:16 * hi:16], span("WS", lo, hi, 2)
             scan(T.WS[:, 16 * lo:16 * hi], T.GW[:, 16 * lo:16 * hi], T.MW[:, 0:16 * n], 0.0, mx, add, span("GW", lo, hi, 2) + "MW", x)
-            ts(T.oP[:, lo:hi], w, c256b, add, r="c256b" + x, w=span("oP", lo, hi, 2))
-            mm1(Bk[bk][:, 0:n], Id, w, False, False, "Id" + x, "#%d" % bk)
-            mm1(Bk[bk][:, n:2 * n], Id, w, False, True, "Id" + x, "#%d" % bk)
-            cp(T.oTQ[:, 2 * lo:2 * hi], Bk[bk][:, 0:2 * n], "#%d" % bk, span("oTQ", 2 * lo, 2 * hi, 4))
+            k = 2 + (lo >= merge)
+            if k == 2:
+                ts(T.oP[:, lo:hi], w, c256b, add, r="c256b" + x, w=span("oP", lo, hi, 2))
+            for j in range(k):
+                mm1(Bk[bk][:, j * n:j * n + n], Id, w, False, j == k - 1, "Id" + x, "#%d" % bk)
+            cp(T.oTQ[:, 3 * lo:3 * lo + k * n], Bk[bk][:, 0:k * n], "#%d" % bk, span("oTQ", 3 * lo, 3 * hi, 6))
 
-    def duels(parts, turn, plain, low, Pt, pk, after):
+    def duels(parts, turn, plain, merge, low, TXw, xk, after):
         calls = []
         for side, lo, hi in turn:
             p0, p1, bk, sh = [p for p in parts if p[0] <= lo < p[1]][0]
             swap = p0 >= plain
             hi2 = hi - (side == "j" and hi == parts[-1][1])
-            y, z = p0 + lo, p1 + lo
-            oy, ry = T.oTQ[:, y:y + hi2 - lo], span("oTQ", y, y + hi - lo, 4)
-            oz, rz = (T.oP[:, lo:hi], span("oP", lo, hi, 2)) if side == "i" else (T.oTQ[:, z:z + hi2 - lo], span("oTQ", z, z + hi - lo, 4))
+            y, z, ry = 2 * p0 + lo, (2 * p1 if side == "i" else p0 + p1) + lo, span("oTQ", 3 * p0, 3 * p1, 6)
+            oy = T.oTQ[:, y:y + hi2 - lo]
+            oz, rz = (T.oP[:, lo:hi], span("oP", lo, hi, 2)) if side == "i" and p0 < merge else (T.oTQ[:, z:z + hi2 - lo], ry)
             at = 16 * lo + (1024 if side == "j" and not swap else 0)
             pg, rg = T.PG[:, at:at + 16 * (hi2 - lo)], span("PG", at, at + 16 * (hi - lo), 32)
             if not swap:
-                act(pg, Pt[:, 0:4096].indirect(oz), r=pk + rz, w=rg)
+                act(pg, Pw.indirect(oz), r="P0" + rz, w=rg)
             elif side == "i":
-                act(pg, TXw.indirect(oy), r="TX" + ry, w=rg)
+                act(pg, TXw.indirect(oy), r=xk + ry, w=rg)
             at = 16 * lo + (low if side == "i" else 1040)
-            calls.append((T.N1[:, at:at + 16 * (hi2 - lo)], Pt[:, 0:4096].indirect(oz) if swap else TXw.indirect(oy), pg,
-                          (pk + rz if swap else "TX" + ry) + rg, span("Q", at, at + 16 * (hi2 - lo), 16), side, hi))
+            calls.append((T.N1[:, at:at + 16 * (hi2 - lo)], Pw.indirect(oz) if swap else TXw.indirect(oy), pg,
+                          ("P0" + rz if swap else xk + ry) + rg, span("Q", at, at + 16 * (hi2 - lo), 16), side, hi))
         for out, in0, pg, r, w, side, hi in calls:
             tt(out, in0, pg, eq, r, w)
             after(side, hi)
 
+    def text(t):
+        send(1, X[t + 1][:, 2048:4096], X[t][:, 2048:4096], "rh%d" % t, "P0 X%d" % t)
+        send(1, X[t + 1][:, 0:2048], X[t][:, 0:2048], "rx%d" % t, "P0 X%d" % t)
+
     def lanes_of(t):
         lo, s0 = 128 * t, 64 * t
-        cp(T.G1[:, lo:lo + 128], T.cdi[:, 0:256].indirect(T.oa[:, 8 * t:8 * t + 8]), "cdi oa", "G1")
+        if t:
+            recv(t, "rc%d" % t, "cd%d" % t)
+        cp(T.G1[:, lo:lo + 128], (T.cdi if t else T.cdo)[:, s0:s0 + 64].indirect(T.oa[:, 0:8]), "cd%d oa" % t, "G1")
         op("v", lambda: v.transpose(T.G2[:, lo:lo + 128], T.G1[:, lo:lo + 128]), "G1", "G2 G2a G2b", cost=(40, 128, 0))
         (cp if t == 0 else act)(T.A[:, s0:s0 + 64], T.G2[:, lo:lo + 128].indirect(T.ob[:, 0:4]), r="G2 G2a G2b ob", w="A%d" % t)
         tt(T.DL[:, s0 + 1:s0 + 64], T.A[:, s0 + 1:s0 + 64], T.A[:, s0:s0 + 63], sub, "A%d" % t, "DL%d" % t)
@@ -471,18 +535,21 @@ def rank_program(g, core, T, topo):
         act(T.Ah[:, s0:s0 + 64], T.A[:, s0:s0 + 64], bias=64.0, r="A%d" % t, w="Ah%d" % t)
         tt(T.Al[:, s0:s0 + 64], T.A64[:, s0:s0 + 64], T.Ah[:, s0:s0 + 64], sub, "A64%d Ah%d" % (t, t), "Al%d" % t)
 
-    dma("y", T.cdi[:], T.cd[:], w="cdi")
+    dma("y", T.cdo[:], T.cd[:], w="cd0")
     dma("a", T.witi[:], T.wit[:], w="witi")
-    dma("y", T.P0[:], T.pat[:], w="P0", lat=5000.0)
-    dma("y", TXw, T.txt[:], w="TX", lat=6800.0)
+    dma("y", T.P0[:], T.pat[:], w="P0", lat=LOADS[0])
+    dma("y", T.X0[:, 0:4096], T.txt[:], w="X0", lat=LOADS[1])
     dma("a", T.prbi[:], T.prb[:], w="prbi")
     iota(T.ip[:, 0:1], [[0, 1]], 0, 1, "ip0")
-    iota(T.ia[:], [[64, 4], [1, 4], [0, 2]], 0, 0, "ia")
+    iota(T.ia[:], [[1, 4], [0, 2]], 0, 0, "ia")
     iota(T.ib[:, 0:4], [[32, 4]], 0, 0, "ib")
     iota(T.iqm[:], [[1, 16]], 0, 0, "iqm", True)
     iota(T.ix[:], [[1, 256]], 0, 0, "ix", True)
     iota(T.iq16[:], [[16, 8], [0, 16]], 0, 0, "iq16", True)
-    ms(T.CT[:, 256:272], 0.0, "CTp")
+    ms(T.nil[:], 0.0, "nil")
+    fill(T.CT[:, 256:272], 16, 0, "CTp")
+    fill(T.CT[:, 0:1], 1, 0, "CT0")
+    fill(T.DL[:, 64:257:64], 4, int(BIG), "DLp")
     ts(T.ip[:, 1:2], T.ip[:, 0:1], 15, ALU.bitwise_and, r="ip0", w="ip1")
     ts(T.ip[:, 2:3], T.ip[:, 0:1], 31, ALU.bitwise_and, r="ip0", w="ip2")
     cp(cP, T.ip[:, 0:1], "ip0", "cP")
@@ -499,12 +566,8 @@ def rank_program(g, core, T, topo):
     ts(T.tm[:, 16:32], T.iqm[:], cR, eq, 256.0, mul, r="iqm cR", w="tm1")
     ts(T.tm[:, 32:48], T.iqm[:], 15.0, eq, -512.0, mul, r="iqm", w="tm2")
     tt(T.tm[:, 48:64], T.tm[:, 0:16], T.tm[:, 16:32], add, "tm0 tm1", "tm3")
-    ms(T.CT[:, 0:1], 0.0, "CT0")
     tt(T.m16[:, 0:16], T.tm[:, 48:64], T.tm[:, 32:48], add, "tm3 tm2", "m0")
-    act(T.CW[:, CW1:CW1 + 256], T.ix[:], AF.Silu, scale=0.0, r="ix", w="CWb")
-    ops[-1][5] = ((1360, 256, 0), 0.0, None)
-    spread(T.MW[:], 0, 64, "m0", "MW")
-    ms(T.DL[:, 64:257:64], BIG, "DLp")
+    spread(T.MW[:], 0, T.MW.shape[1] // 16, "m0", "MW")
     ts(cG15, cG, 15.0, add, r="cG", w="cG15")
     lanes_of(0)
     ms(T.G2[:, 7:8], 4096 - ROUND, "G2")
@@ -515,37 +578,38 @@ def rank_program(g, core, T, topo):
     ts(T.Z[:], T.ix[:, 0:144], cG15, eq, r="ix cG15", w="Z")
     ts(cIs0, cR, 0.0, eq, r="cR", w="cIs0")
     witnesses(PART1, T.CT[:, 0:272], T.oW1[:, 0:64], "CT CT0 CTp oW10")
-    for dst, s, w in ((nI, -1.0, "nI"), (nI8, -1 / 8, "nI8"), (hI, -0.5, "hI")):
-        act(dst, Id, scale=s, r="Id", w=w)
+    for dst, s, w in ((nI, -1.0, "nI"), (hI, -0.5, "hI"), (nI8, -1 / 8, "nI8")):
+        unit(dst, s, w)
     act(T.K0[:, 0:64], T.ix[:, 0:64], scale=0.0, bias=192.0, r="ix", w="K0a")
     act(T.K0[:, 64:128], T.ix[:, 0:64], scale=0.0, bias=c256b, r="ix c256b", w="K0b")
     fill(T.N1[:, 1024:1040], 16, 0, "N1p")
     fill(T.T1[:, 0:2], 2, 0, "T1p")
     fill(T.T2[:, 0:2], 2, 0, "T2p")
-    ts(T.x1[:], T.iqm[:], cR, eq, r="iqm cR", w="x1")
+    ts(T.x1[:], T.iqm[:], cR, eq, r="iqm cR", w="x1 x1b")
     for p in range(16):
-        ts(T.Sel[:, 128 * p:128 * p + 128], BO, T.x1[:, p:p + 1], mul, r="BO x1", w="Sel")
+        ts(T.Sel[:, 128 * p:128 * p + 128], BO, T.x1[:, p:p + 1], mul, r="BO x1 x1b", w="Sel")
+    fill(T.ones[:], 256, 1, "ones")
+    send(1, T.cdi[:, 64:128], T.cdo[:, 64:128], "rc1", "cd0")
+    ops[-1][5] = ((3000, 1, 6),) + ops[-1][5][1:]
+    text(0)
+    put(T.LF[:, 264:272], NONE[1] * TINY, "LFp")
+    fill(T.O[:, 15:160:32], 5, 0, "Op")
+    for dst, s, w in ((Idw, 1 / TINY, "Idw"), (n4I, -4.0, "n4I"), (qI, 0.25, "qI"), (cI, 33 / 128, "cI")):
+        unit(dst, s, w)
     keep(ShI, BO, eq, 0.0, -1, "BO", "ShI")
     keep(ShI, ShI, ne, -1.0, 0, "ShI", "ShI")
     keep(LT, BO, gt, 0.0, 0, "BO", "LT")
-    fill(T.ones[:], 256, 1, "ones")
+    put(cRf, ROUND + 64, "cRf")
+    put(T.two[:], 2.0, "two", [[0, 32], [1, 4]], 3)
+    fill(T.dK[:, 0:128:2], 64, 1, "dK")
+    put(T.m16[:, 16:32], -2 * HOLD, "m1", [[1, 16]], 0)
+    fill(T.m16[:, 96:111], 15, 1, "m6")
+    for c, x, w in ((c75, 7.5, "c75"), (cSn, -255.5, "cSn"), (cX2, (HOLD + BIG + ROUND) / BIG, "cX2")):
+        put(c, x, w)
     fill(T.step[:, 0:16], 16, 0, "stepp")
-    fill(T.sg[:, 0:16], 16, 1, "sgp")
-    fill(T.sg[:, 272:288], 16, 0, "sgq")
-    fill(T.TX[:, 4096:TW], TW - 4096, 0, "TXp")
-    fill(T.CS[:, 256:264], 8, 0, "CSp")
-    fill(T.E[:, 0:98], 98, 0, "E0 E1 KTa")
-    iota(T.YS[:, 0:392], [[0, 8], [1, 49]], 0, 0, "YSa YSb", True)
-    fill(T.W1[:, 4096:WW], WW - 4096, 0, "W1p")
-    fill(T.W0[:, 4096:WW], WW - 4096, 0, "W0p")
-    send(1, T.TL[0], T.CT[:, 0:256], "rt0", False, "CT CT0")
-    ops[-1][5] = ((3000, 1, 6),) + ops[-1][5][1:]
-    send(0, T.P0[:], T.P0[:], "rp0", True, "P0 TX")
 
     def consts(part):
         if part == 0:
-            ms(cRf, ROUND + 64, "cRf")
-            ms(T.LF[:, 264:272], NONE[1] * TINY, "LFp")
             mm(T.B7[:, 0:135], [(Id, T.Z[:, 8:143]), (Id, T.Z[:, 0:135])], "Id Z", "#7")
             act(T.Z2[:, 0:135], T.B7[:, 0:135], scale=1 / 64, r="#7", w="Z2")
             ts(cH0, cR, 8.0, lt, -1.0, mul, r="cR", w="cH0")
@@ -558,39 +622,39 @@ def rank_program(g, core, T, topo):
             for k, c in enumerate((256.0, c256b, 256.0, c512)):
                 act(T.K2[:, 32 * k:32 * k + 32], T.ix[:, 0:32], scale=0.0, bias=c, r="ix c256b c512", w="K2%d" % k)
             ts(cN0, cR, 0.0, gt, 256.0, mul, r="cR", w="cN0")
-            ts(cNs0, cIs0, -1.0, mul, r="cIs0", w="cNs0")
             ts(cNz, cR, 0.0, gt, r="cR", w="cNz")
             ts(cNzB, cR, 0.0, gt, -BIG, mul, r="cR", w="cNzB")
-            ts(cS8k, cIs0, -BIG, mul, r="cIs0", w="cS8k")
-            for dst, src, s, r, w in ((B256, BO, cN0, "cN0", "B256"), (nBO, BO, -1.0, "", "nBO"), (B8k, BO, BIG, "", "B8k"),
-                                      (nB8k, BO, cNzB, "cNzB", "nB8k"), (BN, BO, cNz, "cNz", "BN"), (S0, BO, cIs0, "cIs0", "S0"),
-                                      (Idf, Id, 1.0, "", "Idf"), (Idw, Id, 1 / TINY, "", "Idw"), (qI, Id, 0.25, "", "qI"), (cI, Id, 33 / 128, "", "cI"),
-                                      (n4I, Id, -4.0, "", "n4I"), (nIdf, Id, -1.0, "", "nIdf"), (S0f, BO, cIs0, "cIs0", "S0f"), (nS0, BO, cNs0, "cNs0", "nS0"),
-                                      (nB4k, BO, -HOLD / 16, "", "nB4k"), (nS8k, BO, cS8k, "cS8k", "nS8k"), (nI4k, Id, -4096.0, "", "nI4k"),
-                                      (Bx, BO, 256.0, "", "Bx"), (nBx, BO, -256.0, "", "nBx")):
-                act(dst, src, scale=s, r="BO Id " + r, w=w)
-            act(T.fine[:, 0:256], T.ix[:], scale=0.0, bias=1 / 256, r="ix", w="fine0")
+            for dst, s, r, w in ((B256, cN0, "cN0", "B256"), (B8k, BIG, "", "B8k"), (nB8k, cNzB, "cNzB", "nB8k"), (nB4k, -HOLD / 16, "", "nB4k")):
+                act(dst, BO, scale=s, r="BO " + r, w=w)
         elif part == 1:
-            ms(T.O[:, 15:160:32], 0.0, "Op")
             cp(O(0), T.prbi[:], "prbi", "O0")
             ts(T.iw[:, 0:1], T.ip[:, 0:1], 4, ALU.arith_shift_right, r="ip0", w="iw")
             lanes_of(1)
             halves_of(1)
         elif part == 2:
+            for dst, c, w in ((S0f, 1.0, "S0f"), (S0, 1.0, "S0"), (nS8k, -BIG, "nS8k")):
+                rows(dst, c, 0, 0, w)
+            put(T.LV[:], -2 * HOLD, "LV", [[0, 8], [1, 32]], 0)
+            unit(nI4k, -4096.0, "nI4k")
+            fill(T.sg[:, 0:16], 16, 1, "sgp")
+            fill(T.sg[:, 272:288], 16, 0, "sgq")
+            fill(T.CS[:, 256:264], 8, 0, "CSp")
+            fill(T.E[:, 0:98], 98, 1, "E0 E1 KTa")
+            iota(T.YS[:, 0:392], [[0, 8], [1, 49]], 0, 0, "YSa YSb", True)
+            fill(T.W0[:, 4096:WW], WW - 4096, 0, "W0p")
+            for t in (2, 3):
+                send(t, T.cdi[:, 64 * t:64 * t + 64], T.cdo[:, 64 * t:64 * t + 64], "rc%d" % t, "cd0")
+            for dst, c, lo, hi, w in ((nS0, -1.0, 0, 0, "nS0"), (BN, 1.0, 1, 15, "BN"), (nBO, -1.0, 0, 15, "nBO")):
+                rows(dst, c, lo, hi, w)
             act(cT, cR, scale=68.0, bias=1024.0, r="cR", w="cT")
             act(T.cum[:, 0:1], cT, r="cT", w="cump")
             act(cTl, cR, scale=-68.0, bias=-1088.0, r="cR", w="cTl")
             act(cTe, cTl, scale=-256.0, bias=256.0, r="cTl", w="cTe")
-            ms(T.two[:], 0.0, "two")
-            ms(T.two[:, 3:128:4], 2.0, "two")
-            ms(T.dK[:, 0:128:2], 1.0, "dK")
             act(T.tm[:, 0:32], T.ix[:, 0:32], scale=2.0, bias=cT, r="ix cT", w="tm0 tm1")
             act(T.dK[:, 1:64:2], T.tm[:, 0:32], scale=-1.0, r="tm0 tm1", w="dKe")
             act(T.dK[:, 65:128:2], T.tm[:, 0:32], scale=-1.0, bias=-4.0, r="tm0 tm1", w="dKo")
-            ms(c75, 7.5, "c75")
             act(cH0b, cH0, scale=-7.5 / 64, r="cH0", w="cH0b")
             act(cH1b, cH1, scale=-7.5 / 64, r="cH1", w="cH1b")
-            ms(cSn, -255.5, "cSn")
             tt(L0, LT, Z0, add, "LT Z", "L0")
             act(LTf, LT, r="LT", w="LTf")
             act(L0f, L0, r="L0", w="L0f")
@@ -602,7 +666,6 @@ def rank_program(g, core, T, topo):
             tt(A1, Id, LT, sub, "Id LT", "A1")
             act(A1, A1, scale=4096.0, r="A1", w="A1")
             act(cB1, cR, scale=-4096.0, bias=-18 * 4096.0, r="cR", w="cB1")
-            ts(T.m16[:, 16:32], T.iqm[:], 0.0, eq, -2 * HOLD, mul, r="iqm", w="m1")
             ts(T.tm[:, 0:16], T.iqm[:], cR, gt, -BIG, mul, r="iqm cR", w="tm0")
             ts(T.tm[:, 16:32], T.iqm[:], cR, eq, HOLD, mul, r="iqm cR", w="tm1")
             tt(T.tm[:, 32:48], T.tm[:, 0:16], T.tm[:, 16:32], add, "tm0 tm1", "tm2")
@@ -610,18 +673,14 @@ def rank_program(g, core, T, topo):
             spread(T.MK[:, 0:256], 2, 16, "m2", "MK")
             cp(T.or2[:, 0:16:2], T.orr[:, 0:8], "orr", "or2")
             ts(T.or2[:, 1:16:2], T.orr[:, 0:8], 16.0, add, r="orr", w="or3")
-            act(T.m16[:, 64:80], T.m16[:, 16:32], r="m1", w="m4")
-            act(T.m16[:, 80:96], T.tm[:, 32:48], r="tm2", w="m5")
-            act(T.MK[:, 256:512], T.m16[:, 64:96].indirect(T.or2[:]), r="m4 m5 or2 or3", w="MK2")
-            ms(T.LV[:], 0.0, "LV")
-            ms(T.LV[:, 0:256:32], -2 * HOLD, "LV")
+            act(cN8, cNz, scale=8.0, r="cNz", w="cN8")
+            ts(T.oH[:, 0:16:2], T.ix[:, 0:8], cN8, add, r="ix cN8", w="oH")
+            ts(T.oH[:, 1:16:2], T.ix[:, 0:8], 8.0, add, r="ix", w="oH")
             act(cRm, cR, bias=-1.0, r="cR", w="cRm")
-            ms(cX2, (HOLD + BIG + ROUND) / BIG, "cX2")
             ts(T.tm[:, 0:16], T.iqm[:], cRm, eq, -2.0, mul, r="iqm cRm", w="tm0")
             ts(T.tm[:, 16:32], T.iqm[:], cR, lt, r="iqm cR", w="tm1")
             tt(T.m16[:, 48:64], T.tm[:, 0:16], T.tm[:, 16:32], add, "tm0 tm1", "m3")
             spread(T.MX[:, 0:256], 3, 16, "m3", "MX")
-            act(T.m16[:, 96:111], T.ones[:, 0:15], r="ones", w="m6")
             act(T.m16[:, 111:112], cIs0, scale=-2.0, bias=1.0, r="cIs0", w="m6b")
             act(T.m16[:, 112:128], T.m16[:, 48:64], r="m3", w="m7")
             act(T.MX[:, 256:512], T.m16[:, 96:128].indirect(T.or2[:]), r="m6 m6b m7 or2 or3", w="MX2")
@@ -633,9 +692,9 @@ def rank_program(g, core, T, topo):
             act(cD2, cR, bias=4128.0, r="cR", w="cD2")
         elif part == 3:
             act(cY, cR, bias=33.0, r="cR", w="cY")
-            ts(T.MC[:, 0:392], T.YS[:, 0:392], cY, lt, r="YSa YSb cY", w="MC")
-            act(cW, cR, scale=32.0, bias=4128.0, r="cR", w="cW")
-            act(T.MC[:, 1:392:49], T.ix[:, 0:8], scale=512.0, bias=cW, r="ix cW", w="MC")
+            ts(T.MC[:, 0:392], T.YS[:, 0:392], cY, ge, -2.0, mul, r="YSa YSb cY", w="MC")
+            act(cW, cR, scale=16 / BIG, bias=2064 / BIG, r="cR", w="cW")
+            act(T.MC[:, 1:392:49], T.ix[:, 0:8], scale=256 / BIG, bias=cW, r="ix cW", w="MC")
             tt(Mx, Id, Z0, sub, "Id Z", "Mx")
             act(T.e1[:, 1:2], cR, scale=-0.5, bias=1.0, r="cR", w="e11")
             act(cG0, cIs0, scale=-8.0, bias=T.e1[:, 1:2], r="cIs0 e11", w="cG0")
@@ -657,35 +716,24 @@ def rank_program(g, core, T, topo):
         for q in range(8):
             mm1(out, T.Z2[:, 7 - q:135 - q], T.N1[:, lo + q:lo + 16 * n:8], False, stop and q == 7, r + " Z2", w)
 
-    def expand(t):
-        recv(1, "rt%d" % (t - 1), False, "TL%d" % (t - 1))
-        dma("y", TD[t % 2][:], T.TL[t - 1], "TL%d" % (t - 1), "TD%d" % (t % 2))
-        op("g", lambda: g.indirect_dma_start(W[t % 2][:, 0:4096], None, TD[t % 2][:], IndirectOffsetOnAxis(ap=T.iw[:, 0:1], axis=0),
-                                             bounds_check=7), "TD%d iw" % (t % 2), "W%d" % (t % 2), "d", 1700.0, 6000.0)
+    def expand():
+        dma("y", T.TD[:], T.CT[:, 0:256], "CT CT0", "TD")
+        op("g", lambda: g.indirect_dma_start(T.W0[:, 0:4096], None, T.TD[:], IndirectOffsetOnAxis(ap=T.iw[:, 0:1], axis=0),
+                                             bounds_check=7), "TD iw", "W0", "d", 1700.0, 6000.0)
 
-    def values(t):
-        lo = 128 * t
-        act(T.sv[:, lo:lo + 128], T.B7[:, 0:128], r="#7", w="sv%d" % t)
-        send(1, T.lw[:, lo:lo + 128], T.sv[:, lo:lo + 128], "rv%d" % t, False, "sv%d" % t)
-
-    def keys(t):
-        lo = 16 * t
-        cp(T.su[:, lo:lo + 8], T.YS[:, 0:392:49], "YSa YSb", "su%d" % t)
-        send(1, T.lu[:, lo:lo + 8], T.su[:, lo:lo + 8], "ru%d" % t, False, "su%d" % t)
-
-    def apply_u(t, win, wk):
-        recv(1, "rv%d" % t, False, "lw%d" % t)
-        recv(1, "ru%d" % t, False, "lu%d" % t)
-        cp(win[:, 0:WS].indirect(T.lu[:, 16 * t:16 * t + 8]), T.lw[:, 128 * t:128 * t + 128], "lu%d lw%d %s" % (t, t, wk), wk)
+    def name(lo, hi, x):
+        act(T.sv[:, 16 * lo:16 * hi], T.B7[:, 16 * lo:16 * hi], r="#7", w="sv" + x)
+        ts(T.su[:, lo:hi], T.YS[:, 49 * lo:49 * hi:49], -2 * BIG, mul, r="YS" + x, w="su" + x)
+        cp(T.W0[:, 0:WS].indirect(T.su[:, lo:hi]), T.sv[:, 16 * lo:16 * hi], "su%s sv%s W0 W0p" % (x, x), "W0 W0p")
 
     def equals(lo, hi, x):
         scan(T.KS[:, 16 * lo:16 * hi], T.B6[:, 16 * lo:16 * hi], T.MWk[:, 16 * lo:16 * hi], 0.0, mx, add, "#6 MWk", "KS" + x)
-        act(T.E[:, 49 * lo:49 * hi:49], T.KS[:, 16 * lo + 15:16 * hi:16], bias=BIG, r="KS" + x, w="KT" + x)
+        act(T.E[:, 49 * lo:49 * hi:49], T.KS[:, 16 * lo + 15:16 * hi:16], scale=-0.5 / BIG, bias=-0.5, r="KS" + x, w="KT" + x)
         for k in range(lo, hi):
             n = min(48, 16 * k + 16)
-            ts(T.E[:, 49 * k + 49 - n:49 * k + 49], T.B6[:, 16 * k + 16 - n:16 * k + 16], T.KS[:, 16 * k + 15:16 * k + 16], sub, BIG, eq, r="#6 KS" + x, w="E%d" % k)
+            ts(T.E[:, 49 * k + 49 - n:49 * k + 49], T.B6[:, 16 * k + 16 - n:16 * k + 16], T.KS[:, 16 * k + 15:16 * k + 16], sub, BIG, ne, r="#6 KS" + x, w="E%d" % k)
         back = slice(49 * hi - 1, 49 * lo - 1 if lo else None, -1)
-        scan(T.YS[:, back], T.E[:, back], T.MC[:, back], 0.0, mx, mul, "MC KT%s " % x + " ".join("E%d" % k for k in range(lo, hi)), "YS" + x)
+        scan(T.YS[:, back], T.E[:, back], T.MC[:, back], 1.0, mn, sub, "MC KT%s " % x + " ".join("E%d" % k for k in range(lo, hi)), "YS" + x)
 
     def starts(t):
         for p in range(16):
@@ -698,20 +746,21 @@ def rank_program(g, core, T, topo):
         mm1(T.B1[:, 0:256], BN, st[:, 16:272], True, False, "BN step", "#1")
         mm1(T.B1[:, 0:255], nBO, st[:, 17:272], False, False, "nBO step", "#1")
         mm1(T.B1[:, 0:256], S0, T.G0[:], False, True, "S0 G0", "#1")
-        mm(T.B5[:, 256:512], [(Id, T.G0[:]), (nS0, T.G0[:])], "Id nS0 G0", "#5")
+        mm(T.B3[:, 0:256], [(Id, T.G0[:]), (nS0, T.G0[:])], "Id nS0 G0", "#3")
         act(T.d0[:], T.B1[:, 0:256], AF.Relu, r="#1", w="d0")
-        scan(T.CS[:, 255::-1], T.d0[:, 255::-1], T.B5[:, 511:255:-1], 0.0, mul, add, "d0 #5", "CS")
+        scan(T.CS[:, 255::-1], T.d0[:, 255::-1], T.B3[:, 255::-1], 0.0, mul, add, "d0 #3", "CS")
         tt(T.uo[:], T.CS[:, 0:264].indirect(T.oE[:, 0:1]), T.Dp[:], mul, "CS CSp oE Dp", "uo")
         mm(T.B7[:, 144:160], [(Id, O(t)), (Mx, T.uo[:])], "Id Mx uo O%d" % t, "#7")
-        so, land = (T.so[:, 16 * t:16 * t + 16], O(t + 1)) if t < 3 else (T.o32[:, 0:16], T.o32[:, 16:32])
-        act(so, T.B7[:, 144:160], r="#7", w="so%d" % t)
-        send(1, land, so, "ro%d" % t, False, "so%d" % t)
+        act(O(t + 1) if t < 3 else T.o32[:], T.B7[:, 144:160], r="#7", w="O%d" % (t + 1))
 
-    def held():
+    def held(t):
         scan(T.KX[:, 255::-1], T.B3[:, 255::-1], T.MK[:, 255::-1], -2 * ROUND, mx, add, "#3 MK", "KX")
-        scan(T.KX[:, 511:255:-1], T.B3[:, 255::-1], T.MK[:, 511:255:-1], -2 * ROUND, mx, add, "#3 MK2", "KX2")
-        ts(T.oXg[:], T.KX[:, 0:256:16], HOLD + ROUND, add, r="KX", w="oXg")
-        act(T.FV[:], T.TX[:, 0:TW].indirect(T.oXg[:]), scale=-1.0, bias=255.0, r="TX TXp oXg", w="FV")
+        act(T.xo[:, 0:8], T.KX[:, 16:256:32], r="KX", w="xo0")
+        act(T.xo[:, 8:16], T.KX[:, 16:256:32], bias=2 * HOLD, r="KX", w="xo1")
+        for lo, x in ((0, "a"), (8, "b")):
+            act(T.KX[:, 256 + 16 * lo:384 + 16 * lo], T.xo[:, 0:16].indirect(T.oH[:, lo:lo + 8]), r="xo0 xo1 oH", w="KX2" + x)
+        ts(T.sG[:, 16 * t:16 * t + 16], T.KX[:, 0:256:16], HOLD + ROUND, add, r="KX", w="sG%d" % t)
+        send(1, T.oG[:, 16 * t:16 * t + 16], T.sG[:, 16 * t:16 * t + 16], "rf%d" % t, "sG%d" % t)
         act(T.x1[:, 0:16:2], T.KX[:, 0:256:32], scale=cSi, bias=cX1, r="cSi cX1 KX", w="x1")
         act(T.x1[:, 1:16:2], T.KX[:, 16:256:32], scale=1 / BIG, bias=cX2, r="cX2 KX", w="x1b")
 
@@ -728,49 +777,57 @@ def rank_program(g, core, T, topo):
         signs(out, nB4k, lo, hi, 0, True, "nB4k", bk)
 
     def lifted(lo):
-        return (T.B3[:, 384:512], "#3") if lo else (T.B5[:, 384:512], "#5")
+        k = FLIPS.index(lo)
+        bk, at = ((5, 384), (3, 384), (5, 256))[k]
+        return Bk[bk][:, at:at + FLIPS[k + 1] - lo], "#%d" % bk
 
-    def flip_a(lo, hi, x):
-        k0, k1 = lo // 16, hi // 16
+    def flip_a(t, lo, hi, x):
+        k0, k1, at = lo // 16, hi // 16, 24 * t + 8 * "amb".index(x)
         for j, (s, d) in enumerate(((cSg, cD), (BIG, cD2))):
             y, up = x + str(j), 256 * j
             back = slice(up + hi - 1, up + lo - 1 if up + lo else None, -1)
-            tt(T.ZX[:, up + lo:up + hi], lifted(lo)[0], T.KX[:, up + lo:up + hi], eq, lifted(lo)[1] + " KX KX2", "ZX" + y)
+            tt(T.ZX[:, up + lo:up + hi], lifted(lo)[0], T.KX[:, up + lo:up + hi], eq, lifted(lo)[1] + (" KX2" + "ab"[lo > 0] if j else " KX"), "ZX" + y)
             scan(T.ZS[:, back], T.MX[:, back], T.ZX[:, back], 0.0, mul, add, "MX MX2 ZX" + y, "ZS" + y)
             z = T.x2[:, 16 * j + k0 // 2:16 * j + k1 // 2]
             tt(z, T.ZS[:, up + lo:up + hi:32], T.x1[:, k0 + j:k1:2], add, "x1 x1b ZS" + y, "x2" + y)
-            ts(T.oX2[:, k0 + j:k1:2], z, s, mul, d, mn, r="cSg cD cD2 x2" + y, w="oX2" + y)
+            ts(T.sX[:, at + j:at + k1 - k0:2], z, s, mul, d, mn, r="cSg cD cD2 x2" + y, w="sX%d%s" % (t, y))
+        send(1, T.lX[:, at:at + k1 - k0], T.sX[:, at:at + k1 - k0], "r%s%d" % (x, t), "sX%d%s0 sX%d%s1" % (t, x, t, x))
 
-    def flip_b(lo, hi):
-        for k in range(lo, hi):
-            x = "ab"[k // 4]
-            cp(T.TX[:, 0:TW].indirect(T.oX2[:, 2 * k:2 * k + 2]), T.FV[:, 32 * k:32 * k + 32], "FV oX2%s0 oX2%s1" % (x, x), "TX TXp")
+    def flip_b(t, x):
+        if x == "a":
+            recv(1, "rx%d" % t, "X%d" % (t + 1))
+            recv(1, "rh%d" % t, "X%dh" % (t + 1))
+            recv(1, "rf%d" % t, "oG%d" % t)
+            act(T.FV[:], X[t + 1][:, 0:4096].indirect(T.oG[:, 16 * t:16 * t + 16]), scale=-1.0, bias=255.0, r="X%d X%dh oG%d" % (t + 1, t + 1, t), w="FV")
+        recv(1, "r%s%d" % (x, t), "lX%d%s" % (t, x))
+        n = "amb".index(x)
+        for k in range(FLIPS[n] // 32, FLIPS[n + 1] // 32):
+            at = 24 * t + 8 * n + 2 * k - FLIPS[n] // 16
+            cp(X[t + 1][:, 0:TW].indirect(T.lX[:, at:at + 2]), T.FV[:, 32 * k:32 * k + 32], "lX%d%s FV" % (t, x), "X%d" % (t + 1))
 
     def offsets1(t):
         s0 = 64 * t
-        for lo, hi, bk, sh in PART1:
-            n = hi - lo
-            mm1(Bk[bk][:, 0:2 * n], Id, T.K0[:, 64 - n:64 + n], True, False, "Id K0a K0b", "#%d" % bk)
+        for lo, hi, bk, sh in PARTL if t else PART1:
+            n, k = hi - lo, 2 + (lo >= MERGE[t > 0])
+            mm1(Bk[bk][:, 0:k * n], Id, T.K0[:, 64 - n:64 + (k - 1) * n], True, False, "Id K0a K0b", "#%d" % bk)
             mm1(Bk[bk][:, 0:n], Id, T.Ah[:, s0 + lo:s0 + hi], False, False, "Id Ah%d" % t, "#%d" % bk)
             mm1(Bk[bk][:, 0:n], Id, T.Al[:, s0 + lo:s0 + hi], False, False, "Id Al%d" % t, "#%d" % bk)
             mm1(Bk[bk][:, n:2 * n], nI, T.DB[:, s0 + lo:s0 + hi], False, False, "nI DB%d" % t, "#%d" % bk)
 
     offsets1(0)
     for t in range(4):
-        Pt, pk, ok = P[t], "P%d" % t, "O%d" % t
-        win, wk = (W[t % 2][:, 0:WW], "W%d W%dp" % (t % 2, t % 2)) if t else (T.CT[:, 0:272], "CT CT0 CTp")
+        TXw, xk, ok = X[t][:, 0:4096], "X%d" % t, "O%d" % t
+        win, wk = (T.W0[:, 0:WW], "W0 W0p") if t else (T.CT[:, 0:272], "CT CT0 CTp")
         s0 = 64 * t
         w1, WS1 = T.WS[:, 15:1024:16], span("WS", 0, 64, 2)
-        offsets(PART1)
+        parts, turn, upto = (PARTL, TURNL, COUNTL) if t else (PART1, TURN1, COUNT1)
+        offsets(parts, MERGE[t > 0])
         if t > 0:
-            flip_b(7, 8)
-            recv(t, "rp%d" % t, True, pk)
-            send(1, T.TL[t], T.TS[t], "rt%d" % t, False, "TS%d" % t)
+            text(t)
         else:
             consts(0)
-        ts(T.T1[:, 2:130:2], w1, -256.0, gt, r=WS1, w="T10")
-        act(T.T1[:, 3:130:2], w1, AF.Sign, bias=256.0, r=WS1, w="T11")
         for j in range(2):
+            act(T.T1[:, 2 + j:130:2], w1, AF.Sign, bias=256.0, r=WS1, w="T1%d" % j)
             act(T.A2[:, j:128:2], T.A[:, s0:s0 + 64], scale=TINY, r="A%d" % t, w="A2%d" % j)
             act(T.A2[:, 128 + j:256:2], T.A[:, s0:s0 + 64], scale=-TINY, bias=cA2 if t else 0.0, r="cA2 A%d" % t, w="A2%d" % (j + 2))
         J = T.B1[:, 0:128]
@@ -779,8 +836,8 @@ def rank_program(g, core, T, topo):
         done = {"i": 0, "j": 0}
 
         def counts1(side, hi):
-            lo, last = done[side], [x[2] for x in TURN1 if x[0] == side][-2:]
-            if hi - lo < 26 and hi not in last[side == "i":]:
+            lo = done[side]
+            if hi not in upto[side]:
                 return
             if side == "i":
                 pairs(T.B0[:, 2 * lo:2 * hi], 16 * lo, hi - lo, False, span("Q", 16 * lo, 16 * hi, 16), "#0")
@@ -789,28 +846,30 @@ def rank_program(g, core, T, topo):
             else:
                 lo, up = lo + (lo > 0), min(hi + 1, 64)
                 pairs(J[:, 2 * lo:2 * up], 1024 + 16 * lo, up - lo, hi == 64, "N1p" + span("Q", max(1040, 1024 + 16 * lo), 1024 + 16 * up, 16), "#1")
-                if hi == last[0]:
-                    act(T.TH[:], T.B0[:, 0:128], AF.Sign, scale=-1.0, bias=61 / 256, r="#0", w="TH")
+                if not lo:
                     mm1(J, nI8, T.T1[:, 0:128], False, False, "nI8 T10 T11 T1p", "#1")
+                if hi == upto["j"][-2]:
+                    act(T.TH[:], T.B0[:, 0:128], AF.Sign, scale=-1.0, bias=61 / 256, r="#0", w="TH")
                     mm1(J, hI, T.TH[:], False, False, "hI TH", "#1")
             done[side] = hi
 
-        duels(PART1, TURN1, PLAIN[0], 0, Pt, pk, counts1)
+        duels(parts, turn, PLAIN[t > 0], MERGE[t > 0], 0, TXw, xk, counts1)
         act(T.CW[:, 0:256], T.ix[:], scale=0.0, bias=cRf, r="ix cRf", w="CWa")
         if t > 0:
             act(T.CW[:, CW1:CW1 + 256], T.ix[:], scale=0.0, r="ix", w="CWb")
-            recv(1, "ro%d" % (t - 1), False, ok)
         else:
+            act(T.CW[:, CW1:CW1 + 256], T.ix[:], AF.Silu, scale=0.0, r="ix", w="CWb")
+            ops[-1][5] = ((1360, 256, 0), 0.0, None)
             consts(1)
-            starts(0)
+        starts(t)
         for lo, hi, bk, sh in PART2:
             mm1(Bk[bk][:, 0:2 * (hi - lo)], Id, T.K2[:, 64 * (t > 0) + 32 + lo - hi:64 * (t > 0) + 32 + hi - lo], True, False, "Id K20 K21 K22 K23", "#%d" % bk)
         scan(T.LF[:, 0:128], J, T.A2[:, 0:128], NONE[0] * TINY, mx, mn, "#1 A20 A21", "LFa")
         scan(T.LF[:, 263:135:-1], T.B1[:, 127::-1], T.A2[:, 255:127:-1], NONE[1] * TINY, mx, mn, "#1 A22 A23", "LFb")
         tt(T.nd[:], T.LF[:, 3:128:4], T.LF[:, 140:265:4], add, "LFa LFb LFp", "nd")
         ts(T.oW2[:], T.nd[:], -1 / TINY, mul, c256b if t else 256.0, mn, r="nd c256b", w="oW2")
-        if t < 3:
-            expand(t + 1)
+        if t == 0:
+            expand()
         witnesses(PART2, win, T.oW2, wk + " oW2")
         for lo, hi, bk, sh in PART2:
             mm1(Bk[bk][:, 0:hi - lo], Idw, T.LF[:, 3 + 4 * lo:4 * hi:4], False, False, "Idw LFa", "#%d" % bk)
@@ -831,13 +890,12 @@ def rank_program(g, core, T, topo):
         tt(T.dO[:], O(t), O(t, -1, 15), sub, ok + " Op", "dO")
         tt(XO, T.dO[:, 0:16].indirect(T.orr[:, 0:8]), BO, mul, "dO orr BO", "XO")
         w2, WS2 = T.WS[:, 15:512:16], span("WS", 0, 32, 2)
-        offsets(PART2)
-        ts(T.T2[:, 2:66:2], w2, -256.0, gt, r=WS2, w="T20")
-        act(T.T2[:, 3:66:2], w2, AF.Sign, bias=256.0, r=WS2, w="T21")
+        offsets(PART2, MERGE[2])
+        for j in range(2):
+            act(T.T2[:, 2 + j:66:2], w2, AF.Sign, bias=256.0, r=WS2, w="T2%d" % j)
         mm(T.B5[:, 0:128], [(XO, Id)], "XO Id", "#5")
         act(dOT, T.B5[:, 0:128], scale=cNz, r="#5 cNz", w="dOT")
         act(dO0, T.B5[:, 0:128], scale=cIs0, r="#5 cIs0", w="dO0")
-        act(T.fine[:, 256:384], dOT, scale=1 / 256, r="dOT", w="fine")
         mm(T.B7[:, 128:144], [(ShI, O(t))], "ShI " + ok, "#7")
         act(T.Dp[:], T.B7[:, 128:144], r="#7", w="Dp")
 
@@ -846,10 +904,10 @@ def rank_program(g, core, T, topo):
                 pairs(xi, 512, 32, False, span("Q", 512, 1024, 16), "#0")
                 mm1(xi, nI8, T.T2[:, 2:66], False, True, "nI8 T20 T21", "#0")
                 mm1(xj, nI8, T.T2[:, 0:64], False, False, "nI8 T20 T21 T2p", "#1")
-            elif hi == 32:
+            elif (side, hi) == TURN2[-1][::2]:
                 pairs(xj, 1024, 32, True, "N1p" + span("Q", 1040, 1536, 16), "#1")
 
-        duels(PART2, TURN2, PLAIN[1], 512, Pt, pk, counts2)
+        duels(PART2, TURN2, PLAIN[2], MERGE[2], 512, TXw, xk, counts2)
         if t == 0:
             consts(2)
         if t == 1:
@@ -878,66 +936,57 @@ def rank_program(g, core, T, topo):
         ts(T.CW[:, 0:CW1].indirect(T.oR[:, 0:16]), T.V[:, 0:256], -1.0, mul, ROUND + 64, add, r="oR Re Ro V", w="CWa")
         cp(T.oPP[:], T.B4[:, 256:512], "#4", "oPP")
         ts(T.CW[:, 0:CW1].indirect(T.oR[:, 16:k]), T.V[:, 256:16 * k], -1.0, mul, ROUND + 64, add, r="oR Re Ro V", w="CWa")
+        act(cE, T.cum[:, 128:129], AF.Relu, bias=cTe, scale=-256.0, r="cum cTe", w="cE")
+        act(cE2, cE, bias=cB0, r="cE cB0", w="cE2")
+        ts(T.oE[:, 0:1], base, cE2, add, 256.0, mn, r="cE2 #5", w="oE")
 
         def cuts(h):
             return zip((32 * h,), (32 * h + 32,)) if h else ((0, HEAD), (HEAD, 32))
 
         def items(h):
             for lo, hi in cuts(h):
-                act(T.PG[:, 16 * lo:16 * hi], Pt[:, 0:4096].indirect(T.oPP[:, lo:hi]), r=pk + " oPP", w=span("PG", 16 * lo, 16 * hi, 32))
+                act(T.PG[:, 16 * lo:16 * hi], Pw.indirect(T.oPP[:, lo:hi]), r="P0 oPP", w=span("PG", 16 * lo, 16 * hi, 32))
 
         items(0)
         items(1)
         for lo, hi, x in ((0, FIRST, "G2"), (FIRST, 128, "G2a"), (128, 256, "G2b")):
             scan(T.G2[:, 8 + lo:8 + hi], T.CW[:, CW1 + lo:CW1 + hi], T.CW[:, lo:hi], 0.0, mx, sub, "CWa CWb", x)
             ts(T.oTT[:, lo:hi], T.G2[:, 8 + lo:8 + hi], ROUND, add, r=x, w=span("oTT", lo, hi, 32))
-        if t == 3:
-            recv(1, "rt3", False, "TL3")
-            dma("g", T.CW[0:128:16, 0:4096], T.TL[3], "TL3", "CWa CWb")
-        vv = T.B5[:, 256:384]
-        for k, (l, y) in enumerate(((dO0, T.ones[:]), (dOT, st), (B8k, st), (nB8k, stp))):
-            mm1(vv, l, y[:, 0:128], k == 0, False, "dO0 ones dOT step stepp B8k nB8k", "#5")
-        mm(T.B4[:, 0:256], [(dO0, T.fine[:, 0:256]), (T.fine[:, 256:384], st)], "dO0 step fine0 fine", "#4")
-        mm1(vv, Idf, T.G2[:, 8:136], False, False, "G2 G2a Idf", "#5")
-        mm1(vv, nIdf, T.G2[:, 7:135], False, True, "G2 G2a nIdf", "#5")
-        scan(T.dd[:, 0:128], T.G2[:, 136:264], T.G2[:, 135:263], 0.0, mn, sub, "G2a G2b", "dd")
-        for k, (l, y) in enumerate(((dO0, T.ones[:]), (dOT, st), (B8k, st), (nB8k, stp))):
-            mm1(T.B0[:, 256:384], l, y[:, 128:256], k == 0, False, "dO0 ones dOT step stepp B8k nB8k", "#0")
-        mm1(T.B0[:, 256:384], Id, T.dd[:, 0:128], False, True, "Id dd", "#0")
+        for lo, x, r in ((0, "a", "G2 G2a"), (128, "b", "G2a G2b")):
+            scan(T.dd[:, lo:lo + 128], T.G2[:, 8 + lo:136 + lo], T.G2[:, 7 + lo:135 + lo], 0.0, mn, sub, r, "dd" + x)
+        for k, (l, y) in enumerate(((dO0, T.ones[:]), (dOT, st), (B8k, st), (nB8k, stp), (Id, T.dd[:]))):
+            mm1(T.B0[:, 256:512], l, y, k == 0, k == 4, "dO0 ones dOT step stepp B8k nB8k Id" + " dda ddb" * (k == 4), "#0")
         items(2)
         items(3)
 
         def named(lo, hi, x):
-            mm1(T.B2[:, lo:hi], Id, (T.ones, T.dd)[lo > 0][:, 0:128], True, False, "Id ones" + " dd" * (lo > 0), "#2")
-            mm1(T.B2[:, lo:hi], nI4k, T.sn[:, lo:hi], False, False, "nI4k sn" + x, "#2")
-            signs(T.B2[:, lo:hi], A1, lo, hi, 0, False, "A1", "#2")
-            signs(T.B2[:, lo:hi], nB4k, lo, hi, 1, True, "nB4k", "#2")
-            f = T.t1[:, lo:hi] if lo else T.dd[:, 128:256]
-            act(f, T.B2[:, lo:hi], AF.Relu, bias=cB1, r="#2 cB1", w="t1b" if lo else "f1")
-            if not lo:
-                tt(T.t1[:, lo:hi], vv[:, lo:hi], f, mul, "#5 f1", "t1a")
-            tt(T.t2[:, lo:hi], T.B4[:, lo:hi], f, mn, "#4 " + ("t1b" if lo else "f1"), "t2" + x)
+            for bk, more in ((2, ()), (4, ((dO0, T.ones), (dOT, st)))):
+                out, w = Bk[bk][:, lo:hi], "#%d" % bk
+                for k, (l, y) in enumerate(more + ((Id, T.dd), (nI4k, T.sn))):
+                    mm1(out, l, y[:, lo:hi], k == 0, False, "dO0 ones dOT step Id nI4k" + " dda ddb" * (l is Id) + " sn" * (l is nI4k), w)
+            for bk, y in ((2, "t1"), (4, "t2")):
+                out, w = Bk[bk][:, lo:hi], "#%d" % bk
+                signs(out, A1, lo, hi, 0, False, "A1", w)
+                signs(out, nB4k, lo, hi, 1, True, "nB4k", w)
+                act(T[y][:, lo:hi], out, AF.Relu, bias=cB1, r=w + " cB1", w=y + x)
 
         def slots(lo, hi, x):
-            one = [(BO, T.t1[:, k:hi:2]) for k in (lo, lo + 1)]
-            two = [((nBx, Bx)[lo > 0], T.t2[:, k:hi:2]) for k in (lo, lo + 1)]
             mm1(T.B6[:, lo // 2:hi // 2], B256, T.step[:, 16 + lo:16 + hi:2], True, False, "step B256", "#6")
-            for k, (l, y) in enumerate(one if lo else one + two):
-                mm1(T.B6[:, lo // 2:hi // 2], l, y, False, k == (1 if lo else 3), "BO nBx t1" + x + " t2a" * (k > 1), "#6")
-            mm(T.B7[:, lo // 2:hi // 2], one + two if lo else one, "BO Bx t1" + x + " t2b" * (lo > 0), "#7")
+            for k in (lo, lo + 1):
+                mm1(T.B6[:, lo // 2:hi // 2], BO, T.t1[:, k:hi:2], False, k > lo, "BO t1" + x, "#6")
+            mm(T.B7[:, lo // 2:hi // 2], [(BO, T.t2[:, k:hi:2]) for k in (lo, lo + 1)], "BO t2" + x, "#7")
 
         for h in range(4):
             nk = "N%d N%d" % (2 * h, 2 * h + 1) + " N0x" * (h == 0)
             for j in (2 * h, 2 * h + 1):
                 for lo, hi in cuts(j):
                     tt(T.NN[:, 16 * lo:16 * hi], TXw.indirect(T.oTT[:, lo:hi]), T.PG[:, 16 * lo:16 * hi], eq,
-                       "TX" + span("oTT", lo, hi, 32) + span("PG", 16 * lo, 16 * hi, 32), "N%d" % j + "x" * (hi == HEAD))
+                       xk + span("oTT", lo, hi, 32) + span("PG", 16 * lo, 16 * hi, 32), "N%d" % j + "x" * (hi == HEAD))
             if h == 0:
                 mm1(T.B3[:, 0:128], S0f, T.G2[:, 8:136], True, True, "G2 G2a S0f", "#3")
             if h == 1:
                 mm1(T.B3[:, 128:256], S0f, T.G2[:, 136:264], True, True, "G2b S0f", "#3")
-            if h == 2:
-                held()
+                held(t)
             bk = (6, 1, 7, 1)[h]
             if h < 3:
                 count(Bk[bk][:, 0:64], T.NN, 1024 * h, 64, nk, "#%d" % bk)
@@ -952,47 +1001,37 @@ def rank_program(g, core, T, topo):
                 items(2 * h + 4)
                 items(2 * h + 5)
             if h == 1:
-                act(T.sn[:, 0:128], vv, AF.Sign, bias=cSn, r="#5 cSn", w="sna")
-                act(T.sn[:, 128:256], T.B0[:, 256:384], AF.Sign, bias=cSn, r="#0 cSn", w="snb")
+                act(T.sn[:], T.B0[:, 256:512], AF.Sign, bias=cSn, r="#0 cSn", w="sn")
             if h == 2:
-                accepted(0, 128)
-                named(0, 128, "a")
-                flip_a(0, 128, "a")
+                named(0, NAMES, "a")
+                accepted(0, FLIPS[1])
+                flip_a(t, 0, FLIPS[1], "a")
         if t == 0:
             consts(3)
-        slots(0, 128, "a")
-        named(128, 256, "b")
-        equals(0, 4, "a")
-        flip_b(0, 4)
-        accepted(128, 256)
-        flip_a(128, 256, "b")
-        slots(128, 256, "b")
+        slots(0, NAMES, "a")
+        accepted(FLIPS[1], FLIPS[2])
+        flip_a(t, FLIPS[1], FLIPS[2], "m")
+        accepted(FLIPS[2], 256)
+        named(NAMES, 256, "b")
+        flip_a(t, FLIPS[2], 256, "b")
+        equals(0, NAMES // 32, "a")
+        name(0, NAMES // 32, "a")
+        slots(NAMES, 256, "b")
         signs(T.B0[:, 0:256], L0, 0, 256, 0, True, "L0", "#0", True)
-        values(t)
         act(T.G0[:], T.B0[:, 0:256], AF.Relu, bias=cG0, scale=-0.5, r="#0 cG0", w="G0")
-        act(cE, T.cum[:, 128:129], AF.Relu, bias=cTe, scale=-256.0, r="cum cTe", w="cE")
-        act(cE2, cE, bias=cB0, r="cE cB0", w="cE2")
-        ts(T.oE[:, 0:1], base, cE2, add, 256.0, mn, r="cE2 #5", w="oE")
-        equals(4, 8, "b")
-        keys(t)
-        places(t)
+        equals(NAMES // 32, 8, "b")
+        name(NAMES // 32, 8, "b")
         if t == 0:
             consts(4)
         if t < 3:
-            starts(t + 1)
             offsets1(t + 1)
-            flip_b(4, 7)
-            wn, wnk = W[(t + 1) % 2], "W%d W%dp" % ((t + 1) % 2, (t + 1) % 2)
-            apply_u(t, wn, wnk)
-            witnesses(PART1, wn[:, 0:WW], T.oW1[:, s0 + 64:s0 + 128], wnk + " oW1%d" % (t + 1))
-            dma("y", T.TS[t + 1], wn[0:128:16, 0:4096], wnk, "TS%d" % (t + 1))
-        else:
-            flip_b(4, 8)
-            dma("y", T.yt[:, 0:2048], T.TX[:, 0:2048], "TX", "yta", lat=4500.0)
-            dma("a", T.yt[:, 2048:4096], T.TX[:, 2048:4096], "TX", "ytb", lat=4500.0)
-            recv(1, "ro3", False, "o32")
-            dma("y", T.yo[:], T.o32[:, 16:32], "o32", "yo")
-            apply_u(3, T.CW, "CWa CWb")
-            cp(T.CW[:, 0:4096:256], T.z0[:], "z0 CWa", "CWa CWb")
-            dma("a", T.yw[:], T.CW[0:128:16, 0:4096], "CWa CWb", "yw")
+            witnesses(PARTL, T.W0[:, 0:WW], T.oW1[:, s0 + 64:s0 + 128], "W0 W0p oW1%d" % (t + 1))
+        places(t)
+        for x in "amb":
+            flip_b(t, x)
+    dma("y", T.yt[:, 0:2048], T.X4[:, 0:2048], "X4", "yta", lat=4500.0)
+    dma("a", T.yt[:, 2048:4096], T.X4[:, 2048:4096], "X4", "ytb", lat=4500.0)
+    dma("y", T.yo[:], T.o32[:], "O4", "yo")
+    cp(T.W0[:, 0:4096:256], T.z0[:], "z0 W0", "W0")
+    dma("g", T.yw[:], T.W0[0:128:16, 0:4096], "W0", "yw")
     _emit(g, T, ops)

from concourse.bass import IndirectOffsetOnAxis
from concourse.mybir import AluOpType as ALU, ActivationFunctionType as AF

N = 4
BIG = 8192.0
HOLD = 65536.0
WW = 4112
WS = 8224
TW = 4144
CW1 = 3200
ORDER = []
TRIES, MOVES = 44, 300
PACES = ((0.83, 1.0, 1.9, 150.0, 110.0, 10.0, 400.0, 0.42), (0.87, 1.3, 3.1, 190.0, 128.0, 10.0, 700.0, 0.45),
         (1.1, 1.0, 2.5, 170.0, 122.0, 10.0, 500.0, 0.58), (1.2, 1.9, 6.5, 240.0, 185.0, 20.0, 1000.0, 0.6))
LOADS = (4400.0, 6000.0)
LINK = 1600.0
BULK = 16000.0
TINY = 2.0 ** -21
NONE = (-6000.0, -12000.0)
ROUND = 1.5 * 2.0 ** 23
SHARE = 34
PART1 = ((0, 8, 4, "v8"), (8, 28, 6, "a28"), (28, 64, 5, "v46 a64"))
TURN1 = (("i", 0, 8), ("j", 0, 8), ("i", 8, 28), ("i", 28, 46), ("i", 46, 64), ("j", 8, 28), ("j", 28, 46), ("j", 46, 64))
COUNT1 = {"i": (64,), "j": (28, 46, 64)}
PARTL = ((0, 16, 4, "v16"), (16, 40, 6, "a40"), (40, 64, 5, "a64"))
TURNL = (("i", 0, 16), ("i", 16, 40), ("i", 40, 64), ("j", 0, 16), ("j", 16, 40), ("j", 40, 64))
COUNTL = {"i": (40, 64), "j": (40, 64)}
PART2 = ((0, 12, 4, "v12"), (12, 32, 6, "a32"))
TURN2 = (("i", 0, 12), ("i", 12, 32), ("j", 12, 32), ("j", 0, 12))
PLAIN = (8, 40, 32)
MERGE = (64, 40, 64)
FLIPS = (0, 128, 192, 256)
NAMES = 128
FIRST, HEAD = 32, 12
PIECES = ("V", "Sel")

F, B, I, U = "float32", "bfloat16", "int32", "uint16"
MATS = "BO LT Id A1 nBO nI B256 B8k nB8k BN nB4k nS8k nI8 S0 nS0 ShI L0 Mx dOT dO0 XO nI4k qI hI cI n4I".split()
SCRATCH = {}
for _n, _c, _d in (
    ("X0", TW, B), ("X1", TW, B), ("X2", TW, B), ("X3", TW, B), ("X4", TW, B), ("P0", 4096, B),
    ("W0", WS, B), ("cdo", 256, I), ("CT", 272, B), ("cdi", 256, I), ("witi", 256, I), ("prbi", 16, I),
    ("ip", 8, I), ("iw", 8, I), ("col", 48, F), ("ia", 8, I), ("ib", 16, I), ("oa", 8, U), ("ob", 16, U), ("orr", 64, U),
    ("G1", 512, F), ("G2", 512, F), ("A", 264, F), ("A64", 256, F), ("Ah", 264, B), ("Al", 264, B), ("DL", 264, F), ("DB", 256, B),
    ("KX", 512, F), ("ZX", 512, B), ("ZS", 512, B), ("MX", 512, B), ("MK", 256, B), ("LV", 256, B), ("m16", 128, B), ("or2", 16, U),
    ("W4", 128, B), ("two", 128, B), ("UU", 192, B), ("A2", 256, F), ("LF", 272, F), ("dd", 256, B),
    ("oW1", 256, U), ("ix", 256, B), ("iq16", 128, B), ("iqm", 16, B), ("Z", 144, B), ("M", 128 * len(MATS), B), ("Mf", 512, F),
    ("Sel", 2048, B), ("MW", 16 * max(8, *(p[1] - p[0] for p in PART1 + PART2 + PARTL)), B), ("MWk", 128, B), ("MC", 400, B), ("tm", 64, F),
    ("z0", 16, B), ("xz", 16, B), ("K0", 128, B),
    ("GW", 1024, B), ("WS", 1024, B), ("oP", 64, U), ("oTQ", 192, U), ("PG", 4096, B),
    ("NN", 4096, B), ("N1", 2048, B), ("nd", 32, F), ("T1", 136, B), ("Z2", 136, B), ("TH", 128, B), ("T2", 72, B), ("AE", 128, B),
    ("CJ", 128, B), ("K2", 128, B), ("oW2", 32, U),
    ("cum", 136, F), ("DD", 128, F), ("ones", 256, B), ("dK", 128, F), ("u0", 64, F),
    ("oR", 64, U), ("step", 272, B), ("oPP", 256, U), ("oTT", 256, U),
    ("V", 1024, F), ("CW", 2 * CW1, F), ("dO", 16, B),
    ("sg", 352, B), ("sn", 256, B), ("nil", 256, B), ("G0", 256, B), ("d0", 256, B), ("t1", 256, B), ("t2", 256, B),
    ("KS", 128, F), ("E", 400, F), ("YS", 400, F), ("x1", 16, F), ("xo", 16, F), ("oH", 16, U), ("x2", 32, F),
    ("sG", 64, U), ("oG", 64, U), ("sX", 96, U), ("lX", 96, U), ("FV", 256, B), ("sv", 128, B), ("CS", 264, F), ("e1", 8, F), ("oE", 8, U),
    ("Dp", 16, B), ("uo", 16, B), ("su", 8, U), ("O", 160, B), ("o32", 16, F),
):
    SCRATCH[_n] = ("sbuf", [128, _c], _d)
SCRATCH["TD"] = ("dram", [8, 4096], B)
for _t in range(8):
    SCRATCH["B%d" % _t] = ("psum", [128, 512], F)

NDMA = 60
SEMAPHORES = (["qv", "qa", "qt", "qg", "loc"] + ["d%d" % k for k in range(NDMA)]
              + ["r%s%d" % (k, t) for k in "chxfamb" for t in range(4)])


def _place(ops, before, after, floor, rank):
    n = len(ops)
    left, ready, start, gaps = [len(p) for p in before], list(floor), [0.0] * n, {}
    cand = [j for j in range(n) if not left[j]]
    while cand:
        j = min(cand, key=lambda x: rank[x])
        cand.remove(j)
        s, c = ready[j], ops[j][5][0]
        if ops[j][0] != "r":
            used = gaps.setdefault(ops[j][0], [])
            lo, hi = 0, len(used)
            while lo < hi:
                mid = (lo + hi) // 2
                if used[mid][1] <= s:
                    lo = mid + 1
                else:
                    hi = mid
            while lo < len(used) and s + c > used[lo][0]:
                s = max(s, used[lo][1])
                lo += 1
            used.insert(lo, (s, s + c))
        start[j] = s
        for i, d in after[j]:
            ready[i] = max(ready[i], s + d)
            left[i] -= 1
            if not left[i]:
                cand.append(i)
    return start


def _graph(ops, deps, WAKE):
    n = len(ops)
    pre = [[(i, ops[i][5][1] + WAKE) for i in d] for d in deps]
    last, sent = {}, {o[5][2]: j for j, o in enumerate(ops) if o[1] == "s"}
    for j, o in enumerate(ops):
        if o[1] == "r":
            pre[j].append((sent[o[2][2]], ops[sent[o[2][2]]][5][1]))
        elif o[0] == "t":
            if o[4][0] in last:
                pre[j].append((last[o[4][0]], ops[last[o[4][0]]][5][0]))
            last[o[4][0]] = j
        elif o[0] not in "va":
            if o[0] in last:
                pre[j].append((last[o[0]], ops[last[o[0]]][5][0]))
            last[o[0]] = j
    post = [[] for _ in ops]
    for j in range(n):
        for i, c in pre[j]:
            post[i].append((j, c))
    return pre, post, [[(i, ops[j][5][0] + c - ops[i][5][0]) for i, c in pre[j]] for j in range(n)]


def _order(timed, deps):
    n = len(deps)
    graphs = [_graph(ops, deps, m[3]) for ops, m in zip(timed, PACES)]
    best, rank, seed = None, list(range(n)), 1
    for k in range(TRIES):
        ops, (pre, post, back) = timed[k % len(PACES)], graphs[k % len(PACES)]
        if best:
            rank = []
            for x in best[2][k % len(PACES)]:
                seed = (seed * 1103515245 + 12345) % 2147483648
                rank.append(x + 150.0 * seed / 2147483648)
        start = _place(ops, pre, post, [0.0] * n, rank)
        late = _place(ops, post, back, [o[5][1] - o[5][0] for o in ops], [-start[j] - ops[j][5][0] for j in range(n)])
        start = _place(ops, pre, post, [0.0] * n, [-late[j] - ops[j][5][0] for j in range(n)])
        new = _polish(timed, deps, graphs[0], sorted(range(n), key=lambda j: (start[j], j)))
        if best is None or new[0] < best[0]:
            best = new
    return best[1]


def _polish(timed, deps, graph, order):
    n = len(order)
    pre, post = [[i for i, c in p] for p in graph[0]], [[i for i, c in p] for p in graph[1]]
    sent = {o[5][2]: j for j, o in enumerate(timed[0]) if o[1] == "s"}
    queue = ["vatgyr".index(o[0]) for o in timed[0]]
    need = [[sent[o[2][2]]] if o[1] == "r" else d for o, d in zip(timed[0], deps)]
    busy = [[o[5][0] for o in ops] for ops in timed]
    lat = [[o[5][1] for o in ops] for ops in timed]

    def run(order, k, lo, old):
        end, free, w, b, l = list(old), [None] * 5, PACES[k][3], busy[k], lat[k]
        left, x = 5, lo - 1
        while left and x >= 0:
            j = order[x]
            q = queue[j]
            if q < 5 and free[q] is None:
                free[q] = end[j] - l[j] + b[j]
                left -= 1
            x -= 1
        free = [f or 0.0 for f in free]
        for j in order[lo:]:
            q = queue[j]
            if q == 5:
                end[j] = end[need[j][0]]
                continue
            s = free[q] - w
            for i in need[j]:
                if end[i] > s:
                    s = end[i]
            s += w
            free[q] = s + b[j]
            end[j] = s + l[j]
        return end

    def total(order, lo, old):
        runs = [run(order, k, lo, old[k]) for k in range(len(PACES))]
        return sum((max(e) + 0.1 * sum(e) / n) / m[4] for e, m in zip(runs, PACES)), runs

    def moves(order, k, end, line, at):
        w, b, l = PACES[k][3], busy[k], lat[k]
        own, full, nxt = list(l), [0.0] * n, [None] * 6
        for j in reversed(order):
            q = queue[j]
            f = own[j]
            if q < 5:
                if nxt[q] is not None and b[j] + nxt[q] > f:
                    f = b[j] + nxt[q]
                nxt[q] = f
                full[j] = f
                f += w
            else:
                full[j] = f
            for i in need[j]:
                if l[i] + f > own[i]:
                    own[i] = l[i] + f
        span = max(end)
        j, out = end.index(span), []

        def ready(x):
            return max([end[i] for i in need[x]] + [-w]) + w
        while True:
            q, s0 = queue[j], end[j] - l[j]
            if q == 5:
                j = need[j][0]
                continue
            if ready(j) >= s0 - 1e-6:
                if not need[j]:
                    break
                j = max(need[j], key=lambda i: end[i])
                continue
            ln, p = line[q], at[j]
            if q < 3:
                for a, z, up in [(p - d, p, True) for d in range(1, 7)] + [(p - 1, p + d, False) for d in range(0, 4)]:
                    if a < 0 or z + 1 >= len(ln):
                        continue
                    part = [ln[z]] + ln[a:z] if up else ln[a + 1:z + 1] + [ln[a]]
                    s, far = end[ln[a - 1]] - l[ln[a - 1]] + b[ln[a - 1]] if a else 0.0, 0.0
                    for x in part:
                        s = max(s, ready(x))
                        far = max(far, s + own[x])
                        s += b[x]
                    far = max(far, s + full[ln[z + 1]])
                    if far < span - 8:
                        out.append((span - far, ln[a], ln[z], up))
            if not p:
                break
            j = ln[p - 1]
        return out

    least, runs = total(order, 0, [[0.0] * n] * len(PACES))
    failed, tried, mark = set(), 0, least
    while tried < MOVES:
        line = [[j for j in order if queue[j] == q] for q in range(5)]
        at = {j: x for ln in line for x, j in enumerate(ln)}
        cand = sorted(set(m for k in range(len(PACES)) for m in moves(order, k, runs[k], line, at) if m[1:] not in failed), reverse=True)
        if not cand:
            if least >= mark:
                break
            failed, mark = set(), least
        place = {x: k for k, x in enumerate(order)}
        for gain, i, j, up in cand[:16]:
            if (i, j, up) in failed:
                continue
            failed.add((i, j, up))
            move, todo, lo, hi = set(), [j if up else i], place[i], place[j]
            while todo:
                x = todo.pop()
                if x not in move:
                    move.add(x)
                    todo.extend(y for y in (pre if up else post)[x] if lo <= place[y] <= hi)
            if lo >= hi or (i in move and j in move):
                continue
            a, b = [x for x in order[lo:hi + 1] if x in move], [x for x in order[lo:hi + 1] if x not in move]
            new = order[:lo] + (a + b if up else b + a) + order[hi + 1:]
            span, r = total(new, lo, runs)
            tried += 1
            if span < least:
                order, least, runs = new, span, r
                for k in range(lo, hi + 1):
                    place[order[k]] = k
    return least, order, [[e - x for e, x in zip(r, l)] for r, l in zip(runs, lat)]


def _emit(g, T, ops):
    writers, readers, banks, deps = {}, {}, {}, []
    for j, (q, kind, fn, rd, wr, cost) in enumerate(ops):
        d = set()
        for k in set(rd + wr):
            if k[0] == "#":
                acc = banks.setdefault(k, [])
                n = len(acc) - 1
                while n >= 0 and ops[acc[n]][0] == q:
                    n -= 1
                while n >= 0 and ops[acc[n]][0] != q:
                    d.add(acc[n])
                    n -= 1
                acc.append(j)
        for k in rd:
            d.update(writers.get(k, []))
        for k in wr:
            d.update(readers.get(k, []))
            d.update(i for i in writers.get(k, []) if k not in PIECES or ops[i][0] != q)
        for k in rd:
            if k[0] != "#":
                readers.setdefault(k, []).append(j)
        for k in wr:
            if k in PIECES:
                writers.setdefault(k, []).append(j)
            elif k[0] != "#":
                writers[k] = [j]
                readers[k] = []
        d.discard(j)
        deps.append(sorted(i for i in d if ops[i][1] != "s" and not (q == "t" and ops[i][0] == "t")))
    if not ORDER:
        def timed_by(m):
            busy = [o[5][0][0] + o[5][0][1] * m[o[5][0][2]] + (m[5] if o[0] in "va" and o[1] == "c" and not o[5][0][2] else 0) for o in ops]
            return [o[:5] + [(c, c + o[5][1], o[5][2])] for o, c in zip(ops, busy)]
        ORDER.extend(_order([timed_by(m) for m in PACES], deps))
    order = ORDER
    place = {j: n for n, j in enumerate(order)}
    ops = [ops[j][:5] for j in order]
    deps = [sorted(place[i] for i in deps[j]) for j in order]
    need = set()
    for j, d in enumerate(deps):
        last = {}
        for i in d:
            if ops[i][1] == "c":
                last[ops[i][0]] = i
        deps[j] = [i for i in d if ops[i][1] != "c"] + list(last.values())
        need.update(last.values())
    Q = {"v": g.vector, "a": g.scalar, "t": g.tensor, "g": g, "y": g.sync}
    cnt = {"v": 0, "a": 0, "t": 0, "g": 0}
    tok, seen, ndma, loc = {}, {q: {} for q in Q}, 0, 0
    for j, (q, kind, fn, rd, wr) in enumerate(ops):
        if kind == "r":
            tok[j] = fn[:2]
            continue
        for i in deps[j]:
            s, n = tok[i]
            if seen[q].get(s, 0) < n:
                Q[q].wait_ge(T.sem[s], n)
                seen[q][s] = n
        if kind == "s":
            loc += fn()
            continue
        ins = fn()
        if kind == "d":
            tok[j] = ("d%d" % ndma, 16)
            ndma += 1
            ins.then_inc(T.sem[tok[j][0]], 16)
        elif j in need:
            cnt[q] += 1
            tok[j] = ("q" + q, cnt[q])
            ins.then_inc(T.sem["q" + q], 1)
    end = {}
    for s, n in tok.values():
        end[s] = max(end.get(s, 0), n)
    end["loc"] = loc
    for s, n in end.items():
        if max(seen[q].get(s, 0) for q in Q) < n:
            g.wait_ge(T.sem[s], n)


def rank_program(g, core, T, topo):
    rank = T.rank_of(core)
    helper = [min(h for h in topo.cores_of(c) if T.rank_of(h) is None and topo.die(h) != topo.die(c) and topo.may_write(h, T.cores[(r + 1) % N]))
              for r, c in enumerate(T.cores)]
    if rank is None:
        if core in helper:
            r = helper.index(core)
            dst = T.cores[(r + 1) % N]
            rid, pid, _ = topo.addr(dst)
            for t in range(4):
                g.wait_ge(T.sem["rh%d" % t], len(topo.engines(T.cores[r], core)))
                x = T["X%d" % (t + 1)][:, 2048:4096]
                g.remote_dma(x, x, T.sem["rh%d" % t], T.sem.loc, pid, rid, topo.mask(core, dst))
            g.wait_ge(T.sem.loc, 4 * len(topo.engines(core, dst)))
        return
    ops = []
    v, a, pe = g.vector, g.scalar, g.tensor

    def op(q, fn, r="", w="", kind="c", cost=400.0, lat=0.0, name=None):
        ops.append([q, kind, fn, r.split(), w.split(), (cost if isinstance(cost, tuple) else (cost, 0, 0), lat, name)])

    def ns(out, in_, r, more=(), k=None, fix=0):
        for x in r.split():
            if x[:2] in ("lX", "su", "oR"):
                return (50 + fix, in_.shape[1], 2), out, in_
            if x[0] == "o" and x != "ones":
                return (50 + fix, out.shape[1], 1), out, in_
        if k is None:
            k = 0.5 if all("16" in str(x.dtype) for x in (out, in_) + tuple(more)) else 1.0
        return (fix, max(64, out.shape[1] * k), 0), out, in_

    def ts(out, in0, s1, o0, s2=None, o1=None, r="", w=""):
        c, out, in0 = ns(out, in0, r)
        if o1 is None:
            op("v", lambda: v.tensor_scalar(out, in0, s1, None, o0), r, w, cost=c)
        else:
            op("v", lambda: v.tensor_scalar(out, in0, s1, s2, o0, o1), r, w, cost=c)

    def tt(out, in0, in1, o, r="", w=""):
        c, out, in0 = ns(out, in0, r, k=1.0 if "#" in r else 2.0)
        op("v", lambda: v.tensor_tensor(out, in0, in1, o), r, w, cost=c)

    def cp(out, in_, r="", w=""):
        c, out, in_ = ns(out, in_, r)
        op("v", lambda: v.tensor_copy(out, in_), r, w, cost=c)

    def ms(ap, c, w):
        op("v", lambda: v.memset(ap, c), "", w, cost=(0, 64, 0))

    def scan(out, d0, d1, init, o0, o1, r="", w=""):
        op("v", lambda: v.tensor_tensor_scan(out, d0, d1, init, o0, o1), r, w, cost=ns(out, d0, "", (d1,))[0])

    def act(out, in_, fn=AF.Identity, bias=0.0, scale=1.0, r="", w=""):
        c, out, in_ = ns(out, in_, r, k=1.0, fix=18)
        if bias is None:
            op("a", lambda: a.activation(out, in_, fn), r, w, cost=c)
        else:
            op("a", lambda: a.activation(out, in_, fn, bias=bias, scale=scale), r, w, cost=c)

    def mm1(out, l, x, st, sp, r, w):
        op("t", lambda: pe.matmul(out, l, x, st, sp), r, w, cost=(10, max(64, x.shape[1]) * (4 if "32" in str(x.dtype) else 1), 7))

    def mm(out, terms, r, w):
        for k, (l, x) in enumerate(terms):
            mm1(out, l, x, k == 0, k == len(terms) - 1, r, w)

    def dma(q, out, in_, r="", w="", lat=2600.0):
        e = {"g": g, "y": g.sync, "a": g.scalar}[q]
        op(q, lambda: e.dma_start(out, in_), r, w, "d", 60.0, lat)

    def iota(out, pat, base, cm, w, flt=False):
        if flt:
            op("g", lambda: g.iota(out, pat, base, cm, allow_small_or_imprecise_dtypes=True), "", w, cost=(130, 2 * out.shape[1], 0))
        else:
            op("g", lambda: g.iota(out, pat, base, cm), "", w, cost=(130, 2 * out.shape[1], 0))

    def send(k, out, in_, sem, r):
        dst = helper[rank] if sem[1] == "h" else T.cores[(rank + k) % N]
        rid, pid, _ = topo.addr(dst)

        def fn():
            g.remote_dma(out, in_, T.sem[sem], T.sem.loc, pid, rid, topo.mask(core, dst))
            return len(topo.engines(core, dst))
        op("g", fn, r, "", "s", (0, 1, 6), LINK + {"x": BULK, "h": BULK, "c": 2000}.get(sem[1], 0), sem)

    def recv(k, sem, w):
        ops.append(["r", "r", (sem, len(topo.engines((helper if sem[1] == "h" else T.cores)[(rank - k) % N], core)), sem), [], w.split(), ((0, 0, 0), 0.0, None)])

    def fill(ap, n, c, w):
        iota(ap, [[0, n]], c, 0, w, True)

    def keep(out, in_, cmp, other, base, r, w):
        op("g", lambda: g.affine_select(out, in_, [[1, 128]], cmp, other, base, -1), r, w)

    def span(name, lo, hi, unit):
        return " " + " ".join(name + str(k) for k in range(lo // unit, (hi - 1) // unit + 1)) + " "

    col = T.col
    (cR, cG, cG15, c4R, cM32, c256, c256b, cIs0, cN0, cB1, cG0, cP, cSn, c75, cSg, cRf, cD, cSi, cX1, cE, cN8, cW, cRm, cY,
     cT, cTe, cNz, cNzB, cS8k, cH0, cH1, cTl, cH0b, cH1b, cA2, c512, cB0, cB1x, cBs, cE2, cD2, cX2) = (col[:, k:k + 1] for k in range(42))
    (BO, LT, Id, A1, nBO, nI, B256, B8k, nB8k, BN, nB4k, nS8k, nI8, S0, nS0, ShI, L0, Mx, dOT, dO0, XO, nI4k, qI, hI, cI, n4I
     ) = (T.M[:, 128 * k:128 * k + 128] for k in range(len(MATS)))
    S0f, Idw, LTf, L0f = (T.Mf[:, 128 * k:128 * k + 128] for k in range(4))
    Z0 = T.Z[:, 15:143]
    X = [T["X%d" % t] for t in range(5)]
    Bk = [T["B%d" % t] for t in range(8)]
    add, sub, mul, mx, mn = ALU.add, ALU.subtract, ALU.mult, ALU.max, ALU.min
    eq, ge, gt, lt, le, ne = ALU.is_equal, ALU.is_ge, ALU.is_gt, ALU.is_lt, ALU.is_le, ALU.not_equal
    Pw = T.P0[:, 0:4096]

    def O(t, lo=0, hi=16):
        return T.O[:, 32 * t + 16 + lo:32 * t + 16 + hi]

    def unit(out, c, w):
        keep(out, T.nil[:, 0:128], ne, c, 0, "nil", w)

    def put(out, c, w, pattern=None, at=1):
        n = out.shape[1]
        op("g", lambda: g.affine_select(out, T.nil[:, 0:n], pattern or [[0, n]], ne if pattern else eq, c, -at, 0), "nil", w, cost=(170, 2 * n, 0))

    def rows(out, c, lo, hi, w):
        op("g", lambda: g.affine_select(out, T.nil[:, 0:128], [[16, 8], [0, 16]], ne if lo == hi else gt, c, lo, -1), "nil", w)
        if lo < hi:
            op("g", lambda: g.affine_select(out, out, [[16, 8], [0, 16]], ge, 0.0, hi, -1), w, w)

    def spread(out, k, n, r, w):
        act(out, T.m16[:, 16 * k:16 * k + 16].indirect(T.orr[:, 0:n]), r=r + " orr", w=w)

    def witnesses(parts, win, off, r):
        for lo, hi, bk, shares in parts:
            for sh in shares.split():
                up = int(sh[1:])
                (cp if sh[0] == "v" else act)(T.GW[:, 16 * lo:16 * up], win.indirect(off[:, lo:up]), r=r, w=span("GW", lo, up, 2))
                lo = up

    def offsets(parts, merge):
        for lo, hi, bk, shares in parts:
            n, w, x = hi - lo, T.WS[:, 16 * lo + 15:16 * hi:16], span("WS", lo, hi, 2)
            scan(T.WS[:, 16 * lo:16 * hi], T.GW[:, 16 * lo:16 * hi], T.MW[:, 0:16 * n], 0.0, mx, add, span("GW", lo, hi, 2) + "MW", x)
            k = 2 + (lo >= merge)
            if k == 2:
                ts(T.oP[:, lo:hi], w, c256b, add, r="c256b" + x, w=span("oP", lo, hi, 2))
            for j in range(k):
                mm1(Bk[bk][:, j * n:j * n + n], Id, w, False, j == k - 1, "Id" + x, "#%d" % bk)
            cp(T.oTQ[:, 3 * lo:3 * lo + k * n], Bk[bk][:, 0:k * n], "#%d" % bk, span("oTQ", 3 * lo, 3 * hi, 6))

    def duels(parts, turn, plain, merge, low, TXw, xk, after):
        calls = []
        for side, lo, hi in turn:
            p0, p1, bk, sh = [p for p in parts if p[0] <= lo < p[1]][0]
            swap = p0 >= plain
            hi2 = hi - (side == "j" and hi == parts[-1][1])
            y, z, ry = 2 * p0 + lo, (2 * p1 if side == "i" else p0 + p1) + lo, span("oTQ", 3 * p0, 3 * p1, 6)
            oy = T.oTQ[:, y:y + hi2 - lo]
            oz, rz = (T.oP[:, lo:hi], span("oP", lo, hi, 2)) if side == "i" and p0 < merge else (T.oTQ[:, z:z + hi2 - lo], ry)
            at = 16 * lo + (1024 if side == "j" and not swap else 0)
            pg, rg = T.PG[:, at:at + 16 * (hi2 - lo)], span("PG", at, at + 16 * (hi - lo), 32)
            if not swap:
                act(pg, Pw.indirect(oz), r="P0" + rz, w=rg)
            elif side == "i":
                act(pg, TXw.indirect(oy), r=xk + ry, w=rg)
            at = 16 * lo + (low if side == "i" else 1040)
            calls.append((T.N1[:, at:at + 16 * (hi2 - lo)], Pw.indirect(oz) if swap else TXw.indirect(oy), pg,
                          ("P0" + rz if swap else xk + ry) + rg, span("Q", at, at + 16 * (hi2 - lo), 16), side, hi))
        for out, in0, pg, r, w, side, hi in calls:
            tt(out, in0, pg, eq, r, w)
            after(side, hi)

    def text(t):
        send(1, X[t + 1][:, 2048:4096], X[t][:, 2048:4096], "rh%d" % t, "P0 X%d" % t)
        send(1, X[t + 1][:, 0:2048], X[t][:, 0:2048], "rx%d" % t, "P0 X%d" % t)

    def lanes_of(t):
        lo, s0 = 128 * t, 64 * t
        if t:
            recv(t, "rc%d" % t, "cd%d" % t)
        cp(T.G1[:, lo:lo + 128], (T.cdi if t else T.cdo)[:, s0:s0 + 64].indirect(T.oa[:, 0:8]), "cd%d oa" % t, "G1")
        op("v", lambda: v.transpose(T.G2[:, lo:lo + 128], T.G1[:, lo:lo + 128]), "G1", "G2 G2a G2b", cost=(40, 128, 0))
        (cp if t == 0 else act)(T.A[:, s0:s0 + 64], T.G2[:, lo:lo + 128].indirect(T.ob[:, 0:4]), r="G2 G2a G2b ob", w="A%d" % t)
        tt(T.DL[:, s0 + 1:s0 + 64], T.A[:, s0 + 1:s0 + 64], T.A[:, s0:s0 + 63], sub, "A%d" % t, "DL%d" % t)
        ts(T.DB[:, s0:s0 + 64], T.DL[:, s0 + 1:s0 + 65], 256.0, mn, r="DL%d DLp" % t, w="DB%d" % t)
        if t == 0:
            ts(T.oW1[:, 0:64], T.DL[:, 1:65], 256.0, mn, r="DL0 DLp", w="oW10")
        else:
            ts(T.oW1[:, s0:s0 + 64], T.DL[:, s0 + 1:s0 + 65], 256.0, mn, c256, add, r="DL%d DLp c256" % t, w="oW1%d" % t)

    def halves_of(t):
        s0 = 64 * t
        act(T.A64[:, s0:s0 + 64], T.A[:, s0:s0 + 64], bias=64.0, r="A%d" % t, w="A64%d" % t)
        act(T.Ah[:, s0:s0 + 64], T.A[:, s0:s0 + 64], bias=64.0, r="A%d" % t, w="Ah%d" % t)
        tt(T.Al[:, s0:s0 + 64], T.A64[:, s0:s0 + 64], T.Ah[:, s0:s0 + 64], sub, "A64%d Ah%d" % (t, t), "Al%d" % t)

    dma("y", T.cdo[:], T.cd[:], w="cd0")
    dma("a", T.witi[:], T.wit[:], w="witi")
    dma("y", T.P0[:], T.pat[:], w="P0", lat=LOADS[0])
    dma("y", T.X0[:, 0:4096], T.txt[:], w="X0", lat=LOADS[1])
    dma("a", T.prbi[:], T.prb[:], w="prbi")
    iota(T.ip[:, 0:1], [[0, 1]], 0, 1, "ip0")
    iota(T.ia[:], [[1, 4], [0, 2]], 0, 0, "ia")
    iota(T.ib[:, 0:4], [[32, 4]], 0, 0, "ib")
    iota(T.iqm[:], [[1, 16]], 0, 0, "iqm", True)
    iota(T.ix[:], [[1, 256]], 0, 0, "ix", True)
    iota(T.iq16[:], [[16, 8], [0, 16]], 0, 0, "iq16", True)
    ms(T.nil[:], 0.0, "nil")
    fill(T.CT[:, 256:272], 16, 0, "CTp")
    fill(T.CT[:, 0:1], 1, 0, "CT0")
    fill(T.DL[:, 64:257:64], 4, int(BIG), "DLp")
    ts(T.ip[:, 1:2], T.ip[:, 0:1], 15, ALU.bitwise_and, r="ip0", w="ip1")
    ts(T.ip[:, 2:3], T.ip[:, 0:1], 31, ALU.bitwise_and, r="ip0", w="ip2")
    cp(cP, T.ip[:, 0:1], "ip0", "cP")
    ts(c4R, T.ip[:, 1:2], 4.0, mul, r="ip1", w="c4R")
    cp(cM32, T.ip[:, 2:3], "ip2", "cM32")
    cp(cR, T.ip[:, 1:2], "ip1", "cR")
    ts(T.oa[:], T.ia[:], c4R, add, r="ia c4R", w="oa")
    ts(T.ob[:, 0:4], T.ib[:, 0:4], cM32, add, r="ib cM32", w="ob")
    ts(T.orr[:], T.ix[:, 0:64], 0.0, mul, cR, add, r="ix cR", w="orr")
    tt(cG, cP, cR, sub, "cP cR", "cG")
    ts(c256, cR, 256.0, mul, r="cR", w="c256")
    ts(c256b, cR, 256.0, mul, 256.0, add, r="cR", w="c256b")
    ts(T.tm[:, 0:16], T.iqm[:], cR, lt, -512.0, mul, r="iqm cR", w="tm0")
    ts(T.tm[:, 16:32], T.iqm[:], cR, eq, 256.0, mul, r="iqm cR", w="tm1")
    ts(T.tm[:, 32:48], T.iqm[:], 15.0, eq, -512.0, mul, r="iqm", w="tm2")
    tt(T.tm[:, 48:64], T.tm[:, 0:16], T.tm[:, 16:32], add, "tm0 tm1", "tm3")
    tt(T.m16[:, 0:16], T.tm[:, 48:64], T.tm[:, 32:48], add, "tm3 tm2", "m0")
    spread(T.MW[:], 0, T.MW.shape[1] // 16, "m0", "MW")
    ts(cG15, cG, 15.0, add, r="cG", w="cG15")
    lanes_of(0)
    ms(T.G2[:, 7:8], 4096 - ROUND, "G2")
    halves_of(0)
    cp(T.CT[:, 1:256], T.witi[:, 1:256], "witi", "CT")
    ts(BO, T.iq16[:], cG, eq, r="iq16 cG", w="BO")
    ts(Id, T.ix[:, 0:128], cP, eq, r="ix cP", w="Id")
    ts(T.Z[:], T.ix[:, 0:144], cG15, eq, r="ix cG15", w="Z")
    ts(cIs0, cR, 0.0, eq, r="cR", w="cIs0")
    witnesses(PART1, T.CT[:, 0:272], T.oW1[:, 0:64], "CT CT0 CTp oW10")
    for dst, s, w in ((nI, -1.0, "nI"), (hI, -0.5, "hI"), (nI8, -1 / 8, "nI8")):
        unit(dst, s, w)
    act(T.K0[:, 0:64], T.ix[:, 0:64], scale=0.0, bias=192.0, r="ix", w="K0a")
    act(T.K0[:, 64:128], T.ix[:, 0:64], scale=0.0, bias=c256b, r="ix c256b", w="K0b")
    fill(T.N1[:, 1024:1040], 16, 0, "N1p")
    fill(T.T1[:, 0:2], 2, 0, "T1p")
    fill(T.T2[:, 0:2], 2, 0, "T2p")
    ts(T.x1[:], T.iqm[:], cR, eq, r="iqm cR", w="x1 x1b")
    for p in range(16):
        ts(T.Sel[:, 128 * p:128 * p + 128], BO, T.x1[:, p:p + 1], mul, r="BO x1 x1b", w="Sel")
    fill(T.ones[:], 256, 1, "ones")
    send(1, T.cdi[:, 64:128], T.cdo[:, 64:128], "rc1", "cd0")
    ops[-1][5] = ((3000, 1, 6),) + ops[-1][5][1:]
    text(0)
    put(T.LF[:, 264:272], NONE[1] * TINY, "LFp")
    fill(T.O[:, 15:160:32], 5, 0, "Op")
    for dst, s, w in ((Idw, 1 / TINY, "Idw"), (n4I, -4.0, "n4I"), (qI, 0.25, "qI"), (cI, 33 / 128, "cI")):
        unit(dst, s, w)
    keep(ShI, BO, eq, 0.0, -1, "BO", "ShI")
    keep(ShI, ShI, ne, -1.0, 0, "ShI", "ShI")
    keep(LT, BO, gt, 0.0, 0, "BO", "LT")
    put(cRf, ROUND + 64, "cRf")
    put(T.two[:], 2.0, "two", [[0, 32], [1, 4]], 3)
    fill(T.dK[:, 0:128:2], 64, 1, "dK")
    put(T.m16[:, 16:32], -2 * HOLD, "m1", [[1, 16]], 0)
    fill(T.m16[:, 96:111], 15, 1, "m6")
    for c, x, w in ((c75, 7.5, "c75"), (cSn, -255.5, "cSn"), (cX2, (HOLD + BIG + ROUND) / BIG, "cX2")):
        put(c, x, w)
    fill(T.step[:, 0:16], 16, 0, "stepp")

    def consts(part):
        if part == 0:
            mm(T.B7[:, 0:135], [(Id, T.Z[:, 8:143]), (Id, T.Z[:, 0:135])], "Id Z", "#7")
            act(T.Z2[:, 0:135], T.B7[:, 0:135], scale=1 / 64, r="#7", w="Z2")
            ts(cH0, cR, 8.0, lt, -1.0, mul, r="cR", w="cH0")
            ts(cH1, cR, 8.0, ge, -1.0, mul, r="cR", w="cH1")
            for j, c in enumerate((cH1, cH0)):
                act(T.CJ[:, j:128:2], T.ix[:, 0:64], scale=0.0, bias=c, r="ix cH0 cH1", w="CJ%d" % j)
            act(T.CJ[:], T.CJ[:], scale=2.0, bias=-63 / 128, r="CJ0 CJ1", w="CJ")
            ts(c512, cR, 512.0, mul, 256.0, add, r="cR", w="c512")
            ts(cA2, cR, -256.0 * TINY, mul, r="cR", w="cA2")
            for k, c in enumerate((256.0, c256b, 256.0, c512)):
                act(T.K2[:, 32 * k:32 * k + 32], T.ix[:, 0:32], scale=0.0, bias=c, r="ix c256b c512", w="K2%d" % k)
            ts(cN0, cR, 0.0, gt, 256.0, mul, r="cR", w="cN0")
            ts(cNz, cR, 0.0, gt, r="cR", w="cNz")
            ts(cNzB, cR, 0.0, gt, -BIG, mul, r="cR", w="cNzB")
            for dst, s, r, w in ((B256, cN0, "cN0", "B256"), (B8k, BIG, "", "B8k"), (nB8k, cNzB, "cNzB", "nB8k"), (nB4k, -HOLD / 16, "", "nB4k")):
                act(dst, BO, scale=s, r="BO " + r, w=w)
        elif part == 1:
            cp(O(0), T.prbi[:], "prbi", "O0")
            ts(T.iw[:, 0:1], T.ip[:, 0:1], 4, ALU.arith_shift_right, r="ip0", w="iw")
            lanes_of(1)
            halves_of(1)
        elif part == 2:
            for dst, c, w in ((S0f, 1.0, "S0f"), (S0, 1.0, "S0"), (nS8k, -BIG, "nS8k")):
                rows(dst, c, 0, 0, w)
            put(T.LV[:], -2 * HOLD, "LV", [[0, 8], [1, 32]], 0)
            unit(nI4k, -4096.0, "nI4k")
            fill(T.sg[:, 0:16], 16, 1, "sgp")
            fill(T.sg[:, 272:288], 16, 0, "sgq")
            fill(T.CS[:, 256:264], 8, 0, "CSp")
            fill(T.E[:, 0:98], 98, 1, "E0 E1 KTa")
            iota(T.YS[:, 0:392], [[0, 8], [1, 49]], 0, 0, "YSa YSb", True)
            fill(T.W0[:, 4096:WW], WW - 4096, 0, "W0p")
            for t in (2, 3):
                send(t, T.cdi[:, 64 * t:64 * t + 64], T.cdo[:, 64 * t:64 * t + 64], "rc%d" % t, "cd0")
            for dst, c, lo, hi, w in ((nS0, -1.0, 0, 0, "nS0"), (BN, 1.0, 1, 15, "BN"), (nBO, -1.0, 0, 15, "nBO")):
                rows(dst, c, lo, hi, w)
            act(cT, cR, scale=68.0, bias=1024.0, r="cR", w="cT")
            act(T.cum[:, 0:1], cT, r="cT", w="cump")
            act(cTl, cR, scale=-68.0, bias=-1088.0, r="cR", w="cTl")
            act(cTe, cTl, scale=-256.0, bias=256.0, r="cTl", w="cTe")
            act(T.tm[:, 0:32], T.ix[:, 0:32], scale=2.0, bias=cT, r="ix cT", w="tm0 tm1")
            act(T.dK[:, 1:64:2], T.tm[:, 0:32], scale=-1.0, r="tm0 tm1", w="dKe")
            act(T.dK[:, 65:128:2], T.tm[:, 0:32], scale=-1.0, bias=-4.0, r="tm0 tm1", w="dKo")
            act(cH0b, cH0, scale=-7.5 / 64, r="cH0", w="cH0b")
            act(cH1b, cH1, scale=-7.5 / 64, r="cH1", w="cH1b")
            tt(L0, LT, Z0, add, "LT Z", "L0")
            act(LTf, LT, r="LT", w="LTf")
            act(L0f, L0, r="L0", w="L0f")
            mm(T.B7[:, 176:177], [(LTf, cTl)], "LTf cTl", "#7")
            mm(T.B7[:, 177:178], [(L0f, cTl)], "L0f cTl", "#7")
            act(cB0, T.B7[:, 176:177], r="#7", w="cB0")
            act(cB1x, T.B7[:, 176:177], bias=1.0, r="#7", w="cB1x")
            act(cBs, T.B7[:, 177:178], scale=-1.0, r="#7", w="cBs")
            tt(A1, Id, LT, sub, "Id LT", "A1")
            act(A1, A1, scale=4096.0, r="A1", w="A1")
            act(cB1, cR, scale=-4096.0, bias=-18 * 4096.0, r="cR", w="cB1")
            ts(T.tm[:, 0:16], T.iqm[:], cR, gt, -BIG, mul, r="iqm cR", w="tm0")
            ts(T.tm[:, 16:32], T.iqm[:], cR, eq, HOLD, mul, r="iqm cR", w="tm1")
            tt(T.tm[:, 32:48], T.tm[:, 0:16], T.tm[:, 16:32], add, "tm0 tm1", "tm2")
            tt(T.m16[:, 32:48], T.tm[:, 32:48], T.m16[:, 16:32], add, "tm2 m1", "m2")
            spread(T.MK[:, 0:256], 2, 16, "m2", "MK")
            cp(T.or2[:, 0:16:2], T.orr[:, 0:8], "orr", "or2")
            ts(T.or2[:, 1:16:2], T.orr[:, 0:8], 16.0, add, r="orr", w="or3")
            act(cN8, cNz, scale=8.0, r="cNz", w="cN8")
            ts(T.oH[:, 0:16:2], T.ix[:, 0:8], cN8, add, r="ix cN8", w="oH")
            ts(T.oH[:, 1:16:2], T.ix[:, 0:8], 8.0, add, r="ix", w="oH")
            act(cRm, cR, bias=-1.0, r="cR", w="cRm")
            ts(T.tm[:, 0:16], T.iqm[:], cRm, eq, -2.0, mul, r="iqm cRm", w="tm0")
            ts(T.tm[:, 16:32], T.iqm[:], cR, lt, r="iqm cR", w="tm1")
            tt(T.m16[:, 48:64], T.tm[:, 0:16], T.tm[:, 16:32], add, "tm0 tm1", "m3")
            spread(T.MX[:, 0:256], 3, 16, "m3", "MX")
            act(T.m16[:, 111:112], cIs0, scale=-2.0, bias=1.0, r="cIs0", w="m6b")
            act(T.m16[:, 112:128], T.m16[:, 48:64], r="m3", w="m7")
            act(T.MX[:, 256:512], T.m16[:, 96:128].indirect(T.or2[:]), r="m6 m6b m7 or2 or3", w="MX2")
            act(T.MWk[:], T.MW[:, 0:128], scale=32.0, r="MW", w="MWk")
            act(cSi, cIs0, scale=-2 / BIG, bias=1 / BIG, r="cIs0", w="cSi")
            act(cX1, cSi, scale=HOLD + BIG + ROUND, r="cSi", w="cX1")
            act(cSg, cIs0, scale=-2 * BIG, bias=BIG, r="cIs0", w="cSg")
            ts(cD, cR, 4112.0, add, r="cR", w="cD")
            act(cD2, cR, bias=4128.0, r="cR", w="cD2")
        elif part == 3:
            act(cY, cR, bias=33.0, r="cR", w="cY")
            ts(T.MC[:, 0:392], T.YS[:, 0:392], cY, ge, -2.0, mul, r="YSa YSb cY", w="MC")
            act(cW, cR, scale=16 / BIG, bias=2064 / BIG, r="cR", w="cW")
            act(T.MC[:, 1:392:49], T.ix[:, 0:8], scale=256 / BIG, bias=cW, r="ix cW", w="MC")
            tt(Mx, Id, Z0, sub, "Id Z", "Mx")
            act(T.e1[:, 1:2], cR, scale=-0.5, bias=1.0, r="cR", w="e11")
            act(cG0, cIs0, scale=-8.0, bias=T.e1[:, 1:2], r="cIs0 e11", w="cG0")
        elif part == 4:
            for t in (2, 3):
                lanes_of(t)
                halves_of(t)
        else:
            cp(T.e1[:, 4:5], T.witi[:, 0:1], "witi", "e14")
            ts(T.xz[:], T.iqm[:], cR, eq, T.e1[:, 4:5], mul, r="iqm cR e14", w="xz")
            mm(T.B7[:, 160:176], [(BO, T.xz[:])], "BO xz", "#7")
            act(T.z0[:], T.B7[:, 160:176], r="#7", w="z0")

    def count(out, buf, lo, n, r, w):
        for m in range(16):
            mm1(out, T.Z[:, 15 - m:143 - m], buf[:, lo + m:lo + 16 * n:16], m == 0, m == 15, r + " Z", w)

    def pairs(out, lo, n, stop, r, w):
        for q in range(8):
            mm1(out, T.Z2[:, 7 - q:135 - q], T.N1[:, lo + q:lo + 16 * n:8], False, stop and q == 7, r + " Z2", w)

    def expand():
        dma("y", T.TD[:], T.CT[:, 0:256], "CT CT0", "TD")
        op("g", lambda: g.indirect_dma_start(T.W0[:, 0:4096], None, T.TD[:], IndirectOffsetOnAxis(ap=T.iw[:, 0:1], axis=0),
                                             bounds_check=7), "TD iw", "W0", "d", 1700.0, 6000.0)

    def name(lo, hi, x):
        act(T.sv[:, 16 * lo:16 * hi], T.B7[:, 16 * lo:16 * hi], r="#7", w="sv" + x)
        ts(T.su[:, lo:hi], T.YS[:, 49 * lo:49 * hi:49], -2 * BIG, mul, r="YS" + x, w="su" + x)
        cp(T.W0[:, 0:WS].indirect(T.su[:, lo:hi]), T.sv[:, 16 * lo:16 * hi], "su%s sv%s W0 W0p" % (x, x), "W0 W0p")

    def equals(lo, hi, x):
        scan(T.KS[:, 16 * lo:16 * hi], T.B6[:, 16 * lo:16 * hi], T.MWk[:, 16 * lo:16 * hi], 0.0, mx, add, "#6 MWk", "KS" + x)
        act(T.E[:, 49 * lo:49 * hi:49], T.KS[:, 16 * lo + 15:16 * hi:16], scale=-0.5 / BIG, bias=-0.5, r="KS" + x, w="KT" + x)
        for k in range(lo, hi):
            n = min(48, 16 * k + 16)
            ts(T.E[:, 49 * k + 49 - n:49 * k + 49], T.B6[:, 16 * k + 16 - n:16 * k + 16], T.KS[:, 16 * k + 15:16 * k + 16], sub, BIG, ne, r="#6 KS" + x, w="E%d" % k)
        back = slice(49 * hi - 1, 49 * lo - 1 if lo else None, -1)
        scan(T.YS[:, back], T.E[:, back], T.MC[:, back], 1.0, mn, sub, "MC KT%s " % x + " ".join("E%d" % k for k in range(lo, hi)), "YS" + x)

    def starts(t):
        for p in range(16):
            s = T.Sel[:, 128 * p:128 * p + 128]
            mm(Bk[2 + p // 8][:, 64 * (p % 8):64 * (p % 8) + 64], [(s, T.Ah[:, 64 * t:64 * t + 64]), (s, T.Al[:, 64 * t:64 * t + 64])],
               "Sel Ah%d Al%d" % (t, t), "#%d" % (2 + p // 8))

    def places(t):
        st = T.step
        mm1(T.B1[:, 0:256], BN, st[:, 16:272], True, False, "BN step", "#1")
        mm1(T.B1[:, 0:255], nBO, st[:, 17:272], False, False, "nBO step", "#1")
        mm1(T.B1[:, 0:256], S0, T.G0[:], False, True, "S0 G0", "#1")
        mm(T.B3[:, 0:256], [(Id, T.G0[:]), (nS0, T.G0[:])], "Id nS0 G0", "#3")
        act(T.d0[:], T.B1[:, 0:256], AF.Relu, r="#1", w="d0")
        scan(T.CS[:, 255::-1], T.d0[:, 255::-1], T.B3[:, 255::-1], 0.0, mul, add, "d0 #3", "CS")
        tt(T.uo[:], T.CS[:, 0:264].indirect(T.oE[:, 0:1]), T.Dp[:], mul, "CS CSp oE Dp", "uo")
        mm(T.B7[:, 144:160], [(Id, O(t)), (Mx, T.uo[:])], "Id Mx uo O%d" % t, "#7")
        act(O(t + 1) if t < 3 else T.o32[:], T.B7[:, 144:160], r="#7", w="O%d" % (t + 1))

    def held(t):
        scan(T.KX[:, 255::-1], T.B3[:, 255::-1], T.MK[:, 255::-1], -2 * ROUND, mx, add, "#3 MK", "KX")
        act(T.xo[:, 0:8], T.KX[:, 16:256:32], r="KX", w="xo0")
        act(T.xo[:, 8:16], T.KX[:, 16:256:32], bias=2 * HOLD, r="KX", w="xo1")
        for lo, x in ((0, "a"), (8, "b")):
            act(T.KX[:, 256 + 16 * lo:384 + 16 * lo], T.xo[:, 0:16].indirect(T.oH[:, lo:lo + 8]), r="xo0 xo1 oH", w="KX2" + x)
        ts(T.sG[:, 16 * t:16 * t + 16], T.KX[:, 0:256:16], HOLD + ROUND, add, r="KX", w="sG%d" % t)
        send(1, T.oG[:, 16 * t:16 * t + 16], T.sG[:, 16 * t:16 * t + 16], "rf%d" % t, "sG%d" % t)
        act(T.x1[:, 0:16:2], T.KX[:, 0:256:32], scale=cSi, bias=cX1, r="cSi cX1 KX", w="x1")
        act(T.x1[:, 1:16:2], T.KX[:, 16:256:32], scale=1 / BIG, bias=cX2, r="cX2 KX", w="x1b")

    def signs(out, l, lo, hi, back, stop, r, w, start=False):
        mm1(out, l, T.sg[:, 16 + lo - back:16 + hi - back], start, stop and hi < 256, r + " sgp " + " ".join("sg%d" % k for k in range(hi // 64)), w)
        if hi == 256:
            mm1(out[:, 192 - lo:256 - lo], l, T.sg[:, 288 - back:352 - back], False, stop, r + " sgq sg4", w)

    def accepted(lo, hi):
        out, bk = lifted(lo)
        mm1(out, S0f, T.G2[:, 8 + lo:8 + hi], True, False, "S0f G2 G2a G2b", bk)
        mm1(out, S0, T.LV[:, lo:hi], False, False, "S0 LV", bk)
        mm1(out, nS8k, T.step[:, 16 + lo:16 + hi], False, False, "nS8k step", bk)
        signs(out, nB4k, lo, hi, 0, True, "nB4k", bk)

    def lifted(lo):
        k = FLIPS.index(lo)
        bk, at = ((5, 384), (3, 384), (5, 256))[k]
        return Bk[bk][:, at:at + FLIPS[k + 1] - lo], "#%d" % bk

    def flip_a(t, lo, hi, x):
        k0, k1, at = lo // 16, hi // 16, 24 * t + 8 * "amb".index(x)
        for j, (s, d) in enumerate(((cSg, cD), (BIG, cD2))):
            y, up = x + str(j), 256 * j
            back = slice(up + hi - 1, up + lo - 1 if up + lo else None, -1)
            tt(T.ZX[:, up + lo:up + hi], lifted(lo)[0], T.KX[:, up + lo:up + hi], eq, lifted(lo)[1] + (" KX2" + "ab"[lo > 0] if j else " KX"), "ZX" + y)
            scan(T.ZS[:, back], T.MX[:, back], T.ZX[:, back], 0.0, mul, add, "MX MX2 ZX" + y, "ZS" + y)
            z = T.x2[:, 16 * j + k0 // 2:16 * j + k1 // 2]
            tt(z, T.ZS[:, up + lo:up + hi:32], T.x1[:, k0 + j:k1:2], add, "x1 x1b ZS" + y, "x2" + y)
            ts(T.sX[:, at + j:at + k1 - k0:2], z, s, mul, d, mn, r="cSg cD cD2 x2" + y, w="sX%d%s" % (t, y))
        send(1, T.lX[:, at:at + k1 - k0], T.sX[:, at:at + k1 - k0], "r%s%d" % (x, t), "sX%d%s0 sX%d%s1" % (t, x, t, x))

    def flip_b(t, x):
        if x == "a":
            recv(1, "rx%d" % t, "X%d" % (t + 1))
            recv(1, "rh%d" % t, "X%dh" % (t + 1))
            recv(1, "rf%d" % t, "oG%d" % t)
            act(T.FV[:], X[t + 1][:, 0:4096].indirect(T.oG[:, 16 * t:16 * t + 16]), scale=-1.0, bias=255.0, r="X%d X%dh oG%d" % (t + 1, t + 1, t), w="FV")
        recv(1, "r%s%d" % (x, t), "lX%d%s" % (t, x))
        n = "amb".index(x)
        for k in range(FLIPS[n] // 32, FLIPS[n + 1] // 32):
            at = 24 * t + 8 * n + 2 * k - FLIPS[n] // 16
            cp(X[t + 1][:, 0:TW].indirect(T.lX[:, at:at + 2]), T.FV[:, 32 * k:32 * k + 32], "lX%d%s FV" % (t, x), "X%d" % (t + 1))

    def offsets1(t):
        s0 = 64 * t
        for lo, hi, bk, sh in PARTL if t else PART1:
            n, k = hi - lo, 2 + (lo >= MERGE[t > 0])
            mm1(Bk[bk][:, 0:k * n], Id, T.K0[:, 64 - n:64 + (k - 1) * n], True, False, "Id K0a K0b", "#%d" % bk)
            mm1(Bk[bk][:, 0:n], Id, T.Ah[:, s0 + lo:s0 + hi], False, False, "Id Ah%d" % t, "#%d" % bk)
            mm1(Bk[bk][:, 0:n], Id, T.Al[:, s0 + lo:s0 + hi], False, False, "Id Al%d" % t, "#%d" % bk)
            mm1(Bk[bk][:, n:2 * n], nI, T.DB[:, s0 + lo:s0 + hi], False, False, "nI DB%d" % t, "#%d" % bk)

    offsets1(0)
    for t in range(4):
        TXw, xk, ok = X[t][:, 0:4096], "X%d" % t, "O%d" % t
        win, wk = (T.W0[:, 0:WW], "W0 W0p") if t else (T.CT[:, 0:272], "CT CT0 CTp")
        s0 = 64 * t
        w1, WS1 = T.WS[:, 15:1024:16], span("WS", 0, 64, 2)
        parts, turn, upto = (PARTL, TURNL, COUNTL) if t else (PART1, TURN1, COUNT1)
        offsets(parts, MERGE[t > 0])
        if t > 0:
            text(t)
        else:
            consts(0)
        for j in range(2):
            act(T.T1[:, 2 + j:130:2], w1, AF.Sign, bias=256.0, r=WS1, w="T1%d" % j)
            act(T.A2[:, j:128:2], T.A[:, s0:s0 + 64], scale=TINY, r="A%d" % t, w="A2%d" % j)
            act(T.A2[:, 128 + j:256:2], T.A[:, s0:s0 + 64], scale=-TINY, bias=cA2 if t else 0.0, r="cA2 A%d" % t, w="A2%d" % (j + 2))
        J = T.B1[:, 0:128]
        mm1(J, Id, T.CJ[:], True, False, "Id CJ", "#1")
        mm1(T.B0[:, 0:128], hI, T.CJ[:], True, False, "hI CJ", "#0")
        done = {"i": 0, "j": 0}

        def counts1(side, hi):
            lo = done[side]
            if hi not in upto[side]:
                return
            if side == "i":
                pairs(T.B0[:, 2 * lo:2 * hi], 16 * lo, hi - lo, False, span("Q", 16 * lo, 16 * hi, 16), "#0")
                if hi == 64:
                    mm1(T.B0[:, 0:128], nI8, T.T1[:, 2:130], False, True, "nI8 T10 T11", "#0")
            else:
                lo, up = lo + (lo > 0), min(hi + 1, 64)
                pairs(J[:, 2 * lo:2 * up], 1024 + 16 * lo, up - lo, hi == 64, "N1p" + span("Q", max(1040, 1024 + 16 * lo), 1024 + 16 * up, 16), "#1")
                if not lo:
                    mm1(J, nI8, T.T1[:, 0:128], False, False, "nI8 T10 T11 T1p", "#1")
                if hi == upto["j"][-2]:
                    act(T.TH[:], T.B0[:, 0:128], AF.Sign, scale=-1.0, bias=61 / 256, r="#0", w="TH")
                    mm1(J, hI, T.TH[:], False, False, "hI TH", "#1")
            done[side] = hi

        duels(parts, turn, PLAIN[t > 0], MERGE[t > 0], 0, TXw, xk, counts1)
        act(T.CW[:, 0:256], T.ix[:], scale=0.0, bias=cRf, r="ix cRf", w="CWa")
        if t > 0:
            act(T.CW[:, CW1:CW1 + 256], T.ix[:], scale=0.0, r="ix", w="CWb")
        else:
            act(T.CW[:, CW1:CW1 + 256], T.ix[:], AF.Silu, scale=0.0, r="ix", w="CWb")
            ops[-1][5] = ((1360, 256, 0), 0.0, None)
            consts(1)
        starts(t)
        for lo, hi, bk, sh in PART2:
            mm1(Bk[bk][:, 0:2 * (hi - lo)], Id, T.K2[:, 64 * (t > 0) + 32 + lo - hi:64 * (t > 0) + 32 + hi - lo], True, False, "Id K20 K21 K22 K23", "#%d" % bk)
        scan(T.LF[:, 0:128], J, T.A2[:, 0:128], NONE[0] * TINY, mx, mn, "#1 A20 A21", "LFa")
        scan(T.LF[:, 263:135:-1], T.B1[:, 127::-1], T.A2[:, 255:127:-1], NONE[1] * TINY, mx, mn, "#1 A22 A23", "LFb")
        tt(T.nd[:], T.LF[:, 3:128:4], T.LF[:, 140:265:4], add, "LFa LFb LFp", "nd")
        ts(T.oW2[:], T.nd[:], -1 / TINY, mul, c256b if t else 256.0, mn, r="nd c256b", w="oW2")
        if t == 0:
            expand()
        witnesses(PART2, win, T.oW2, wk + " oW2")
        for lo, hi, bk, sh in PART2:
            mm1(Bk[bk][:, 0:hi - lo], Idw, T.LF[:, 3 + 4 * lo:4 * hi:4], False, False, "Idw LFa", "#%d" % bk)
            mm1(Bk[bk][:, hi - lo:2 * (hi - lo)], Idw, T.nd[:, lo:hi], False, False, "Idw nd", "#%d" % bk)
        for k in range(4):
            act(T.AE[:, 64 * (k // 2) + k % 2:64 * (k // 2) + 64:2], T.B1[:, k:128:4], AF.Sign, r="#1", w="AE%d" % k)
        ae, ao, AE = T.AE[:, 0:64], T.AE[:, 64:128], " AE0 AE1 AE2 AE3"
        mm(T.B7[:, 192:256], [(Id, ae), (n4I, ao)], "Id n4I" + AE, "#7")
        act(T.UU[:, 128:192], T.B7[:, 192:256], bias=3.5 + 47.5 / 64, r="#7", w="TI")
        xi, xj = T.B0[:, 0:64], T.B1[:, 128:192]
        mm1(xi, Id, ae, True, False, "Id" + AE, "#0")
        mm1(xi, qI, ao, False, False, "qI" + AE, "#0")
        mm1(xj, cI, T.ones[:, 0:64], True, False, "cI ones", "#1")
        mm1(xj, qI, ae, False, False, "qI" + AE, "#1")
        for p in range(16):
            act(T.V[:, p:1024:16], Bk[2 + p // 8][:, 64 * (p % 8):64 * (p % 8) + 64], bias=O(t, p, p + 1),
                r="#%d %s" % (2 + p // 8, ok), w="V")
        tt(T.dO[:], O(t), O(t, -1, 15), sub, ok + " Op", "dO")
        tt(XO, T.dO[:, 0:16].indirect(T.orr[:, 0:8]), BO, mul, "dO orr BO", "XO")
        w2, WS2 = T.WS[:, 15:512:16], span("WS", 0, 32, 2)
        offsets(PART2, MERGE[2])
        for j in range(2):
            act(T.T2[:, 2 + j:66:2], w2, AF.Sign, bias=256.0, r=WS2, w="T2%d" % j)
        mm(T.B5[:, 0:128], [(XO, Id)], "XO Id", "#5")
        act(dOT, T.B5[:, 0:128], scale=cNz, r="#5 cNz", w="dOT")
        act(dO0, T.B5[:, 0:128], scale=cIs0, r="#5 cIs0", w="dO0")
        mm(T.B7[:, 128:144], [(ShI, O(t))], "ShI " + ok, "#7")
        act(T.Dp[:], T.B7[:, 128:144], r="#7", w="Dp")

        def counts2(side, hi):
            if side == "i" and hi == 32:
                pairs(xi, 512, 32, False, span("Q", 512, 1024, 16), "#0")
                mm1(xi, nI8, T.T2[:, 2:66], False, True, "nI8 T20 T21", "#0")
                mm1(xj, nI8, T.T2[:, 0:64], False, False, "nI8 T20 T21 T2p", "#1")
            elif (side, hi) == TURN2[-1][::2]:
                pairs(xj, 1024, 32, True, "N1p" + span("Q", 1040, 1536, 16), "#1")

        duels(PART2, TURN2, PLAIN[2], MERGE[2], 512, TXw, xk, counts2)
        if t == 0:
            consts(2)
        if t == 1:
            consts(5)
        ts(T.UU[:, 0:64], xi, 47.5 / 64, lt, 0.5, add, r="#0", w="Ue")
        tt(T.UU[:, 64:128], xi, T.UU[:, 128:192], lt, "#0 TI", "Uo")
        mm1(T.B4[:, 256:512], dO0, T.ones[:], True, False, "dO0 ones", "#4")
        tt(T.W4[:, 0:128:2], xj, T.UU[:, 0:64], gt, "#1 Ue", "We")
        tt(T.W4[:, 1:128:2], xj, T.UU[:, 64:128], gt, "#1 Uo", "Wo")
        scan(T.cum[:, 1:129], T.W4[:], T.two[:], cT, add, add, "We Wo two cT", "cum")
        for j, x in enumerate("eo"):
            scan(T.DD[:, 64 * j:64 * j + 64], T.W4[:, j:128:2], T.dK[:, 64 * j:64 * j + 64], 0.0, mx, mul, "dK dKe dKo W" + x, "D" + x)
        base = T.B5[:, 128:129]
        mm(base, [(LTf, T.cum[:, 128:129])], "LTf cum", "#5")
        mm(T.B7[:, 128:129], [(L0f, T.cum[:, 128:129])], "L0f cum", "#7")
        for j, x in enumerate("eo"):
            tt(T.u0[:, 32 * j:32 * j + 32], T.cum[:, 4 * j:128 + j:4], T.DD[:, 64 * j + 1:64 * j + 64:2], add, "cum cump D" + x, "u" + x)
        for j, x in enumerate("eo"):
            ts(T.oR[:, j:64:2], T.u0[:, 32 * j:32 * j + 32], base, add, (cB0, cB1x)[j], add, r="#5 cB0 cB1x u" + x, w="R" + x)
        st, stp = T.step[:, 16:272], T.step[:, 15:271]
        ts(st, T.ix[:], cBs, add, T.B7[:, 128:129], ge, r="ix cBs #7", w="step")
        mm1(T.B4[:, 256:512], dOT, st, False, False, "dOT step", "#4")
        mm1(T.B4[:, 256:512], B256, st, False, True, "B256 step", "#4")
        k = 64 - SHARE
        act(T.CW[:, CW1:2 * CW1].indirect(T.oR[:, k:64]), T.V[:, 16 * k:1024], AF.Silu, bias=None, r="oR Re Ro V", w="CWb")
        ts(T.CW[:, 0:CW1].indirect(T.oR[:, 0:16]), T.V[:, 0:256], -1.0, mul, ROUND + 64, add, r="oR Re Ro V", w="CWa")
        cp(T.oPP[:], T.B4[:, 256:512], "#4", "oPP")
        ts(T.CW[:, 0:CW1].indirect(T.oR[:, 16:k]), T.V[:, 256:16 * k], -1.0, mul, ROUND + 64, add, r="oR Re Ro V", w="CWa")
        act(cE, T.cum[:, 128:129], AF.Relu, bias=cTe, scale=-256.0, r="cum cTe", w="cE")
        act(cE2, cE, bias=cB0, r="cE cB0", w="cE2")
        ts(T.oE[:, 0:1], base, cE2, add, 256.0, mn, r="cE2 #5", w="oE")

        def cuts(h):
            return zip((32 * h,), (32 * h + 32,)) if h else ((0, HEAD), (HEAD, 32))

        def items(h):
            for lo, hi in cuts(h):
                act(T.PG[:, 16 * lo:16 * hi], Pw.indirect(T.oPP[:, lo:hi]), r="P0 oPP", w=span("PG", 16 * lo, 16 * hi, 32))

        items(0)
        items(1)
        for lo, hi, x in ((0, FIRST, "G2"), (FIRST, 128, "G2a"), (128, 256, "G2b")):
            scan(T.G2[:, 8 + lo:8 + hi], T.CW[:, CW1 + lo:CW1 + hi], T.CW[:, lo:hi], 0.0, mx, sub, "CWa CWb", x)
            ts(T.oTT[:, lo:hi], T.G2[:, 8 + lo:8 + hi], ROUND, add, r=x, w=span("oTT", lo, hi, 32))
        for lo, x, r in ((0, "a", "G2 G2a"), (128, "b", "G2a G2b")):
            scan(T.dd[:, lo:lo + 128], T.G2[:, 8 + lo:136 + lo], T.G2[:, 7 + lo:135 + lo], 0.0, mn, sub, r, "dd" + x)
        for k, (l, y) in enumerate(((dO0, T.ones[:]), (dOT, st), (B8k, st), (nB8k, stp), (Id, T.dd[:]))):
            mm1(T.B0[:, 256:512], l, y, k == 0, k == 4, "dO0 ones dOT step stepp B8k nB8k Id" + " dda ddb" * (k == 4), "#0")
        items(2)
        items(3)

        def named(lo, hi, x):
            for bk, more in ((2, ()), (4, ((dO0, T.ones), (dOT, st)))):
                out, w = Bk[bk][:, lo:hi], "#%d" % bk
                for k, (l, y) in enumerate(more + ((Id, T.dd), (nI4k, T.sn))):
                    mm1(out, l, y[:, lo:hi], k == 0, False, "dO0 ones dOT step Id nI4k" + " dda ddb" * (l is Id) + " sn" * (l is nI4k), w)
            for bk, y in ((2, "t1"), (4, "t2")):
                out, w = Bk[bk][:, lo:hi], "#%d" % bk
                signs(out, A1, lo, hi, 0, False, "A1", w)
                signs(out, nB4k, lo, hi, 1, True, "nB4k", w)
                act(T[y][:, lo:hi], out, AF.Relu, bias=cB1, r=w + " cB1", w=y + x)

        def slots(lo, hi, x):
            mm1(T.B6[:, lo // 2:hi // 2], B256, T.step[:, 16 + lo:16 + hi:2], True, False, "step B256", "#6")
            for k in (lo, lo + 1):
                mm1(T.B6[:, lo // 2:hi // 2], BO, T.t1[:, k:hi:2], False, k > lo, "BO t1" + x, "#6")
            mm(T.B7[:, lo // 2:hi // 2], [(BO, T.t2[:, k:hi:2]) for k in (lo, lo + 1)], "BO t2" + x, "#7")

        for h in range(4):
            nk = "N%d N%d" % (2 * h, 2 * h + 1) + " N0x" * (h == 0)
            for j in (2 * h, 2 * h + 1):
                for lo, hi in cuts(j):
                    tt(T.NN[:, 16 * lo:16 * hi], TXw.indirect(T.oTT[:, lo:hi]), T.PG[:, 16 * lo:16 * hi], eq,
                       xk + span("oTT", lo, hi, 32) + span("PG", 16 * lo, 16 * hi, 32), "N%d" % j + "x" * (hi == HEAD))
            if h == 0:
                mm1(T.B3[:, 0:128], S0f, T.G2[:, 8:136], True, True, "G2 G2a S0f", "#3")
            if h == 1:
                mm1(T.B3[:, 128:256], S0f, T.G2[:, 136:264], True, True, "G2b S0f", "#3")
                held(t)
            bk = (6, 1, 7, 1)[h]
            if h < 3:
                count(Bk[bk][:, 0:64], T.NN, 1024 * h, 64, nk, "#%d" % bk)
                act(T.sg[:, 16 + 64 * h:80 + 64 * h], Bk[bk][:, 0:64], AF.Sign, bias=c75, scale=-1.0, r="#%d c75" % bk, w="sg%d" % h)
            else:
                for j in (6, 7):
                    mm(T.B1[:, 64 * j - 384:64 * j - 320], [(T.Z2[:, 7 - q:135 - q], T.NN[:, 512 * j + q:512 * j + 512:8]) for q in range(8)],
                       "Z2 N%d" % j, "#1")
                act(T.sg[:, 208:272], T.B1[:, 0:128:2], AF.Sign, bias=cH0b, scale=cH0, r="#1 cH0 cH0b", w="sg3")
                act(T.sg[:, 288:352], T.B1[:, 1:128:2], AF.Sign, bias=cH1b, scale=cH1, r="#1 cH1 cH1b", w="sg4")
            if h < 2:
                items(2 * h + 4)
                items(2 * h + 5)
            if h == 1:
                act(T.sn[:], T.B0[:, 256:512], AF.Sign, bias=cSn, r="#0 cSn", w="sn")
            if h == 2:
                named(0, NAMES, "a")
                accepted(0, FLIPS[1])
                flip_a(t, 0, FLIPS[1], "a")
        if t == 0:
            consts(3)
        slots(0, NAMES, "a")
        accepted(FLIPS[1], FLIPS[2])
        flip_a(t, FLIPS[1], FLIPS[2], "m")
        accepted(FLIPS[2], 256)
        named(NAMES, 256, "b")
        flip_a(t, FLIPS[2], 256, "b")
        equals(0, NAMES // 32, "a")
        name(0, NAMES // 32, "a")
        slots(NAMES, 256, "b")
        signs(T.B0[:, 0:256], L0, 0, 256, 0, True, "L0", "#0", True)
        act(T.G0[:], T.B0[:, 0:256], AF.Relu, bias=cG0, scale=-0.5, r="#0 cG0", w="G0")
        equals(NAMES // 32, 8, "b")
        name(NAMES // 32, 8, "b")
        if t == 0:
            consts(4)
        if t < 3:
            offsets1(t + 1)
            witnesses(PARTL, T.W0[:, 0:WW], T.oW1[:, s0 + 64:s0 + 128], "W0 W0p oW1%d" % (t + 1))
        places(t)
        for x in "amb":
            flip_b(t, x)
    dma("y", T.yt[:, 0:2048], T.X4[:, 0:2048], "X4", "yta", lat=4500.0)
    dma("a", T.yt[:, 2048:4096], T.X4[:, 2048:4096], "X4", "ytb", lat=4500.0)
    dma("y", T.yo[:], T.o32[:], "O4", "yo")
    cp(T.W0[:, 0:4096:256], T.z0[:], "z0 W0", "W0")
    dma("g", T.yw[:], T.W0[0:128:16, 0:4096], "W0", "yw")
    _emit(g, T, ops)
